import numpy as np
import ml_dtypes


def mxq(x, axis, fmt="e4m3"):
    dtype, down = {"e4m3": (ml_dtypes.float8_e4m3fn, 7), "e5m2": (ml_dtypes.float8_e5m2, 14)}[fmt]
    v = np.moveaxis(np.asarray(x, np.float32).astype(ml_dtypes.bfloat16).astype(np.float64), axis, -1)
    blocks = v.reshape(v.shape[:-1] + (-1, 32))
    amax = np.abs(blocks).max(-1, keepdims=True)
    byte = np.maximum(np.where(amax > 0, np.frexp(amax)[1] - 1 + 127, 0) - down, 1)
    scale = np.exp2(byte - 127.0)
    codes = (blocks / scale).astype(np.float32).astype(dtype).astype(np.float64)
    return np.moveaxis((codes * scale).reshape(v.shape), -1, axis)


WIDE = False


def mx_kscale(k):
    if not WIDE:
        return np.ones(k)
    levels = np.array([10, -10, 5, -5, 0])
    if k % 512:
        return np.exp2(np.random.permutation(np.resize(levels, k // 32))).repeat(32)
    a = np.empty((k // 512, 16))
    for p in range(k // 512):
        a[p, :8] = np.random.permutation(np.resize(levels, 8))
        for g in range(8):
            far = levels[np.abs(levels - a[p, g]) >= 10]
            a[p, g + 8] = far[np.random.randint(len(far))]
    return np.exp2(a.ravel()).repeat(32)


BF16 = ml_dtypes.bfloat16


def bf(x):
    return np.asarray(x, np.float32).astype(BF16)


def f64(x):
    return np.asarray(x).astype(np.float64)

def planes(Y):
    n, m = Y.shape
    b = f64(bf(Y)).reshape(n // 32, 32, m)
    amax = np.abs(b).max(1)
    byte = np.clip(np.where(amax > 0, np.frexp(amax)[1] - 1 + 127 - 7, 1), 1, 254)
    codes = (b * np.exp2(127.0 - byte)[:, None, :]).reshape(n, m).astype(np.float32).astype(ml_dtypes.float8_e4m3fn).view(np.uint8)
    words = codes.reshape(n // 512, 128, 4, m).transpose(0, 1, 3, 2)
    return np.ascontiguousarray(words), np.ascontiguousarray(byte.astype(np.uint8).reshape(n // 512, 16, m))


R, G, M = 1024, 512, 4


def setup_inputs():
    s, u = mx_kscale(G), mx_kscale(R)
    return {
        "flux": bf(np.random.standard_normal((R, G)) * s[None, :] / u[:, None]),
        "scat": bf(np.random.standard_normal((M, G, G)) / np.sqrt(G) / s[None, :, None]),
        "dens": bf(np.random.uniform(0.2, 0.8, (R, M))),
        "nusf": bf(np.random.uniform(0.5, 1.5, (M, G)) / np.sqrt(G) / s[None, :]),
        "chi": bf(np.random.uniform(0.5, 1.5, G)),
        "kern": bf(np.random.standard_normal((R, R)) / np.sqrt(R) * u[None, :]),
        "sigt": bf(np.random.uniform(0.5, 1.5, (M, G))),
    }


def scattering_source(flux, scat, dens):
    a = mxq(flux, 1, "e4m3") @ mxq(scat, 1, "e4m3")
    return np.sum(dens.T[:, :, None] * a, axis=0)


def fission_rate(flux, nusf, dens):
    per_material = np.sum(flux[:, None, :] * nusf[None, :, :], axis=-1)
    return np.sum(dens * per_material, axis=1)


def core(flux, scat, dens, nusf, chi, kern, sigt):
    flux, scat, dens, nusf = f64(flux), f64(scat), f64(dens), f64(nusf)
    s = scattering_source(flux, scat, dens)
    f = fission_rate(flux, nusf, dens)
    q = s + f[:, None] * f64(chi)[None, :]
    c = mxq(f64(kern), 1, "e4m3") @ mxq(q, 0, "e4m3")
    st = np.sum(dens[:, :, None] * f64(sigt)[None, :, :], axis=1)
    return c / st


def reference(flux, scat, dens, nusf, chi, kern, sigt):
    R_out = core(flux, scat, dens, nusf, chi, kern, sigt)
    words, scales = planes(R_out)
    return R_out, words, scales

@@ -1,0 +1,471 @@
+from contextlib import ExitStack
+
+import concourse.mybir as mybir
+from concourse.masks import make_identity
+
+F32 = mybir.dt.float32
+BF16 = mybir.dt.bfloat16
+U32 = mybir.dt.uint32
+I32 = mybir.dt.int32
+U8 = mybir.dt.uint8
+FP8X4 = mybir.dt.float8_e4m3fn_x4
+ALU = mybir.AluOpType
+ACT = mybir.ActivationFunctionType
+AX = mybir.AxisListType
+
+P = 128
+R, G, M = 1024, 512, 4
+NT = 8
+H = 256
+FLOPS = 2 * R * G * G * M + 2 * R * R * G
+
+
+def tile_multigroupintegraltransportsourceiterati_x1_kernel(tc, flux, scat, dens, nusf, chi, kern, sigt, out_0, out_1, out_2):
+    nc = tc.nc
+    V, S, T, GP = nc.vector, nc.scalar, nc.tensor, nc.gpsimd
+    with ExitStack() as ctx:
+        keep = ctx.enter_context(tc.tile_pool(name="keep", bufs=1))
+        psum = ctx.enter_context(tc.psum_pool(name="psum", bufs=1))
+        ctx.enter_context(tc.manual_schedule())
+
+        def tile(name, shape, dtype):
+            return keep.tile(shape, dtype, align_bytes=64, name=name)
+
+        sig4 = tile("sig4", [M, G], BF16)
+        pad = tile("pad", [P, G], BF16)
+        dens_pad = tile("dens_pad", [P, NT, P], BF16)
+        dens_sb = tile("dens_sb", [P, 2, 16], BF16)
+        nusf_t = tile("nusf_t", [P, M, 4], BF16)
+        flux_raw = tile("flux_raw", [P, 2, 4, G], BF16)
+        scat_raw = tile("scat_raw", [P, M, 4, G], BF16)
+        kern_raw = tile("kern_raw", [P, 2, 4, R], BF16)
+        id32 = tile("id32", [P, P], F32)
+        id16 = tile("id16", [P, P], BF16)
+        dens32 = tile("dens32", [P, NT, M], F32)
+        dens_t = tile("dens_t", [P, NT, P], BF16)
+        flux_grp = tile("flux_grp", [P, NT, P, 4], BF16)
+        flux_codes = tile("flux_codes", [P, NT, P], U32)
+        flux_sc = tile("flux_sc", [P, NT, P], U8)
+        chi_b = tile("chi_b", [P, G], BF16)
+        scat_grp = tile("scat_grp", [P, M, G, 4], BF16)
+        scat_codes = tile("scat_codes", [P, M, G], U32)
+        scat_sc = tile("scat_sc", [P, M, G], U8)
+        pd = tile("pd", [P, NT, M], F32)
+        f = tile("f", [P, NT], F32)
+        x = tile("x", [P, NT, G], F32)
+        fchi_t = tile("fchi_t", [P, NT, G], F32)
+        rs = tile("rs", [P, 3, G], F32)
+        sg = tile("sg", [P, 3, G], F32)
+        rst = tile("rst", [P, NT, G], F32)
+        kern_grp = tile("kern_grp", [P, 2, 2, 4, P, 4], BF16)
+        kern_codes = tile("kern_codes", [P, 2, 2, 4, P], U32)
+        kern_sc = tile("kern_sc", [P, 2, 2, 4, P], U8)
+        q_grp = tile("q_grp", [P, 2, G, 4], BF16)
+        q_codes = tile("q_codes", [P, 2, G], U32)
+        q_sc = tile("q_sc", [P, 2, G], U8)
+        res = tile("res", [P, 2, 4, G], F32)
+        r_grp = tile("r_grp", [P, 2, G, 4], BF16)
+        r_codes = tile("r_codes", [P, 2, G], U32)
+        r_sc = tile("r_sc", [P, 2, G], U8)
+
+        dens_v = dens_sb[:].rearrange("p g (t m) -> p (g t) m", m=M)
+        flux_v = flux.rearrange("(g p t) k -> g p t k", g=2, t=4)
+        kern_v = kern.rearrange("(g p t) k -> g p t k", g=2, t=4)
+        out0_v = out_0.rearrange("(g p t) n -> g p t n", g=2, t=4)
+        out1_v = out_1.rearrange("g p n t -> g p (n t)").bitcast(I32)
+        out2_v = out_2.bitcast(I32)
+
+        bank = {}
+
+        def mm_bank(shape):
+            return psum.tile(shape, F32, tag="mm", bufs=4, name="mm")
+
+        def tp_bank(shape, dtype=F32):
+            return psum.tile(shape, dtype, tag="tp", bufs=2, name="tp")
+
+        p_ps = psum.tile([P, NT, M], F32, tag="p", bufs=1, name="p_ps")
+
+        def move(eng, out, in_):
+            if eng == "S":
+                S.copy(out=out, in_=in_)
+            else:
+                V.tensor_copy(out=out, in_=in_)
+
+        def t_dens():
+            bank["dens"] = tp_bank([P, NT, P], BF16)
+            for i in range(NT):
+                T.transpose(bank["dens"][:, i], dens_pad[:, i], id16[:])
+
+        def t_flux(b):
+            bank["flux", b] = tp_bank([P, 2, 2, P])
+            for a in range(2):
+                words = flux_raw[:, b // 2, 2 * (b % 2) + a].bitcast(F32)
+                for u in range(2):
+                    T.transpose(bank["flux", b][:, a, u], words[:, u:256:2], id32[:])
+
+        def t_kern(i):
+            bank["kern", i] = tp_bank([P, 2, 2, P])
+            words = kern_raw[:, i // 4, i % 4].bitcast(F32)
+            for ks in range(2):
+                for u in range(2):
+                    T.transpose(bank["kern", i][:, ks, u], words[:, 256 * ks + u:256 * ks + 256:2], id32[:])
+
+        def st(i):
+            bank["st", i] = psum.tile([P, G], F32, tag="st", bufs=1, name="st")
+            T.matmul(bank["st", i][:], lhsT=dens_t[:, i], rhs=pad[:], start=True, stop=True)
+
+        def mx(i, m):
+            bank["a", i, m] = mm_bank([P, G])
+            T.matmul_mx(out=bank["a", i, m][:], lhsT=flux_codes[:, i].bitcast(FP8X4), lhsT_scale=flux_sc[:, i],
+                        rhs=scat_codes[:, m].bitcast(FP8X4), rhs_scale=scat_sc[:, m], start=True, stop=True)
+
+        def fis(i):
+            for j in range(4):
+                T.matmul(p_ps[:, i], lhsT=flux_grp[:, i, :, j], rhs=nusf_t[:, :, j], start=(j == 0), stop=(j == 3))
+
+        def tr(g, c0):
+            bank["c", g, c0] = mm_bank([P, 4, P])
+            for t in range(4):
+                for gs in range(2):
+                    T.matmul_mx(out=bank["c", g, c0][:, t], lhsT=kern_codes[:, g, gs, t].bitcast(FP8X4),
+                                lhsT_scale=kern_sc[:, g, gs, t], rhs=q_codes[:, gs, c0:c0 + P].bitcast(FP8X4),
+                                rhs_scale=q_sc[:, gs, c0:c0 + P], start=(gs == 0), stop=(gs == 1))
+
+        def c_dens():
+            S.copy(out=dens_t[:], in_=bank["dens"][:])
+
+        def c_pad():
+            S.copy(out=pad[0:M], in_=sig4[:])
+
+        def c_flux(b, eng):
+            dst = flux_grp[:, 2 * b:2 * b + 2].rearrange("p a r f -> p a (r f)").bitcast(F32).rearrange("p a (r u) -> p a r u", u=2)
+            move(eng, dst, bank["flux", b][:].rearrange("p a u r -> p a r u"))
+
+        def c_kern(i, eng):
+            dst = kern_grp[:, i // 4, :, i % 4].rearrange("p k r f -> p k (r f)").bitcast(F32).rearrange("p k (r u) -> p k r u", u=2)
+            move(eng, dst, bank["kern", i][:].rearrange("p k u r -> p k r u"))
+
+        def x0(i, eng):
+            if eng == "S":
+                S.activation(out=x[:, i], in_=bank["a", i, 0][:], func=ACT.Copy, scale=dens32[:, i, 0:1])
+            else:
+                V.tensor_scalar(out=x[:, i], in0=bank["a", i, 0][:], scalar1=dens32[:, i, 0:1], scalar2=None, op0=ALU.mult)
+
+        def ars(i):
+            S.activation(out=rs[:, i % 3], in_=bank["st", i][:], func=ACT.Abs_reciprocal_sqrt)
+
+        def sgn(i):
+            S.activation(out=sg[:, i % 3], in_=bank["st", i][:], func=ACT.Sign)
+
+        def sqr(i):
+            S.activation(out=rs[:, i % 3], in_=rs[:, i % 3], func=ACT.Square)
+
+        def fchi(i, eng):
+            if eng == "S":
+                S.activation(out=fchi_t[:, i], in_=chi_b[:], func=ACT.Copy, scale=f[:, i:i + 1])
+            else:
+                (V if eng == "V" else GP).tensor_scalar(out=fchi_t[:, i], in0=chi_b[:], scalar1=f[:, i:i + 1], scalar2=0.0, op0=ALU.mult, op1=ALU.add)
+
+        def inv(i):
+            ars(i)
+            sgn(i)
+            sqr(i)
+
+        def r_int(g, c0, w, eng):
+            move(eng, r_grp[:, g, c0:c0 + w].rearrange("p (c i) t -> p c t i", i=4),
+                 res[:, g, :, c0:c0 + w].rearrange("p t (c i) -> p c t i", i=4))
+
+        def s_piece(m, c0, eng):
+            if eng == "V":
+                V.tensor_copy(out=scat_grp[:, m, c0:c0 + H].rearrange("p (c i) t -> p c t i", i=4),
+                              in_=scat_raw[:, m, :, c0:c0 + H].rearrange("p t (c i) -> p c t i", i=4))
+            elif eng == "S":
+                S.copy(out=scat_grp[:, m, c0:c0 + H].rearrange("p (c i) t -> p c t i", i=4),
+                       in_=scat_raw[:, m, :, c0:c0 + H].rearrange("p t (c i) -> p c t i", i=4))
+            else:
+                for b0 in (c0, c0 + P):
+                    GP.tensor_scalar(out=scat_grp[:, m, b0:b0 + P], in0=scat_raw[:, m, :, b0:b0 + P].rearrange("p t n -> p n t"),
+                                     scalar1=1.0, scalar2=0.0, op0=ALU.mult, op1=ALU.add)
+
+        def rmul(i, eng):
+            if eng == "V":
+                V.tensor_tensor(out=rst[:, i], in0=rs[:, i % 3], in1=sg[:, i % 3], op=ALU.mult)
+            else:
+                for c0 in (0, H):
+                    GP.tensor_tensor(out=rst[:, i, c0:c0 + H], in0=rs[:, i % 3, c0:c0 + H], in1=sg[:, i % 3, c0:c0 + H], op=ALU.mult)
+
+        def s_int(m):
+            V.tensor_copy(out=scat_grp[:, m].rearrange("p (c i) t -> p c t i", i=4),
+                          in_=scat_raw[:, m].rearrange("p t (c i) -> p c t i", i=4))
+
+        def q_scat(m):
+            V.quantize_mx(out=scat_codes[:, m].bitcast(FP8X4), scales=scat_sc[:, m], in_=scat_grp[:, m].rearrange("p n j -> p (n j)"))
+
+        def q_flux(b):
+            V.quantize_mx(out=flux_codes[:, 2 * b:2 * b + 2].rearrange("p a r -> p (a r)").bitcast(FP8X4),
+                          scales=flux_sc[:, 2 * b:2 * b + 2].rearrange("p a r -> p (a r)"),
+                          in_=flux_grp[:, 2 * b:2 * b + 2].rearrange("p a r f -> p (a r f)"))
+
+        def q_kern(g, ks):
+            V.quantize_mx(out=kern_codes[:, g, ks].rearrange("p t r -> p (t r)").bitcast(FP8X4),
+                          scales=kern_sc[:, g, ks].rearrange("p t r -> p (t r)"), in_=kern_grp[:, g, ks].rearrange("p t r f -> p (t r f)"))
+
+        def stt(i, m):
+            V.scalar_tensor_tensor(out=x[:, i], in0=bank["a", i, m][:], scalar=dens32[:, i, m:m + 1], in1=x[:, i], op0=ALU.mult, op1=ALU.add)
+
+        def f_mul(g):
+            V.tensor_tensor(out=pd[:, 4 * g:4 * g + 4], in0=p_ps[:, 4 * g:4 * g + 4], in1=dens32[:, 4 * g:4 * g + 4], op=ALU.mult)
+
+        def f_sum(g):
+            V.tensor_reduce(out=f[:, 4 * g:4 * g + 4], in_=pd[:, 4 * g:4 * g + 4], axis=AX.X, op=ALU.add)
+
+        def q_int(g, c0, w):
+            t4 = slice(4 * g, 4 * g + 4)
+            V.tensor_tensor(out=q_grp[:, g, c0:c0 + w].rearrange("p (c i) t -> p c t i", i=4),
+                            in0=x[:, t4, c0:c0 + w].rearrange("p t (c i) -> p c t i", i=4),
+                            in1=fchi_t[:, t4, c0:c0 + w].rearrange("p t (c i) -> p c t i", i=4), op=ALU.add)
+
+        def q_q(g, c0, w):
+            V.quantize_mx(out=q_codes[:, g, c0:c0 + w].bitcast(FP8X4), scales=q_sc[:, g, c0:c0 + w],
+                          in_=q_grp[:, g, c0:c0 + w].rearrange("p n t -> p (n t)"))
+
+        def out(g, c0):
+            V.tensor_tensor(out=res[:, g, :, c0:c0 + P], in0=bank["c", g, c0][:], in1=rst[:, 4 * g:4 * g + 4, c0:c0 + P], op=ALU.mult)
+
+        def q_r(g, c0, w):
+            V.quantize_mx(out=r_codes[:, g, c0:c0 + w].bitcast(FP8X4), scales=r_sc[:, g, c0:c0 + w],
+                          in_=r_grp[:, g, c0:c0 + w].rearrange("p n t -> p (n t)"))
+
+        def v_pad():
+            V.memset(pad[:], 0.0)
+
+        def v_id():
+            V.tensor_copy(out=id16[:], in_=id32[:])
+
+        def v_dens():
+            V.tensor_copy(out=dens_pad[:, :, 0:M], in_=dens_v)
+
+        def v_dens32():
+            V.tensor_copy(out=dens32[:], in_=dens_v)
+
+        warm = tile("warm", [P, 2], F32)
+
+        def v_warm():
+            V.memset(warm[:], 1.0)
+
+        def s_warm():
+            S.activation(out=warm[:, 1:2], in_=warm[:, 0:1], func=ACT.Abs_reciprocal_sqrt)
+
+        def store(g, c0, w):
+            nc.sync.dma_start(out=out0_v[g, :, :, c0:c0 + w], in_=res[:, g, :, c0:c0 + w])
+
+        def store_w(g, c0, w):
+            nc.sync.dma_start(out=out1_v[g, :, c0:c0 + w], in_=r_codes[:, g, c0:c0 + w].bitcast(I32))
+
+        def store_s(g, k, eng):
+            (nc.scalar if eng == "S" else nc.sync).dma_start(out=out2_v[g, 4 * k:4 * k + 4, :], in_=r_sc[32 * k:32 * k + 4, g, :].bitcast(I32))
+
+        def load_scat(m):
+            nc.sync.dma_start(out=scat_raw[:, m], in_=scat[m].rearrange("(p j) n -> p j n", j=4))
+
+        def load_flux(g):
+            nc.sync.dma_start(out=flux_raw[:, g], in_=flux_v[g])
+
+        def load_kern(g):
+            nc.sync.dma_start(out=kern_raw[:, g], in_=kern_v[g])
+
+        def load_small():
+            nc.scalar.dma_start(out=dens_sb[:], in_=dens.rearrange("(g p t) m -> p g (t m)", g=2, t=4))
+            nc.scalar.dma_start(out=sig4[:], in_=sigt)
+            with nc.allow_non_contiguous_dma("512 short runs of nusf"):
+                nc.scalar.dma_start(out=nusf_t[:], in_=nusf.rearrange("m (p j) -> p m j", j=4))
+
+        def load_chi():
+            nc.sync.dma_start(out=chi_b[:], in_=chi.partition_broadcast(P))
+
+        def g_start():
+            GP.memset(dens_pad[:], 0.0)
+            make_identity(nc, id32[:])
+
+        load_small()
+        load_flux(0)
+        load_scat(0)
+        load_flux(1)
+        load_scat(1)
+        load_scat(2)
+        load_scat(3)
+        load_chi()
+        load_kern(0)
+        load_kern(1)
+        g_start()
+        v_warm()
+        s_warm()
+        v_pad()
+        v_id()
+        v_dens()
+        v_dens32()
+        t_dens()
+        c_dens()
+        c_pad()
+        s_int(0)
+        for b in range(2):
+            t_flux(b)
+            c_flux(b, "S")
+        st(0)
+        inv(0)
+        q_flux(0)
+        q_scat(0)
+        for b in range(2, 4):
+            t_flux(b)
+            c_flux(b, "S")
+        s_int(1)
+        q_flux(1)
+        q_scat(1)
+        s_piece(2, 0, "G")
+        s_piece(2, H, "V")
+        s_piece(3, H, "G")
+        q_flux(2)
+        q_flux(3)
+        s_piece(3, 0, "V")
+        rmul(0, "G")
+        mx(0, 0)
+        x0(0, "S")
+        st(1)
+        ars(1)
+        sgn(1)
+        fis(0)
+        mx(1, 0)
+        x0(1, "S")
+        mx(2, 0)
+        x0(2, "S")
+        for k in range(5):
+            mx(k, 1)
+            stt(k, 1)
+            if k == 1:
+                st(2)
+            mx(k + 3, 0)
+            x0(k + 3, "S")
+            if k == 0:
+                fis(1)
+        sqr(1)
+        rmul(1, "G")
+        inv(2)
+        rmul(2, "G")
+        mx(5, 1)
+        stt(5, 1)
+        t_kern(0)
+        q_scat(2)
+        q_scat(3)
+        for k in (6, 7):
+            mx(k, 1)
+            stt(k, 1)
+        fis(2)
+        fis(3)
+        mx(0, 2)
+        stt(0, 2)
+        f_mul(0)
+        st(3)
+        ars(3)
+        sgn(3)
+        c_kern(0, "S")
+        sqr(3)
+        rmul(3, "G")
+        mx(1, 2)
+        stt(1, 2)
+        f_sum(0)
+        for k in (2, 3):
+            mx(k, 2)
+            stt(k, 2)
+        fchi(0, "G")
+        fchi(1, "G")
+        mx(0, 3)
+        stt(0, 3)
+        fis(4)
+        st(4)
+        inv(4)
+        rmul(4, "G")
+        for k in (1, 2):
+            mx(k, 3)
+            stt(k, 3)
+        t_kern(1)
+        c_kern(1, "S")
+        mx(3, 3)
+        stt(3, 3)
+        for k in range(4, 8):
+            mx(k, 2)
+            stt(k, 2)
+            if k == 5:
+                st(5)
+                ars(5)
+                fis(5)
+        fchi(2, "S")
+        fchi(3, "S")
+        sgn(5)
+        sqr(5)
+        rmul(5, "G")
+        fis(6)
+        fis(7)
+        f_mul(1)
+        mx(4, 3)
+        stt(4, 3)
+        f_sum(1)
+        q_int(0, 0, H)
+        q_int(0, H, H)
+        for k in range(5, 8):
+            mx(k, 3)
+            stt(k, 3)
+        fchi(4, "S")
+        st(6)
+        for i in range(2, 6):
+            t_kern(i)
+            c_kern(i, "S")
+            if i == 2:
+                fchi(5, "S")
+                fchi(6, "S")
+            if i == 4:
+                fchi(7, "S")
+        inv(6)
+        for i in range(6, 8):
+            t_kern(i)
+            c_kern(i, "S")
+        st(7)
+        inv(7)
+        rmul(7, "G")
+        q_kern(0, 0)
+        q_kern(0, 1)
+        q_int(1, 0, H)
+        q_q(0, 0, G)
+        q_q(1, 0, H)
+        q_int(1, H, H)
+        rmul(6, "V")
+        q_q(1, H, H)
+        q_kern(1, 0)
+        q_kern(1, 1)
+        for g, c0 in ((0, 0), (1, 0), (0, H)):
+            for b0 in (c0, c0 + P):
+                tr(g, b0)
+                out(g, b0)
+            store(g, c0, H)
+            r_int(g, c0, H, "S")
+        tr(1, H)
+        out(1, H)
+        store(1, H, P)
+        q_r(0, 0, H)
+        store_w(0, 0, H)
+        tr(1, H + P)
+        out(1, H + P)
+        store(1, H + P, P)
+        r_int(1, H, P, "S")
+        q_r(1, 0, H)
+        store_w(1, 0, H)
+        r_int(1, H + P, P, "V")
+        q_r(0, H, H)
+        store_w(0, H, H)
+        q_r(1, H, P)
+        q_r(1, H + P, P)
+        for k in range(4):
+            store_s(0, k, "S")
+        store_w(1, H, P)
+        store_w(1, H + P, P)
+        for k in range(4):
+            store_s(1, k, "S" if k % 2 else "Y")

@@ -31,42 +31,45 @@ def tile_multigroupintegraltransportsourceiterati_x1_kernel(tc, flux, scat, dens
         def tile(name, shape, dtype):
             return keep.tile(shape, dtype, align_bytes=64, name=name)
 
+        def tiles(name, n, shape, dtype):
+            return [tile("%s%d" % (name, k), shape, dtype) for k in range(n)]
+
         sig4 = tile("sig4", [M, G], BF16)
         pad = tile("pad", [P, G], BF16)
         dens_pad = tile("dens_pad", [P, NT, P], BF16)
         dens_sb = tile("dens_sb", [P, 2, 16], BF16)
         nusf_t = tile("nusf_t", [P, M, 4], BF16)
-        flux_raw = tile("flux_raw", [P, 2, 4, G], BF16)
-        scat_raw = tile("scat_raw", [P, M, 4, G], BF16)
-        kern_raw = tile("kern_raw", [P, 2, 4, R], BF16)
+        flux_raw = tiles("flux_raw", 4, [P, 2, G], BF16)
+        scat_raw = tiles("scat_raw", M, [P, 4, G], BF16)
+        kern_raw = tiles("kern_raw", 2, [P, 4, R], BF16)
         id32 = tile("id32", [P, P], F32)
         id16 = tile("id16", [P, P], BF16)
         dens32 = tile("dens32", [P, NT, M], F32)
         dens_t = tile("dens_t", [P, NT, P], BF16)
-        flux_grp = tile("flux_grp", [P, NT, P, 4], BF16)
+        flux_grp = tiles("flux_grp", 2, [P, 4, P, 4], BF16)
         flux_codes = tile("flux_codes", [P, NT, P], U32)
         flux_sc = tile("flux_sc", [P, NT, P], U8)
         chi_b = tile("chi_b", [P, G], BF16)
-        scat_grp = tile("scat_grp", [P, M, G, 4], BF16)
+        scat_grp = tiles("scat_grp", M, [P, G, 4], BF16)
         scat_codes = tile("scat_codes", [P, M, G], U32)
         scat_sc = tile("scat_sc", [P, M, G], U8)
         pd = tile("pd", [P, NT, M], F32)
         f = tile("f", [P, NT], F32)
-        x = tile("x", [P, NT, G], F32)
-        fchi_t = tile("fchi_t", [P, NT, G], F32)
-        rs = tile("rs", [P, 3, G], F32)
-        sg = tile("sg", [P, 3, G], F32)
-        rst = tile("rst", [P, NT, G], F32)
-        kern_grp = tile("kern_grp", [P, 2, 2, 4, P, 4], BF16)
+        x = tiles("x", 2, [P, 4, G], F32)
+        fx = tiles("fx", 2, [P, 4, G], F32)
+        sg = tiles("sg", NT, [P, G], BF16)
+        rst = tiles("rst", 2, [P, 4, G], F32)
+        kern_grp = tiles("kern_grp", 2, [P, 2, 4, P, 4], BF16)
         kern_codes = tile("kern_codes", [P, 2, 2, 4, P], U32)
         kern_sc = tile("kern_sc", [P, 2, 2, 4, P], U8)
         q_grp = tile("q_grp", [P, 2, G, 4], BF16)
         q_codes = tile("q_codes", [P, 2, G], U32)
         q_sc = tile("q_sc", [P, 2, G], U8)
-        res = tile("res", [P, 2, 4, G], F32)
+        res = tiles("res", 2, [P, 4, G], F32)
         r_grp = tile("r_grp", [P, 2, G, 4], BF16)
         r_codes = tile("r_codes", [P, 2, G], U32)
-        r_sc = tile("r_sc", [P, 2, G], U8)
+        r_sc = tile("r_sc", [P, G], U8)
+        warm = tile("warm", [P, 2], F32)
 
         dens_v = dens_sb[:].rearrange("p g (t m) -> p (g t) m", m=M)
         flux_v = flux.rearrange("(g p t) k -> g p t k", g=2, t=4)
@@ -76,396 +79,326 @@ def tile_multigroupintegraltransportsourceiterati_x1_kernel(tc, flux, scat, dens
         out2_v = out_2.bitcast(I32)
 
         bank = {}
+        rings = {"mm": 4, "tp": 2, "st": 2}
+        turn = {"mm": [], "tp": [], "st": []}
 
-        def mm_bank(shape):
-            return psum.tile(shape, F32, tag="mm", bufs=4, name="mm")
+        def step(run, needs, gives):
+            return (run, list(needs), list(gives))
 
-        def tp_bank(shape, dtype=F32):
-            return psum.tile(shape, dtype, tag="tp", bufs=2, name="tp")
+        def take(ring, key, shape, dtype=F32):
+            turn[ring].append(key)
+            before = turn[ring][-1 - rings[ring]:-rings[ring]]
 
-        p_ps = psum.tile([P, NT, M], F32, tag="p", bufs=1, name="p_ps")
+            def alloc():
+                bank[key] = psum.tile(shape, dtype, tag=ring, bufs=rings[ring], name=ring)
+                return bank[key]
+
+            return alloc, [("read", k) for k in before]
 
         def move(eng, out, in_):
-            if eng == "S":
+            if eng is S:
                 S.copy(out=out, in_=in_)
-            else:
+            elif eng is V:
                 V.tensor_copy(out=out, in_=in_)
+            else:
+                GP.tensor_scalar(out=out, in0=in_, scalar1=1.0, scalar2=0.0, op0=ALU.mult, op1=ALU.add)
+
+        def blocks(dst, src):
+            return dst.rearrange("p (c i) t -> p c t i", i=4), src.rearrange("p t (c i) -> p c t i", i=4)
+
+        def weave(eng, dst, src):
+            if eng is GP:
+                move(eng, dst, src.rearrange("p t n -> p n t"))
+            else:
+                move(eng, *blocks(dst, src))
+
+        def cols(name, g, c0, w):
+            return [(name, g, c) for c in range(c0, c0 + w, P)]
 
         def t_dens():
-            bank["dens"] = tp_bank([P, NT, P], BF16)
-            for i in range(NT):
-                T.transpose(bank["dens"][:, i], dens_pad[:, i], id16[:])
+            alloc, free = take("tp", "dens", [P, NT, P], BF16)
+
+            def run():
+                b = alloc()
+                for i in range(NT):
+                    T.transpose(b[:, i], dens_pad[:, i], id16[:])
+            return step(run, free + ["dens_pad", "id16"], ["dens"])
 
         def t_flux(b):
-            bank["flux", b] = tp_bank([P, 2, 2, P])
-            for a in range(2):
-                words = flux_raw[:, b // 2, 2 * (b % 2) + a].bitcast(F32)
-                for u in range(2):
-                    T.transpose(bank["flux", b][:, a, u], words[:, u:256:2], id32[:])
+            alloc, free = take("tp", ("flux", b), [P, 2, 2, P])
+
+            def run():
+                ps = alloc()
+                for a in range(2):
+                    words = flux_raw[b][:, a].bitcast(F32)
+                    for u in range(2):
+                        T.transpose(ps[:, a, u], words[:, u:256:2], id32[:])
+            return step(run, free + ["id32"], [("flux", b)])
 
         def t_kern(i):
-            bank["kern", i] = tp_bank([P, 2, 2, P])
-            words = kern_raw[:, i // 4, i % 4].bitcast(F32)
-            for ks in range(2):
-                for u in range(2):
-                    T.transpose(bank["kern", i][:, ks, u], words[:, 256 * ks + u:256 * ks + 256:2], id32[:])
+            alloc, free = take("tp", ("kern", i), [P, 2, 2, P])
+
+            def run():
+                ps = alloc()
+                words = kern_raw[i // 4][:, i % 4].bitcast(F32)
+                for ks in range(2):
+                    for u in range(2):
+                        T.transpose(ps[:, ks, u], words[:, 256 * ks + u:256 * ks + 256:2], id32[:])
+            return step(run, free, [("kern", i)])
 
         def st(i):
-            bank["st", i] = psum.tile([P, G], F32, tag="st", bufs=1, name="st")
-            T.matmul(bank["st", i][:], lhsT=dens_t[:, i], rhs=pad[:], start=True, stop=True)
+            alloc, free = take("st", ("st", i), [P, G])
+            return step(lambda: T.matmul(alloc()[:], lhsT=dens_t[:, i], rhs=pad[:], start=True, stop=True), free + ["dens_t", "pad"], [("st", i)])
 
-        def mx(i, m):
-            bank["a", i, m] = mm_bank([P, G])
-            T.matmul_mx(out=bank["a", i, m][:], lhsT=flux_codes[:, i].bitcast(FP8X4), lhsT_scale=flux_sc[:, i],
-                        rhs=scat_codes[:, m].bitcast(FP8X4), rhs_scale=scat_sc[:, m], start=True, stop=True)
+        def mx(i, m, c0=0, w=G):
+            alloc, free = take("mm", ("a", i, m, c0), [P, w])
+            return step(lambda: T.matmul_mx(out=alloc()[:], lhsT=flux_codes[:, i].bitcast(FP8X4), lhsT_scale=flux_sc[:, i],
+                                            rhs=scat_codes[:, m, c0:c0 + w].bitcast(FP8X4), rhs_scale=scat_sc[:, m, c0:c0 + w], start=True, stop=True),
+                        free + [("fq", i), ("sq", m)], [("a", i, m, c0)])
 
-        def fis(i):
-            for j in range(4):
-                T.matmul(p_ps[:, i], lhsT=flux_grp[:, i, :, j], rhs=nusf_t[:, :, j], start=(j == 0), stop=(j == 3))
+        def fis(i0, n, ring="mm"):
+            alloc, free = take(ring, ("p", i0), [P, n, M])
 
-        def tr(g, c0):
-            bank["c", g, c0] = mm_bank([P, 4, P])
+            def run():
+                ps = alloc()
+                for a in range(n):
+                    i = i0 + a
+                    for j in range(4):
+                        T.matmul(ps[:, a], lhsT=flux_grp[i // 4][:, i % 4, :, j], rhs=nusf_t[:, :, j], start=(j == 0), stop=(j == 3))
+            return step(run, free + [("fg", i // 2) for i in range(i0, i0 + n)], [("p", i0)])
+
+        def tr_pass(ps, g, c0, gs):
             for t in range(4):
-                for gs in range(2):
-                    T.matmul_mx(out=bank["c", g, c0][:, t], lhsT=kern_codes[:, g, gs, t].bitcast(FP8X4),
-                                lhsT_scale=kern_sc[:, g, gs, t], rhs=q_codes[:, gs, c0:c0 + P].bitcast(FP8X4),
-                                rhs_scale=q_sc[:, gs, c0:c0 + P], start=(gs == 0), stop=(gs == 1))
+                T.matmul_mx(out=ps[:, t], lhsT=kern_codes[:, g, gs, t].bitcast(FP8X4), lhsT_scale=kern_sc[:, g, gs, t],
+                            rhs=q_codes[:, gs, c0:c0 + P].bitcast(FP8X4), rhs_scale=q_sc[:, gs, c0:c0 + P],
+                            start=(gs == 0 and t == 0), stop=(gs == 1 and t == 3))
 
-        def c_dens():
-            S.copy(out=dens_t[:], in_=bank["dens"][:])
+        def tr0(g, c0, ring):
+            alloc, free = take(ring, ("c", g, c0), [P, 4, P])
+            return step(lambda: tr_pass(alloc(), g, c0, 0), free + [("kq", g), ("qq", 0, c0)], [("c0", g, c0)])
 
-        def c_pad():
-            S.copy(out=pad[0:M], in_=sig4[:])
+        def tr1(g, c0):
+            return step(lambda: tr_pass(bank["c", g, c0], g, c0, 1), [("c0", g, c0), ("qq", 1, c0)], [("c", g, c0)])
+
+        def c_dens(eng):
+            return step(lambda: move(eng, dens_t[:], bank["dens"][:]), ["dens"], ["dens_t", ("read", "dens")])
 
         def c_flux(b, eng):
-            dst = flux_grp[:, 2 * b:2 * b + 2].rearrange("p a r f -> p a (r f)").bitcast(F32).rearrange("p a (r u) -> p a r u", u=2)
-            move(eng, dst, bank["flux", b][:].rearrange("p a u r -> p a r u"))
+            a0 = 2 * (b % 2)
+            dst = flux_grp[b // 2][:, a0:a0 + 2].rearrange("p a r f -> p a (r f)").bitcast(F32).rearrange("p a (r u) -> p a r u", u=2)
+            return step(lambda: move(eng, dst, bank["flux", b][:].rearrange("p a u r -> p a r u")), [("flux", b)], [("fg", b), ("read", ("flux", b))])
 
         def c_kern(i, eng):
-            dst = kern_grp[:, i // 4, :, i % 4].rearrange("p k r f -> p k (r f)").bitcast(F32).rearrange("p k (r u) -> p k r u", u=2)
-            move(eng, dst, bank["kern", i][:].rearrange("p k u r -> p k r u"))
-
-        def x0(i, eng):
-            if eng == "S":
-                S.activation(out=x[:, i], in_=bank["a", i, 0][:], func=ACT.Copy, scale=dens32[:, i, 0:1])
-            else:
-                V.tensor_scalar(out=x[:, i], in0=bank["a", i, 0][:], scalar1=dens32[:, i, 0:1], scalar2=None, op0=ALU.mult)
+            dst = kern_grp[i // 4][:, :, i % 4].rearrange("p k r f -> p k (r f)").bitcast(F32).rearrange("p k (r u) -> p k r u", u=2)
+            return step(lambda: move(eng, dst, bank["kern", i][:].rearrange("p k u r -> p k r u")), [("kern", i)], [("kg", i), ("read", ("kern", i))])
 
         def ars(i):
-            S.activation(out=rs[:, i % 3], in_=bank["st", i][:], func=ACT.Abs_reciprocal_sqrt)
+            return step(lambda: S.activation(out=rst[i // 4][:, i % 4], in_=bank["st", i][:], func=ACT.Abs_reciprocal_sqrt), [("st", i)], [("w", i)])
 
         def sgn(i):
-            S.activation(out=sg[:, i % 3], in_=bank["st", i][:], func=ACT.Sign)
+            return step(lambda: S.activation(out=sg[i][:], in_=bank["st", i][:], func=ACT.Sign), [("w", i)], [("sg", i), ("read", ("st", i))])
 
         def sqr(i):
-            S.activation(out=rs[:, i % 3], in_=rs[:, i % 3], func=ACT.Square)
-
-        def fchi(i, eng):
-            if eng == "S":
-                S.activation(out=fchi_t[:, i], in_=chi_b[:], func=ACT.Copy, scale=f[:, i:i + 1])
-            else:
-                (V if eng == "V" else GP).tensor_scalar(out=fchi_t[:, i], in0=chi_b[:], scalar1=f[:, i:i + 1], scalar2=0.0, op0=ALU.mult, op1=ALU.add)
+            r = rst[i // 4][:, i % 4]
+            return step(lambda: S.activation(out=r, in_=r, func=ACT.Square), [("w", i)], [("r", i)])
 
         def inv(i):
-            ars(i)
-            sgn(i)
-            sqr(i)
+            return [ars(i), sgn(i), sqr(i)]
+
+        def rmul(i, eng, c0=0, w=G):
+            r = rst[i // 4][:, i % 4, c0:c0 + w]
+            return step(lambda: eng.tensor_tensor(out=r, in0=r, in1=sg[i][:, c0:c0 + w], op=ALU.mult), [("r", i), ("sg", i)], cols("rst", i, c0, w))
+
+        def fchi(i, eng, dst):
+            def run():
+                if eng is S:
+                    S.activation(out=dst[i // 4][:, i % 4], in_=chi_b[:], func=ACT.Copy, scale=f[:, i:i + 1])
+                else:
+                    eng.tensor_scalar(out=dst[i // 4][:, i % 4], in0=chi_b[:], scalar1=f[:, i:i + 1], scalar2=0.0, op0=ALU.mult, op1=ALU.add)
+            return step(run, [("f", i)], [("fx", i)] if dst is fx else cols(("x", -1), i, 0, G))
+
+        def x0(i, eng):
+            def run():
+                if eng is S:
+                    S.activation(out=x[i // 4][:, i % 4], in_=bank["a", i, 0, 0][:], func=ACT.Copy, scale=dens32[:, i, 0:1])
+                else:
+                    V.tensor_scalar(out=x[i // 4][:, i % 4], in0=bank["a", i, 0, 0][:], scalar1=dens32[:, i, 0:1], scalar2=None, op0=ALU.mult)
+            return step(run, [("a", i, 0, 0), "dens32"], cols(("x", 0), i, 0, G) + [("read", ("a", i, 0, 0))])
+
+        def s_int(m, c0, w, eng):
+            return step(lambda: weave(eng, scat_grp[m][:, c0:c0 + w], scat_raw[m][:, :, c0:c0 + w]), [], cols("sg", ("s", m), c0, w))
+
+        def q_int(g, c0, w, eng):
+            needs = [k for i in range(4 * g, 4 * g + 4) for k in cols(("x", 3), i, c0, w)]
+            return step(lambda: weave(eng, q_grp[:, g, c0:c0 + w], x[g][:, :, c0:c0 + w]), needs, cols("qg", g, c0, w))
+
+        def q_add(g, c0, w, eng):
+            needs = [k for i in range(4 * g, 4 * g + 4) for k in cols(("x", 3), i, c0, w) + [("fx", i)]]
+
+            def run():
+                if eng is V:
+                    dst, a = blocks(q_grp[:, g, c0:c0 + w], x[g][:, :, c0:c0 + w])
+                    b = fx[g][:, :, c0:c0 + w].rearrange("p t (c i) -> p c t i", i=4)
+                else:
+                    dst = q_grp[:, g, c0:c0 + w]
+                    a = x[g][:, :, c0:c0 + w].rearrange("p t n -> p n t")
+                    b = fx[g][:, :, c0:c0 + w].rearrange("p t n -> p n t")
+                eng.tensor_tensor(out=dst, in0=a, in1=b, op=ALU.add)
+            return step(run, needs, cols("qg", g, c0, w))
 
         def r_int(g, c0, w, eng):
-            move(eng, r_grp[:, g, c0:c0 + w].rearrange("p (c i) t -> p c t i", i=4),
-                 res[:, g, :, c0:c0 + w].rearrange("p t (c i) -> p c t i", i=4))
-
-        def s_piece(m, c0, eng):
-            if eng == "V":
-                V.tensor_copy(out=scat_grp[:, m, c0:c0 + H].rearrange("p (c i) t -> p c t i", i=4),
-                              in_=scat_raw[:, m, :, c0:c0 + H].rearrange("p t (c i) -> p c t i", i=4))
-            elif eng == "S":
-                S.copy(out=scat_grp[:, m, c0:c0 + H].rearrange("p (c i) t -> p c t i", i=4),
-                       in_=scat_raw[:, m, :, c0:c0 + H].rearrange("p t (c i) -> p c t i", i=4))
-            else:
-                for b0 in (c0, c0 + P):
-                    GP.tensor_scalar(out=scat_grp[:, m, b0:b0 + P], in0=scat_raw[:, m, :, b0:b0 + P].rearrange("p t n -> p n t"),
-                                     scalar1=1.0, scalar2=0.0, op0=ALU.mult, op1=ALU.add)
-
-        def rmul(i, eng):
-            if eng == "V":
-                V.tensor_tensor(out=rst[:, i], in0=rs[:, i % 3], in1=sg[:, i % 3], op=ALU.mult)
-            else:
-                for c0 in (0, H):
-                    GP.tensor_tensor(out=rst[:, i, c0:c0 + H], in0=rs[:, i % 3, c0:c0 + H], in1=sg[:, i % 3, c0:c0 + H], op=ALU.mult)
-
-        def s_int(m):
-            V.tensor_copy(out=scat_grp[:, m].rearrange("p (c i) t -> p c t i", i=4),
-                          in_=scat_raw[:, m].rearrange("p t (c i) -> p c t i", i=4))
+            return step(lambda: weave(eng, r_grp[:, g, c0:c0 + w], res[g][:, :, c0:c0 + w]), cols("res", g, c0, w), cols("rg", g, c0, w))
 
         def q_scat(m):
-            V.quantize_mx(out=scat_codes[:, m].bitcast(FP8X4), scales=scat_sc[:, m], in_=scat_grp[:, m].rearrange("p n j -> p (n j)"))
+            return step(lambda: V.quantize_mx(out=scat_codes[:, m].bitcast(FP8X4), scales=scat_sc[:, m], in_=scat_grp[m][:].rearrange("p n j -> p (n j)")),
+                        cols("sg", ("s", m), 0, G), [("sq", m)])
 
-        def q_flux(b):
-            V.quantize_mx(out=flux_codes[:, 2 * b:2 * b + 2].rearrange("p a r -> p (a r)").bitcast(FP8X4),
-                          scales=flux_sc[:, 2 * b:2 * b + 2].rearrange("p a r -> p (a r)"),
-                          in_=flux_grp[:, 2 * b:2 * b + 2].rearrange("p a r f -> p (a r f)"))
+        def q_flux(i0, n):
+            return step(lambda: V.quantize_mx(out=flux_codes[:, i0:i0 + n].rearrange("p a r -> p (a r)").bitcast(FP8X4),
+                                              scales=flux_sc[:, i0:i0 + n].rearrange("p a r -> p (a r)"),
+                                              in_=flux_grp[i0 // 4][:, i0 % 4:i0 % 4 + n].rearrange("p a r f -> p (a r f)")),
+                        [("fg", i // 2) for i in range(i0, i0 + n)], [("fq", i) for i in range(i0, i0 + n)])
 
-        def q_kern(g, ks):
-            V.quantize_mx(out=kern_codes[:, g, ks].rearrange("p t r -> p (t r)").bitcast(FP8X4),
-                          scales=kern_sc[:, g, ks].rearrange("p t r -> p (t r)"), in_=kern_grp[:, g, ks].rearrange("p t r f -> p (t r f)"))
+        def q_kern(g):
+            return step(lambda: V.quantize_mx(out=kern_codes[:, g].rearrange("p k t r -> p (k t r)").bitcast(FP8X4),
+                                              scales=kern_sc[:, g].rearrange("p k t r -> p (k t r)"),
+                                              in_=kern_grp[g][:].rearrange("p k t r f -> p (k t r f)")),
+                        [("kg", i) for i in range(4 * g, 4 * g + 4)], [("kq", g)])
 
-        def stt(i, m):
-            V.scalar_tensor_tensor(out=x[:, i], in0=bank["a", i, m][:], scalar=dens32[:, i, m:m + 1], in1=x[:, i], op0=ALU.mult, op1=ALU.add)
+        def stt(i, m, c0=0, w=G):
+            xi = x[i // 4][:, i % 4, c0:c0 + w]
+            return step(lambda: V.scalar_tensor_tensor(out=xi, in0=bank["a", i, m, c0][:], scalar=dens32[:, i, m:m + 1], in1=xi, op0=ALU.mult, op1=ALU.add),
+                        [("a", i, m, c0)] + cols(("x", m - 1), i, c0, w), cols(("x", m), i, c0, w) + [("read", ("a", i, m, c0))])
 
-        def f_mul(g):
-            V.tensor_tensor(out=pd[:, 4 * g:4 * g + 4], in0=p_ps[:, 4 * g:4 * g + 4], in1=dens32[:, 4 * g:4 * g + 4], op=ALU.mult)
+        def f_mul(i0, n):
+            return step(lambda: V.tensor_tensor(out=pd[:, i0:i0 + n], in0=bank["p", i0][:], in1=dens32[:, i0:i0 + n], op=ALU.mult),
+                        [("p", i0), "dens32"], [("pd", i0), ("read", ("p", i0))])
 
-        def f_sum(g):
-            V.tensor_reduce(out=f[:, 4 * g:4 * g + 4], in_=pd[:, 4 * g:4 * g + 4], axis=AX.X, op=ALU.add)
-
-        def q_int(g, c0, w):
-            t4 = slice(4 * g, 4 * g + 4)
-            V.tensor_tensor(out=q_grp[:, g, c0:c0 + w].rearrange("p (c i) t -> p c t i", i=4),
-                            in0=x[:, t4, c0:c0 + w].rearrange("p t (c i) -> p c t i", i=4),
-                            in1=fchi_t[:, t4, c0:c0 + w].rearrange("p t (c i) -> p c t i", i=4), op=ALU.add)
+        def f_sum(i0, n):
+            return step(lambda: V.tensor_reduce(out=f[:, i0:i0 + n], in_=pd[:, i0:i0 + n], axis=AX.X, op=ALU.add), [("pd", i0)], [("f", i) for i in range(i0, i0 + n)])
 
         def q_q(g, c0, w):
-            V.quantize_mx(out=q_codes[:, g, c0:c0 + w].bitcast(FP8X4), scales=q_sc[:, g, c0:c0 + w],
-                          in_=q_grp[:, g, c0:c0 + w].rearrange("p n t -> p (n t)"))
+            return step(lambda: V.quantize_mx(out=q_codes[:, g, c0:c0 + w].bitcast(FP8X4), scales=q_sc[:, g, c0:c0 + w],
+                                              in_=q_grp[:, g, c0:c0 + w].rearrange("p n t -> p (n t)")), cols("qg", g, c0, w), cols("qq", g, c0, w))
 
         def out(g, c0):
-            V.tensor_tensor(out=res[:, g, :, c0:c0 + P], in0=bank["c", g, c0][:], in1=rst[:, 4 * g:4 * g + 4, c0:c0 + P], op=ALU.mult)
+            return step(lambda: V.tensor_tensor(out=res[g][:, :, c0:c0 + P], in0=bank["c", g, c0][:], in1=rst[g][:, :, c0:c0 + P], op=ALU.mult),
+                        [("c", g, c0)] + [("rst", i, c0) for i in range(4 * g, 4 * g + 4)], [("res", g, c0), ("read", ("c", g, c0))])
 
         def q_r(g, c0, w):
-            V.quantize_mx(out=r_codes[:, g, c0:c0 + w].bitcast(FP8X4), scales=r_sc[:, g, c0:c0 + w],
-                          in_=r_grp[:, g, c0:c0 + w].rearrange("p n t -> p (n t)"))
-
-        def v_pad():
-            V.memset(pad[:], 0.0)
-
-        def v_id():
-            V.tensor_copy(out=id16[:], in_=id32[:])
-
-        def v_dens():
-            V.tensor_copy(out=dens_pad[:, :, 0:M], in_=dens_v)
-
-        def v_dens32():
-            V.tensor_copy(out=dens32[:], in_=dens_v)
-
-        warm = tile("warm", [P, 2], F32)
-
-        def v_warm():
-            V.memset(warm[:], 1.0)
-
-        def s_warm():
-            S.activation(out=warm[:, 1:2], in_=warm[:, 0:1], func=ACT.Abs_reciprocal_sqrt)
+            return step(lambda: V.quantize_mx(out=r_codes[:, g, c0:c0 + w].bitcast(FP8X4), scales=r_sc[4 * g:P, c0:c0 + w],
+                                              in_=r_grp[:, g, c0:c0 + w].rearrange("p n t -> p (n t)")), cols("rg", g, c0, w), cols("rq", g, c0, w))
 
         def store(g, c0, w):
-            nc.sync.dma_start(out=out0_v[g, :, :, c0:c0 + w], in_=res[:, g, :, c0:c0 + w])
+            return step(lambda: nc.sync.dma_start(out=out0_v[g, :, :, c0:c0 + w], in_=res[g][:, :, c0:c0 + w]), cols("res", g, c0, w), [])
 
         def store_w(g, c0, w):
-            nc.sync.dma_start(out=out1_v[g, :, c0:c0 + w], in_=r_codes[:, g, c0:c0 + w].bitcast(I32))
+            return step(lambda: nc.sync.dma_start(out=out1_v[g, :, c0:c0 + w], in_=r_codes[:, g, c0:c0 + w].bitcast(I32)), cols("rq", g, c0, w), [])
 
-        def store_s(g, k, eng):
-            (nc.scalar if eng == "S" else nc.sync).dma_start(out=out2_v[g, 4 * k:4 * k + 4, :], in_=r_sc[32 * k:32 * k + 4, g, :].bitcast(I32))
+        def store_s(k, eng):
+            return step(lambda: eng.dma_start(out=out2_v[:, 4 * k:4 * k + 4, :], in_=r_sc[32 * k:32 * k + 8, :].bitcast(I32)), cols("rq", 0, 0, G) + cols("rq", 1, 0, G), [])
 
         def load_scat(m):
-            nc.sync.dma_start(out=scat_raw[:, m], in_=scat[m].rearrange("(p j) n -> p j n", j=4))
+            nc.sync.dma_start(out=scat_raw[m][:], in_=scat[m].rearrange("(p j) n -> p j n", j=4))
 
-        def load_flux(g):
-            nc.sync.dma_start(out=flux_raw[:, g], in_=flux_v[g])
+        def load_flux(b):
+            nc.sync.dma_start(out=flux_raw[b][:], in_=flux_v[b // 2, :, 2 * (b % 2):2 * (b % 2) + 2])
 
         def load_kern(g):
-            nc.sync.dma_start(out=kern_raw[:, g], in_=kern_v[g])
+            nc.sync.dma_start(out=kern_raw[g][:], in_=kern_v[g])
 
         def load_small():
             nc.scalar.dma_start(out=dens_sb[:], in_=dens.rearrange("(g p t) m -> p g (t m)", g=2, t=4))
             nc.scalar.dma_start(out=sig4[:], in_=sigt)
             with nc.allow_non_contiguous_dma("512 short runs of nusf"):
                 nc.scalar.dma_start(out=nusf_t[:], in_=nusf.rearrange("m (p j) -> p m j", j=4))
+            nc.scalar.dma_start(out=chi_b[:], in_=chi.partition_broadcast(P))
 
-        def load_chi():
-            nc.sync.dma_start(out=chi_b[:], in_=chi.partition_broadcast(P))
-
-        def g_start():
-            GP.memset(dens_pad[:], 0.0)
+        def setup():
+            V.memset(warm[:], 1.0)
+            S.activation(out=warm[:, 1:2], in_=warm[:, 0:1], func=ACT.Abs_reciprocal_sqrt)
             make_identity(nc, id32[:])
+            V.memset(pad[:], 0.0)
+            V.memset(dens_pad[:], 0.0)
+            V.tensor_copy(out=id16[:], in_=id32[:])
+            V.tensor_copy(out=dens_pad[:, :, 0:M], in_=dens_v)
+            V.tensor_copy(out=pad[0:M], in_=sig4[:])
+            V.tensor_copy(out=dens32[:], in_=dens_v)
+
+        def emit(queues):
+            have = {"id32", "id16", "dens_pad", "pad", "dens32"}
+            at = [0] * len(queues)
+            while any(at[e] < len(qu) for e, qu in enumerate(queues)):
+                moved = False
+                for e, qu in enumerate(queues):
+                    while at[e] < len(qu) and all(k in have for k in qu[at[e]][1]):
+                        qu[at[e]][0]()
+                        for k in qu[at[e]][2]:
+                            have.add(k)
+                        at[e] = at[e] + 1
+                        moved = True
+                assert moved, [[k for k in qu[at[e]][1] if k not in have] for e, qu in enumerate(queues) if at[e] < len(qu)]
 
         load_small()
         load_flux(0)
         load_scat(0)
         load_flux(1)
         load_scat(1)
+        load_flux(2)
+        load_flux(3)
         load_scat(2)
         load_scat(3)
-        load_chi()
         load_kern(0)
         load_kern(1)
-        g_start()
-        v_warm()
-        s_warm()
-        v_pad()
-        v_id()
-        v_dens()
-        v_dens32()
-        t_dens()
-        c_dens()
-        c_pad()
-        s_int(0)
-        for b in range(2):
-            t_flux(b)
-            c_flux(b, "S")
-        st(0)
-        inv(0)
-        q_flux(0)
-        q_scat(0)
-        for b in range(2, 4):
-            t_flux(b)
-            c_flux(b, "S")
-        s_int(1)
-        q_flux(1)
-        q_scat(1)
-        s_piece(2, 0, "G")
-        s_piece(2, H, "V")
-        s_piece(3, H, "G")
-        q_flux(2)
-        q_flux(3)
-        s_piece(3, 0, "V")
-        rmul(0, "G")
-        mx(0, 0)
-        x0(0, "S")
-        st(1)
-        ars(1)
-        sgn(1)
-        fis(0)
-        mx(1, 0)
-        x0(1, "S")
-        mx(2, 0)
-        x0(2, "S")
-        for k in range(5):
-            mx(k, 1)
-            stt(k, 1)
-            if k == 1:
-                st(2)
-            mx(k + 3, 0)
-            x0(k + 3, "S")
-            if k == 0:
-                fis(1)
-        sqr(1)
-        rmul(1, "G")
-        inv(2)
-        rmul(2, "G")
-        mx(5, 1)
-        stt(5, 1)
-        t_kern(0)
-        q_scat(2)
-        q_scat(3)
-        for k in (6, 7):
-            mx(k, 1)
-            stt(k, 1)
-        fis(2)
-        fis(3)
-        mx(0, 2)
-        stt(0, 2)
-        f_mul(0)
-        st(3)
-        ars(3)
-        sgn(3)
-        c_kern(0, "S")
-        sqr(3)
-        rmul(3, "G")
-        mx(1, 2)
-        stt(1, 2)
-        f_sum(0)
-        for k in (2, 3):
-            mx(k, 2)
-            stt(k, 2)
-        fchi(0, "G")
-        fchi(1, "G")
-        mx(0, 3)
-        stt(0, 3)
-        fis(4)
-        st(4)
-        inv(4)
-        rmul(4, "G")
-        for k in (1, 2):
-            mx(k, 3)
-            stt(k, 3)
-        t_kern(1)
-        c_kern(1, "S")
-        mx(3, 3)
-        stt(3, 3)
-        for k in range(4, 8):
-            mx(k, 2)
-            stt(k, 2)
-            if k == 5:
-                st(5)
-                ars(5)
-                fis(5)
-        fchi(2, "S")
-        fchi(3, "S")
-        sgn(5)
-        sqr(5)
-        rmul(5, "G")
-        fis(6)
-        fis(7)
-        f_mul(1)
-        mx(4, 3)
-        stt(4, 3)
-        f_sum(1)
-        q_int(0, 0, H)
-        q_int(0, H, H)
-        for k in range(5, 8):
-            mx(k, 3)
-            stt(k, 3)
-        fchi(4, "S")
-        st(6)
-        for i in range(2, 6):
-            t_kern(i)
-            c_kern(i, "S")
-            if i == 2:
-                fchi(5, "S")
-                fchi(6, "S")
-            if i == 4:
-                fchi(7, "S")
-        inv(6)
-        for i in range(6, 8):
-            t_kern(i)
-            c_kern(i, "S")
-        st(7)
-        inv(7)
-        rmul(7, "G")
-        q_kern(0, 0)
-        q_kern(0, 1)
-        q_int(1, 0, H)
-        q_q(0, 0, G)
-        q_q(1, 0, H)
-        q_int(1, H, H)
-        rmul(6, "V")
-        q_q(1, H, H)
-        q_kern(1, 0)
-        q_kern(1, 1)
-        for g, c0 in ((0, 0), (1, 0), (0, H)):
-            for b0 in (c0, c0 + P):
-                tr(g, b0)
-                out(g, b0)
-            store(g, c0, H)
-            r_int(g, c0, H, "S")
-        tr(1, H)
-        out(1, H)
-        store(1, H, P)
-        q_r(0, 0, H)
-        store_w(0, 0, H)
-        tr(1, H + P)
-        out(1, H + P)
-        store(1, H + P, P)
-        r_int(1, H, P, "S")
-        q_r(1, 0, H)
-        store_w(1, 0, H)
-        r_int(1, H + P, P, "V")
-        q_r(0, H, H)
-        store_w(0, H, H)
-        q_r(1, H, P)
-        q_r(1, H + P, P)
+        setup()
+        Y = nc.sync
+        lo, hi = range(4), range(4, 8)
+        pair = [[(2 * b, 0), (2 * b + 1, 0), (2 * b, 1), (2 * b + 1, 1)] for b in range(4)]
+        qt = [t_flux(0), t_dens(), fis(0, 2), t_flux(1), st(0), st(1), fis(2, 2)]
+        for b in range(4):
+            a = [mx(i, m) for i, m in pair[b][:2]]
+            if b < 2:
+                a.append(t_flux(b + 2))
+            a += [mx(i, m) for i, m in pair[b][2:]]
+            if b < 2:
+                a.append(fis(2 * b + 4, 2))
+            else:
+                a.append(st(b))
+            qt += a
+        rest = [(i, m) for m in (2, 3) for i in lo] + [(i, 2) for i in hi]
+        side = [[t_kern(0), t_kern(1)], [], [st(4)], [t_kern(2), t_kern(3)], [], [st(5)], [t_kern(4), t_kern(5)], [], [st(6)], [t_kern(6), t_kern(7)], [], [st(7)]]
+        for k, (i, m) in enumerate(rest):
+            qt += [mx(i, m)] + side[k]
+        qt += [mx(i, 3, 0, H) for i in hi] + [tr0(0, 0, "tp"), tr0(0, P, "tp")] + [mx(i, 3, H, H) for i in hi]
+        qt += [tr0(0, H, "mm"), tr0(0, H + P, "mm"), tr1(0, 0), tr1(0, P), tr0(1, 0, "mm"), tr0(1, P, "mm"), tr1(0, H), tr1(0, H + P), tr1(1, 0), tr1(1, P)]
+        qt += [tr0(1, H, "st"), tr1(1, H), tr0(1, H + P, "st"), tr1(1, H + P)]
+
+        qv = [s_int(0, 0, G, V), q_flux(0, 2), q_scat(0), f_mul(0, 2), s_int(1, 0, H, V), f_sum(0, 2), s_int(1, H, H, V), q_flux(2, 2), q_scat(1)]
+        for b in range(4):
+            a = [stt(i, m) for i, m in pair[b]]
+            if b < 3:
+                a = a[:1] + [f_mul(2 * b + 2, 2)] + a[1:2] + [f_sum(2 * b + 2, 2)] + a[2:]
+            if b < 2:
+                a.append(q_flux(2 * b + 4, 2))
+            if b == 3:
+                a = a[:1] + [q_scat(2)] + a[1:]
+            qv += a
+        qv += [stt(0, 2), q_scat(3), stt(1, 2), stt(2, 2), stt(3, 2)] + [stt(i, 3) for i in lo]
+        qv += [stt(4, 2), stt(5, 2), q_kern(0), stt(6, 2), stt(7, 2), q_q(0, 0, G)]
+        qv += [stt(i, 3, 0, H) for i in hi] + [stt(i, 3, H, H) for i in hi]
+        qv += [q_q(1, 0, H), q_kern(1), out(0, 0), q_q(1, H, H), out(0, P), out(0, H), out(0, H + P), out(1, 0), q_r(0, 0, H), out(1, P), out(1, H), q_r(0, H, H)]
+        qv += [out(1, H + P), q_r(1, 0, H), r_int(1, H + P, P, V), q_r(1, H, P), q_r(1, H + P, P)]
+
+        qs = [c_flux(0, S), c_dens(S), c_flux(1, S), fchi(0, S, x), fchi(1, S, x), ars(0), sgn(0), c_flux(2, S), ars(1), sgn(1), c_flux(3, S), s_int(2, 0, G, S), sqr(0), sqr(1)]
+        qs += inv(2) + inv(3)
         for k in range(4):
-            store_s(0, k, "S")
-        store_w(1, H, P)
-        store_w(1, H + P, P)
-        for k in range(4):
-            store_s(1, k, "S" if k % 2 else "Y")
+            if k == 3:
+                qs.append(q_int(0, 0, G, S))
+            qs += [c_kern(2 * k, S), c_kern(2 * k + 1, S)] + (inv(4 + k) if k < 3 else [])
+        qs += [q_int(1, 0, H, S), q_int(1, H, H, S)] + inv(7) + [r_int(g, c, P, S) for g in range(2) for c in range(0, G, P)][:7]
+        qs += [store_s(1, S), store_s(3, S)]
+
+        qg = [fchi(i, GP, x) for i in range(2, 8)] + [s_int(3, c, P, GP) for c in range(0, G, P)] + [rmul(i, GP) for i in range(8)]
+
+        qy = [store(0, 0, H), store(0, H, H), store(1, 0, H), store(1, H, P), store_w(0, 0, G), store(1, H + P, P), store_w(1, 0, H), store_w(1, H, H), store_s(0, Y), store_s(2, Y)]
+        emit([qt, qv, qs, qg, qy])

@@ -50,7 +50,8 @@ def tile_multigroupintegraltransportsourceiterati_x1_kernel(tc, flux, scat, dens
         flux_codes = tile("flux_codes", [P, NT, P], U32)
         flux_sc = tile("flux_sc", [P, NT, P], U8)
         chi_b = tile("chi_b", [P, G], BF16)
-        scat_grp = tiles("scat_grp", M, [P, G, 4], BF16)
+        scat_grp = tiles("scat_grp", M - 1, [P, G, 4], BF16)
+        scat_grp.append(scat_grp[2])
         scat_codes = tile("scat_codes", [P, M, G], U32)
         scat_sc = tile("scat_sc", [P, M, G], U8)
         pd = tile("pd", [P, NT, M], F32)
@@ -86,14 +87,11 @@ def tile_multigroupintegraltransportsourceiterati_x1_kernel(tc, flux, scat, dens
             return (run, list(needs), list(gives))
 
         def take(ring, key, shape, dtype=F32):
-            turn[ring].append(key)
-            before = turn[ring][-1 - rings[ring]:-rings[ring]]
-
             def alloc():
                 bank[key] = psum.tile(shape, dtype, tag=ring, bufs=rings[ring], name=ring)
                 return bank[key]
 
-            return alloc, [("read", k) for k in before]
+            return alloc, [("bank", ring, key)]
 
         def move(eng, out, in_):
             if eng is S:
@@ -116,7 +114,7 @@ def tile_multigroupintegraltransportsourceiterati_x1_kernel(tc, flux, scat, dens
             return [(name, g, c) for c in range(c0, c0 + w, P)]
 
         def t_dens():
-            alloc, free = take("tp", "dens", [P, NT, P], BF16)
+            alloc, free = take("st", "dens", [P, NT, P], BF16)
 
             def run():
                 b = alloc()
@@ -124,8 +122,8 @@ def tile_multigroupintegraltransportsourceiterati_x1_kernel(tc, flux, scat, dens
                     T.transpose(b[:, i], dens_pad[:, i], id16[:])
             return step(run, free + ["dens_pad", "id16"], ["dens"])
 
-        def t_flux(b):
-            alloc, free = take("tp", ("flux", b), [P, 2, 2, P])
+        def t_flux(b, ring):
+            alloc, free = take(ring, ("flux", b), [P, 2, 2, P])
 
             def run():
                 ps = alloc()
@@ -156,16 +154,15 @@ def tile_multigroupintegraltransportsourceiterati_x1_kernel(tc, flux, scat, dens
                                             rhs=scat_codes[:, m, c0:c0 + w].bitcast(FP8X4), rhs_scale=scat_sc[:, m, c0:c0 + w], start=True, stop=True),
                         free + [("fq", i), ("sq", m)], [("a", i, m, c0)])
 
-        def fis(i0, n, ring="mm"):
-            alloc, free = take(ring, ("p", i0), [P, n, M])
+        def fis(i, ring="tp"):
+            i0 = 4 * (i // 4)
+            alloc, free = take(ring, ("p", i0), [P, 4, M])
 
             def run():
-                ps = alloc()
-                for a in range(n):
-                    i = i0 + a
-                    for j in range(4):
-                        T.matmul(ps[:, a], lhsT=flux_grp[i // 4][:, i % 4, :, j], rhs=nusf_t[:, :, j], start=(j == 0), stop=(j == 3))
-            return step(run, free + [("fg", i // 2) for i in range(i0, i0 + n)], [("p", i0)])
+                ps = alloc() if i == i0 else bank["p", i0]
+                for j in range(4):
+                    T.matmul(ps[:, i - i0], lhsT=flux_grp[i // 4][:, i % 4, :, j], rhs=nusf_t[:, :, j], start=(j == 0), stop=(j == 3))
+            return step(run, (free if i == i0 else []) + [("fg", i // 2)], [("p", i0)] if i == i0 + 3 else [])
 
         def tr_pass(ps, g, c0, gs):
             for t in range(4):
@@ -175,10 +172,22 @@ def tile_multigroupintegraltransportsourceiterati_x1_kernel(tc, flux, scat, dens
 
         def tr0(g, c0, ring):
             alloc, free = take(ring, ("c", g, c0), [P, 4, P])
-            return step(lambda: tr_pass(alloc(), g, c0, 0), free + [("kq", g), ("qq", 0, c0)], [("c0", g, c0)])
+            return step(lambda: tr_pass(alloc(), g, c0, 0), free + [("kq", g, 0), ("qq", 0, c0)], [("c0", g, c0)])
 
         def tr1(g, c0):
-            return step(lambda: tr_pass(bank["c", g, c0], g, c0, 1), [("c0", g, c0), ("qq", 1, c0)], [("c", g, c0)])
+            return step(lambda: tr_pass(bank["c", g, c0], g, c0, 1), [("c0", g, c0), ("kq", g, 1), ("qq", 1, c0)], [("c", g, c0)])
+
+        def t_scat(m, c0, ring):
+            alloc, free = take(ring, ("scat", m, c0), [P, H, 4], BF16)
+
+            def run():
+                ps = alloc()
+                for b0 in (0, P):
+                    T.matmul(ps[:, b0:b0 + P], lhsT=id16[:], rhs=scat_raw[m][:, :, c0 + b0:c0 + b0 + P].rearrange("p t n -> p n t"), start=True, stop=True)
+            return step(run, free + ["id16"], [("scat", m, c0)])
+
+        def c_scat(m, c0, eng):
+            return step(lambda: move(eng, scat_grp[m][:, c0:c0 + H], bank["scat", m, c0][:]), [("scat", m, c0)], cols("sg", ("s", m), c0, H) + [("read", ("scat", m, c0))])
 
         def c_dens(eng):
             return step(lambda: move(eng, dens_t[:], bank["dens"][:]), ["dens"], ["dens_t", ("read", "dens")])
@@ -226,7 +235,7 @@ def tile_multigroupintegraltransportsourceiterati_x1_kernel(tc, flux, scat, dens
             return step(run, [("a", i, 0, 0), "dens32"], cols(("x", 0), i, 0, G) + [("read", ("a", i, 0, 0))])
 
         def s_int(m, c0, w, eng):
-            return step(lambda: weave(eng, scat_grp[m][:, c0:c0 + w], scat_raw[m][:, :, c0:c0 + w]), [], cols("sg", ("s", m), c0, w))
+            return step(lambda: weave(eng, scat_grp[m][:, c0:c0 + w], scat_raw[m][:, :, c0:c0 + w]), [("sq", 2)] if m == 3 else [], cols("sg", ("s", m), c0, w))
 
         def q_int(g, c0, w, eng):
             needs = [k for i in range(4 * g, 4 * g + 4) for k in cols(("x", 3), i, c0, w)]
@@ -259,23 +268,23 @@ def tile_multigroupintegraltransportsourceiterati_x1_kernel(tc, flux, scat, dens
                                               in_=flux_grp[i0 // 4][:, i0 % 4:i0 % 4 + n].rearrange("p a r f -> p (a r f)")),
                         [("fg", i // 2) for i in range(i0, i0 + n)], [("fq", i) for i in range(i0, i0 + n)])
 
-        def q_kern(g):
-            return step(lambda: V.quantize_mx(out=kern_codes[:, g].rearrange("p k t r -> p (k t r)").bitcast(FP8X4),
-                                              scales=kern_sc[:, g].rearrange("p k t r -> p (k t r)"),
-                                              in_=kern_grp[g][:].rearrange("p k t r f -> p (k t r f)")),
-                        [("kg", i) for i in range(4 * g, 4 * g + 4)], [("kq", g)])
+        def q_kern(g, k0, n):
+            return step(lambda: V.quantize_mx(out=kern_codes[:, g, k0:k0 + n].rearrange("p k t r -> p (k t r)").bitcast(FP8X4),
+                                              scales=kern_sc[:, g, k0:k0 + n].rearrange("p k t r -> p (k t r)"),
+                                              in_=kern_grp[g][:, k0:k0 + n].rearrange("p k t r f -> p (k t r f)")),
+                        [("kg", i) for i in range(4 * g, 4 * g + 4)], [("kq", g, k) for k in range(k0, k0 + n)])
 
         def stt(i, m, c0=0, w=G):
             xi = x[i // 4][:, i % 4, c0:c0 + w]
-            return step(lambda: V.scalar_tensor_tensor(out=xi, in0=bank["a", i, m, c0][:], scalar=dens32[:, i, m:m + 1], in1=xi, op0=ALU.mult, op1=ALU.add),
-                        [("a", i, m, c0)] + cols(("x", m - 1), i, c0, w), cols(("x", m), i, c0, w) + [("read", ("a", i, m, c0))])
+            return step(lambda: V.scalar_tensor_tensor(out=xi, in0=bank["a", i, m, 0][:, c0:c0 + w], scalar=dens32[:, i, m:m + 1], in1=xi, op0=ALU.mult, op1=ALU.add),
+                        [("a", i, m, 0)] + cols(("x", m - 1), i, c0, w), cols(("x", m), i, c0, w) + ([("read", ("a", i, m, 0))] if c0 + w == G else []))
 
         def f_mul(i0, n):
             return step(lambda: V.tensor_tensor(out=pd[:, i0:i0 + n], in0=bank["p", i0][:], in1=dens32[:, i0:i0 + n], op=ALU.mult),
-                        [("p", i0), "dens32"], [("pd", i0), ("read", ("p", i0))])
+                        [("p", i0), "dens32"], [("pd", i) for i in range(i0, i0 + n)] + [("read", ("p", i0))])
 
         def f_sum(i0, n):
-            return step(lambda: V.tensor_reduce(out=f[:, i0:i0 + n], in_=pd[:, i0:i0 + n], axis=AX.X, op=ALU.add), [("pd", i0)], [("f", i) for i in range(i0, i0 + n)])
+            return step(lambda: V.tensor_reduce(out=f[:, i0:i0 + n], in_=pd[:, i0:i0 + n], axis=AX.X, op=ALU.add), [("pd", i) for i in range(i0, i0 + n)], [("f", i) for i in range(i0, i0 + n)])
 
         def q_q(g, c0, w):
             return step(lambda: V.quantize_mx(out=q_codes[:, g, c0:c0 + w].bitcast(FP8X4), scales=q_sc[:, g, c0:c0 + w],
@@ -327,6 +336,11 @@ def tile_multigroupintegraltransportsourceiterati_x1_kernel(tc, flux, scat, dens
 
         def emit(queues):
             have = {"id32", "id16", "dens_pad", "pad", "dens32"}
+            for run, needs, gives in queues[0]:
+                for k in [k for k in needs if k[0] == "bank"]:
+                    needs.remove(k)
+                    turn[k[1]].append(k[2])
+                    needs.extend(("read", b) for b in turn[k[1]][-1 - rings[k[1]]:-rings[k[1]]])
             at = [0] * len(queues)
             while any(at[e] < len(qu) for e, qu in enumerate(queues)):
                 moved = False
@@ -340,12 +354,11 @@ def tile_multigroupintegraltransportsourceiterati_x1_kernel(tc, flux, scat, dens
                 assert moved, [[k for k in qu[at[e]][1] if k not in have] for e, qu in enumerate(queues) if at[e] < len(qu)]
 
         load_small()
-        load_flux(0)
         load_scat(0)
-        load_flux(1)
+        load_flux(0)
         load_scat(1)
-        load_flux(2)
-        load_flux(3)
+        for b in range(1, 4):
+            load_flux(b)
         load_scat(2)
         load_scat(3)
         load_kern(0)
@@ -353,52 +366,29 @@ def tile_multigroupintegraltransportsourceiterati_x1_kernel(tc, flux, scat, dens
         setup()
         Y = nc.sync
         lo, hi = range(4), range(4, 8)
-        pair = [[(2 * b, 0), (2 * b + 1, 0), (2 * b, 1), (2 * b + 1, 1)] for b in range(4)]
-        qt = [t_flux(0), t_dens(), fis(0, 2), t_flux(1), st(0), st(1), fis(2, 2)]
-        for b in range(4):
-            a = [mx(i, m) for i, m in pair[b][:2]]
-            if b < 2:
-                a.append(t_flux(b + 2))
-            a += [mx(i, m) for i, m in pair[b][2:]]
-            if b < 2:
-                a.append(fis(2 * b + 4, 2))
-            else:
-                a.append(st(b))
-            qt += a
-        rest = [(i, m) for m in (2, 3) for i in lo] + [(i, 2) for i in hi]
-        side = [[t_kern(0), t_kern(1)], [], [st(4)], [t_kern(2), t_kern(3)], [], [st(5)], [t_kern(4), t_kern(5)], [], [st(6)], [t_kern(6), t_kern(7)], [], [st(7)]]
-        for k, (i, m) in enumerate(rest):
-            qt += [mx(i, m)] + side[k]
-        qt += [mx(i, 3, 0, H) for i in hi] + [tr0(0, 0, "tp"), tr0(0, P, "tp")] + [mx(i, 3, H, H) for i in hi]
-        qt += [tr0(0, H, "mm"), tr0(0, H + P, "mm"), tr1(0, 0), tr1(0, P), tr0(1, 0, "mm"), tr0(1, P, "mm"), tr1(0, H), tr1(0, H + P), tr1(1, 0), tr1(1, P)]
-        qt += [tr0(1, H, "st"), tr1(1, H), tr0(1, H + P, "st"), tr1(1, H + P)]
+        qt = [t_dens(), t_flux(0, "tp"), st(0), t_flux(1, "tp"), mx(0, 0), mx(1, 0), t_flux(2, "tp"), t_flux(3, "tp"), mx(0, 1), mx(2, 0), mx(3, 0), st(1)]
+        qt += [mx(1, 1), mx(4, 0), fis(0), mx(2, 1), mx(5, 0), fis(1), mx(3, 1), mx(6, 0), fis(2), mx(0, 2), mx(7, 0), fis(3)]
+        slots = [(i, 2) for i in (1, 2, 3)] + [(i, 1) for i in hi] + [(i, 3) for i in lo] + [(i, 2) for i in hi]
+        side = {1: [st(2)], 3: [t_kern(0)], 4: [t_kern(1), st(3)], 8: [st(4)], 11: [st(5)]}
+        for k, (i, m) in enumerate(slots):
+            qt += [mx(i, m)] + side.get(k, []) + ([fis(k - 4)] if 8 <= k < 12 else [])
+        qt += [mx(4, 3), mx(5, 3), mx(6, 3), t_kern(2), t_kern(3), st(6), mx(7, 3), t_kern(4), t_kern(5), st(7), t_kern(6), t_kern(7)]
+        qt += [tr0(0, 0, "mm"), tr0(0, P, "mm"), tr0(0, H, "mm"), tr0(0, H + P, "mm"), tr0(1, 0, "tp"), tr1(0, 0), tr1(0, P), tr0(1, P, "tp"), tr1(0, H), tr1(0, H + P)]
+        qt += [tr1(1, 0), tr1(1, P), tr0(1, H, "mm"), tr1(1, H), tr0(1, H + P, "mm"), tr1(1, H + P)]
 
-        qv = [s_int(0, 0, G, V), q_flux(0, 2), q_scat(0), f_mul(0, 2), s_int(1, 0, H, V), f_sum(0, 2), s_int(1, H, H, V), q_flux(2, 2), q_scat(1)]
-        for b in range(4):
-            a = [stt(i, m) for i, m in pair[b]]
-            if b < 3:
-                a = a[:1] + [f_mul(2 * b + 2, 2)] + a[1:2] + [f_sum(2 * b + 2, 2)] + a[2:]
-            if b < 2:
-                a.append(q_flux(2 * b + 4, 2))
-            if b == 3:
-                a = a[:1] + [q_scat(2)] + a[1:]
-            qv += a
-        qv += [stt(0, 2), q_scat(3), stt(1, 2), stt(2, 2), stt(3, 2)] + [stt(i, 3) for i in lo]
-        qv += [stt(4, 2), stt(5, 2), q_kern(0), stt(6, 2), stt(7, 2), q_q(0, 0, G)]
-        qv += [stt(i, 3, 0, H) for i in hi] + [stt(i, 3, H, H) for i in hi]
-        qv += [q_q(1, 0, H), q_kern(1), out(0, 0), q_q(1, H, H), out(0, P), out(0, H), out(0, H + P), out(1, 0), q_r(0, 0, H), out(1, P), out(1, H), q_r(0, H, H)]
-        qv += [out(1, H + P), q_r(1, 0, H), r_int(1, H + P, P, V), q_r(1, H, P), q_r(1, H + P, P)]
+        qv = [s_int(0, 0, G, V), s_int(1, 0, H, V), q_scat(0), q_flux(0, 2), s_int(1, H, H, V), q_scat(1), q_flux(2, 2), s_int(2, 0, G, V), stt(0, 1), q_flux(4, 4), q_scat(2)]
+        qv += [stt(i, 1) for i in (1, 2, 3)] + [stt(i, 2) for i in (0, 1, 2)] + [f_mul(0, 4), q_scat(3), f_sum(0, 4), stt(3, 2)] + [stt(i, 1) for i in hi]
+        qv += [stt(i, 3) for i in lo] + [stt(4, 2), f_mul(4, 4), stt(5, 2), f_sum(4, 4), stt(6, 2), stt(7, 2)]
+        qv += [q_add(0, 0, H, V), q_add(0, H, H, V), q_q(0, 0, G), q_kern(0, 0, 2)] + [stt(i, 3) for i in hi]
+        qv += [q_add(1, 0, H, V), q_kern(1, 0, 1), q_q(1, 0, H), q_add(1, H, H, V), out(0, 0), q_q(1, H, H), q_kern(1, 1, 1), out(0, P), out(0, H), out(0, H + P)]
+        qv += [out(1, 0), out(1, P), out(1, H), q_r(0, 0, G), out(1, H + P), q_r(1, 0, H), r_int(1, H + P, P, V), q_r(1, H, P), q_r(1, H + P, P)]
 
-        qs = [c_flux(0, S), c_dens(S), c_flux(1, S), fchi(0, S, x), fchi(1, S, x), ars(0), sgn(0), c_flux(2, S), ars(1), sgn(1), c_flux(3, S), s_int(2, 0, G, S), sqr(0), sqr(1)]
-        qs += inv(2) + inv(3)
-        for k in range(4):
-            if k == 3:
-                qs.append(q_int(0, 0, G, S))
-            qs += [c_kern(2 * k, S), c_kern(2 * k + 1, S)] + (inv(4 + k) if k < 3 else [])
-        qs += [q_int(1, 0, H, S), q_int(1, H, H, S)] + inv(7) + [r_int(g, c, P, S) for g in range(2) for c in range(0, G, P)][:7]
-        qs += [store_s(1, S), store_s(3, S)]
+        qs = [c_dens(S), c_flux(0, S), ars(0), c_flux(1, S), x0(0, S), x0(1, S), c_flux(2, S), c_flux(3, S), x0(2, S), x0(3, S), sgn(0)]
+        qs += [x0(4, S), sqr(0), x0(5, S), x0(6, S), x0(7, S)] + inv(1) + inv(2) + [c_kern(0, S), c_kern(1, S)] + inv(3) + inv(4) + [ars(5), sgn(5)]
+        qs += [fchi(i, S, fx) for i in (4, 5, 6)] + [c_kern(2, S), c_kern(3, S), fchi(7, S, fx), ars(6), sqr(5), sgn(6), c_kern(4, S), sqr(6), c_kern(5, S), c_kern(6, S), c_kern(7, S), ars(7), sgn(7)]
+        weaves = [r_int(g, c, P, S) for g in range(2) for c in range(0, G, P)]
+        qs += weaves[:1] + [sqr(7)] + weaves[1:7] + [store_s(1, S), store_s(3, S)]
 
-        qg = [fchi(i, GP, x) for i in range(2, 8)] + [s_int(3, c, P, GP) for c in range(0, G, P)] + [rmul(i, GP) for i in range(8)]
-
-        qy = [store(0, 0, H), store(0, H, H), store(1, 0, H), store(1, H, P), store_w(0, 0, G), store(1, H + P, P), store_w(1, 0, H), store_w(1, H, H), store_s(0, Y), store_s(2, Y)]
+        qg = [s_int(3, c, P, GP) for c in range(0, G, P)] + [rmul(0, GP)] + [fchi(i, GP, fx) for i in lo] + [rmul(i, GP, c, H) for i in range(1, 8) for c in (0, H)]
+        qy = [store(0, 0, P), store(0, P, P), store(0, H, H), store(1, 0, H), store(1, H, P), store_w(0, 0, G), store(1, H + P, P), store_w(1, 0, H), store_w(1, H, H), store_s(0, Y), store_s(2, Y)]
         emit([qt, qv, qs, qg, qy])

@@ -321,7 +321,6 @@ def tile_multigroupintegraltransportsourceiterati_x1_kernel(tc, flux, scat, dens
             nc.scalar.dma_start(out=sig4[:], in_=sigt)
             with nc.allow_non_contiguous_dma("512 short runs of nusf"):
                 nc.scalar.dma_start(out=nusf_t[:], in_=nusf.rearrange("m (p j) -> p m j", j=4))
-            nc.scalar.dma_start(out=chi_b[:], in_=chi.partition_broadcast(P))
 
         def setup():
             V.memset(warm[:], 1.0)
@@ -361,6 +360,7 @@ def tile_multigroupintegraltransportsourceiterati_x1_kernel(tc, flux, scat, dens
             load_flux(b)
         load_scat(2)
         load_scat(3)
+        nc.sync.dma_start(out=chi_b[:], in_=chi.partition_broadcast(P))
         load_kern(0)
         load_kern(1)
         setup()

@@ -144,8 +144,8 @@ def tile_multigroupintegraltransportsourceiterati_x1_kernel(tc, flux, scat, dens
                         T.transpose(ps[:, ks, u], words[:, 256 * ks + u:256 * ks + 256:2], id32[:])
             return step(run, free, [("kern", i)])
 
-        def st(i):
-            alloc, free = take("st", ("st", i), [P, G])
+        def st(i, ring="st"):
+            alloc, free = take(ring, ("st", i), [P, G])
             return step(lambda: T.matmul(alloc()[:], lhsT=dens_t[:, i], rhs=pad[:], start=True, stop=True), free + ["dens_t", "pad"], [("st", i)])
 
         def mx(i, m, c0=0, w=G):
@@ -319,8 +319,6 @@ def tile_multigroupintegraltransportsourceiterati_x1_kernel(tc, flux, scat, dens
         def load_small():
             nc.scalar.dma_start(out=dens_sb[:], in_=dens.rearrange("(g p t) m -> p g (t m)", g=2, t=4))
             nc.scalar.dma_start(out=sig4[:], in_=sigt)
-            with nc.allow_non_contiguous_dma("512 short runs of nusf"):
-                nc.scalar.dma_start(out=nusf_t[:], in_=nusf.rearrange("m (p j) -> p m j", j=4))
 
         def setup():
             V.memset(warm[:], 1.0)
@@ -360,35 +358,37 @@ def tile_multigroupintegraltransportsourceiterati_x1_kernel(tc, flux, scat, dens
             load_flux(b)
         load_scat(2)
         load_scat(3)
-        nc.sync.dma_start(out=chi_b[:], in_=chi.partition_broadcast(P))
+        with nc.allow_non_contiguous_dma("512 short runs of nusf"):
+            nc.sync.dma_start(out=nusf_t[:], in_=nusf.rearrange("m (p j) -> p m j", j=4))
         load_kern(0)
+        nc.sync.dma_start(out=chi_b[:], in_=chi.partition_broadcast(P))
         load_kern(1)
         setup()
         Y = nc.sync
         lo, hi = range(4), range(4, 8)
-        qt = [t_dens(), t_flux(0, "tp"), st(0), t_flux(1, "tp"), mx(0, 0), mx(1, 0), t_flux(2, "tp"), t_flux(3, "tp"), mx(0, 1), mx(2, 0), mx(3, 0), st(1)]
-        qt += [mx(1, 1), mx(4, 0), fis(0), mx(2, 1), mx(5, 0), fis(1), mx(3, 1), mx(6, 0), fis(2), mx(0, 2), mx(7, 0), fis(3)]
+        qt = [t_dens(), t_flux(0, "tp"), st(0), t_flux(1, "tp"), mx(0, 0), mx(1, 0), t_flux(2, "tp"), t_flux(3, "tp"), mx(0, 1), mx(2, 0), mx(3, 0), st(1), fis(0), fis(1)]
+        qt += [mx(1, 1), mx(4, 0), mx(2, 1), mx(5, 0), mx(3, 1), mx(6, 0), mx(0, 2), mx(7, 0)]
         slots = [(i, 2) for i in (1, 2, 3)] + [(i, 1) for i in hi] + [(i, 3) for i in lo] + [(i, 2) for i in hi]
-        side = {1: [st(2)], 3: [t_kern(0)], 4: [t_kern(1), st(3)], 8: [st(4)], 11: [st(5)]}
+        side = [[fis(2)], [st(2)], [fis(3)], [fis(4)], [fis(5), st(3)], [fis(6)], [fis(7)], [st(4)], [t_kern(0)], [], [t_kern(1)], [st(5)], [], [], []]
         for k, (i, m) in enumerate(slots):
-            qt += [mx(i, m)] + side.get(k, []) + ([fis(k - 4)] if 8 <= k < 12 else [])
-        qt += [mx(4, 3), mx(5, 3), mx(6, 3), t_kern(2), t_kern(3), st(6), mx(7, 3), t_kern(4), t_kern(5), st(7), t_kern(6), t_kern(7)]
+            qt += [mx(i, m)] + side[k]
+        qt += [mx(4, 3), mx(5, 3), t_kern(2), t_kern(3), mx(6, 3), mx(7, 3), t_kern(4), t_kern(5), st(6), t_kern(6), t_kern(7), st(7)]
         qt += [tr0(0, 0, "mm"), tr0(0, P, "mm"), tr0(0, H, "mm"), tr0(0, H + P, "mm"), tr0(1, 0, "tp"), tr1(0, 0), tr1(0, P), tr0(1, P, "tp"), tr1(0, H), tr1(0, H + P)]
         qt += [tr1(1, 0), tr1(1, P), tr0(1, H, "mm"), tr1(1, H), tr0(1, H + P, "mm"), tr1(1, H + P)]
 
         qv = [s_int(0, 0, G, V), s_int(1, 0, H, V), q_scat(0), q_flux(0, 2), s_int(1, H, H, V), q_scat(1), q_flux(2, 2), s_int(2, 0, G, V), stt(0, 1), q_flux(4, 4), q_scat(2)]
-        qv += [stt(i, 1) for i in (1, 2, 3)] + [stt(i, 2) for i in (0, 1, 2)] + [f_mul(0, 4), q_scat(3), f_sum(0, 4), stt(3, 2)] + [stt(i, 1) for i in hi]
-        qv += [stt(i, 3) for i in lo] + [stt(4, 2), f_mul(4, 4), stt(5, 2), f_sum(4, 4), stt(6, 2), stt(7, 2)]
-        qv += [q_add(0, 0, H, V), q_add(0, H, H, V), q_q(0, 0, G), q_kern(0, 0, 2)] + [stt(i, 3) for i in hi]
+        qv += [stt(i, 1) for i in (1, 2, 3)] + [stt(i, 2) for i in lo] + [stt(4, 1), f_mul(0, 4), q_scat(3), f_sum(0, 4)] + [stt(i, 1) for i in (5, 6, 7)]
+        qv += [stt(0, 3), f_mul(4, 4), stt(1, 3), f_sum(4, 4), stt(2, 3), stt(3, 3)] + [stt(i, 2) for i in hi]
+        qv += [q_add(0, 0, H, V), q_add(0, H, H, V), q_q(0, 0, H), q_q(0, H, H), q_kern(0, 0, 2)] + [stt(i, 3) for i in hi]
         qv += [q_add(1, 0, H, V), q_kern(1, 0, 1), q_q(1, 0, H), q_add(1, H, H, V), out(0, 0), q_q(1, H, H), q_kern(1, 1, 1), out(0, P), out(0, H), out(0, H + P)]
         qv += [out(1, 0), out(1, P), out(1, H), q_r(0, 0, G), out(1, H + P), q_r(1, 0, H), r_int(1, H + P, P, V), q_r(1, H, P), q_r(1, H + P, P)]
 
         qs = [c_dens(S), c_flux(0, S), ars(0), c_flux(1, S), x0(0, S), x0(1, S), c_flux(2, S), c_flux(3, S), x0(2, S), x0(3, S), sgn(0)]
-        qs += [x0(4, S), sqr(0), x0(5, S), x0(6, S), x0(7, S)] + inv(1) + inv(2) + [c_kern(0, S), c_kern(1, S)] + inv(3) + inv(4) + [ars(5), sgn(5)]
-        qs += [fchi(i, S, fx) for i in (4, 5, 6)] + [c_kern(2, S), c_kern(3, S), fchi(7, S, fx), ars(6), sqr(5), sgn(6), c_kern(4, S), sqr(6), c_kern(5, S), c_kern(6, S), c_kern(7, S), ars(7), sgn(7)]
-        weaves = [r_int(g, c, P, S) for g in range(2) for c in range(0, G, P)]
-        qs += weaves[:1] + [sqr(7)] + weaves[1:7] + [store_s(1, S), store_s(3, S)]
+        qs += [x0(i, S) for i in hi] + [sqr(0)] + inv(1) + inv(2) + inv(3) + [fchi(3, S, fx), c_kern(0, S), ars(4), sgn(4), c_kern(1, S), fchi(4, S, fx), fchi(5, S, fx), ars(5), sgn(5)]
+        qs += [c_kern(2, S), c_kern(3, S), fchi(6, S, fx), c_kern(4, S), sqr(4), c_kern(5, S), sqr(5), fchi(7, S, fx), c_kern(6, S), c_kern(7, S)] + inv(6) + inv(7)
+        qs += [r_int(g, c, P, S) for g in range(2) for c in range(0, G, P)][:7] + [store_s(1, S), store_s(3, S)]
 
-        qg = [s_int(3, c, P, GP) for c in range(0, G, P)] + [rmul(0, GP)] + [fchi(i, GP, fx) for i in lo] + [rmul(i, GP, c, H) for i in range(1, 8) for c in (0, H)]
-        qy = [store(0, 0, P), store(0, P, P), store(0, H, H), store(1, 0, H), store(1, H, P), store_w(0, 0, G), store(1, H + P, P), store_w(1, 0, H), store_w(1, H, H), store_s(0, Y), store_s(2, Y)]
+        qg = [s_int(3, c, P, GP) for c in range(0, G, P)] + [fchi(i, GP, fx) for i in range(3)] + [rmul(i, GP) for i in range(6)] + [rmul(i, GP, c, H) for c in (0, H) for i in (6, 7)]
+        qy = [store(g, c, P) for g in range(2) for c in range(0, G, P)]
+        qy = qy[:7] + [store_w(0, 0, G)] + qy[7:] + [store_w(1, 0, H), store_w(1, H, H), store_s(0, Y), store_s(2, Y)]
         emit([qt, qv, qs, qg, qy])

@@ -34,11 +34,11 @@ def tile_multigroupintegraltransportsourceiterati_x1_kernel(tc, flux, scat, dens
         def tiles(name, n, shape, dtype):
             return [tile("%s%d" % (name, k), shape, dtype) for k in range(n)]
 
-        sig4 = tile("sig4", [M, G], BF16)
+        rows = tile("rows", [16, G], BF16)
         pad = tile("pad", [P, G], BF16)
         dens_pad = tile("dens_pad", [P, NT, P], BF16)
         dens_sb = tile("dens_sb", [P, 2, 16], BF16)
-        nusf_t = tile("nusf_t", [P, M, 4], BF16)
+        nusf_t = tile("nusf_t", [P, 4, M], BF16)
         flux_raw = tiles("flux_raw", 4, [P, 2, G], BF16)
         scat_raw = tiles("scat_raw", M, [P, 4, G], BF16)
         kern_raw = tiles("kern_raw", 2, [P, 4, R], BF16)
@@ -161,8 +161,8 @@ def tile_multigroupintegraltransportsourceiterati_x1_kernel(tc, flux, scat, dens
             def run():
                 ps = alloc() if i == i0 else bank["p", i0]
                 for j in range(4):
-                    T.matmul(ps[:, i - i0], lhsT=flux_grp[i // 4][:, i % 4, :, j], rhs=nusf_t[:, :, j], start=(j == 0), stop=(j == 3))
-            return step(run, (free if i == i0 else []) + [("fg", i // 2)], [("p", i0)] if i == i0 + 3 else [])
+                    T.matmul(ps[:, i - i0], lhsT=flux_grp[i // 4][:, i % 4, :, j], rhs=nusf_t[:, j], start=(j == 0), stop=(j == 3))
+            return step(run, (free if i == i0 else []) + [("fg", i // 2), "nusf_t"], [("p", i0)] if i == i0 + 3 else [])
 
         def tr_pass(ps, g, c0, gs):
             for t in range(4):
@@ -188,6 +188,25 @@ def tile_multigroupintegraltransportsourceiterati_x1_kernel(tc, flux, scat, dens
 
         def c_scat(m, c0, eng):
             return step(lambda: move(eng, scat_grp[m][:, c0:c0 + H], bank["scat", m, c0][:]), [("scat", m, c0)], cols("sg", ("s", m), c0, H) + [("read", ("scat", m, c0))])
+
+        def t_nusf(ring):
+            alloc, free = take(ring, "nusf", [P, 4, P], BF16)
+
+            def run():
+                ps = alloc()
+                for j in range(4):
+                    T.transpose(ps[:, j], pad[:, j:G:4], id16[:])
+            return step(run, free, ["nusf"])
+
+        def c_nusf(eng):
+            return step(lambda: move(eng, nusf_t[:], bank["nusf"][:, :, M:2 * M]), ["nusf"], ["nusf_t", ("read", "nusf")])
+
+        def t_chi(ring):
+            alloc, free = take(ring, "chi", [P, G], BF16)
+            return step(lambda: T.matmul(alloc()[:], lhsT=id16[:, 2 * M:2 * M + 1].to_broadcast([P, P]), rhs=pad[:], start=True, stop=True), free, ["chi"])
+
+        def c_chi(eng):
+            return step(lambda: move(eng, chi_b[:], bank["chi"][:]), ["chi"], ["chi_b", ("read", "chi")])
 
         def c_dens(eng):
             return step(lambda: move(eng, dens_t[:], bank["dens"][:]), ["dens"], ["dens_t", ("read", "dens")])
@@ -224,7 +243,7 @@ def tile_multigroupintegraltransportsourceiterati_x1_kernel(tc, flux, scat, dens
                     S.activation(out=dst[i // 4][:, i % 4], in_=chi_b[:], func=ACT.Copy, scale=f[:, i:i + 1])
                 else:
                     eng.tensor_scalar(out=dst[i // 4][:, i % 4], in0=chi_b[:], scalar1=f[:, i:i + 1], scalar2=0.0, op0=ALU.mult, op1=ALU.add)
-            return step(run, [("f", i)], [("fx", i)] if dst is fx else cols(("x", -1), i, 0, G))
+            return step(run, [("f", i), "chi_b"], [("fx", i)] if dst is fx else cols(("x", -1), i, 0, G))
 
         def x0(i, eng):
             def run():
@@ -318,7 +337,9 @@ def tile_multigroupintegraltransportsourceiterati_x1_kernel(tc, flux, scat, dens
 
         def load_small():
             nc.scalar.dma_start(out=dens_sb[:], in_=dens.rearrange("(g p t) m -> p g (t m)", g=2, t=4))
-            nc.scalar.dma_start(out=sig4[:], in_=sigt)
+            nc.scalar.dma_start(out=rows[0:M], in_=sigt)
+            nc.scalar.dma_start(out=rows[M:2 * M], in_=nusf)
+            nc.scalar.dma_start(out=rows[2 * M:2 * M + 1], in_=chi.rearrange("(o g) -> o g", o=1))
 
         def setup():
             V.memset(warm[:], 1.0)
@@ -328,7 +349,7 @@ def tile_multigroupintegraltransportsourceiterati_x1_kernel(tc, flux, scat, dens
             V.memset(dens_pad[:], 0.0)
             V.tensor_copy(out=id16[:], in_=id32[:])
             V.tensor_copy(out=dens_pad[:, :, 0:M], in_=dens_v)
-            V.tensor_copy(out=pad[0:M], in_=sig4[:])
+            V.tensor_copy(out=pad[0:2 * M + 1], in_=rows[0:2 * M + 1])
             V.tensor_copy(out=dens32[:], in_=dens_v)
 
         def emit(queues):
@@ -358,16 +379,13 @@ def tile_multigroupintegraltransportsourceiterati_x1_kernel(tc, flux, scat, dens
             load_flux(b)
         load_scat(2)
         load_scat(3)
-        with nc.allow_non_contiguous_dma("512 short runs of nusf"):
-            nc.sync.dma_start(out=nusf_t[:], in_=nusf.rearrange("m (p j) -> p m j", j=4))
         load_kern(0)
-        nc.sync.dma_start(out=chi_b[:], in_=chi.partition_broadcast(P))
         load_kern(1)
         setup()
         Y = nc.sync
         lo, hi = range(4), range(4, 8)
-        qt = [t_dens(), t_flux(0, "tp"), st(0), t_flux(1, "tp"), mx(0, 0), mx(1, 0), t_flux(2, "tp"), t_flux(3, "tp"), mx(0, 1), mx(2, 0), mx(3, 0), st(1), fis(0), fis(1)]
-        qt += [mx(1, 1), mx(4, 0), mx(2, 1), mx(5, 0), mx(3, 1), mx(6, 0), mx(0, 2), mx(7, 0)]
+        qt = [t_dens(), t_flux(0, "tp"), t_chi("mm"), st(0), t_flux(1, "tp"), mx(0, 0), mx(1, 0), t_flux(2, "tp"), t_flux(3, "tp"), mx(0, 1), mx(2, 0), mx(3, 0), st(1), t_nusf("tp")]
+        qt += [mx(1, 1), mx(4, 0), mx(2, 1), mx(5, 0), mx(3, 1), mx(6, 0), fis(0), mx(0, 2), mx(7, 0), fis(1)]
         slots = [(i, 2) for i in (1, 2, 3)] + [(i, 1) for i in hi] + [(i, 3) for i in lo] + [(i, 2) for i in hi]
         side = [[fis(2)], [st(2)], [fis(3)], [fis(4)], [fis(5), st(3)], [fis(6)], [fis(7)], [st(4)], [t_kern(0)], [], [t_kern(1)], [st(5)], [], [], []]
         for k, (i, m) in enumerate(slots):
@@ -383,12 +401,11 @@ def tile_multigroupintegraltransportsourceiterati_x1_kernel(tc, flux, scat, dens
         qv += [q_add(1, 0, H, V), q_kern(1, 0, 1), q_q(1, 0, H), q_add(1, H, H, V), out(0, 0), q_q(1, H, H), q_kern(1, 1, 1), out(0, P), out(0, H), out(0, H + P)]
         qv += [out(1, 0), out(1, P), out(1, H), q_r(0, 0, G), out(1, H + P), q_r(1, 0, H), r_int(1, H + P, P, V), q_r(1, H, P), q_r(1, H + P, P)]
 
-        qs = [c_dens(S), c_flux(0, S), ars(0), c_flux(1, S), x0(0, S), x0(1, S), c_flux(2, S), c_flux(3, S), x0(2, S), x0(3, S), sgn(0)]
+        qs = [c_dens(S), c_flux(0, S), c_chi(S), ars(0), c_flux(1, S), x0(0, S), x0(1, S), c_flux(2, S), c_flux(3, S), x0(2, S), x0(3, S), c_nusf(S), sgn(0)]
         qs += [x0(i, S) for i in hi] + [sqr(0)] + inv(1) + inv(2) + inv(3) + [fchi(3, S, fx), c_kern(0, S), ars(4), sgn(4), c_kern(1, S), fchi(4, S, fx), fchi(5, S, fx), ars(5), sgn(5)]
         qs += [c_kern(2, S), c_kern(3, S), fchi(6, S, fx), c_kern(4, S), sqr(4), c_kern(5, S), sqr(5), fchi(7, S, fx), c_kern(6, S), c_kern(7, S)] + inv(6) + inv(7)
         qs += [r_int(g, c, P, S) for g in range(2) for c in range(0, G, P)][:7] + [store_s(1, S), store_s(3, S)]
 
         qg = [s_int(3, c, P, GP) for c in range(0, G, P)] + [fchi(i, GP, fx) for i in range(3)] + [rmul(i, GP) for i in range(6)] + [rmul(i, GP, c, H) for c in (0, H) for i in (6, 7)]
-        qy = [store(g, c, P) for g in range(2) for c in range(0, G, P)]
-        qy = qy[:7] + [store_w(0, 0, G)] + qy[7:] + [store_w(1, 0, H), store_w(1, H, H), store_s(0, Y), store_s(2, Y)]
+        qy = [store(0, 0, P), store(0, P, P), store(0, H, H), store(1, 0, H), store(1, H, P), store_w(0, 0, G), store(1, H + P, P), store_w(1, 0, H), store_w(1, H, H), store_s(0, Y), store_s(2, Y)]
         emit([qt, qv, qs, qg, qy])

@@ -34,7 +34,8 @@ def tile_multigroupintegraltransportsourceiterati_x1_kernel(tc, flux, scat, dens
         def tiles(name, n, shape, dtype):
             return [tile("%s%d" % (name, k), shape, dtype) for k in range(n)]
 
-        rows = tile("rows", [16, G], BF16)
+        pad_nu = tile("pad_nu", [P, G], BF16)
+        pad_chi = tile("pad_chi", [P, G], BF16)
         pad = tile("pad", [P, G], BF16)
         dens_pad = tile("dens_pad", [P, NT, P], BF16)
         dens_sb = tile("dens_sb", [P, 2, 16], BF16)
@@ -60,7 +61,8 @@ def tile_multigroupintegraltransportsourceiterati_x1_kernel(tc, flux, scat, dens
         fx = tiles("fx", 2, [P, 4, G], F32)
         sg = tiles("sg", NT, [P, G], BF16)
         rst = tiles("rst", 2, [P, 4, G], F32)
-        kern_grp = tiles("kern_grp", 2, [P, 2, 4, P, 4], BF16)
+        kern_grp = [keep.tile([P, 2, 4, P, 4], BF16, align_bytes=64, name="kern_grp%d" % g, tag="late%d" % g) for g in range(2)]
+        inv_hi = {}
         kern_codes = tile("kern_codes", [P, 2, 2, 4, P], U32)
         kern_sc = tile("kern_sc", [P, 2, 2, 4, P], U8)
         q_grp = tile("q_grp", [P, 2, G, 4], BF16)
@@ -195,15 +197,15 @@ def tile_multigroupintegraltransportsourceiterati_x1_kernel(tc, flux, scat, dens
             def run():
                 ps = alloc()
                 for j in range(4):
-                    T.transpose(ps[:, j], pad[:, j:G:4], id16[:])
+                    T.transpose(ps[:, j], pad_nu[:, j:G:4], id16[:])
             return step(run, free, ["nusf"])
 
         def c_nusf(eng):
-            return step(lambda: move(eng, nusf_t[:], bank["nusf"][:, :, M:2 * M]), ["nusf"], ["nusf_t", ("read", "nusf")])
+            return step(lambda: move(eng, nusf_t[:], bank["nusf"][:, :, 0:M]), ["nusf"], ["nusf_t", ("read", "nusf")])
 
         def t_chi(ring):
             alloc, free = take(ring, "chi", [P, G], BF16)
-            return step(lambda: T.matmul(alloc()[:], lhsT=id16[:, 2 * M:2 * M + 1].to_broadcast([P, P]), rhs=pad[:], start=True, stop=True), free, ["chi"])
+            return step(lambda: T.matmul(alloc()[:], lhsT=id16[:, 0:1].to_broadcast([P, P]), rhs=pad_chi[:], start=True, stop=True), free, ["chi"])
 
         def c_chi(eng):
             return step(lambda: move(eng, chi_b[:], bank["chi"][:]), ["chi"], ["chi_b", ("read", "chi")])
@@ -235,7 +237,17 @@ def tile_multigroupintegraltransportsourceiterati_x1_kernel(tc, flux, scat, dens
 
         def rmul(i, eng, c0=0, w=G):
             r = rst[i // 4][:, i % 4, c0:c0 + w]
-            return step(lambda: eng.tensor_tensor(out=r, in0=r, in1=sg[i][:, c0:c0 + w], op=ALU.mult), [("r", i), ("sg", i)], cols("rst", i, c0, w))
+
+            def run():
+                if i < 4:
+                    dst = r
+                else:
+                    h = (i - 4) // 2
+                    if h not in inv_hi:
+                        inv_hi[h] = keep.tile([P, 2, G], F32, align_bytes=64, name="inv_hi%d" % h, tag="late%d" % h)
+                    dst = inv_hi[h][:, i % 2, c0:c0 + w]
+                eng.tensor_tensor(out=dst, in0=r, in1=sg[i][:, c0:c0 + w], op=ALU.mult)
+            return step(run, [("r", i), ("sg", i)] + ([("kq", (i - 4) // 2, 1)] if i >= 4 else []), cols("rst", i, c0, w))
 
         def fchi(i, eng, dst):
             def run():
@@ -310,8 +322,13 @@ def tile_multigroupintegraltransportsourceiterati_x1_kernel(tc, flux, scat, dens
                                               in_=q_grp[:, g, c0:c0 + w].rearrange("p n t -> p (n t)")), cols("qg", g, c0, w), cols("qq", g, c0, w))
 
         def out(g, c0):
-            return step(lambda: V.tensor_tensor(out=res[g][:, :, c0:c0 + P], in0=bank["c", g, c0][:], in1=rst[g][:, :, c0:c0 + P], op=ALU.mult),
-                        [("c", g, c0)] + [("rst", i, c0) for i in range(4 * g, 4 * g + 4)], [("res", g, c0), ("read", ("c", g, c0))])
+            def run():
+                if g == 0:
+                    V.tensor_tensor(out=res[g][:, :, c0:c0 + P], in0=bank["c", g, c0][:], in1=rst[g][:, :, c0:c0 + P], op=ALU.mult)
+                else:
+                    for h in range(2):
+                        V.tensor_tensor(out=res[g][:, 2 * h:2 * h + 2, c0:c0 + P], in0=bank["c", g, c0][:, 2 * h:2 * h + 2], in1=inv_hi[h][:, :, c0:c0 + P], op=ALU.mult)
+            return step(run, [("c", g, c0)] + [("rst", i, c0) for i in range(4 * g, 4 * g + 4)], [("res", g, c0), ("read", ("c", g, c0))])
 
         def q_r(g, c0, w):
             return step(lambda: V.quantize_mx(out=r_codes[:, g, c0:c0 + w].bitcast(FP8X4), scales=r_sc[4 * g:P, c0:c0 + w],
@@ -337,19 +354,19 @@ def tile_multigroupintegraltransportsourceiterati_x1_kernel(tc, flux, scat, dens
 
         def load_small():
             nc.scalar.dma_start(out=dens_sb[:], in_=dens.rearrange("(g p t) m -> p g (t m)", g=2, t=4))
-            nc.scalar.dma_start(out=rows[0:M], in_=sigt)
-            nc.scalar.dma_start(out=rows[M:2 * M], in_=nusf)
-            nc.scalar.dma_start(out=rows[2 * M:2 * M + 1], in_=chi.rearrange("(o g) -> o g", o=1))
 
         def setup():
+            for t in (pad, pad_nu, pad_chi):
+                V.memset(t[:], 0.0)
+            nc.scalar.dma_start(out=pad[0:M], in_=sigt)
+            nc.scalar.dma_start(out=pad_chi[0:1], in_=chi.rearrange("(o g) -> o g", o=1))
+            nc.scalar.dma_start(out=pad_nu[0:M], in_=nusf)
             V.memset(warm[:], 1.0)
             S.activation(out=warm[:, 1:2], in_=warm[:, 0:1], func=ACT.Abs_reciprocal_sqrt)
             make_identity(nc, id32[:])
-            V.memset(pad[:], 0.0)
             V.memset(dens_pad[:], 0.0)
             V.tensor_copy(out=id16[:], in_=id32[:])
             V.tensor_copy(out=dens_pad[:, :, 0:M], in_=dens_v)
-            V.tensor_copy(out=pad[0:2 * M + 1], in_=rows[0:2 * M + 1])
             V.tensor_copy(out=dens32[:], in_=dens_v)
 
         def emit(queues):
@@ -387,7 +404,7 @@ def tile_multigroupintegraltransportsourceiterati_x1_kernel(tc, flux, scat, dens
         qt = [t_dens(), t_flux(0, "tp"), t_chi("mm"), st(0), t_flux(1, "tp"), mx(0, 0), mx(1, 0), t_flux(2, "tp"), t_flux(3, "tp"), mx(0, 1), mx(2, 0), mx(3, 0), st(1), t_nusf("tp")]
         qt += [mx(1, 1), mx(4, 0), mx(2, 1), mx(5, 0), mx(3, 1), mx(6, 0), fis(0), mx(0, 2), mx(7, 0), fis(1)]
         slots = [(i, 2) for i in (1, 2, 3)] + [(i, 1) for i in hi] + [(i, 3) for i in lo] + [(i, 2) for i in hi]
-        side = [[fis(2)], [st(2)], [fis(3)], [fis(4)], [fis(5), st(3)], [fis(6)], [fis(7)], [st(4)], [t_kern(0)], [], [t_kern(1)], [st(5)], [], [], []]
+        side = [[fis(2)], [fis(3)], [st(2)], [fis(4)], [fis(5), st(3)], [fis(6)], [fis(7)], [st(4)], [t_kern(0)], [], [t_kern(1)], [st(5)], [], [], []]
         for k, (i, m) in enumerate(slots):
             qt += [mx(i, m)] + side[k]
         qt += [mx(4, 3), mx(5, 3), t_kern(2), t_kern(3), mx(6, 3), mx(7, 3), t_kern(4), t_kern(5), st(6), t_kern(6), t_kern(7), st(7)]
@@ -395,7 +412,7 @@ def tile_multigroupintegraltransportsourceiterati_x1_kernel(tc, flux, scat, dens
         qt += [tr1(1, 0), tr1(1, P), tr0(1, H, "mm"), tr1(1, H), tr0(1, H + P, "mm"), tr1(1, H + P)]
 
         qv = [s_int(0, 0, G, V), s_int(1, 0, H, V), q_scat(0), q_flux(0, 2), s_int(1, H, H, V), q_scat(1), q_flux(2, 2), s_int(2, 0, G, V), stt(0, 1), q_flux(4, 4), q_scat(2)]
-        qv += [stt(i, 1) for i in (1, 2, 3)] + [stt(i, 2) for i in lo] + [stt(4, 1), f_mul(0, 4), q_scat(3), f_sum(0, 4)] + [stt(i, 1) for i in (5, 6, 7)]
+        qv += [stt(i, 1) for i in (1, 2, 3)] + [stt(i, 2) for i in lo] + [f_mul(0, 4), q_scat(3), f_sum(0, 4)] + [stt(i, 1) for i in hi]
         qv += [stt(0, 3), f_mul(4, 4), stt(1, 3), f_sum(4, 4), stt(2, 3), stt(3, 3)] + [stt(i, 2) for i in hi]
         qv += [q_add(0, 0, H, V), q_add(0, H, H, V), q_q(0, 0, H), q_q(0, H, H), q_kern(0, 0, 2)] + [stt(i, 3) for i in hi]
         qv += [q_add(1, 0, H, V), q_kern(1, 0, 1), q_q(1, 0, H), q_add(1, H, H, V), out(0, 0), q_q(1, H, H), q_kern(1, 1, 1), out(0, P), out(0, H), out(0, H + P)]

@@ -15,14 +15,16 @@ AX = mybir.AxisListType
 
 P = 128
 R, G, M = 1024, 512, 4
-NT = 8
-H = 256
+NT = R // P
+H = G // 2
+BANKS = {"mm": 4, "tp": 2, "st": 2}
+F_ON_GPSIMD = 3
 FLOPS = 2 * R * G * G * M + 2 * R * R * G
 
 
 def tile_multigroupintegraltransportsourceiterati_x1_kernel(tc, flux, scat, dens, nusf, chi, kern, sigt, out_0, out_1, out_2):
     nc = tc.nc
-    V, S, T, GP = nc.vector, nc.scalar, nc.tensor, nc.gpsimd
+    V, S, T, GP, SP = nc.vector, nc.scalar, nc.tensor, nc.gpsimd, nc.sync
     with ExitStack() as ctx:
         keep = ctx.enter_context(tc.tile_pool(name="keep", bufs=1))
         psum = ctx.enter_context(tc.psum_pool(name="psum", bufs=1))
@@ -34,11 +36,14 @@ def tile_multigroupintegraltransportsourceiterati_x1_kernel(tc, flux, scat, dens
         def tiles(name, n, shape, dtype):
             return [tile("%s%d" % (name, k), shape, dtype) for k in range(n)]
 
-        pad_nu = tile("pad_nu", [P, G], BF16)
-        pad_chi = tile("pad_chi", [P, G], BF16)
-        pad = tile("pad", [P, G], BF16)
+        def shared(name, h, shape, dtype):
+            return keep.tile(shape, dtype, align_bytes=64, name="%s%d" % (name, h), tag="shared%d" % h)
+
+        nu_pad = tile("nu_pad", [P, G], BF16)
+        chi_pad = tile("chi_pad", [P, G], BF16)
+        sig_pad = tile("sig_pad", [P, G], BF16)
         dens_pad = tile("dens_pad", [P, NT, P], BF16)
-        dens_sb = tile("dens_sb", [P, 2, 16], BF16)
+        dens_sb = tile("dens_sb", [P, 2, 4 * M], BF16)
         nusf_t = tile("nusf_t", [P, 4, M], BF16)
         flux_raw = tiles("flux_raw", 4, [P, 2, G], BF16)
         scat_raw = tiles("scat_raw", M, [P, 4, G], BF16)
@@ -59,9 +64,9 @@ def tile_multigroupintegraltransportsourceiterati_x1_kernel(tc, flux, scat, dens
         f = tile("f", [P, NT], F32)
         x = tiles("x", 2, [P, 4, G], F32)
         fx = tiles("fx", 2, [P, 4, G], F32)
-        sg = tiles("sg", NT, [P, G], BF16)
+        sg = tile("sg", [P, NT, G], BF16)
         rst = tiles("rst", 2, [P, 4, G], F32)
-        kern_grp = [keep.tile([P, 2, 4, P, 4], BF16, align_bytes=64, name="kern_grp%d" % g, tag="late%d" % g) for g in range(2)]
+        kern_grp = [shared("kern_grp", g, [P, 2, 4, P, 4], BF16) for g in range(2)]
         inv_hi = {}
         kern_codes = tile("kern_codes", [P, 2, 2, 4, P], U32)
         kern_sc = tile("kern_sc", [P, 2, 2, 4, P], U8)
@@ -82,347 +87,333 @@ def tile_multigroupintegraltransportsourceiterati_x1_kernel(tc, flux, scat, dens
         out2_v = out_2.bitcast(I32)
 
         bank = {}
-        rings = {"mm": 4, "tp": 2, "st": 2}
-        turn = {"mm": [], "tp": [], "st": []}
-
-        def step(run, needs, gives):
-            return (run, list(needs), list(gives))
 
         def take(ring, key, shape, dtype=F32):
             def alloc():
-                bank[key] = psum.tile(shape, dtype, tag=ring, bufs=rings[ring], name=ring)
+                bank[key] = psum.tile(shape, dtype, tag=ring, bufs=BANKS[ring], name=ring)
                 return bank[key]
-
             return alloc, [("bank", ring, key)]
 
-        def move(eng, out, in_):
-            if eng is S:
-                S.copy(out=out, in_=in_)
-            elif eng is V:
-                V.tensor_copy(out=out, in_=in_)
-            else:
-                GP.tensor_scalar(out=out, in0=in_, scalar1=1.0, scalar2=0.0, op0=ALU.mult, op1=ALU.add)
+        def cols(name, g, c0, w):
+            return [(name, g, c) for c in range(c0, c0 + w, P)]
 
         def blocks(dst, src):
             return dst.rearrange("p (c i) t -> p c t i", i=4), src.rearrange("p t (c i) -> p c t i", i=4)
 
         def weave(eng, dst, src):
             if eng is GP:
-                move(eng, dst, src.rearrange("p t n -> p n t"))
+                GP.tensor_scalar(out=dst, in0=src.rearrange("p t n -> p n t"), scalar1=1.0, scalar2=0.0, op0=ALU.mult, op1=ALU.add)
+            elif eng is S:
+                out, in_ = blocks(dst, src)
+                S.copy(out=out, in_=in_)
             else:
-                move(eng, *blocks(dst, src))
-
-        def cols(name, g, c0, w):
-            return [(name, g, c) for c in range(c0, c0 + w, P)]
+                out, in_ = blocks(dst, src)
+                V.tensor_copy(out=out, in_=in_)
 
         def t_dens():
-            alloc, free = take("st", "dens", [P, NT, P], BF16)
+            alloc, needs = take("st", "dens", [P, NT, P], BF16)
 
             def run():
-                b = alloc()
+                ps = alloc()
                 for i in range(NT):
-                    T.transpose(b[:, i], dens_pad[:, i], id16[:])
-            return step(run, free + ["dens_pad", "id16"], ["dens"])
+                    T.transpose(ps[:, i], dens_pad[:, i], id16[:])
+            return run, needs, ["dens"]
 
-        def t_flux(b, ring):
-            alloc, free = take(ring, ("flux", b), [P, 2, 2, P])
+        def t_flux(b):
+            alloc, needs = take("tp", ("flux", b), [P, 2, 2, P])
 
             def run():
                 ps = alloc()
                 for a in range(2):
                     words = flux_raw[b][:, a].bitcast(F32)
                     for u in range(2):
-                        T.transpose(ps[:, a, u], words[:, u:256:2], id32[:])
-            return step(run, free + ["id32"], [("flux", b)])
+                        T.transpose(ps[:, a, u], words[:, u:H:2], id32[:])
+            return run, needs, [("flux", b)]
 
         def t_kern(i):
-            alloc, free = take("tp", ("kern", i), [P, 2, 2, P])
+            alloc, needs = take("tp", ("kern", i), [P, 2, 2, P])
 
             def run():
                 ps = alloc()
                 words = kern_raw[i // 4][:, i % 4].bitcast(F32)
                 for ks in range(2):
                     for u in range(2):
-                        T.transpose(ps[:, ks, u], words[:, 256 * ks + u:256 * ks + 256:2], id32[:])
-            return step(run, free, [("kern", i)])
+                        T.transpose(ps[:, ks, u], words[:, H * ks + u:H * ks + H:2], id32[:])
+            return run, needs, [("kern", i)]
 
-        def st(i, ring="st"):
-            alloc, free = take(ring, ("st", i), [P, G])
-            return step(lambda: T.matmul(alloc()[:], lhsT=dens_t[:, i], rhs=pad[:], start=True, stop=True), free + ["dens_t", "pad"], [("st", i)])
+        def t_nusf():
+            alloc, needs = take("tp", "nusf", [P, 4, P], BF16)
 
-        def mx(i, m, c0=0, w=G):
-            alloc, free = take("mm", ("a", i, m, c0), [P, w])
-            return step(lambda: T.matmul_mx(out=alloc()[:], lhsT=flux_codes[:, i].bitcast(FP8X4), lhsT_scale=flux_sc[:, i],
-                                            rhs=scat_codes[:, m, c0:c0 + w].bitcast(FP8X4), rhs_scale=scat_sc[:, m, c0:c0 + w], start=True, stop=True),
-                        free + [("fq", i), ("sq", m)], [("a", i, m, c0)])
+            def run():
+                ps = alloc()
+                for j in range(4):
+                    T.transpose(ps[:, j], nu_pad[:, j:G:4], id16[:])
+            return run, needs, ["nusf"]
 
-        def fis(i, ring="tp"):
+        def spread_chi():
+            alloc, needs = take("tp", "chi", [P, G], BF16)
+            return (lambda: T.matmul(alloc()[:], lhsT=id16[:, 0:1].to_broadcast([P, P]), rhs=chi_pad[:], start=True, stop=True)), needs, ["chi"]
+
+        def total(i):
+            alloc, needs = take("st", ("st", i), [P, G])
+            return (lambda: T.matmul(alloc()[:], lhsT=dens_t[:, i], rhs=sig_pad[:], start=True, stop=True)), needs + ["dens_t"], [("st", i)]
+
+        def scatter(i, m):
+            alloc, needs = take("mm", ("a", i, m), [P, G])
+
+            def run():
+                T.matmul_mx(out=alloc()[:], lhsT=flux_codes[:, i].bitcast(FP8X4), lhsT_scale=flux_sc[:, i],
+                            rhs=scat_codes[:, m].bitcast(FP8X4), rhs_scale=scat_sc[:, m], start=True, stop=True)
+            return run, needs + [("flux_q", i), ("scat_q", m)], [("a", i, m)]
+
+        def fission(i):
             i0 = 4 * (i // 4)
-            alloc, free = take(ring, ("p", i0), [P, 4, M])
+            alloc, needs = take("tp", ("p", i0), [P, 4, M])
 
             def run():
                 ps = alloc() if i == i0 else bank["p", i0]
                 for j in range(4):
                     T.matmul(ps[:, i - i0], lhsT=flux_grp[i // 4][:, i % 4, :, j], rhs=nusf_t[:, j], start=(j == 0), stop=(j == 3))
-            return step(run, (free if i == i0 else []) + [("fg", i // 2), "nusf_t"], [("p", i0)] if i == i0 + 3 else [])
+            return run, (needs if i == i0 else []) + [("flux_grp", i // 2), "nusf_t"], [("p", i0)] if i == i0 + 3 else []
 
-        def tr_pass(ps, g, c0, gs):
-            for t in range(4):
-                T.matmul_mx(out=ps[:, t], lhsT=kern_codes[:, g, gs, t].bitcast(FP8X4), lhsT_scale=kern_sc[:, g, gs, t],
-                            rhs=q_codes[:, gs, c0:c0 + P].bitcast(FP8X4), rhs_scale=q_sc[:, gs, c0:c0 + P],
-                            start=(gs == 0 and t == 0), stop=(gs == 1 and t == 3))
+        def transport_pass(ps, g, h, c0, gs):
+            for a in range(2):
+                t = 2 * h + a
+                T.matmul_mx(out=ps[:, a], lhsT=kern_codes[:, g, gs, t].bitcast(FP8X4), lhsT_scale=kern_sc[:, g, gs, t],
+                            rhs=q_codes[:, gs, c0:c0 + H].bitcast(FP8X4), rhs_scale=q_sc[:, gs, c0:c0 + H],
+                            start=(gs == 0 and a == 0), stop=(gs == 1 and a == 1))
 
-        def tr0(g, c0, ring):
-            alloc, free = take(ring, ("c", g, c0), [P, 4, P])
-            return step(lambda: tr_pass(alloc(), g, c0, 0), free + [("kq", g, 0), ("qq", 0, c0)], [("c0", g, c0)])
+        def open_unit(unit, ring):
+            g, h, c0 = unit
+            alloc, needs = take(ring, ("c", unit), [P, 2, H])
+            return (lambda: transport_pass(alloc(), g, h, c0, 0)), needs + [("kern_q", g, 0)] + cols("q_q", 0, c0, H), [("open", unit)]
 
-        def tr1(g, c0):
-            return step(lambda: tr_pass(bank["c", g, c0], g, c0, 1), [("c0", g, c0), ("kq", g, 1), ("qq", 1, c0)], [("c", g, c0)])
+        def close_unit(unit):
+            g, h, c0 = unit
+            return (lambda: transport_pass(bank["c", unit], g, h, c0, 1)), [("open", unit), ("kern_q", g, 1)] + cols("q_q", 1, c0, H), [("c", unit)]
 
-        def t_scat(m, c0, ring):
-            alloc, free = take(ring, ("scat", m, c0), [P, H, 4], BF16)
+        def c_dens():
+            return (lambda: S.copy(out=dens_t[:], in_=bank["dens"][:])), ["dens"], ["dens_t", ("read", "dens")]
 
-            def run():
-                ps = alloc()
-                for b0 in (0, P):
-                    T.matmul(ps[:, b0:b0 + P], lhsT=id16[:], rhs=scat_raw[m][:, :, c0 + b0:c0 + b0 + P].rearrange("p t n -> p n t"), start=True, stop=True)
-            return step(run, free + ["id16"], [("scat", m, c0)])
+        def c_nusf():
+            return (lambda: S.copy(out=nusf_t[:], in_=bank["nusf"][:, :, 0:M])), ["nusf"], ["nusf_t", ("read", "nusf")]
 
-        def c_scat(m, c0, eng):
-            return step(lambda: move(eng, scat_grp[m][:, c0:c0 + H], bank["scat", m, c0][:]), [("scat", m, c0)], cols("sg", ("s", m), c0, H) + [("read", ("scat", m, c0))])
+        def c_chi():
+            return (lambda: S.copy(out=chi_b[:], in_=bank["chi"][:])), ["chi"], ["chi_b", ("read", "chi")]
 
-        def t_nusf(ring):
-            alloc, free = take(ring, "nusf", [P, 4, P], BF16)
-
-            def run():
-                ps = alloc()
-                for j in range(4):
-                    T.transpose(ps[:, j], pad_nu[:, j:G:4], id16[:])
-            return step(run, free, ["nusf"])
-
-        def c_nusf(eng):
-            return step(lambda: move(eng, nusf_t[:], bank["nusf"][:, :, 0:M]), ["nusf"], ["nusf_t", ("read", "nusf")])
-
-        def t_chi(ring):
-            alloc, free = take(ring, "chi", [P, G], BF16)
-            return step(lambda: T.matmul(alloc()[:], lhsT=id16[:, 0:1].to_broadcast([P, P]), rhs=pad_chi[:], start=True, stop=True), free, ["chi"])
-
-        def c_chi(eng):
-            return step(lambda: move(eng, chi_b[:], bank["chi"][:]), ["chi"], ["chi_b", ("read", "chi")])
-
-        def c_dens(eng):
-            return step(lambda: move(eng, dens_t[:], bank["dens"][:]), ["dens"], ["dens_t", ("read", "dens")])
-
-        def c_flux(b, eng):
+        def c_flux(b):
             a0 = 2 * (b % 2)
             dst = flux_grp[b // 2][:, a0:a0 + 2].rearrange("p a r f -> p a (r f)").bitcast(F32).rearrange("p a (r u) -> p a r u", u=2)
-            return step(lambda: move(eng, dst, bank["flux", b][:].rearrange("p a u r -> p a r u")), [("flux", b)], [("fg", b), ("read", ("flux", b))])
+            return (lambda: S.copy(out=dst, in_=bank["flux", b][:].rearrange("p a u r -> p a r u"))), [("flux", b)], [("flux_grp", b), ("read", ("flux", b))]
 
-        def c_kern(i, eng):
+        def c_kern(i):
             dst = kern_grp[i // 4][:, :, i % 4].rearrange("p k r f -> p k (r f)").bitcast(F32).rearrange("p k (r u) -> p k r u", u=2)
-            return step(lambda: move(eng, dst, bank["kern", i][:].rearrange("p k u r -> p k r u")), [("kern", i)], [("kg", i), ("read", ("kern", i))])
+            return (lambda: S.copy(out=dst, in_=bank["kern", i][:].rearrange("p k u r -> p k r u"))), [("kern", i)], [("kern_grp", i), ("read", ("kern", i))]
 
-        def ars(i):
-            return step(lambda: S.activation(out=rst[i // 4][:, i % 4], in_=bank["st", i][:], func=ACT.Abs_reciprocal_sqrt), [("st", i)], [("w", i)])
+        def weigh_first(i):
+            def run():
+                S.activation(out=x[i // 4][:, i % 4], in_=bank["a", i, 0][:], func=ACT.Copy, scale=dens32[:, i, 0:1])
+            return run, [("a", i, 0)], [("x", i, 0), ("read", ("a", i, 0))]
 
-        def sgn(i):
-            return step(lambda: S.activation(out=sg[i][:], in_=bank["st", i][:], func=ACT.Sign), [("w", i)], [("sg", i), ("read", ("st", i))])
+        def root(i):
+            return (lambda: S.activation(out=rst[i // 4][:, i % 4], in_=bank["st", i][:], func=ACT.Abs_reciprocal_sqrt)), [("st", i)], [("root", i)]
 
-        def sqr(i):
+        def sign(i):
+            return (lambda: S.activation(out=sg[:, i], in_=bank["st", i][:], func=ACT.Sign)), [("root", i)], [("sign", i), ("read", ("st", i))]
+
+        def square(i):
             r = rst[i // 4][:, i % 4]
-            return step(lambda: S.activation(out=r, in_=r, func=ACT.Square), [("w", i)], [("r", i)])
+            return (lambda: S.activation(out=r, in_=r, func=ACT.Square)), [("root", i)], [("size", i)]
 
-        def inv(i):
-            return [ars(i), sgn(i), sqr(i)]
+        def inverse(i):
+            return [root(i), sign(i), square(i)]
 
-        def rmul(i, eng, c0=0, w=G):
-            r = rst[i // 4][:, i % 4, c0:c0 + w]
-
-            def run():
-                if i < 4:
-                    dst = r
-                else:
-                    h = (i - 4) // 2
-                    if h not in inv_hi:
-                        inv_hi[h] = keep.tile([P, 2, G], F32, align_bytes=64, name="inv_hi%d" % h, tag="late%d" % h)
-                    dst = inv_hi[h][:, i % 2, c0:c0 + w]
-                eng.tensor_tensor(out=dst, in0=r, in1=sg[i][:, c0:c0 + w], op=ALU.mult)
-            return step(run, [("r", i), ("sg", i)] + ([("kq", (i - 4) // 2, 1)] if i >= 4 else []), cols("rst", i, c0, w))
-
-        def fchi(i, eng, dst):
+        def f_chi(i, eng):
             def run():
                 if eng is S:
-                    S.activation(out=dst[i // 4][:, i % 4], in_=chi_b[:], func=ACT.Copy, scale=f[:, i:i + 1])
+                    S.activation(out=fx[i // 4][:, i % 4], in_=chi_b[:], func=ACT.Copy, scale=f[:, i:i + 1])
                 else:
-                    eng.tensor_scalar(out=dst[i // 4][:, i % 4], in0=chi_b[:], scalar1=f[:, i:i + 1], scalar2=0.0, op0=ALU.mult, op1=ALU.add)
-            return step(run, [("f", i), "chi_b"], [("fx", i)] if dst is fx else cols(("x", -1), i, 0, G))
+                    GP.tensor_scalar(out=fx[i // 4][:, i % 4], in0=chi_b[:], scalar1=f[:, i:i + 1], scalar2=0.0, op0=ALU.mult, op1=ALU.add)
+            return run, [("f", i), "chi_b"], [("fx", i)]
 
-        def x0(i, eng):
-            def run():
-                if eng is S:
-                    S.activation(out=x[i // 4][:, i % 4], in_=bank["a", i, 0, 0][:], func=ACT.Copy, scale=dens32[:, i, 0:1])
-                else:
-                    V.tensor_scalar(out=x[i // 4][:, i % 4], in0=bank["a", i, 0, 0][:], scalar1=dens32[:, i, 0:1], scalar2=None, op0=ALU.mult)
-            return step(run, [("a", i, 0, 0), "dens32"], cols(("x", 0), i, 0, G) + [("read", ("a", i, 0, 0))])
-
-        def s_int(m, c0, w, eng):
-            return step(lambda: weave(eng, scat_grp[m][:, c0:c0 + w], scat_raw[m][:, :, c0:c0 + w]), [("sq", 2)] if m == 3 else [], cols("sg", ("s", m), c0, w))
-
-        def q_int(g, c0, w, eng):
-            needs = [k for i in range(4 * g, 4 * g + 4) for k in cols(("x", 3), i, c0, w)]
-            return step(lambda: weave(eng, q_grp[:, g, c0:c0 + w], x[g][:, :, c0:c0 + w]), needs, cols("qg", g, c0, w))
-
-        def q_add(g, c0, w, eng):
-            needs = [k for i in range(4 * g, 4 * g + 4) for k in cols(("x", 3), i, c0, w) + [("fx", i)]]
+        def signed(i, c0=0, w=G):
+            r = rst[i // 4][:, i % 4:i % 4 + 2, c0:c0 + w]
+            h = (i - 4) // 2
 
             def run():
-                if eng is V:
-                    dst, a = blocks(q_grp[:, g, c0:c0 + w], x[g][:, :, c0:c0 + w])
-                    b = fx[g][:, :, c0:c0 + w].rearrange("p t (c i) -> p c t i", i=4)
-                else:
-                    dst = q_grp[:, g, c0:c0 + w]
-                    a = x[g][:, :, c0:c0 + w].rearrange("p t n -> p n t")
-                    b = fx[g][:, :, c0:c0 + w].rearrange("p t n -> p n t")
-                eng.tensor_tensor(out=dst, in0=a, in1=b, op=ALU.add)
-            return step(run, needs, cols("qg", g, c0, w))
+                if i >= 4 and h not in inv_hi:
+                    inv_hi[h] = shared("inv_hi", h, [P, 2, G], F32)
+                dst = inv_hi[h][:, :, c0:c0 + w] if i >= 4 else r
+                GP.tensor_tensor(out=dst, in0=r, in1=sg[:, i:i + 2, c0:c0 + w], op=ALU.mult)
+            needs = [(k, j) for k in ("size", "sign") for j in (i, i + 1)] + ([("kern_q", h, 1)] if i >= 4 else [])
+            return run, needs, cols("inv", i, c0, w) + cols("inv", i + 1, c0, w)
 
-        def r_int(g, c0, w, eng):
-            return step(lambda: weave(eng, r_grp[:, g, c0:c0 + w], res[g][:, :, c0:c0 + w]), cols("res", g, c0, w), cols("rg", g, c0, w))
+        def weave_scat(m, c0, w, eng):
+            return (lambda: weave(eng, scat_grp[m][:, c0:c0 + w], scat_raw[m][:, :, c0:c0 + w])), [("scat_q", 2)] if m == 3 else [], cols("scat_grp", m, c0, w)
 
-        def q_scat(m):
-            return step(lambda: V.quantize_mx(out=scat_codes[:, m].bitcast(FP8X4), scales=scat_sc[:, m], in_=scat_grp[m][:].rearrange("p n j -> p (n j)")),
-                        cols("sg", ("s", m), 0, G), [("sq", m)])
+        def weave_res(g, c0, eng):
+            needs = cols(("res", 0), g, c0, P) + cols(("res", 1), g, c0, P)
+            return (lambda: weave(eng, r_grp[:, g, c0:c0 + P], res[g][:, :, c0:c0 + P])), needs, cols("r_grp", g, c0, P)
 
-        def q_flux(i0, n):
-            return step(lambda: V.quantize_mx(out=flux_codes[:, i0:i0 + n].rearrange("p a r -> p (a r)").bitcast(FP8X4),
-                                              scales=flux_sc[:, i0:i0 + n].rearrange("p a r -> p (a r)"),
-                                              in_=flux_grp[i0 // 4][:, i0 % 4:i0 % 4 + n].rearrange("p a r f -> p (a r f)")),
-                        [("fg", i // 2) for i in range(i0, i0 + n)], [("fq", i) for i in range(i0, i0 + n)])
-
-        def q_kern(g, k0, n):
-            return step(lambda: V.quantize_mx(out=kern_codes[:, g, k0:k0 + n].rearrange("p k t r -> p (k t r)").bitcast(FP8X4),
-                                              scales=kern_sc[:, g, k0:k0 + n].rearrange("p k t r -> p (k t r)"),
-                                              in_=kern_grp[g][:, k0:k0 + n].rearrange("p k t r f -> p (k t r f)")),
-                        [("kg", i) for i in range(4 * g, 4 * g + 4)], [("kq", g, k) for k in range(k0, k0 + n)])
-
-        def stt(i, m, c0=0, w=G):
-            xi = x[i // 4][:, i % 4, c0:c0 + w]
-            return step(lambda: V.scalar_tensor_tensor(out=xi, in0=bank["a", i, m, 0][:, c0:c0 + w], scalar=dens32[:, i, m:m + 1], in1=xi, op0=ALU.mult, op1=ALU.add),
-                        [("a", i, m, 0)] + cols(("x", m - 1), i, c0, w), cols(("x", m), i, c0, w) + ([("read", ("a", i, m, 0))] if c0 + w == G else []))
-
-        def f_mul(i0, n):
-            return step(lambda: V.tensor_tensor(out=pd[:, i0:i0 + n], in0=bank["p", i0][:], in1=dens32[:, i0:i0 + n], op=ALU.mult),
-                        [("p", i0), "dens32"], [("pd", i) for i in range(i0, i0 + n)] + [("read", ("p", i0))])
-
-        def f_sum(i0, n):
-            return step(lambda: V.tensor_reduce(out=f[:, i0:i0 + n], in_=pd[:, i0:i0 + n], axis=AX.X, op=ALU.add), [("pd", i) for i in range(i0, i0 + n)], [("f", i) for i in range(i0, i0 + n)])
-
-        def q_q(g, c0, w):
-            return step(lambda: V.quantize_mx(out=q_codes[:, g, c0:c0 + w].bitcast(FP8X4), scales=q_sc[:, g, c0:c0 + w],
-                                              in_=q_grp[:, g, c0:c0 + w].rearrange("p n t -> p (n t)")), cols("qg", g, c0, w), cols("qq", g, c0, w))
-
-        def out(g, c0):
+        def quant_scat(m):
             def run():
-                if g == 0:
-                    V.tensor_tensor(out=res[g][:, :, c0:c0 + P], in0=bank["c", g, c0][:], in1=rst[g][:, :, c0:c0 + P], op=ALU.mult)
-                else:
-                    for h in range(2):
-                        V.tensor_tensor(out=res[g][:, 2 * h:2 * h + 2, c0:c0 + P], in0=bank["c", g, c0][:, 2 * h:2 * h + 2], in1=inv_hi[h][:, :, c0:c0 + P], op=ALU.mult)
-            return step(run, [("c", g, c0)] + [("rst", i, c0) for i in range(4 * g, 4 * g + 4)], [("res", g, c0), ("read", ("c", g, c0))])
+                V.quantize_mx(out=scat_codes[:, m].bitcast(FP8X4), scales=scat_sc[:, m], in_=scat_grp[m][:].rearrange("p n j -> p (n j)"))
+            return run, cols("scat_grp", m, 0, G), [("scat_q", m)]
 
-        def q_r(g, c0, w):
-            return step(lambda: V.quantize_mx(out=r_codes[:, g, c0:c0 + w].bitcast(FP8X4), scales=r_sc[4 * g:P, c0:c0 + w],
-                                              in_=r_grp[:, g, c0:c0 + w].rearrange("p n t -> p (n t)")), cols("rg", g, c0, w), cols("rq", g, c0, w))
+        def quant_flux(i0, n):
+            def run():
+                V.quantize_mx(out=flux_codes[:, i0:i0 + n].rearrange("p a r -> p (a r)").bitcast(FP8X4),
+                              scales=flux_sc[:, i0:i0 + n].rearrange("p a r -> p (a r)"),
+                              in_=flux_grp[i0 // 4][:, i0 % 4:i0 % 4 + n].rearrange("p a r f -> p (a r f)"))
+            return run, [("flux_grp", i // 2) for i in range(i0, i0 + n)], [("flux_q", i) for i in range(i0, i0 + n)]
 
-        def store(g, c0, w):
-            return step(lambda: nc.sync.dma_start(out=out0_v[g, :, :, c0:c0 + w], in_=res[g][:, :, c0:c0 + w]), cols("res", g, c0, w), [])
+        def quant_kern(g, k0, n):
+            def run():
+                V.quantize_mx(out=kern_codes[:, g, k0:k0 + n].rearrange("p k t r -> p (k t r)").bitcast(FP8X4),
+                              scales=kern_sc[:, g, k0:k0 + n].rearrange("p k t r -> p (k t r)"),
+                              in_=kern_grp[g][:, k0:k0 + n].rearrange("p k t r f -> p (k t r f)"))
+            return run, [("kern_grp", i) for i in range(4 * g, 4 * g + 4)], [("kern_q", g, k) for k in range(k0, k0 + n)]
 
-        def store_w(g, c0, w):
-            return step(lambda: nc.sync.dma_start(out=out1_v[g, :, c0:c0 + w], in_=r_codes[:, g, c0:c0 + w].bitcast(I32)), cols("rq", g, c0, w), [])
+        def quant_q(g, c0):
+            def run():
+                V.quantize_mx(out=q_codes[:, g, c0:c0 + H].bitcast(FP8X4), scales=q_sc[:, g, c0:c0 + H],
+                              in_=q_grp[:, g, c0:c0 + H].rearrange("p n t -> p (n t)"))
+            return run, cols("q_grp", g, c0, H), cols("q_q", g, c0, H)
 
-        def store_s(k, eng):
-            return step(lambda: eng.dma_start(out=out2_v[:, 4 * k:4 * k + 4, :], in_=r_sc[32 * k:32 * k + 8, :].bitcast(I32)), cols("rq", 0, 0, G) + cols("rq", 1, 0, G), [])
+        def quant_res(g, c0, w):
+            def run():
+                V.quantize_mx(out=r_codes[:, g, c0:c0 + w].bitcast(FP8X4), scales=r_sc[4 * g:P, c0:c0 + w],
+                              in_=r_grp[:, g, c0:c0 + w].rearrange("p n t -> p (n t)"))
+            return run, cols("r_grp", g, c0, w), cols("r_q", g, c0, w)
 
-        def load_scat(m):
-            nc.sync.dma_start(out=scat_raw[m][:], in_=scat[m].rearrange("(p j) n -> p j n", j=4))
+        def weigh_add(i, m):
+            xi = x[i // 4][:, i % 4]
 
-        def load_flux(b):
-            nc.sync.dma_start(out=flux_raw[b][:], in_=flux_v[b // 2, :, 2 * (b % 2):2 * (b % 2) + 2])
+            def run():
+                V.scalar_tensor_tensor(out=xi, in0=bank["a", i, m][:], scalar=dens32[:, i, m:m + 1], in1=xi, op0=ALU.mult, op1=ALU.add)
+            return run, [("a", i, m), ("x", i, m - 1)], [("x", i, m), ("read", ("a", i, m))]
 
-        def load_kern(g):
-            nc.sync.dma_start(out=kern_raw[g][:], in_=kern_v[g])
+        def f_weigh(g):
+            def run():
+                V.tensor_tensor(out=pd[:, 4 * g:4 * g + 4], in0=bank["p", 4 * g][:], in1=dens32[:, 4 * g:4 * g + 4], op=ALU.mult)
+            return run, [("p", 4 * g)], [("pd", g), ("read", ("p", 4 * g))]
 
-        def load_small():
-            nc.scalar.dma_start(out=dens_sb[:], in_=dens.rearrange("(g p t) m -> p g (t m)", g=2, t=4))
+        def f_sum(g):
+            def run():
+                V.tensor_reduce(out=f[:, 4 * g:4 * g + 4], in_=pd[:, 4 * g:4 * g + 4], axis=AX.X, op=ALU.add)
+            return run, [("pd", g)], [("f", i) for i in range(4 * g, 4 * g + 4)]
 
-        def setup():
-            for t in (pad, pad_nu, pad_chi):
-                V.memset(t[:], 0.0)
-            nc.scalar.dma_start(out=pad[0:M], in_=sigt)
-            nc.scalar.dma_start(out=pad_chi[0:1], in_=chi.rearrange("(o g) -> o g", o=1))
-            nc.scalar.dma_start(out=pad_nu[0:M], in_=nusf)
-            V.memset(warm[:], 1.0)
-            S.activation(out=warm[:, 1:2], in_=warm[:, 0:1], func=ACT.Abs_reciprocal_sqrt)
-            make_identity(nc, id32[:])
-            V.memset(dens_pad[:], 0.0)
-            V.tensor_copy(out=id16[:], in_=id32[:])
-            V.tensor_copy(out=dens_pad[:, :, 0:M], in_=dens_v)
-            V.tensor_copy(out=dens32[:], in_=dens_v)
+        def source(g, c0):
+            def run():
+                dst, s = blocks(q_grp[:, g, c0:c0 + H], x[g][:, :, c0:c0 + H])
+                V.tensor_tensor(out=dst, in0=s, in1=fx[g][:, :, c0:c0 + H].rearrange("p t (c i) -> p c t i", i=4), op=ALU.add)
+            return run, [k for i in range(4 * g, 4 * g + 4) for k in (("x", i, M - 1), ("fx", i))], cols("q_grp", g, c0, H)
+
+        def divide(unit):
+            g, h, c0 = unit
+
+            def run():
+                inv = inv_hi[h][:, :, c0:c0 + H] if g else rst[0][:, 2 * h:2 * h + 2, c0:c0 + H]
+                V.tensor_tensor(out=res[g][:, 2 * h:2 * h + 2, c0:c0 + H], in0=bank["c", unit][:], in1=inv, op=ALU.mult)
+            needs = [k for i in (4 * g + 2 * h, 4 * g + 2 * h + 1) for k in cols("inv", i, c0, H)]
+            return run, [("c", unit)] + needs, cols(("res", h), g, c0, H) + [("read", ("c", unit))]
+
+        def store(unit):
+            g, h, c0 = unit
+            return (lambda: SP.dma_start(out=out0_v[g, :, 2 * h:2 * h + 2, c0:c0 + H], in_=res[g][:, 2 * h:2 * h + 2, c0:c0 + H])), cols(("res", h), g, c0, H), []
+
+        def store_codes(g, c0, w):
+            return (lambda: SP.dma_start(out=out1_v[g, :, c0:c0 + w], in_=r_codes[:, g, c0:c0 + w].bitcast(I32))), cols("r_q", g, c0, w), []
+
+        def store_scales(k, eng):
+            def run():
+                eng.dma_start(out=out2_v[:, 4 * k:4 * k + 4, :], in_=r_sc[32 * k:32 * k + 8, :].bitcast(I32))
+            return run, cols("r_q", 0, 0, G) + cols("r_q", 1, 0, G), []
 
         def emit(queues):
-            have = {"id32", "id16", "dens_pad", "pad", "dens32"}
+            have = set()
+            turn = {ring: [] for ring in BANKS}
             for run, needs, gives in queues[0]:
                 for k in [k for k in needs if k[0] == "bank"]:
                     needs.remove(k)
                     turn[k[1]].append(k[2])
-                    needs.extend(("read", b) for b in turn[k[1]][-1 - rings[k[1]]:-rings[k[1]]])
+                    needs.extend(("read", b) for b in turn[k[1]][-1 - BANKS[k[1]]:-BANKS[k[1]]])
             at = [0] * len(queues)
-            while any(at[e] < len(qu) for e, qu in enumerate(queues)):
-                moved = False
-                for e, qu in enumerate(queues):
-                    while at[e] < len(qu) and all(k in have for k in qu[at[e]][1]):
-                        qu[at[e]][0]()
-                        for k in qu[at[e]][2]:
+            while any(at[e] < len(queue) for e, queue in enumerate(queues)):
+                for e, queue in enumerate(queues):
+                    while at[e] < len(queue) and all(k in have for k in queue[at[e]][1]):
+                        queue[at[e]][0]()
+                        for k in queue[at[e]][2]:
                             have.add(k)
                         at[e] = at[e] + 1
-                        moved = True
-                assert moved, [[k for k in qu[at[e]][1] if k not in have] for e, qu in enumerate(queues) if at[e] < len(qu)]
 
-        load_small()
-        load_scat(0)
-        load_flux(0)
-        load_scat(1)
-        for b in range(1, 4):
-            load_flux(b)
-        load_scat(2)
-        load_scat(3)
-        load_kern(0)
-        load_kern(1)
-        setup()
-        Y = nc.sync
-        lo, hi = range(4), range(4, 8)
-        qt = [t_dens(), t_flux(0, "tp"), t_chi("mm"), st(0), t_flux(1, "tp"), mx(0, 0), mx(1, 0), t_flux(2, "tp"), t_flux(3, "tp"), mx(0, 1), mx(2, 0), mx(3, 0), st(1), t_nusf("tp")]
-        qt += [mx(1, 1), mx(4, 0), mx(2, 1), mx(5, 0), mx(3, 1), mx(6, 0), fis(0), mx(0, 2), mx(7, 0), fis(1)]
-        slots = [(i, 2) for i in (1, 2, 3)] + [(i, 1) for i in hi] + [(i, 3) for i in lo] + [(i, 2) for i in hi]
-        side = [[fis(2)], [fis(3)], [st(2)], [fis(4)], [fis(5), st(3)], [fis(6)], [fis(7)], [st(4)], [t_kern(0)], [], [t_kern(1)], [st(5)], [], [], []]
-        for k, (i, m) in enumerate(slots):
-            qt += [mx(i, m)] + side[k]
-        qt += [mx(4, 3), mx(5, 3), t_kern(2), t_kern(3), mx(6, 3), mx(7, 3), t_kern(4), t_kern(5), st(6), t_kern(6), t_kern(7), st(7)]
-        qt += [tr0(0, 0, "mm"), tr0(0, P, "mm"), tr0(0, H, "mm"), tr0(0, H + P, "mm"), tr0(1, 0, "tp"), tr1(0, 0), tr1(0, P), tr0(1, P, "tp"), tr1(0, H), tr1(0, H + P)]
-        qt += [tr1(1, 0), tr1(1, P), tr0(1, H, "mm"), tr1(1, H), tr0(1, H + P, "mm"), tr1(1, H + P)]
+        for t in (sig_pad, nu_pad, chi_pad):
+            V.memset(t[:], 0.0)
+        S.dma_start(out=dens_sb[:], in_=dens.rearrange("(g p t) m -> p g (t m)", g=2, t=4))
+        S.dma_start(out=sig_pad[0:M], in_=sigt)
 
-        qv = [s_int(0, 0, G, V), s_int(1, 0, H, V), q_scat(0), q_flux(0, 2), s_int(1, H, H, V), q_scat(1), q_flux(2, 2), s_int(2, 0, G, V), stt(0, 1), q_flux(4, 4), q_scat(2)]
-        qv += [stt(i, 1) for i in (1, 2, 3)] + [stt(i, 2) for i in lo] + [f_mul(0, 4), q_scat(3), f_sum(0, 4)] + [stt(i, 1) for i in hi]
-        qv += [stt(0, 3), f_mul(4, 4), stt(1, 3), f_sum(4, 4), stt(2, 3), stt(3, 3)] + [stt(i, 2) for i in hi]
-        qv += [q_add(0, 0, H, V), q_add(0, H, H, V), q_q(0, 0, H), q_q(0, H, H), q_kern(0, 0, 2)] + [stt(i, 3) for i in hi]
-        qv += [q_add(1, 0, H, V), q_kern(1, 0, 1), q_q(1, 0, H), q_add(1, H, H, V), out(0, 0), q_q(1, H, H), q_kern(1, 1, 1), out(0, P), out(0, H), out(0, H + P)]
-        qv += [out(1, 0), out(1, P), out(1, H), q_r(0, 0, G), out(1, H + P), q_r(1, 0, H), r_int(1, H + P, P, V), q_r(1, H, P), q_r(1, H + P, P)]
+        def load_scat(m):
+            SP.dma_start(out=scat_raw[m][:], in_=scat[m].rearrange("(p j) n -> p j n", j=4))
 
-        qs = [c_dens(S), c_flux(0, S), c_chi(S), ars(0), c_flux(1, S), x0(0, S), x0(1, S), c_flux(2, S), c_flux(3, S), x0(2, S), x0(3, S), c_nusf(S), sgn(0)]
-        qs += [x0(i, S) for i in hi] + [sqr(0)] + inv(1) + inv(2) + inv(3) + [fchi(3, S, fx), c_kern(0, S), ars(4), sgn(4), c_kern(1, S), fchi(4, S, fx), fchi(5, S, fx), ars(5), sgn(5)]
-        qs += [c_kern(2, S), c_kern(3, S), fchi(6, S, fx), c_kern(4, S), sqr(4), c_kern(5, S), sqr(5), fchi(7, S, fx), c_kern(6, S), c_kern(7, S)] + inv(6) + inv(7)
-        qs += [r_int(g, c, P, S) for g in range(2) for c in range(0, G, P)][:7] + [store_s(1, S), store_s(3, S)]
+        def load_flux(b):
+            SP.dma_start(out=flux_raw[b][:], in_=flux_v[b // 2, :, 2 * (b % 2):2 * (b % 2) + 2])
 
-        qg = [s_int(3, c, P, GP) for c in range(0, G, P)] + [fchi(i, GP, fx) for i in range(3)] + [rmul(i, GP) for i in range(6)] + [rmul(i, GP, c, H) for c in (0, H) for i in (6, 7)]
-        qy = [store(0, 0, P), store(0, P, P), store(0, H, H), store(1, 0, H), store(1, H, P), store_w(0, 0, G), store(1, H + P, P), store_w(1, 0, H), store_w(1, H, H), store_s(0, Y), store_s(2, Y)]
+        for k in range(2):
+            load_scat(k)
+            load_flux(k)
+        SP.dma_start(out=nu_pad[0:M], in_=nusf)
+        SP.dma_start(out=chi_pad[0:1], in_=chi.rearrange("(o g) -> o g", o=1))
+        for k in (2, 3):
+            load_flux(k)
+        for k in (2, 3):
+            load_scat(k)
+        for g in range(2):
+            SP.dma_start(out=kern_raw[g][:], in_=kern_v[g])
+
+        V.memset(warm[:], 1.0)
+        S.activation(out=warm[:, 1:2], in_=warm[:, 0:1], func=ACT.Abs_reciprocal_sqrt)
+        make_identity(nc, id32[:])
+        V.memset(dens_pad[:], 0.0)
+        V.tensor_copy(out=id16[:], in_=id32[:])
+        V.tensor_copy(out=dens_pad[:, :, 0:M], in_=dens_v)
+        V.tensor_copy(out=dens32[:], in_=dens_v)
+
+        lo, hi = range(4), range(4, NT)
+        units = [(g, h, c0) for g in range(2) for c0 in (0, H) for h in range(2)]
+
+        qt = [t_dens(), t_flux(0), total(0), total(1), t_flux(1), scatter(0, 0), scatter(1, 0), t_flux(2), t_flux(3)]
+        qt += [scatter(0, 1), scatter(2, 0), scatter(3, 0), t_nusf(), spread_chi()]
+        qt += [scatter(1, 1), scatter(4, 0), scatter(2, 1), scatter(5, 0), scatter(3, 1), scatter(6, 0), fission(0), scatter(0, 2), scatter(7, 0), fission(1)]
+        passes = [(i, 2) for i in lo[1:]] + [(i, 1) for i in hi] + [(i, 3) for i in lo] + [(i, 2) for i in hi]
+        side = [fission(2), fission(3), total(2), fission(4), fission(5), total(3), fission(6), fission(7), total(4), t_kern(0), t_kern(1), total(5)]
+        for k, (i, m) in enumerate(passes):
+            qt += [scatter(i, m)] + side[k:k + 1]
+        qt += [scatter(4, 3), scatter(5, 3), t_kern(2), t_kern(3), scatter(6, 3), scatter(7, 3), t_kern(4), t_kern(5), total(6), t_kern(6), t_kern(7), total(7)]
+        qt += [open_unit(u, "mm") for u in units[:4]] + [open_unit(units[4], "tp"), close_unit(units[0]), close_unit(units[1]), open_unit(units[5], "tp")]
+        qt += [close_unit(u) for u in units[2:6]]
+        for u in units[6:]:
+            qt += [open_unit(u, "mm"), close_unit(u)]
+
+        qv = [weave_scat(0, 0, G, V), quant_scat(0), weave_scat(1, 0, H, V), quant_flux(0, 2), weave_scat(1, H, H, V), quant_scat(1)]
+        qv += [weave_scat(2, 0, H, V), quant_flux(2, 2), weave_scat(2, H, H, V), weigh_add(0, 1), quant_flux(4, 4), quant_scat(2)]
+        qv += [weigh_add(i, 1) for i in lo[1:]] + [weigh_add(i, 2) for i in lo] + [f_weigh(0), quant_scat(3), f_sum(0)]
+        qv += [weigh_add(i, 1) for i in hi] + [weigh_add(0, 3), f_weigh(1), weigh_add(1, 3), f_sum(1), weigh_add(2, 3), weigh_add(3, 3)]
+        qv += [weigh_add(i, 2) for i in hi]
+        qv += [source(0, 0), source(0, H), quant_q(0, 0), quant_q(0, H), quant_kern(0, 0, 2)] + [weigh_add(i, 3) for i in hi]
+        qv += [source(1, 0), quant_kern(1, 0, 1), quant_q(1, 0), source(1, H), divide(units[0]), quant_q(1, H), divide(units[1]), quant_kern(1, 1, 1)]
+        qv += [divide(u) for u in units[2:7]] + [quant_res(0, 0, G), divide(units[7]), quant_res(1, 0, H)]
+        qv += [weave_res(1, H + P, V), quant_res(1, H + P, P), quant_res(1, H, P)]
+
+        qs = [c_dens(), c_flux(0), root(0), sign(0), c_flux(1), weigh_first(0), weigh_first(1), c_flux(2), c_flux(3), weigh_first(2), weigh_first(3)]
+        qs += [c_nusf(), c_chi()] + [weigh_first(i) for i in hi] + [square(0)] + inverse(1) + inverse(2) + inverse(3)
+        qs += [f_chi(i, S) for i in lo[F_ON_GPSIMD:]] + [c_kern(0)] + inverse(4) + [c_kern(1)] + inverse(5)
+        for i in (2, 4):
+            qs += [c_kern(i), c_kern(i + 1), f_chi(i + 2, S), f_chi(i + 3, S)]
+        qs += [c_kern(6), c_kern(7)] + inverse(6) + inverse(7)
+        qs += [weave_res(g, c, S) for g in range(2) for c in range(0, G, P)][:-1] + [store_scales(1, S), store_scales(3, S)]
+
+        qg = [weave_scat(3, 0, G, GP)] + [f_chi(i, GP) for i in lo[:F_ON_GPSIMD]] + [signed(0), signed(2), signed(4), signed(6, 0, H), signed(6, H, H)]
+
+        qy = [store(u) for u in units[:7]] + [store_codes(0, 0, G), store(units[7]), store_codes(1, 0, H), store_codes(1, H, H)]
+        qy += [store_scales(0, SP), store_scales(2, SP)]
         emit([qt, qv, qs, qg, qy])

@@ -142,7 +142,7 @@ def tile_multigroupintegraltransportsourceiterati_x1_kernel(tc, flux, scat, dens
             return run, needs, [("kern", i)]
 
         def t_nusf():
-            alloc, needs = take("tp", "nusf", [P, 4, P], BF16)
+            alloc, needs = take("mm", "nusf", [P, 4, P], BF16)
 
             def run():
                 ps = alloc()
@@ -381,13 +381,14 @@ def tile_multigroupintegraltransportsourceiterati_x1_kernel(tc, flux, scat, dens
         lo, hi = range(4), range(4, NT)
         units = [(g, h, c0) for g in range(2) for c0 in (0, H) for h in range(2)]
 
-        qt = [t_dens(), t_flux(0), total(0), total(1), t_flux(1), scatter(0, 0), scatter(1, 0), t_flux(2), t_flux(3)]
-        qt += [scatter(0, 1), scatter(2, 0), scatter(3, 0), t_nusf(), spread_chi()]
-        qt += [scatter(1, 1), scatter(4, 0), scatter(2, 1), scatter(5, 0), scatter(3, 1), scatter(6, 0), fission(0), scatter(0, 2), scatter(7, 0), fission(1)]
+        qt = [t_dens(), t_flux(0), total(0), total(1), t_flux(1), t_nusf(), scatter(0, 0), scatter(1, 0), t_flux(2), t_flux(3)]
+        qt += [scatter(0, 1), scatter(2, 0), scatter(3, 0), scatter(1, 1), spread_chi()] + [fission(i) for i in lo[:2]]
+        qt += [scatter(4, 0), scatter(2, 1), scatter(5, 0), scatter(3, 1), scatter(6, 0), scatter(0, 2), scatter(7, 0)]
         passes = [(i, 2) for i in lo[1:]] + [(i, 1) for i in hi] + [(i, 3) for i in lo] + [(i, 2) for i in hi]
-        side = [fission(2), fission(3), total(2), fission(4), fission(5), total(3), fission(6), fission(7), total(4), t_kern(0), t_kern(1), total(5)]
-        for k, (i, m) in enumerate(passes):
-            qt += [scatter(i, m)] + side[k:k + 1]
+        pairs = [[fission(2), fission(3)], [None, t_kern(0)], [None, t_kern(1)], [fission(4), fission(5)], [fission(6), fission(7)]]
+        side = [w for k, pair in enumerate(pairs) for w in pair + [total(2 + k) if k < 4 else None]]
+        for (i, m), w in zip(passes, side):
+            qt += [scatter(i, m)] + ([w] if w else [])
         qt += [scatter(4, 3), scatter(5, 3), t_kern(2), t_kern(3), scatter(6, 3), scatter(7, 3), t_kern(4), t_kern(5), total(6), t_kern(6), t_kern(7), total(7)]
         qt += [open_unit(u, "mm") for u in units[:4]] + [open_unit(units[4], "tp"), close_unit(units[0]), close_unit(units[1]), open_unit(units[5], "tp")]
         qt += [close_unit(u) for u in units[2:6]]
@@ -397,16 +398,16 @@ def tile_multigroupintegraltransportsourceiterati_x1_kernel(tc, flux, scat, dens
         qv = [weave_scat(0, 0, G, V), quant_scat(0), weave_scat(1, 0, H, V), quant_flux(0, 2), weave_scat(1, H, H, V), quant_scat(1)]
         qv += [weave_scat(2, 0, H, V), quant_flux(2, 2), weave_scat(2, H, H, V), weigh_add(0, 1), quant_flux(4, 4), quant_scat(2)]
         qv += [weigh_add(i, 1) for i in lo[1:]] + [weigh_add(i, 2) for i in lo] + [f_weigh(0), quant_scat(3), f_sum(0)]
-        qv += [weigh_add(i, 1) for i in hi] + [weigh_add(0, 3), f_weigh(1), weigh_add(1, 3), f_sum(1), weigh_add(2, 3), weigh_add(3, 3)]
-        qv += [weigh_add(i, 2) for i in hi]
+        qv += [weigh_add(i, 1) for i in hi] + [weigh_add(i, 3) for i in lo]
+        qv += [weigh_add(4, 2), weigh_add(5, 2), weigh_add(6, 2), f_weigh(1), weigh_add(7, 2), f_sum(1)]
         qv += [source(0, 0), source(0, H), quant_q(0, 0), quant_q(0, H), quant_kern(0, 0, 2)] + [weigh_add(i, 3) for i in hi]
         qv += [source(1, 0), quant_kern(1, 0, 1), quant_q(1, 0), source(1, H), divide(units[0]), quant_q(1, H), divide(units[1]), quant_kern(1, 1, 1)]
         qv += [divide(u) for u in units[2:7]] + [quant_res(0, 0, G), divide(units[7]), quant_res(1, 0, H)]
         qv += [weave_res(1, H + P, V), quant_res(1, H + P, P), quant_res(1, H, P)]
 
-        qs = [c_dens(), c_flux(0), root(0), sign(0), c_flux(1), weigh_first(0), weigh_first(1), c_flux(2), c_flux(3), weigh_first(2), weigh_first(3)]
-        qs += [c_nusf(), c_chi()] + [weigh_first(i) for i in hi] + [square(0)] + inverse(1) + inverse(2) + inverse(3)
-        qs += [f_chi(i, S) for i in lo[F_ON_GPSIMD:]] + [c_kern(0)] + inverse(4) + [c_kern(1)] + inverse(5)
+        qs = [c_dens(), c_flux(0), root(0), sign(0), c_flux(1), c_nusf(), weigh_first(0), weigh_first(1), c_flux(2), c_flux(3), weigh_first(2), weigh_first(3)]
+        qs += [c_chi()] + [weigh_first(i) for i in hi] + [square(0)] + inverse(1) + inverse(2) + [c_kern(0)] + inverse(3)
+        qs += [f_chi(i, S) for i in lo[F_ON_GPSIMD:]] + [c_kern(1)] + inverse(4) + inverse(5)
         for i in (2, 4):
             qs += [c_kern(i), c_kern(i + 1), f_chi(i + 2, S), f_chi(i + 3, S)]
         qs += [c_kern(6), c_kern(7)] + inverse(6) + inverse(7)

@@ -17,8 +17,9 @@ P = 128
 R, G, M = 1024, 512, 4
 NT = R // P
 H = G // 2
+CHI_AT, NU_AT = 4, 8
+PIECES = 3
 BANKS = {"mm": 4, "tp": 2, "st": 2}
-F_ON_GPSIMD = 3
 FLOPS = 2 * R * G * G * M + 2 * R * R * G
 
 
@@ -36,15 +37,11 @@ def tile_multigroupintegraltransportsourceiterati_x1_kernel(tc, flux, scat, dens
         def tiles(name, n, shape, dtype):
             return [tile("%s%d" % (name, k), shape, dtype) for k in range(n)]
 
-        def shared(name, h, shape, dtype):
-            return keep.tile(shape, dtype, align_bytes=64, name="%s%d" % (name, h), tag="shared%d" % h)
-
-        nu_pad = tile("nu_pad", [P, G], BF16)
-        chi_pad = tile("chi_pad", [P, G], BF16)
+        rows = tile("rows", [P, G], BF16)
         sig_pad = tile("sig_pad", [P, G], BF16)
         dens_pad = tile("dens_pad", [P, NT, P], BF16)
         dens_sb = tile("dens_sb", [P, 2, 4 * M], BF16)
-        nusf_t = tile("nusf_t", [P, 4, M], BF16)
+        nusf_t = tile("nusf_t", [P, 2, M], F32)
         flux_raw = tiles("flux_raw", 4, [P, 2, G], BF16)
         scat_raw = tiles("scat_raw", M, [P, 4, G], BF16)
         kern_raw = tiles("kern_raw", 2, [P, 4, R], BF16)
@@ -52,25 +49,20 @@ def tile_multigroupintegraltransportsourceiterati_x1_kernel(tc, flux, scat, dens
         id16 = tile("id16", [P, P], BF16)
         dens32 = tile("dens32", [P, NT, M], F32)
         dens_t = tile("dens_t", [P, NT, P], BF16)
+        f_t = tile("f_t", [P, NT, P], BF16)
         flux_grp = tiles("flux_grp", 2, [P, 4, P, 4], BF16)
         flux_codes = tile("flux_codes", [P, NT, P], U32)
         flux_sc = tile("flux_sc", [P, NT, P], U8)
-        chi_b = tile("chi_b", [P, G], BF16)
-        scat_grp = tiles("scat_grp", M - 1, [P, G, 4], BF16)
-        scat_grp.append(scat_grp[2])
         scat_codes = tile("scat_codes", [P, M, G], U32)
         scat_sc = tile("scat_sc", [P, M, G], U8)
         pd = tile("pd", [P, NT, M], F32)
         f = tile("f", [P, NT], F32)
+        f_rest = tile("f_rest", [P, NT], F32)
         x = tiles("x", 2, [P, 4, G], F32)
-        fx = tiles("fx", 2, [P, 4, G], F32)
         sg = tile("sg", [P, NT, G], BF16)
         rst = tiles("rst", 2, [P, 4, G], F32)
-        kern_grp = [shared("kern_grp", g, [P, 2, 4, P, 4], BF16) for g in range(2)]
-        inv_hi = {}
         kern_codes = tile("kern_codes", [P, 2, 2, 4, P], U32)
         kern_sc = tile("kern_sc", [P, 2, 2, 4, P], U8)
-        q_grp = tile("q_grp", [P, 2, G, 4], BF16)
         q_codes = tile("q_codes", [P, 2, G], U32)
         q_sc = tile("q_sc", [P, 2, G], U8)
         res = tiles("res", 2, [P, 4, G], F32)
@@ -79,7 +71,15 @@ def tile_multigroupintegraltransportsourceiterati_x1_kernel(tc, flux, scat, dens
         r_sc = tile("r_sc", [P, G], U8)
         warm = tile("warm", [P, 2], F32)
 
+        held = {}
+
+        def tenant(buffer, name, shape, dtype):
+            if name not in held:
+                held[name] = keep.tile(shape, dtype, align_bytes=64, name=name, tag=buffer)
+            return held[name]
+
         dens_v = dens_sb[:].rearrange("p g (t m) -> p (g t) m", m=M)
+        nusf_k = nusf_t[:].bitcast(BF16).rearrange("p u (m e) -> p u m e", e=2)
         flux_v = flux.rearrange("(g p t) k -> g p t k", g=2, t=4)
         kern_v = kern.rearrange("(g p t) k -> g p t k", g=2, t=4)
         out0_v = out_0.rearrange("(g p t) n -> g p t n", g=2, t=4)
@@ -110,14 +110,31 @@ def tile_multigroupintegraltransportsourceiterati_x1_kernel(tc, flux, scat, dens
                 out, in_ = blocks(dst, src)
                 V.tensor_copy(out=out, in_=in_)
 
-        def t_dens():
-            alloc, needs = take("st", "dens", [P, NT, P], BF16)
+        def scat_grp(m, c0, w):
+            for buffer, b0, bw in SCAT_PIECES[m]:
+                if b0 <= c0 and c0 + w <= b0 + bw:
+                    return tenant(buffer, "scat_grp%d_%d" % (m, b0), [P, bw, 4], BF16)[:, c0 - b0:c0 - b0 + w]
+
+        def kern_grp(g):
+            return tenant("kern%d" % g, "kern_grp%d" % g, [P, 2, 4, P, 4], BF16)
+
+        def q_grp(g):
+            return tenant("q%d" % g, "q_grp%d" % g, [P, G, 4], BF16)
+
+        def inv(i, n):
+            buffer = INV_IN[i // 2]
+            if buffer is None:
+                return rst[i // 4][:, i % 4:i % 4 + n]
+            return tenant(buffer, "inv%d" % (i // 2), [P, 2, G], F32)[:, i % 2:i % 2 + n]
+
+        def t_pad(name, i0, n, ring):
+            alloc, needs = take(ring, (name, i0), [P, n, P], BF16)
 
             def run():
                 ps = alloc()
-                for i in range(NT):
-                    T.transpose(ps[:, i], dens_pad[:, i], id16[:])
-            return run, needs, ["dens"]
+                for i in range(n):
+                    T.transpose(ps[:, i], dens_pad[:, i0 + i], id16[:])
+            return run, needs + ([("pieces", i0 // 4)] if name == "f" else []), [(name, i0)]
 
         def t_flux(b):
             alloc, needs = take("tp", ("flux", b), [P, 2, 2, P])
@@ -142,21 +159,17 @@ def tile_multigroupintegraltransportsourceiterati_x1_kernel(tc, flux, scat, dens
             return run, needs, [("kern", i)]
 
         def t_nusf():
-            alloc, needs = take("mm", "nusf", [P, 4, P], BF16)
+            alloc, needs = take("mm", "nusf", [P, 2, P])
 
             def run():
                 ps = alloc()
-                for j in range(4):
-                    T.transpose(ps[:, j], nu_pad[:, j:G:4], id16[:])
+                for u in range(2):
+                    T.transpose(ps[:, u], rows[:].bitcast(F32)[:, u:H:2], id32[:])
             return run, needs, ["nusf"]
-
-        def spread_chi():
-            alloc, needs = take("tp", "chi", [P, G], BF16)
-            return (lambda: T.matmul(alloc()[:], lhsT=id16[:, 0:1].to_broadcast([P, P]), rhs=chi_pad[:], start=True, stop=True)), needs, ["chi"]
 
         def total(i):
             alloc, needs = take("st", ("st", i), [P, G])
-            return (lambda: T.matmul(alloc()[:], lhsT=dens_t[:, i], rhs=sig_pad[:], start=True, stop=True)), needs + ["dens_t"], [("st", i)]
+            return (lambda: T.matmul(alloc()[:], lhsT=dens_t[:, i], rhs=sig_pad[:], start=True, stop=True)), needs + [("dens_t", i)], [("st", i)]
 
         def scatter(i, m):
             alloc, needs = take("mm", ("a", i, m), [P, G])
@@ -164,51 +177,65 @@ def tile_multigroupintegraltransportsourceiterati_x1_kernel(tc, flux, scat, dens
             def run():
                 T.matmul_mx(out=alloc()[:], lhsT=flux_codes[:, i].bitcast(FP8X4), lhsT_scale=flux_sc[:, i],
                             rhs=scat_codes[:, m].bitcast(FP8X4), rhs_scale=scat_sc[:, m], start=True, stop=True)
-            return run, needs + [("flux_q", i), ("scat_q", m)], [("a", i, m)]
+            return run, needs + [("flux_q", i)] + cols("scat_q", m, 0, G), [("a", i, m)]
 
         def fission(i):
-            i0 = 4 * (i // 4)
-            alloc, needs = take("tp", ("p", i0), [P, 4, M])
+            alloc, needs = take("tp", "p", [P, NT, M])
 
             def run():
-                ps = alloc() if i == i0 else bank["p", i0]
+                ps = alloc() if i == 0 else bank["p"]
                 for j in range(4):
-                    T.matmul(ps[:, i - i0], lhsT=flux_grp[i // 4][:, i % 4, :, j], rhs=nusf_t[:, j], start=(j == 0), stop=(j == 3))
-            return run, (needs if i == i0 else []) + [("flux_grp", i // 2), "nusf_t"], [("p", i0)] if i == i0 + 3 else []
+                    T.matmul(ps[:, i], lhsT=flux_grp[i // 4][:, i % 4, :, j], rhs=nusf_k[:, j // 2, :, j % 2], start=(j == 0), stop=(j == 3))
+            return run, (needs if i == 0 else []) + [("flux_grp", i // 2), "nusf_t"], ["p"] if i == NT - 1 else []
 
-        def transport_pass(ps, g, h, c0, gs):
-            for a in range(2):
-                t = 2 * h + a
+        def emission(g, c0):
+            alloc, needs = take("mm", ("e", g, c0), [P, 4, P])
+
+            def run():
+                ps = alloc()
+                for t in range(4):
+                    T.matmul(ps[:, t], lhsT=f_t[:, 4 * g + t], rhs=rows[:, c0:c0 + P], start=True, stop=True)
+            return run, needs + [("f_t", 4 * g), "chi"], [("e", g, c0)]
+
+        def transport_pass(ps, unit, gs):
+            g, t0, n, c0, w = unit
+            for a in range(n):
+                t = t0 + a
                 T.matmul_mx(out=ps[:, a], lhsT=kern_codes[:, g, gs, t].bitcast(FP8X4), lhsT_scale=kern_sc[:, g, gs, t],
-                            rhs=q_codes[:, gs, c0:c0 + H].bitcast(FP8X4), rhs_scale=q_sc[:, gs, c0:c0 + H],
-                            start=(gs == 0 and a == 0), stop=(gs == 1 and a == 1))
+                            rhs=q_codes[:, gs, c0:c0 + w].bitcast(FP8X4), rhs_scale=q_sc[:, gs, c0:c0 + w],
+                            start=(gs == 0 and a == 0), stop=(gs == 1 and a == n - 1))
 
         def open_unit(unit, ring):
-            g, h, c0 = unit
-            alloc, needs = take(ring, ("c", unit), [P, 2, H])
-            return (lambda: transport_pass(alloc(), g, h, c0, 0)), needs + [("kern_q", g, 0)] + cols("q_q", 0, c0, H), [("open", unit)]
+            g, t0, n, c0, w = unit
+            alloc, needs = take(ring, ("c", unit), [P, n, w])
+            return (lambda: transport_pass(alloc(), unit, 0)), needs + [("kern_q", g, 0)] + cols("q_q", 0, c0, w), [("open", unit)]
 
         def close_unit(unit):
-            g, h, c0 = unit
-            return (lambda: transport_pass(bank["c", unit], g, h, c0, 1)), [("open", unit), ("kern_q", g, 1)] + cols("q_q", 1, c0, H), [("c", unit)]
+            g, t0, n, c0, w = unit
+            return (lambda: transport_pass(bank["c", unit], unit, 1)), [("open", unit), ("kern_q", g, 1)] + cols("q_q", 1, c0, w), [("c", unit)]
 
-        def c_dens():
-            return (lambda: S.copy(out=dens_t[:], in_=bank["dens"][:])), ["dens"], ["dens_t", ("read", "dens")]
+        def c_pad(name, dst, i0, n):
+            return (lambda: S.copy(out=dst[:, i0:i0 + n], in_=bank[name, i0][:])), [(name, i0)], [(name + "_t", i) for i in range(i0, i0 + n)] + [("read", (name, i0))]
 
         def c_nusf():
-            return (lambda: S.copy(out=nusf_t[:], in_=bank["nusf"][:, :, 0:M])), ["nusf"], ["nusf_t", ("read", "nusf")]
+            return (lambda: S.copy(out=nusf_t[:], in_=bank["nusf"][:, :, NU_AT:NU_AT + M])), ["nusf"], ["nusf_t", ("read", "nusf")]
 
-        def c_chi():
-            return (lambda: S.copy(out=chi_b[:], in_=bank["chi"][:])), ["chi"], ["chi_b", ("read", "chi")]
+        def words_out(eng, dst, src):
+            if eng is S:
+                S.copy(out=dst, in_=src)
+            else:
+                V.tensor_copy(out=dst, in_=src)
 
-        def c_flux(b):
+        def c_flux(b, eng=S):
             a0 = 2 * (b % 2)
             dst = flux_grp[b // 2][:, a0:a0 + 2].rearrange("p a r f -> p a (r f)").bitcast(F32).rearrange("p a (r u) -> p a r u", u=2)
-            return (lambda: S.copy(out=dst, in_=bank["flux", b][:].rearrange("p a u r -> p a r u"))), [("flux", b)], [("flux_grp", b), ("read", ("flux", b))]
+            return (lambda: words_out(eng, dst, bank["flux", b][:].rearrange("p a u r -> p a r u"))), [("flux", b)], [("flux_grp", b), ("read", ("flux", b))]
 
-        def c_kern(i):
-            dst = kern_grp[i // 4][:, :, i % 4].rearrange("p k r f -> p k (r f)").bitcast(F32).rearrange("p k (r u) -> p k r u", u=2)
-            return (lambda: S.copy(out=dst, in_=bank["kern", i][:].rearrange("p k u r -> p k r u"))), [("kern", i)], [("kern_grp", i), ("read", ("kern", i))]
+        def c_kern(i, eng=S):
+            def run():
+                dst = kern_grp(i // 4)[:, :, i % 4].rearrange("p k r f -> p k (r f)").bitcast(F32).rearrange("p k (r u) -> p k r u", u=2)
+                words_out(eng, dst, bank["kern", i][:].rearrange("p k u r -> p k r u"))
+            return run, [("kern", i)], [("kern_grp", i), ("read", ("kern", i))]
 
         def weigh_first(i):
             def run():
@@ -228,37 +255,22 @@ def tile_multigroupintegraltransportsourceiterati_x1_kernel(tc, flux, scat, dens
         def inverse(i):
             return [root(i), sign(i), square(i)]
 
-        def f_chi(i, eng):
+        def signed(i, n=1, c0=0, w=G, after=()):
             def run():
-                if eng is S:
-                    S.activation(out=fx[i // 4][:, i % 4], in_=chi_b[:], func=ACT.Copy, scale=f[:, i:i + 1])
-                else:
-                    GP.tensor_scalar(out=fx[i // 4][:, i % 4], in0=chi_b[:], scalar1=f[:, i:i + 1], scalar2=0.0, op0=ALU.mult, op1=ALU.add)
-            return run, [("f", i), "chi_b"], [("fx", i)]
+                GP.tensor_tensor(out=inv(i, n)[:, :, c0:c0 + w], in0=rst[i // 4][:, i % 4:i % 4 + n, c0:c0 + w], in1=sg[:, i:i + n, c0:c0 + w], op=ALU.mult)
+            return run, [(k, j) for k in ("size", "sign") for j in range(i, i + n)] + list(after), [k for j in range(i, i + n) for k in cols("inv", j, c0, w)]
 
-        def signed(i, c0=0, w=G):
-            r = rst[i // 4][:, i % 4:i % 4 + 2, c0:c0 + w]
-            h = (i - 4) // 2
-
-            def run():
-                if i >= 4 and h not in inv_hi:
-                    inv_hi[h] = shared("inv_hi", h, [P, 2, G], F32)
-                dst = inv_hi[h][:, :, c0:c0 + w] if i >= 4 else r
-                GP.tensor_tensor(out=dst, in0=r, in1=sg[:, i:i + 2, c0:c0 + w], op=ALU.mult)
-            needs = [(k, j) for k in ("size", "sign") for j in (i, i + 1)] + ([("kern_q", h, 1)] if i >= 4 else [])
-            return run, needs, cols("inv", i, c0, w) + cols("inv", i + 1, c0, w)
-
-        def weave_scat(m, c0, w, eng):
-            return (lambda: weave(eng, scat_grp[m][:, c0:c0 + w], scat_raw[m][:, :, c0:c0 + w])), [("scat_q", 2)] if m == 3 else [], cols("scat_grp", m, c0, w)
+        def weave_scat(m, c0, w, eng, after=()):
+            return (lambda: weave(eng, scat_grp(m, c0, w), scat_raw[m][:, :, c0:c0 + w])), list(after), cols("scat_grp", m, c0, w)
 
         def weave_res(g, c0, eng):
-            needs = cols(("res", 0), g, c0, P) + cols(("res", 1), g, c0, P)
+            needs = [k for t in range(4) for k in cols(("res", t), g, c0, P)]
             return (lambda: weave(eng, r_grp[:, g, c0:c0 + P], res[g][:, :, c0:c0 + P])), needs, cols("r_grp", g, c0, P)
 
-        def quant_scat(m):
+        def quant_scat(m, c0, w):
             def run():
-                V.quantize_mx(out=scat_codes[:, m].bitcast(FP8X4), scales=scat_sc[:, m], in_=scat_grp[m][:].rearrange("p n j -> p (n j)"))
-            return run, cols("scat_grp", m, 0, G), [("scat_q", m)]
+                V.quantize_mx(out=scat_codes[:, m, c0:c0 + w].bitcast(FP8X4), scales=scat_sc[:, m, c0:c0 + w], in_=scat_grp(m, c0, w).rearrange("p n j -> p (n j)"))
+            return run, cols("scat_grp", m, c0, w), cols("scat_q", m, c0, w)
 
         def quant_flux(i0, n):
             def run():
@@ -271,14 +283,14 @@ def tile_multigroupintegraltransportsourceiterati_x1_kernel(tc, flux, scat, dens
             def run():
                 V.quantize_mx(out=kern_codes[:, g, k0:k0 + n].rearrange("p k t r -> p (k t r)").bitcast(FP8X4),
                               scales=kern_sc[:, g, k0:k0 + n].rearrange("p k t r -> p (k t r)"),
-                              in_=kern_grp[g][:, k0:k0 + n].rearrange("p k t r f -> p (k t r f)"))
+                              in_=kern_grp(g)[:, k0:k0 + n].rearrange("p k t r f -> p (k t r f)"))
             return run, [("kern_grp", i) for i in range(4 * g, 4 * g + 4)], [("kern_q", g, k) for k in range(k0, k0 + n)]
 
-        def quant_q(g, c0):
+        def quant_q(g, c0, w):
             def run():
-                V.quantize_mx(out=q_codes[:, g, c0:c0 + H].bitcast(FP8X4), scales=q_sc[:, g, c0:c0 + H],
-                              in_=q_grp[:, g, c0:c0 + H].rearrange("p n t -> p (n t)"))
-            return run, cols("q_grp", g, c0, H), cols("q_q", g, c0, H)
+                V.quantize_mx(out=q_codes[:, g, c0:c0 + w].bitcast(FP8X4), scales=q_sc[:, g, c0:c0 + w],
+                              in_=q_grp(g)[:, c0:c0 + w].rearrange("p n t -> p (n t)"))
+            return run, cols("q_grp", g, c0, w), cols("q_q", g, c0, w)
 
         def quant_res(g, c0, w):
             def run():
@@ -286,41 +298,51 @@ def tile_multigroupintegraltransportsourceiterati_x1_kernel(tc, flux, scat, dens
                               in_=r_grp[:, g, c0:c0 + w].rearrange("p n t -> p (n t)"))
             return run, cols("r_grp", g, c0, w), cols("r_q", g, c0, w)
 
-        def weigh_add(i, m):
-            xi = x[i // 4][:, i % 4]
+        def weigh_add(i, m, c0=0, w=G):
+            xi = x[i // 4][:, i % 4, c0:c0 + w]
 
             def run():
-                V.scalar_tensor_tensor(out=xi, in0=bank["a", i, m][:], scalar=dens32[:, i, m:m + 1], in1=xi, op0=ALU.mult, op1=ALU.add)
-            return run, [("a", i, m), ("x", i, m - 1)], [("x", i, m), ("read", ("a", i, m))]
+                V.scalar_tensor_tensor(out=xi, in0=bank["a", i, m][:, c0:c0 + w], scalar=dens32[:, i, m:m + 1], in1=xi, op0=ALU.mult, op1=ALU.add)
+            return run, [("a", i, m), ("x", i, m - 1)], [("x", i, m), ("read", ("a", i, m))] if c0 + w == G else []
 
-        def f_weigh(g):
-            def run():
-                V.tensor_tensor(out=pd[:, 4 * g:4 * g + 4], in0=bank["p", 4 * g][:], in1=dens32[:, 4 * g:4 * g + 4], op=ALU.mult)
-            return run, [("p", 4 * g)], [("pd", g), ("read", ("p", 4 * g))]
+        def f_weigh():
+            return (lambda: V.tensor_tensor(out=pd[:], in0=bank["p"][:], in1=dens32[:], op=ALU.mult)), ["p"], ["pd", ("read", "p")]
 
-        def f_sum(g):
+        def f_sums():
             def run():
-                V.tensor_reduce(out=f[:, 4 * g:4 * g + 4], in_=pd[:, 4 * g:4 * g + 4], axis=AX.X, op=ALU.add)
-            return run, [("pd", g)], [("f", i) for i in range(4 * g, 4 * g + 4)]
+                V.tensor_reduce(out=f[:], in_=pd[:], axis=AX.X, op=ALU.add)
+                with nc.allow_low_precision(reason="the first bf16 piece of f; the later pieces carry the rest"):
+                    V.tensor_reduce(out=dens_pad[:, :, CHI_AT], in_=pd[:], axis=AX.X, op=ALU.add)
+            return run, ["pd"], ["f"]
+
+        def f_less_first():
+            return (lambda: V.tensor_tensor(out=f_rest[:], in0=f[:], in1=dens_pad[:, :, CHI_AT], op=ALU.subtract)), ["f"], ["f_rest"]
+
+        def f_second():
+            return (lambda: V.tensor_copy(out=dens_pad[:, :, CHI_AT + 1], in_=f_rest[:])), ["f_rest"], ["f_mid"]
+
+        def f_third():
+            return (lambda: V.tensor_tensor(out=dens_pad[:, :, CHI_AT + 2], in0=f_rest[:], in1=dens_pad[:, :, CHI_AT + 1], op=ALU.subtract)), ["f_mid"], [("pieces", 0), ("pieces", 1)]
 
         def source(g, c0):
             def run():
-                dst, s = blocks(q_grp[:, g, c0:c0 + H], x[g][:, :, c0:c0 + H])
-                V.tensor_tensor(out=dst, in0=s, in1=fx[g][:, :, c0:c0 + H].rearrange("p t (c i) -> p c t i", i=4), op=ALU.add)
-            return run, [k for i in range(4 * g, 4 * g + 4) for k in (("x", i, M - 1), ("fx", i))], cols("q_grp", g, c0, H)
+                dst, s = blocks(q_grp(g)[:, c0:c0 + P], x[g][:, :, c0:c0 + P])
+                V.tensor_tensor(out=dst, in0=bank["e", g, c0][:].rearrange("p t (c i) -> p c t i", i=4), in1=s, op=ALU.add)
+            return run, [("x", i, M - 1) for i in range(4 * g, 4 * g + 4)] + [("e", g, c0)], cols("q_grp", g, c0, P) + [("read", ("e", g, c0))]
 
         def divide(unit):
-            g, h, c0 = unit
+            g, t0, n, c0, w = unit
+            i0 = 4 * g + t0
 
             def run():
-                inv = inv_hi[h][:, :, c0:c0 + H] if g else rst[0][:, 2 * h:2 * h + 2, c0:c0 + H]
-                V.tensor_tensor(out=res[g][:, 2 * h:2 * h + 2, c0:c0 + H], in0=bank["c", unit][:], in1=inv, op=ALU.mult)
-            needs = [k for i in (4 * g + 2 * h, 4 * g + 2 * h + 1) for k in cols("inv", i, c0, H)]
-            return run, [("c", unit)] + needs, cols(("res", h), g, c0, H) + [("read", ("c", unit))]
+                V.tensor_tensor(out=res[g][:, t0:t0 + n, c0:c0 + w], in0=bank["c", unit][:], in1=inv(i0, n)[:, :, c0:c0 + w], op=ALU.mult)
+            needs = [k for i in range(i0, i0 + n) for k in cols("inv", i, c0, w)]
+            return run, [("c", unit)] + needs, [k for t in range(t0, t0 + n) for k in cols(("res", t), g, c0, w)] + [("read", ("c", unit))]
 
         def store(unit):
-            g, h, c0 = unit
-            return (lambda: SP.dma_start(out=out0_v[g, :, 2 * h:2 * h + 2, c0:c0 + H], in_=res[g][:, 2 * h:2 * h + 2, c0:c0 + H])), cols(("res", h), g, c0, H), []
+            g, t0, n, c0, w = unit
+            needs = [k for t in range(t0, t0 + n) for k in cols(("res", t), g, c0, w)]
+            return (lambda: SP.dma_start(out=out0_v[g, :, t0:t0 + n, c0:c0 + w], in_=res[g][:, t0:t0 + n, c0:c0 + w])), needs, []
 
         def store_codes(g, c0, w):
             return (lambda: SP.dma_start(out=out1_v[g, :, c0:c0 + w], in_=r_codes[:, g, c0:c0 + w].bitcast(I32))), cols("r_q", g, c0, w), []
@@ -340,17 +362,14 @@ def tile_multigroupintegraltransportsourceiterati_x1_kernel(tc, flux, scat, dens
                     needs.extend(("read", b) for b in turn[k[1]][-1 - BANKS[k[1]]:-BANKS[k[1]]])
             at = [0] * len(queues)
             while any(at[e] < len(queue) for e, queue in enumerate(queues)):
+                before = sum(at)
                 for e, queue in enumerate(queues):
                     while at[e] < len(queue) and all(k in have for k in queue[at[e]][1]):
                         queue[at[e]][0]()
                         for k in queue[at[e]][2]:
                             have.add(k)
                         at[e] = at[e] + 1
-
-        for t in (sig_pad, nu_pad, chi_pad):
-            V.memset(t[:], 0.0)
-        S.dma_start(out=dens_sb[:], in_=dens.rearrange("(g p t) m -> p g (t m)", g=2, t=4))
-        S.dma_start(out=sig_pad[0:M], in_=sigt)
+                assert sum(at) > before, [[k for k in queue[at[e]][1] if k not in have] for e, queue in enumerate(queues) if at[e] < len(queue)]
 
         def load_scat(m):
             SP.dma_start(out=scat_raw[m][:], in_=scat[m].rearrange("(p j) n -> p j n", j=4))
@@ -358,63 +377,69 @@ def tile_multigroupintegraltransportsourceiterati_x1_kernel(tc, flux, scat, dens
         def load_flux(b):
             SP.dma_start(out=flux_raw[b][:], in_=flux_v[b // 2, :, 2 * (b % 2):2 * (b % 2) + 2])
 
-        for k in range(2):
-            load_scat(k)
-            load_flux(k)
-        SP.dma_start(out=nu_pad[0:M], in_=nusf)
-        SP.dma_start(out=chi_pad[0:1], in_=chi.rearrange("(o g) -> o g", o=1))
-        for k in (2, 3):
-            load_flux(k)
-        for k in (2, 3):
-            load_scat(k)
+        V.memset(warm[:], 1.0)
+        for t in (sig_pad, rows, dens_pad):
+            V.memset(t[:], 0.0)
+        make_identity(nc, id32[:])
+        S.dma_start(out=dens_sb[:], in_=dens.rearrange("(g p t) m -> p g (t m)", g=2, t=4))
+        S.dma_start(out=sig_pad[0:M], in_=sigt)
+        load_scat(0)
+        SP.dma_start(out=rows[NU_AT:NU_AT + M], in_=nusf)
+        load_flux(0)
+        load_scat(1)
+        load_flux(1)
+        load_flux(2)
+        load_scat(2)
+        load_flux(3)
+        load_scat(3)
         for g in range(2):
             SP.dma_start(out=kern_raw[g][:], in_=kern_v[g])
 
-        V.memset(warm[:], 1.0)
         S.activation(out=warm[:, 1:2], in_=warm[:, 0:1], func=ACT.Abs_reciprocal_sqrt)
-        make_identity(nc, id32[:])
-        V.memset(dens_pad[:], 0.0)
-        V.tensor_copy(out=id16[:], in_=id32[:])
         V.tensor_copy(out=dens_pad[:, :, 0:M], in_=dens_v)
+        V.tensor_copy(out=id16[:], in_=id32[:])
         V.tensor_copy(out=dens32[:], in_=dens_v)
 
         lo, hi = range(4), range(4, NT)
-        units = [(g, h, c0) for g in range(2) for c0 in (0, H) for h in range(2)]
+        units = [(g, 2 * h, 2, c0, H) for g in range(2) for c0 in (0, H) for h in range(2)]
+        quarters = range(0, G, P)
+        SCAT_PIECES = [[("a", 0, G)], [("b", 0, G)], [("c", 0, G)], [("c", 0, G)]]
+        INV_IN = [None, "c", None, "kern0"]
 
-        qt = [t_dens(), t_flux(0), total(0), total(1), t_flux(1), t_nusf(), scatter(0, 0), scatter(1, 0), t_flux(2), t_flux(3)]
-        qt += [scatter(0, 1), scatter(2, 0), scatter(3, 0), scatter(1, 1), spread_chi()] + [fission(i) for i in lo[:2]]
-        qt += [scatter(4, 0), scatter(2, 1), scatter(5, 0), scatter(3, 1), scatter(6, 0), scatter(0, 2), scatter(7, 0)]
-        passes = [(i, 2) for i in lo[1:]] + [(i, 1) for i in hi] + [(i, 3) for i in lo] + [(i, 2) for i in hi]
-        pairs = [[fission(2), fission(3)], [None, t_kern(0)], [None, t_kern(1)], [fission(4), fission(5)], [fission(6), fission(7)]]
-        side = [w for k, pair in enumerate(pairs) for w in pair + [total(2 + k) if k < 4 else None]]
-        for (i, m), w in zip(passes, side):
-            qt += [scatter(i, m)] + ([w] if w else [])
-        qt += [scatter(4, 3), scatter(5, 3), t_kern(2), t_kern(3), scatter(6, 3), scatter(7, 3), t_kern(4), t_kern(5), total(6), t_kern(6), t_kern(7), total(7)]
-        qt += [open_unit(u, "mm") for u in units[:4]] + [open_unit(units[4], "tp"), close_unit(units[0]), close_unit(units[1]), open_unit(units[5], "tp")]
-        qt += [close_unit(u) for u in units[2:6]]
-        for u in units[6:]:
-            qt += [open_unit(u, "mm"), close_unit(u)]
+        qt = [t_pad("dens", 0, NT, "st"), t_flux(0), t_nusf(), total(0), t_flux(1), t_flux(2), scatter(0, 0), scatter(1, 0), t_flux(3), total(1)]
+        qt += [scatter(2, 0), scatter(3, 0), scatter(0, 1), scatter(1, 1), fission(0), fission(1), scatter(2, 1), fission(2), scatter(4, 0), fission(3)]
+        qt += [scatter(3, 1), scatter(5, 0), scatter(0, 2), scatter(6, 0), scatter(1, 2), scatter(7, 0), scatter(2, 2), total(2), scatter(3, 2)]
+        for i in hi:
+            qt += [scatter(i, 1), fission(i)]
+        qt += [total(3), scatter(4, 2), scatter(5, 2), t_kern(0), t_kern(1), scatter(6, 2), total(4), scatter(7, 2)]
+        qt += [scatter(0, 3), scatter(1, 3), t_pad("f", 0, NT, "st"), scatter(2, 3), scatter(3, 3), total(5)]
+        qt += [emission(0, c) for c in quarters] + [t_kern(2), t_kern(3)]
+        qt += [scatter(4, 3), total(6), scatter(5, 3), t_kern(4), t_kern(5), scatter(6, 3), scatter(7, 3), total(7)]
+        qt += [emission(1, c) for c in quarters]
+        qt += [open_unit(units[0], "st"), open_unit(units[1], "st"), t_kern(6), t_kern(7), close_unit(units[0]), close_unit(units[1])]
+        qt += [open_unit(units[2], "mm"), open_unit(units[3], "mm"), close_unit(units[2]), close_unit(units[3])]
+        qt += [open_unit(u, ring) for u, ring in zip(units[4:], ("mm", "mm", "tp", "tp"))] + [close_unit(u) for u in units[4:]]
 
-        qv = [weave_scat(0, 0, G, V), quant_scat(0), weave_scat(1, 0, H, V), quant_flux(0, 2), weave_scat(1, H, H, V), quant_scat(1)]
-        qv += [weave_scat(2, 0, H, V), quant_flux(2, 2), weave_scat(2, H, H, V), weigh_add(0, 1), quant_flux(4, 4), quant_scat(2)]
-        qv += [weigh_add(i, 1) for i in lo[1:]] + [weigh_add(i, 2) for i in lo] + [f_weigh(0), quant_scat(3), f_sum(0)]
-        qv += [weigh_add(i, 1) for i in hi] + [weigh_add(i, 3) for i in lo]
-        qv += [weigh_add(4, 2), weigh_add(5, 2), weigh_add(6, 2), f_weigh(1), weigh_add(7, 2), f_sum(1)]
-        qv += [source(0, 0), source(0, H), quant_q(0, 0), quant_q(0, H), quant_kern(0, 0, 2)] + [weigh_add(i, 3) for i in hi]
-        qv += [source(1, 0), quant_kern(1, 0, 1), quant_q(1, 0), source(1, H), divide(units[0]), quant_q(1, H), divide(units[1]), quant_kern(1, 1, 1)]
-        qv += [divide(u) for u in units[2:7]] + [quant_res(0, 0, G), divide(units[7]), quant_res(1, 0, H)]
-        qv += [weave_res(1, H + P, V), quant_res(1, H + P, P), quant_res(1, H, P)]
+        qv = [weave_scat(0, 0, H, V), weave_scat(0, H, H, V), quant_scat(0, 0, H), quant_scat(0, H, H), weave_scat(1, 0, H, V), quant_flux(0, 2), weave_scat(1, H, H, V)]
+        qv += [quant_scat(1, 0, H), quant_scat(1, H, H), quant_flux(2, 2), weave_scat(2, 0, H, V), quant_flux(4, 2), weave_scat(2, H, H, V)]
+        qv += [quant_scat(2, 0, H), quant_flux(6, 2), quant_scat(2, H, H)]
+        qv += [weigh_add(i, 1) for i in lo] + [weigh_add(i, 2) for i in lo] + [weigh_add(i, 1) for i in hi] + [f_weigh(), weigh_add(4, 2), f_sums(), weigh_add(5, 2)]
+        qv += [f_less_first(), quant_scat(3, 0, H), f_second(), quant_scat(3, H, P), f_third(), quant_scat(3, H + P, P)]
+        qv += [weigh_add(6, 2), weigh_add(7, 2)] + [weigh_add(i, 3) for i in lo[:3]] + [weigh_add(3, 3, 0, H), weigh_add(3, 3, H, H)] + [source(0, c) for c in quarters]
+        qv += [weigh_add(4, 3), quant_q(0, 0, G), quant_kern(0, 0, 2), weigh_add(5, 3), weigh_add(6, 3), weigh_add(7, 3, 0, H), weigh_add(7, 3, H, H)]
+        qv += [source(1, c) for c in quarters[:3]] + [quant_q(1, 0, H), source(1, quarters[3]), divide(units[0]), quant_q(1, H, H), divide(units[1]), quant_kern(1, 0, 1)]
+        qv += [divide(units[2]), quant_kern(1, 1, 1), divide(units[3]), quant_res(0, 0, H)] + [divide(u) for u in units[4:7]] + [quant_res(0, H, H), divide(units[7]), quant_res(1, 0, H)]
+        qv += [weave_res(1, H + P, V), quant_res(1, H, P), quant_res(1, H + P, P)]
 
-        qs = [c_dens(), c_flux(0), root(0), sign(0), c_flux(1), c_nusf(), weigh_first(0), weigh_first(1), c_flux(2), c_flux(3), weigh_first(2), weigh_first(3)]
-        qs += [c_chi()] + [weigh_first(i) for i in hi] + [square(0)] + inverse(1) + inverse(2) + [c_kern(0)] + inverse(3)
-        qs += [f_chi(i, S) for i in lo[F_ON_GPSIMD:]] + [c_kern(1)] + inverse(4) + inverse(5)
-        for i in (2, 4):
-            qs += [c_kern(i), c_kern(i + 1), f_chi(i + 2, S), f_chi(i + 3, S)]
-        qs += [c_kern(6), c_kern(7)] + inverse(6) + inverse(7)
-        qs += [weave_res(g, c, S) for g in range(2) for c in range(0, G, P)][:-1] + [store_scales(1, S), store_scales(3, S)]
+        qs = [c_pad("dens", dens_t, 0, NT), c_flux(0), c_nusf(), root(0), c_flux(1), c_flux(2), weigh_first(0), weigh_first(1), c_flux(3), weigh_first(2), weigh_first(3), sign(0)]
+        qs += [weigh_first(4), square(0)] + [weigh_first(i) for i in hi[1:]] + inverse(1) + inverse(2) + inverse(3) + [c_kern(0), c_kern(1), root(4), sign(4), c_pad("f", f_t, 0, NT), square(4)]
+        qs += inverse(5) + [c_kern(2), c_kern(3)] + inverse(6) + inverse(7) + [c_kern(i) for i in hi]
+        qs += [weave_res(g, c, S) for g in range(2) for c in quarters][:-1] + [store_scales(1, S), store_scales(3, S)]
 
-        qg = [weave_scat(3, 0, G, GP)] + [f_chi(i, GP) for i in lo[:F_ON_GPSIMD]] + [signed(0), signed(2), signed(4), signed(6, 0, H), signed(6, H, H)]
+        qg = [weave_scat(3, 0, G, GP, cols("scat_q", 2, 0, G)), signed(0), signed(1)]
+        qg += [signed(2, after=cols("scat_q", 3, 0, G)), signed(3), signed(4), signed(5), signed(6, after=[("kern_q", 0, 1)]), signed(7)]
 
-        qy = [store(u) for u in units[:7]] + [store_codes(0, 0, G), store(units[7]), store_codes(1, 0, H), store_codes(1, H, H)]
+        load_chi = (lambda: SP.dma_start(out=rows[CHI_AT:CHI_AT + PIECES], in_=chi.partition_broadcast(PIECES))), ["nusf"], ["chi"]
+        qy = [load_chi] + [store(u) for u in units[:7]] + [store_codes(0, 0, G), store(units[7]), store_codes(1, 0, H), store_codes(1, H, H)]
         qy += [store_scales(0, SP), store_scales(2, SP)]
         emit([qt, qv, qs, qg, qy])

@@ -18,8 +18,7 @@ R, G, M = 1024, 512, 4
 NT = R // P
 H = G // 2
 CHI_AT, NU_AT = 4, 8
-PIECES = 3
-BANKS = {"mm": 4, "tp": 2, "st": 2}
+BANKS = {"mm": 4, "tp": 2, "sa": 1, "sb": 1}
 FLOPS = 2 * R * G * G * M + 2 * R * R * G
 
 
@@ -38,6 +37,7 @@ def tile_multigroupintegraltransportsourceiterati_x1_kernel(tc, flux, scat, dens
             return [tile("%s%d" % (name, k), shape, dtype) for k in range(n)]
 
         rows = tile("rows", [P, G], BF16)
+        chi_pad = tile("chi_pad", [P, G], BF16)
         sig_pad = tile("sig_pad", [P, G], BF16)
         dens_pad = tile("dens_pad", [P, NT, P], BF16)
         dens_sb = tile("dens_sb", [P, 2, 4 * M], BF16)
@@ -49,7 +49,8 @@ def tile_multigroupintegraltransportsourceiterati_x1_kernel(tc, flux, scat, dens
         id16 = tile("id16", [P, P], BF16)
         dens32 = tile("dens32", [P, NT, M], F32)
         dens_t = tile("dens_t", [P, NT, P], BF16)
-        f_t = tile("f_t", [P, NT, P], BF16)
+        chi_b = tile("chi_b", [P, G], BF16)
+        fx = tiles("fx", 2, [P, 4, G], F32)
         flux_grp = tiles("flux_grp", 2, [P, 4, P, 4], BF16)
         flux_codes = tile("flux_codes", [P, NT, P], U32)
         flux_sc = tile("flux_sc", [P, NT, P], U8)
@@ -57,12 +58,11 @@ def tile_multigroupintegraltransportsourceiterati_x1_kernel(tc, flux, scat, dens
         scat_sc = tile("scat_sc", [P, M, G], U8)
         pd = tile("pd", [P, NT, M], F32)
         f = tile("f", [P, NT], F32)
-        f_rest = tile("f_rest", [P, NT], F32)
         x = tiles("x", 2, [P, 4, G], F32)
         sg = tile("sg", [P, NT, G], BF16)
         rst = tiles("rst", 2, [P, 4, G], F32)
-        kern_codes = tile("kern_codes", [P, 2, 2, 4, P], U32)
-        kern_sc = tile("kern_sc", [P, 2, 2, 4, P], U8)
+        kern_codes = tile("kern_codes", [P, NT, 2, P], U32)
+        kern_sc = tile("kern_sc", [P, NT, 2, P], U8)
         q_codes = tile("q_codes", [P, 2, G], U32)
         q_sc = tile("q_sc", [P, 2, G], U8)
         res = tiles("res", 2, [P, 4, G], F32)
@@ -115,8 +115,8 @@ def tile_multigroupintegraltransportsourceiterati_x1_kernel(tc, flux, scat, dens
                 if b0 <= c0 and c0 + w <= b0 + bw:
                     return tenant(buffer, "scat_grp%d_%d" % (m, b0), [P, bw, 4], BF16)[:, c0 - b0:c0 - b0 + w]
 
-        def kern_grp(g):
-            return tenant("kern%d" % g, "kern_grp%d" % g, [P, 2, 4, P, 4], BF16)
+        def kern_grp(h):
+            return tenant("kern%d" % h, "kern_grp%d" % h, [P, 2, 2, P, 4], BF16)
 
         def q_grp(g):
             return tenant("q%d" % g, "q_grp%d" % g, [P, G, 4], BF16)
@@ -134,7 +134,7 @@ def tile_multigroupintegraltransportsourceiterati_x1_kernel(tc, flux, scat, dens
                 ps = alloc()
                 for i in range(n):
                     T.transpose(ps[:, i], dens_pad[:, i0 + i], id16[:])
-            return run, needs + ([("pieces", i0 // 4)] if name == "f" else []), [(name, i0)]
+            return run, needs, [(name, i0)]
 
         def t_flux(b):
             alloc, needs = take("tp", ("flux", b), [P, 2, 2, P])
@@ -167,12 +167,12 @@ def tile_multigroupintegraltransportsourceiterati_x1_kernel(tc, flux, scat, dens
                     T.transpose(ps[:, u], rows[:].bitcast(F32)[:, u:H:2], id32[:])
             return run, needs, ["nusf"]
 
-        def total(i):
-            alloc, needs = take("st", ("st", i), [P, G])
+        def total(i, ring):
+            alloc, needs = take(ring, ("st", i), [P, G])
             return (lambda: T.matmul(alloc()[:], lhsT=dens_t[:, i], rhs=sig_pad[:], start=True, stop=True)), needs + [("dens_t", i)], [("st", i)]
 
-        def scatter(i, m):
-            alloc, needs = take("mm", ("a", i, m), [P, G])
+        def scatter(i, m, ring="mm"):
+            alloc, needs = take(ring, ("a", i, m), [P, G])
 
             def run():
                 T.matmul_mx(out=alloc()[:], lhsT=flux_codes[:, i].bitcast(FP8X4), lhsT_scale=flux_sc[:, i],
@@ -180,7 +180,7 @@ def tile_multigroupintegraltransportsourceiterati_x1_kernel(tc, flux, scat, dens
             return run, needs + [("flux_q", i)] + cols("scat_q", m, 0, G), [("a", i, m)]
 
         def fission(i):
-            alloc, needs = take("tp", "p", [P, NT, M])
+            alloc, needs = take("sb", "p", [P, NT, M])
 
             def run():
                 ps = alloc() if i == 0 else bank["p"]
@@ -188,37 +188,35 @@ def tile_multigroupintegraltransportsourceiterati_x1_kernel(tc, flux, scat, dens
                     T.matmul(ps[:, i], lhsT=flux_grp[i // 4][:, i % 4, :, j], rhs=nusf_k[:, j // 2, :, j % 2], start=(j == 0), stop=(j == 3))
             return run, (needs if i == 0 else []) + [("flux_grp", i // 2), "nusf_t"], ["p"] if i == NT - 1 else []
 
-        def emission(g, c0):
-            alloc, needs = take("mm", ("e", g, c0), [P, 4, P])
-
-            def run():
-                ps = alloc()
-                for t in range(4):
-                    T.matmul(ps[:, t], lhsT=f_t[:, 4 * g + t], rhs=rows[:, c0:c0 + P], start=True, stop=True)
-            return run, needs + [("f_t", 4 * g), "chi"], [("e", g, c0)]
+        def spread_chi():
+            alloc, needs = take("tp", "chi", [P, G], BF16)
+            return (lambda: T.matmul(alloc()[:], lhsT=id16[:, 0:1].to_broadcast([P, P]), rhs=chi_pad[:], start=True, stop=True)), needs, ["chi"]
 
         def transport_pass(ps, unit, gs):
             g, t0, n, c0, w = unit
             for a in range(n):
                 t = t0 + a
-                T.matmul_mx(out=ps[:, a], lhsT=kern_codes[:, g, gs, t].bitcast(FP8X4), lhsT_scale=kern_sc[:, g, gs, t],
+                T.matmul_mx(out=ps[:, a], lhsT=kern_codes[:, 4 * g + t, gs].bitcast(FP8X4), lhsT_scale=kern_sc[:, 4 * g + t, gs],
                             rhs=q_codes[:, gs, c0:c0 + w].bitcast(FP8X4), rhs_scale=q_sc[:, gs, c0:c0 + w],
                             start=(gs == 0 and a == 0), stop=(gs == 1 and a == n - 1))
 
         def open_unit(unit, ring):
             g, t0, n, c0, w = unit
             alloc, needs = take(ring, ("c", unit), [P, n, w])
-            return (lambda: transport_pass(alloc(), unit, 0)), needs + [("kern_q", g, 0)] + cols("q_q", 0, c0, w), [("open", unit)]
+            return (lambda: transport_pass(alloc(), unit, 0)), needs + [("kern_q", i // 2) for i in range(4 * g + t0, 4 * g + t0 + n)] + cols("q_q", 0, c0, w), [("open", unit)]
 
         def close_unit(unit):
             g, t0, n, c0, w = unit
-            return (lambda: transport_pass(bank["c", unit], unit, 1)), [("open", unit), ("kern_q", g, 1)] + cols("q_q", 1, c0, w), [("c", unit)]
+            return (lambda: transport_pass(bank["c", unit], unit, 1)), [("open", unit)] + cols("q_q", 1, c0, w), [("c", unit)]
 
         def c_pad(name, dst, i0, n):
             return (lambda: S.copy(out=dst[:, i0:i0 + n], in_=bank[name, i0][:])), [(name, i0)], [(name + "_t", i) for i in range(i0, i0 + n)] + [("read", (name, i0))]
 
         def c_nusf():
             return (lambda: S.copy(out=nusf_t[:], in_=bank["nusf"][:, :, NU_AT:NU_AT + M])), ["nusf"], ["nusf_t", ("read", "nusf")]
+
+        def c_chi():
+            return (lambda: S.copy(out=chi_b[:], in_=bank["chi"][:])), ["chi"], ["chi_b", ("read", "chi")]
 
         def words_out(eng, dst, src):
             if eng is S:
@@ -233,7 +231,7 @@ def tile_multigroupintegraltransportsourceiterati_x1_kernel(tc, flux, scat, dens
 
         def c_kern(i, eng=S):
             def run():
-                dst = kern_grp(i // 4)[:, :, i % 4].rearrange("p k r f -> p k (r f)").bitcast(F32).rearrange("p k (r u) -> p k r u", u=2)
+                dst = kern_grp(i // 2)[:, i % 2].rearrange("p k r f -> p k (r f)").bitcast(F32).rearrange("p k (r u) -> p k r u", u=2)
                 words_out(eng, dst, bank["kern", i][:].rearrange("p k u r -> p k r u"))
             return run, [("kern", i)], [("kern_grp", i), ("read", ("kern", i))]
 
@@ -279,12 +277,12 @@ def tile_multigroupintegraltransportsourceiterati_x1_kernel(tc, flux, scat, dens
                               in_=flux_grp[i0 // 4][:, i0 % 4:i0 % 4 + n].rearrange("p a r f -> p (a r f)"))
             return run, [("flux_grp", i // 2) for i in range(i0, i0 + n)], [("flux_q", i) for i in range(i0, i0 + n)]
 
-        def quant_kern(g, k0, n):
+        def quant_kern(h):
             def run():
-                V.quantize_mx(out=kern_codes[:, g, k0:k0 + n].rearrange("p k t r -> p (k t r)").bitcast(FP8X4),
-                              scales=kern_sc[:, g, k0:k0 + n].rearrange("p k t r -> p (k t r)"),
-                              in_=kern_grp(g)[:, k0:k0 + n].rearrange("p k t r f -> p (k t r f)"))
-            return run, [("kern_grp", i) for i in range(4 * g, 4 * g + 4)], [("kern_q", g, k) for k in range(k0, k0 + n)]
+                V.quantize_mx(out=kern_codes[:, 2 * h:2 * h + 2].rearrange("p t k r -> p (t k r)").bitcast(FP8X4),
+                              scales=kern_sc[:, 2 * h:2 * h + 2].rearrange("p t k r -> p (t k r)"),
+                              in_=kern_grp(h)[:].rearrange("p t k r f -> p (t k r f)"))
+            return run, [("kern_grp", 2 * h), ("kern_grp", 2 * h + 1)], [("kern_q", h)]
 
         def quant_q(g, c0, w):
             def run():
@@ -308,27 +306,22 @@ def tile_multigroupintegraltransportsourceiterati_x1_kernel(tc, flux, scat, dens
         def f_weigh():
             return (lambda: V.tensor_tensor(out=pd[:], in0=bank["p"][:], in1=dens32[:], op=ALU.mult)), ["p"], ["pd", ("read", "p")]
 
-        def f_sums():
+        def f_sum():
+            return (lambda: V.tensor_reduce(out=f[:], in_=pd[:], axis=AX.X, op=ALU.add)), ["pd"], ["f"]
+
+        def f_chi(i, eng):
             def run():
-                V.tensor_reduce(out=f[:], in_=pd[:], axis=AX.X, op=ALU.add)
-                with nc.allow_low_precision(reason="the first bf16 piece of f; the later pieces carry the rest"):
-                    V.tensor_reduce(out=dens_pad[:, :, CHI_AT], in_=pd[:], axis=AX.X, op=ALU.add)
-            return run, ["pd"], ["f"]
-
-        def f_less_first():
-            return (lambda: V.tensor_tensor(out=f_rest[:], in0=f[:], in1=dens_pad[:, :, CHI_AT], op=ALU.subtract)), ["f"], ["f_rest"]
-
-        def f_second():
-            return (lambda: V.tensor_copy(out=dens_pad[:, :, CHI_AT + 1], in_=f_rest[:])), ["f_rest"], ["f_mid"]
-
-        def f_third():
-            return (lambda: V.tensor_tensor(out=dens_pad[:, :, CHI_AT + 2], in0=f_rest[:], in1=dens_pad[:, :, CHI_AT + 1], op=ALU.subtract)), ["f_mid"], [("pieces", 0), ("pieces", 1)]
+                if eng is S:
+                    S.activation(out=fx[i // 4][:, i % 4], in_=chi_b[:], func=ACT.Copy, scale=f[:, i:i + 1])
+                else:
+                    GP.tensor_scalar(out=fx[i // 4][:, i % 4], in0=chi_b[:], scalar1=f[:, i:i + 1], scalar2=0.0, op0=ALU.mult, op1=ALU.add)
+            return run, ["f", "chi_b"], [("fx", i)]
 
         def source(g, c0):
             def run():
-                dst, s = blocks(q_grp(g)[:, c0:c0 + P], x[g][:, :, c0:c0 + P])
-                V.tensor_tensor(out=dst, in0=bank["e", g, c0][:].rearrange("p t (c i) -> p c t i", i=4), in1=s, op=ALU.add)
-            return run, [("x", i, M - 1) for i in range(4 * g, 4 * g + 4)] + [("e", g, c0)], cols("q_grp", g, c0, P) + [("read", ("e", g, c0))]
+                dst, s = blocks(q_grp(g)[:, c0:c0 + H], x[g][:, :, c0:c0 + H])
+                V.tensor_tensor(out=dst, in0=s, in1=fx[g][:, :, c0:c0 + H].rearrange("p t (c i) -> p c t i", i=4), op=ALU.add)
+            return run, [k for i in range(4 * g, 4 * g + 4) for k in (("x", i, M - 1), ("fx", i))], cols("q_grp", g, c0, H)
 
         def divide(unit):
             g, t0, n, c0, w = unit
@@ -378,7 +371,7 @@ def tile_multigroupintegraltransportsourceiterati_x1_kernel(tc, flux, scat, dens
             SP.dma_start(out=flux_raw[b][:], in_=flux_v[b // 2, :, 2 * (b % 2):2 * (b % 2) + 2])
 
         V.memset(warm[:], 1.0)
-        for t in (sig_pad, rows, dens_pad):
+        for t in (sig_pad, rows, chi_pad, dens_pad):
             V.memset(t[:], 0.0)
         make_identity(nc, id32[:])
         S.dma_start(out=dens_sb[:], in_=dens.rearrange("(g p t) m -> p g (t m)", g=2, t=4))
@@ -388,10 +381,11 @@ def tile_multigroupintegraltransportsourceiterati_x1_kernel(tc, flux, scat, dens
         load_flux(0)
         load_scat(1)
         load_flux(1)
-        load_flux(2)
+        SP.dma_start(out=chi_pad[0:1], in_=chi.rearrange("(o g) -> o g", o=1))
         load_scat(2)
-        load_flux(3)
         load_scat(3)
+        load_flux(2)
+        load_flux(3)
         for g in range(2):
             SP.dma_start(out=kern_raw[g][:], in_=kern_v[g])
 
@@ -404,42 +398,35 @@ def tile_multigroupintegraltransportsourceiterati_x1_kernel(tc, flux, scat, dens
         units = [(g, 2 * h, 2, c0, H) for g in range(2) for c0 in (0, H) for h in range(2)]
         quarters = range(0, G, P)
         SCAT_PIECES = [[("a", 0, G)], [("b", 0, G)], [("c", 0, G)], [("c", 0, G)]]
-        INV_IN = [None, "c", None, "kern0"]
+        INV_IN = ["c", None, "kern1", "kern3"]
 
-        qt = [t_pad("dens", 0, NT, "st"), t_flux(0), t_nusf(), total(0), t_flux(1), t_flux(2), scatter(0, 0), scatter(1, 0), t_flux(3), total(1)]
-        qt += [scatter(2, 0), scatter(3, 0), scatter(0, 1), scatter(1, 1), fission(0), fission(1), scatter(2, 1), fission(2), scatter(4, 0), fission(3)]
-        qt += [scatter(3, 1), scatter(5, 0), scatter(0, 2), scatter(6, 0), scatter(1, 2), scatter(7, 0), scatter(2, 2), total(2), scatter(3, 2)]
-        for i in hi:
-            qt += [scatter(i, 1), fission(i)]
-        qt += [total(3), scatter(4, 2), scatter(5, 2), t_kern(0), t_kern(1), scatter(6, 2), total(4), scatter(7, 2)]
-        qt += [scatter(0, 3), scatter(1, 3), t_pad("f", 0, NT, "st"), scatter(2, 3), scatter(3, 3), total(5)]
-        qt += [emission(0, c) for c in quarters] + [t_kern(2), t_kern(3)]
-        qt += [scatter(4, 3), total(6), scatter(5, 3), t_kern(4), t_kern(5), scatter(6, 3), scatter(7, 3), total(7)]
-        qt += [emission(1, c) for c in quarters]
-        qt += [open_unit(units[0], "st"), open_unit(units[1], "st"), t_kern(6), t_kern(7), close_unit(units[0]), close_unit(units[1])]
-        qt += [open_unit(units[2], "mm"), open_unit(units[3], "mm"), close_unit(units[2]), close_unit(units[3])]
-        qt += [open_unit(u, ring) for u, ring in zip(units[4:], ("mm", "mm", "tp", "tp"))] + [close_unit(u) for u in units[4:]]
+        qt = [t_pad("dens", 0, NT, "sa"), t_flux(0), t_nusf(), total(0, "sb"), t_flux(1), total(1, "sa"), scatter(0, 0), scatter(1, 0), fission(0), scatter(2, 0), scatter(3, 0), scatter(0, 1), scatter(1, 1)]
+        qt += [t_flux(2), scatter(2, 1), scatter(3, 1), t_flux(3), scatter(0, 2), scatter(1, 2), total(2, "sa"), scatter(2, 2), fission(1), scatter(3, 2), spread_chi()] + [fission(i) for i in range(2, 6)]
+        qt += [scatter(0, 3), total(3, "sa"), scatter(1, 3), fission(6), scatter(4, 0, "tp"), fission(7), scatter(2, 3), scatter(5, 0, "tp"), scatter(3, 3), scatter(4, 1)]
+        qt += [scatter(6, 0, "tp"), scatter(5, 1), scatter(7, 0, "tp"), scatter(6, 1), scatter(7, 1), total(4, "sb"), scatter(4, 2), t_kern(0), scatter(5, 2), scatter(6, 2), t_kern(1), scatter(7, 2), total(5, "sa"), t_kern(2), t_kern(3)]
+        qt += [scatter(4, 3), total(6, "sb"), scatter(5, 3), scatter(6, 3), t_kern(4), t_kern(5), total(7, "sa"), scatter(7, 3)]
+        qt += [open_unit(u, "mm") for u in units[:3]] + [t_kern(6), t_kern(7), open_unit(units[3], "mm"), close_unit(units[0]), close_unit(units[1]), open_unit(units[4], "sb"), close_unit(units[4])]
+        qt += [close_unit(units[2]), close_unit(units[3]), open_unit(units[5], "tp"), close_unit(units[5]), open_unit(units[6], "tp"), close_unit(units[6])]
+        qt += [open_unit(units[7], "sa"), close_unit(units[7])]
 
         qv = [weave_scat(0, 0, H, V), weave_scat(0, H, H, V), quant_scat(0, 0, H), quant_scat(0, H, H), weave_scat(1, 0, H, V), quant_flux(0, 2), weave_scat(1, H, H, V)]
-        qv += [quant_scat(1, 0, H), quant_scat(1, H, H), quant_flux(2, 2), weave_scat(2, 0, H, V), quant_flux(4, 2), weave_scat(2, H, H, V)]
-        qv += [quant_scat(2, 0, H), quant_flux(6, 2), quant_scat(2, H, H)]
-        qv += [weigh_add(i, 1) for i in lo] + [weigh_add(i, 2) for i in lo] + [weigh_add(i, 1) for i in hi] + [f_weigh(), weigh_add(4, 2), f_sums(), weigh_add(5, 2)]
-        qv += [f_less_first(), quant_scat(3, 0, H), f_second(), quant_scat(3, H, P), f_third(), quant_scat(3, H + P, P)]
-        qv += [weigh_add(6, 2), weigh_add(7, 2)] + [weigh_add(i, 3) for i in lo[:3]] + [weigh_add(3, 3, 0, H), weigh_add(3, 3, H, H)] + [source(0, c) for c in quarters]
-        qv += [weigh_add(4, 3), quant_q(0, 0, G), quant_kern(0, 0, 2), weigh_add(5, 3), weigh_add(6, 3), weigh_add(7, 3, 0, H), weigh_add(7, 3, H, H)]
-        qv += [source(1, c) for c in quarters[:3]] + [quant_q(1, 0, H), source(1, quarters[3]), divide(units[0]), quant_q(1, H, H), divide(units[1]), quant_kern(1, 0, 1)]
-        qv += [divide(units[2]), quant_kern(1, 1, 1), divide(units[3]), quant_res(0, 0, H)] + [divide(u) for u in units[4:7]] + [quant_res(0, H, H), divide(units[7]), quant_res(1, 0, H)]
-        qv += [weave_res(1, H + P, V), quant_res(1, H, P), quant_res(1, H + P, P)]
+        qv += [weave_scat(2, 0, H, V), quant_flux(2, 2), quant_scat(1, 0, G), weave_scat(2, H, H, V), quant_scat(2, 0, H), quant_scat(2, H, H)]
+        qv += [weigh_add(i, 1) for i in lo] + [weigh_add(i, 2) for i in lo[:3]]
+        qv += [quant_scat(3, 0, G), quant_flux(4, 4), weigh_add(3, 2), weigh_add(0, 3), weigh_add(1, 3), f_weigh(), weigh_add(2, 3), f_sum(), weigh_add(3, 3)]
+        qv += [weigh_add(i, m) for m in (1, 2) for i in hi][:-1]
+        qv += [source(0, 0), source(0, H), quant_kern(0), quant_q(0, 0, G), quant_kern(1), weigh_add(7, 2)] + [weigh_add(i, 3) for i in hi[:3]] + [weigh_add(7, 3, 0, H), weigh_add(7, 3, H, H)]
+        qv += [source(1, 0), quant_kern(2), quant_q(1, 0, H), source(1, H), divide(units[0]), quant_q(1, H, H), divide(units[1]), quant_kern(3)]
+        qv += [divide(u) for u in units[2:]] + [quant_res(0, 0, G)]
+        qv += [weave_res(1, H + P, V), quant_res(1, 0, H), quant_res(1, H, H)]
 
-        qs = [c_pad("dens", dens_t, 0, NT), c_flux(0), c_nusf(), root(0), c_flux(1), c_flux(2), weigh_first(0), weigh_first(1), c_flux(3), weigh_first(2), weigh_first(3), sign(0)]
-        qs += [weigh_first(4), square(0)] + [weigh_first(i) for i in hi[1:]] + inverse(1) + inverse(2) + inverse(3) + [c_kern(0), c_kern(1), root(4), sign(4), c_pad("f", f_t, 0, NT), square(4)]
-        qs += inverse(5) + [c_kern(2), c_kern(3)] + inverse(6) + inverse(7) + [c_kern(i) for i in hi]
-        qs += [weave_res(g, c, S) for g in range(2) for c in quarters][:-1] + [store_scales(1, S), store_scales(3, S)]
+        qs = [c_pad("dens", dens_t, 0, NT), c_flux(0), c_nusf(), root(0), c_flux(1), sign(0), weigh_first(0), weigh_first(1), weigh_first(2), weigh_first(3), root(1), c_flux(2), sign(1), c_flux(3), square(0), square(1), root(2), sign(2), square(2), c_chi()]
+        qs += [root(3), weigh_first(4), weigh_first(5), weigh_first(6), weigh_first(7), sign(3), square(3), root(4), sign(4), c_kern(0), c_kern(1), square(4), root(5), sign(5), c_kern(2), c_kern(3), square(5)]
+        qs += [f_chi(i, S) for i in hi] + [c_kern(4), c_kern(5), root(6), sign(6), c_kern(6), c_kern(7), square(6)] + inverse(7)
+        qs += [weave_res(0, c, S) for c in quarters] + [weave_res(1, 0, S), weave_res(1, H, S)] + [store_scales(1, S), store_scales(3, S)]
 
-        qg = [weave_scat(3, 0, G, GP, cols("scat_q", 2, 0, G)), signed(0), signed(1)]
-        qg += [signed(2, after=cols("scat_q", 3, 0, G)), signed(3), signed(4), signed(5), signed(6, after=[("kern_q", 0, 1)]), signed(7)]
+        qg = [weave_scat(3, 0, G, GP, cols("scat_q", 2, 0, G)), signed(0, after=cols("scat_q", 3, 0, G))] + [signed(1), signed(2)] + [f_chi(i, GP) for i in lo] + [signed(3)]
+        qg += [signed(4, after=[("kern_q", 1)]), signed(5), signed(6, 2, 0, H, after=[("kern_q", 3)]), signed(6, 2, H, H), weave_res(1, P, GP)]
 
-        load_chi = (lambda: SP.dma_start(out=rows[CHI_AT:CHI_AT + PIECES], in_=chi.partition_broadcast(PIECES))), ["nusf"], ["chi"]
-        qy = [load_chi] + [store(u) for u in units[:7]] + [store_codes(0, 0, G), store(units[7]), store_codes(1, 0, H), store_codes(1, H, H)]
+        qy = [store(units[k]) for k in range(8)] + [store_codes(0, 0, G), store_codes(1, 0, H), store_codes(1, H, H)]
         qy += [store_scales(0, SP), store_scales(2, SP)]
         emit([qt, qv, qs, qg, qy])

@@ -57,7 +57,7 @@ def tile_multigroupintegraltransportsourceiterati_x1_kernel(tc, flux, scat, dens
         scat_codes = tile("scat_codes", [P, M, G], U32)
         scat_sc = tile("scat_sc", [P, M, G], U8)
         pd = tile("pd", [P, NT, M], F32)
-        f = tile("f", [P, NT], F32)
+        f = tiles("f", 2, [P, 4], F32)
         x = tiles("x", 2, [P, 4, G], F32)
         sg = tile("sg", [P, NT, G], BF16)
         rst = tiles("rst", 2, [P, 4, G], F32)
@@ -180,13 +180,14 @@ def tile_multigroupintegraltransportsourceiterati_x1_kernel(tc, flux, scat, dens
             return run, needs + [("flux_q", i)] + cols("scat_q", m, 0, G), [("a", i, m)]
 
         def fission(i):
-            alloc, needs = take("sb", "p", [P, NT, M])
+            i0 = 4 * (i // 4)
+            alloc, needs = take("sb", ("p", i0), [P, 4, M])
 
             def run():
-                ps = alloc() if i == 0 else bank["p"]
+                ps = alloc() if i == i0 else bank["p", i0]
                 for j in range(4):
-                    T.matmul(ps[:, i], lhsT=flux_grp[i // 4][:, i % 4, :, j], rhs=nusf_k[:, j // 2, :, j % 2], start=(j == 0), stop=(j == 3))
-            return run, (needs if i == 0 else []) + [("flux_grp", i // 2), "nusf_t"], ["p"] if i == NT - 1 else []
+                    T.matmul(ps[:, i - i0], lhsT=flux_grp[i // 4][:, i % 4, :, j], rhs=nusf_k[:, j // 2, :, j % 2], start=(j == 0), stop=(j == 3))
+            return run, (needs if i == i0 else []) + [("flux_grp", i // 2), "nusf_t"], [("p", i0)] if i == i0 + 3 else []
 
         def spread_chi():
             alloc, needs = take("tp", "chi", [P, G], BF16)
@@ -303,19 +304,21 @@ def tile_multigroupintegraltransportsourceiterati_x1_kernel(tc, flux, scat, dens
                 V.scalar_tensor_tensor(out=xi, in0=bank["a", i, m][:, c0:c0 + w], scalar=dens32[:, i, m:m + 1], in1=xi, op0=ALU.mult, op1=ALU.add)
             return run, [("a", i, m), ("x", i, m - 1)], [("x", i, m), ("read", ("a", i, m))] if c0 + w == G else []
 
-        def f_weigh():
-            return (lambda: V.tensor_tensor(out=pd[:], in0=bank["p"][:], in1=dens32[:], op=ALU.mult)), ["p"], ["pd", ("read", "p")]
+        def f_weigh(g):
+            def run():
+                V.tensor_tensor(out=pd[:, 4 * g:4 * g + 4], in0=bank["p", 4 * g][:], in1=dens32[:, 4 * g:4 * g + 4], op=ALU.mult)
+            return run, [("p", 4 * g)], [("pd", g), ("read", ("p", 4 * g))]
 
-        def f_sum():
-            return (lambda: V.tensor_reduce(out=f[:], in_=pd[:], axis=AX.X, op=ALU.add)), ["pd"], ["f"]
+        def f_sum(g):
+            return (lambda: V.tensor_reduce(out=f[g][:], in_=pd[:, 4 * g:4 * g + 4], axis=AX.X, op=ALU.add)), [("pd", g)], [("f", g)]
 
         def f_chi(i, eng):
             def run():
                 if eng is S:
-                    S.activation(out=fx[i // 4][:, i % 4], in_=chi_b[:], func=ACT.Copy, scale=f[:, i:i + 1])
+                    S.activation(out=fx[i // 4][:, i % 4], in_=chi_b[:], func=ACT.Copy, scale=f[i // 4][:, i % 4:i % 4 + 1])
                 else:
-                    GP.tensor_scalar(out=fx[i // 4][:, i % 4], in0=chi_b[:], scalar1=f[:, i:i + 1], scalar2=0.0, op0=ALU.mult, op1=ALU.add)
-            return run, ["f", "chi_b"], [("fx", i)]
+                    GP.tensor_scalar(out=fx[i // 4][:, i % 4], in0=chi_b[:], scalar1=f[i // 4][:, i % 4:i % 4 + 1], scalar2=0.0, op0=ALU.mult, op1=ALU.add)
+            return run, [("f", i // 4), "chi_b"], [("fx", i)]
 
         def source(g, c0):
             def run():
@@ -398,34 +401,34 @@ def tile_multigroupintegraltransportsourceiterati_x1_kernel(tc, flux, scat, dens
         units = [(g, 2 * h, 2, c0, H) for g in range(2) for c0 in (0, H) for h in range(2)]
         quarters = range(0, G, P)
         SCAT_PIECES = [[("a", 0, G)], [("b", 0, G)], [("c", 0, G)], [("c", 0, G)]]
-        INV_IN = ["c", None, "kern1", "kern3"]
+        INV_IN = [None, "c", "kern0", "kern3"]
 
         qt = [t_pad("dens", 0, NT, "sa"), t_flux(0), t_nusf(), total(0, "sb"), t_flux(1), total(1, "sa"), scatter(0, 0), scatter(1, 0), fission(0), scatter(2, 0), scatter(3, 0), scatter(0, 1), scatter(1, 1)]
-        qt += [t_flux(2), scatter(2, 1), scatter(3, 1), t_flux(3), scatter(0, 2), scatter(1, 2), total(2, "sa"), scatter(2, 2), fission(1), scatter(3, 2), spread_chi()] + [fission(i) for i in range(2, 6)]
-        qt += [scatter(0, 3), total(3, "sa"), scatter(1, 3), fission(6), scatter(4, 0, "tp"), fission(7), scatter(2, 3), scatter(5, 0, "tp"), scatter(3, 3), scatter(4, 1)]
-        qt += [scatter(6, 0, "tp"), scatter(5, 1), scatter(7, 0, "tp"), scatter(6, 1), scatter(7, 1), total(4, "sb"), scatter(4, 2), t_kern(0), scatter(5, 2), scatter(6, 2), t_kern(1), scatter(7, 2), total(5, "sa"), t_kern(2), t_kern(3)]
-        qt += [scatter(4, 3), total(6, "sb"), scatter(5, 3), scatter(6, 3), t_kern(4), t_kern(5), total(7, "sa"), scatter(7, 3)]
-        qt += [open_unit(u, "mm") for u in units[:3]] + [t_kern(6), t_kern(7), open_unit(units[3], "mm"), close_unit(units[0]), close_unit(units[1]), open_unit(units[4], "sb"), close_unit(units[4])]
-        qt += [close_unit(units[2]), close_unit(units[3]), open_unit(units[5], "tp"), close_unit(units[5]), open_unit(units[6], "tp"), close_unit(units[6])]
-        qt += [open_unit(units[7], "sa"), close_unit(units[7])]
+        qt += [t_flux(2), scatter(2, 1), scatter(3, 1), t_flux(3), scatter(0, 2), scatter(1, 2), total(2, "sa"), scatter(2, 2), fission(1), scatter(3, 2), spread_chi(), fission(2), fission(3)]
+        qt += [scatter(0, 3), total(3, "sa"), scatter(1, 3), scatter(4, 0, "tp"), scatter(2, 3), scatter(5, 0, "tp"), fission(4), scatter(3, 3), scatter(4, 1)]
+        qt += [scatter(6, 0, "tp"), scatter(5, 1), scatter(7, 0, "tp"), fission(5), scatter(6, 1), scatter(7, 1), fission(6), total(4, "sa"), scatter(4, 2), fission(7), scatter(5, 2), scatter(6, 2), total(5, "sb")]
+        qt += [t_kern(0), t_kern(1), scatter(7, 2), scatter(4, 3), total(6, "sa"), scatter(5, 3), scatter(6, 3), t_kern(2), t_kern(3), total(7, "sb"), t_kern(4), scatter(7, 3), t_kern(5)]
+        qt += [open_unit(units[0], "mm"), open_unit(units[2], "mm"), t_kern(6), t_kern(7), open_unit(units[1], "mm"), close_unit(units[0]), close_unit(units[1]), open_unit(units[3], "mm")]
+        qt += [close_unit(units[2]), close_unit(units[3]), open_unit(units[4], "sa"), close_unit(units[4]), open_unit(units[5], "tp"), close_unit(units[5]), open_unit(units[6], "tp"), close_unit(units[6])]
+        qt += [open_unit(units[7], "sb"), close_unit(units[7])]
 
         qv = [weave_scat(0, 0, H, V), weave_scat(0, H, H, V), quant_scat(0, 0, H), quant_scat(0, H, H), weave_scat(1, 0, H, V), quant_flux(0, 2), weave_scat(1, H, H, V)]
         qv += [weave_scat(2, 0, H, V), quant_flux(2, 2), quant_scat(1, 0, G), weave_scat(2, H, H, V), quant_scat(2, 0, H), quant_scat(2, H, H)]
         qv += [weigh_add(i, 1) for i in lo] + [weigh_add(i, 2) for i in lo[:3]]
-        qv += [quant_scat(3, 0, G), quant_flux(4, 4), weigh_add(3, 2), weigh_add(0, 3), weigh_add(1, 3), f_weigh(), weigh_add(2, 3), f_sum(), weigh_add(3, 3)]
-        qv += [weigh_add(i, m) for m in (1, 2) for i in hi][:-1]
-        qv += [source(0, 0), source(0, H), quant_kern(0), quant_q(0, 0, G), quant_kern(1), weigh_add(7, 2)] + [weigh_add(i, 3) for i in hi[:3]] + [weigh_add(7, 3, 0, H), weigh_add(7, 3, H, H)]
-        qv += [source(1, 0), quant_kern(2), quant_q(1, 0, H), source(1, H), divide(units[0]), quant_q(1, H, H), divide(units[1]), quant_kern(3)]
+        qv += [quant_scat(3, 0, G), quant_flux(4, 4), weigh_add(3, 2), f_weigh(0), weigh_add(0, 3), f_sum(0)] + [weigh_add(i, 3) for i in lo[1:]]
+        qv += [weigh_add(i, 1) for i in hi] + [weigh_add(4, 2), f_weigh(1), weigh_add(5, 2), f_sum(1), weigh_add(6, 2)]
+        qv += [source(0, 0), source(0, H), quant_q(0, 0, H), quant_q(0, H, H), quant_kern(0), weigh_add(7, 2)] + [weigh_add(i, 3) for i in hi[:3]] + [weigh_add(7, 3, 0, H), weigh_add(7, 3, H, H)]
+        qv += [source(1, 0), quant_kern(1), quant_q(1, 0, H), source(1, H), divide(units[0]), quant_q(1, H, H), divide(units[1]), quant_kern(2), quant_kern(3)]
         qv += [divide(u) for u in units[2:]] + [quant_res(0, 0, G)]
         qv += [weave_res(1, H + P, V), quant_res(1, 0, H), quant_res(1, H, H)]
 
-        qs = [c_pad("dens", dens_t, 0, NT), c_flux(0), c_nusf(), root(0), c_flux(1), sign(0), weigh_first(0), weigh_first(1), weigh_first(2), weigh_first(3), root(1), c_flux(2), sign(1), c_flux(3), square(0), square(1), root(2), sign(2), square(2), c_chi()]
-        qs += [root(3), weigh_first(4), weigh_first(5), weigh_first(6), weigh_first(7), sign(3), square(3), root(4), sign(4), c_kern(0), c_kern(1), square(4), root(5), sign(5), c_kern(2), c_kern(3), square(5)]
-        qs += [f_chi(i, S) for i in hi] + [c_kern(4), c_kern(5), root(6), sign(6), c_kern(6), c_kern(7), square(6)] + inverse(7)
+        qs = [c_pad("dens", dens_t, 0, NT), c_flux(0), c_nusf(), root(0), c_flux(1), sign(0), weigh_first(0), weigh_first(1), weigh_first(2), weigh_first(3), root(1), c_flux(2), sign(1), square(0), c_flux(3), square(1), root(2), sign(2), square(2), c_chi()]
+        qs += [root(3), weigh_first(4), weigh_first(5), weigh_first(6), weigh_first(7), sign(3), square(3), root(4), sign(4), square(4), root(5), sign(5), c_kern(0), c_kern(1), square(5)]
+        qs += [f_chi(4, S), f_chi(5, S), c_kern(2), c_kern(3), f_chi(6, S), f_chi(7, S), c_kern(4), c_kern(5), root(6), sign(6), c_kern(6), c_kern(7), square(6)] + inverse(7)
         qs += [weave_res(0, c, S) for c in quarters] + [weave_res(1, 0, S), weave_res(1, H, S)] + [store_scales(1, S), store_scales(3, S)]
 
-        qg = [weave_scat(3, 0, G, GP, cols("scat_q", 2, 0, G)), signed(0, after=cols("scat_q", 3, 0, G))] + [signed(1), signed(2)] + [f_chi(i, GP) for i in lo] + [signed(3)]
-        qg += [signed(4, after=[("kern_q", 1)]), signed(5), signed(6, 2, 0, H, after=[("kern_q", 3)]), signed(6, 2, H, H), weave_res(1, P, GP)]
+        qg = [weave_scat(3, 0, G, GP, cols("scat_q", 2, 0, G)), signed(0, 1, 0, H), signed(2, after=cols("scat_q", 3, 0, G))] + [f_chi(i, GP) for i in lo] + [signed(0, 1, H, H), signed(1), signed(3)]
+        qg += [signed(4, after=[("kern_q", 0)]), signed(5), signed(6, 2, 0, H, after=[("kern_q", 3)]), signed(6, 2, H, H), weave_res(1, P, GP)]
 
         qy = [store(units[k]) for k in range(8)] + [store_codes(0, 0, G), store_codes(1, 0, H), store_codes(1, H, H)]
         qy += [store_scales(0, SP), store_scales(2, SP)]

@@ -37,7 +37,6 @@ def tile_multigroupintegraltransportsourceiterati_x1_kernel(tc, flux, scat, dens
             return [tile("%s%d" % (name, k), shape, dtype) for k in range(n)]
 
         rows = tile("rows", [P, G], BF16)
-        chi_pad = tile("chi_pad", [P, G], BF16)
         sig_pad = tile("sig_pad", [P, G], BF16)
         dens_pad = tile("dens_pad", [P, NT, P], BF16)
         dens_sb = tile("dens_sb", [P, 2, 4 * M], BF16)
@@ -189,10 +188,6 @@ def tile_multigroupintegraltransportsourceiterati_x1_kernel(tc, flux, scat, dens
                     T.matmul(ps[:, i - i0], lhsT=flux_grp[i // 4][:, i % 4, :, j], rhs=nusf_k[:, j // 2, :, j % 2], start=(j == 0), stop=(j == 3))
             return run, (needs if i == i0 else []) + [("flux_grp", i // 2), "nusf_t"], [("p", i0)] if i == i0 + 3 else []
 
-        def spread_chi():
-            alloc, needs = take("tp", "chi", [P, G], BF16)
-            return (lambda: T.matmul(alloc()[:], lhsT=id16[:, 0:1].to_broadcast([P, P]), rhs=chi_pad[:], start=True, stop=True)), needs, ["chi"]
-
         def transport_pass(ps, unit, gs):
             g, t0, n, c0, w = unit
             for a in range(n):
@@ -215,9 +210,6 @@ def tile_multigroupintegraltransportsourceiterati_x1_kernel(tc, flux, scat, dens
 
         def c_nusf():
             return (lambda: S.copy(out=nusf_t[:], in_=bank["nusf"][:, :, NU_AT:NU_AT + M])), ["nusf"], ["nusf_t", ("read", "nusf")]
-
-        def c_chi():
-            return (lambda: S.copy(out=chi_b[:], in_=bank["chi"][:])), ["chi"], ["chi_b", ("read", "chi")]
 
         def words_out(eng, dst, src):
             if eng is S:
@@ -318,7 +310,7 @@ def tile_multigroupintegraltransportsourceiterati_x1_kernel(tc, flux, scat, dens
                     S.activation(out=fx[i // 4][:, i % 4], in_=chi_b[:], func=ACT.Copy, scale=f[i // 4][:, i % 4:i % 4 + 1])
                 else:
                     GP.tensor_scalar(out=fx[i // 4][:, i % 4], in0=chi_b[:], scalar1=f[i // 4][:, i % 4:i % 4 + 1], scalar2=0.0, op0=ALU.mult, op1=ALU.add)
-            return run, [("f", i // 4), "chi_b"], [("fx", i)]
+            return run, [("f", i // 4)], [("fx", i)]
 
         def source(g, c0):
             def run():
@@ -374,23 +366,23 @@ def tile_multigroupintegraltransportsourceiterati_x1_kernel(tc, flux, scat, dens
             SP.dma_start(out=flux_raw[b][:], in_=flux_v[b // 2, :, 2 * (b % 2):2 * (b % 2) + 2])
 
         V.memset(warm[:], 1.0)
-        for t in (sig_pad, rows, chi_pad, dens_pad):
+        for t in (sig_pad, rows, dens_pad):
             V.memset(t[:], 0.0)
         make_identity(nc, id32[:])
         S.dma_start(out=dens_sb[:], in_=dens.rearrange("(g p t) m -> p g (t m)", g=2, t=4))
         S.dma_start(out=sig_pad[0:M], in_=sigt)
         load_scat(0)
-        SP.dma_start(out=rows[NU_AT:NU_AT + M], in_=nusf)
         load_flux(0)
+        SP.dma_start(out=rows[NU_AT:NU_AT + M], in_=nusf)
         load_scat(1)
         load_flux(1)
-        SP.dma_start(out=chi_pad[0:1], in_=chi.rearrange("(o g) -> o g", o=1))
         load_scat(2)
         load_scat(3)
         load_flux(2)
         load_flux(3)
-        for g in range(2):
-            SP.dma_start(out=kern_raw[g][:], in_=kern_v[g])
+        SP.dma_start(out=kern_raw[0][:], in_=kern_v[0])
+        SP.dma_start(out=chi_b[:], in_=chi.partition_broadcast(P))
+        SP.dma_start(out=kern_raw[1][:], in_=kern_v[1])
 
         S.activation(out=warm[:, 1:2], in_=warm[:, 0:1], func=ACT.Abs_reciprocal_sqrt)
         V.tensor_copy(out=dens_pad[:, :, 0:M], in_=dens_v)
@@ -401,34 +393,34 @@ def tile_multigroupintegraltransportsourceiterati_x1_kernel(tc, flux, scat, dens
         units = [(g, 2 * h, 2, c0, H) for g in range(2) for c0 in (0, H) for h in range(2)]
         quarters = range(0, G, P)
         SCAT_PIECES = [[("a", 0, G)], [("b", 0, G)], [("c", 0, G)], [("c", 0, G)]]
-        INV_IN = [None, "c", "kern0", "kern3"]
+        INV_IN = ["c", None, "kern0", "kern3"]
 
         qt = [t_pad("dens", 0, NT, "sa"), t_flux(0), t_nusf(), total(0, "sb"), t_flux(1), total(1, "sa"), scatter(0, 0), scatter(1, 0), fission(0), scatter(2, 0), scatter(3, 0), scatter(0, 1), scatter(1, 1)]
-        qt += [t_flux(2), scatter(2, 1), scatter(3, 1), t_flux(3), scatter(0, 2), scatter(1, 2), total(2, "sa"), scatter(2, 2), fission(1), scatter(3, 2), spread_chi(), fission(2), fission(3)]
-        qt += [scatter(0, 3), total(3, "sa"), scatter(1, 3), scatter(4, 0, "tp"), scatter(2, 3), scatter(5, 0, "tp"), fission(4), scatter(3, 3), scatter(4, 1)]
-        qt += [scatter(6, 0, "tp"), scatter(5, 1), scatter(7, 0, "tp"), fission(5), scatter(6, 1), scatter(7, 1), fission(6), total(4, "sa"), scatter(4, 2), fission(7), scatter(5, 2), scatter(6, 2), total(5, "sb")]
-        qt += [t_kern(0), t_kern(1), scatter(7, 2), scatter(4, 3), total(6, "sa"), scatter(5, 3), scatter(6, 3), t_kern(2), t_kern(3), total(7, "sb"), t_kern(4), scatter(7, 3), t_kern(5)]
-        qt += [open_unit(units[0], "mm"), open_unit(units[2], "mm"), t_kern(6), t_kern(7), open_unit(units[1], "mm"), close_unit(units[0]), close_unit(units[1]), open_unit(units[3], "mm")]
-        qt += [close_unit(units[2]), close_unit(units[3]), open_unit(units[4], "sa"), close_unit(units[4]), open_unit(units[5], "tp"), close_unit(units[5]), open_unit(units[6], "tp"), close_unit(units[6])]
-        qt += [open_unit(units[7], "sb"), close_unit(units[7])]
+        qt += [t_flux(2), scatter(2, 1), scatter(3, 1), t_flux(3), scatter(0, 2), scatter(1, 2), total(2, "sa"), scatter(2, 2), fission(1), scatter(3, 2), fission(2), total(3, "tp"), fission(3)]
+        qt += [scatter(0, 3), scatter(1, 3), scatter(4, 0, "tp"), scatter(2, 3), scatter(3, 3), scatter(5, 0, "tp"), total(4, "sa"), scatter(4, 1), fission(4)]
+        qt += [scatter(6, 0, "tp"), scatter(5, 1), scatter(7, 0, "tp"), scatter(6, 1), fission(5), scatter(7, 1), scatter(4, 2), fission(6), scatter(5, 2), scatter(6, 2), fission(7), total(5, "sa")]
+        qt += [t_kern(0), t_kern(1), scatter(7, 2), scatter(4, 3), total(6, "sb"), scatter(5, 3), scatter(6, 3), t_kern(2), t_kern(3), total(7, "sa"), scatter(7, 3), t_kern(4), open_unit(units[0], "mm"), open_unit(units[2], "mm"), t_kern(5)]
+        qt += [open_unit(units[1], "mm"), open_unit(units[3], "mm"), t_kern(6), t_kern(7), close_unit(units[0]), close_unit(units[1])]
+        qt += [close_unit(units[2]), close_unit(units[3]), open_unit(units[4], "sb"), close_unit(units[4]), open_unit(units[5], "tp"), close_unit(units[5]), open_unit(units[6], "tp"), close_unit(units[6])]
+        qt += [open_unit(units[7], "sa"), close_unit(units[7])]
 
         qv = [weave_scat(0, 0, H, V), weave_scat(0, H, H, V), quant_scat(0, 0, H), quant_scat(0, H, H), weave_scat(1, 0, H, V), quant_flux(0, 2), weave_scat(1, H, H, V)]
         qv += [weave_scat(2, 0, H, V), quant_flux(2, 2), quant_scat(1, 0, G), weave_scat(2, H, H, V), quant_scat(2, 0, H), quant_scat(2, H, H)]
         qv += [weigh_add(i, 1) for i in lo] + [weigh_add(i, 2) for i in lo[:3]]
         qv += [quant_scat(3, 0, G), quant_flux(4, 4), weigh_add(3, 2), f_weigh(0), weigh_add(0, 3), f_sum(0)] + [weigh_add(i, 3) for i in lo[1:]]
-        qv += [weigh_add(i, 1) for i in hi] + [weigh_add(4, 2), f_weigh(1), weigh_add(5, 2), f_sum(1), weigh_add(6, 2)]
-        qv += [source(0, 0), source(0, H), quant_q(0, 0, H), quant_q(0, H, H), quant_kern(0), weigh_add(7, 2)] + [weigh_add(i, 3) for i in hi[:3]] + [weigh_add(7, 3, 0, H), weigh_add(7, 3, H, H)]
-        qv += [source(1, 0), quant_kern(1), quant_q(1, 0, H), source(1, H), divide(units[0]), quant_q(1, H, H), divide(units[1]), quant_kern(2), quant_kern(3)]
+        qv += [weigh_add(i, 1) for i in hi] + [weigh_add(i, 2) for i in hi[:3]]
+        qv += [f_weigh(1), source(0, 0), f_sum(1), source(0, H), quant_q(0, 0, H), quant_q(0, H, H), quant_kern(0), weigh_add(7, 2)] + [weigh_add(i, 3) for i in hi]
+        qv += [quant_kern(1), source(1, 0), source(1, H), quant_q(1, 0, H), quant_q(1, H, H), quant_kern(2), divide(units[0]), divide(units[1]), quant_kern(3)]
         qv += [divide(u) for u in units[2:]] + [quant_res(0, 0, G)]
         qv += [weave_res(1, H + P, V), quant_res(1, 0, H), quant_res(1, H, H)]
 
-        qs = [c_pad("dens", dens_t, 0, NT), c_flux(0), c_nusf(), root(0), c_flux(1), sign(0), weigh_first(0), weigh_first(1), weigh_first(2), weigh_first(3), root(1), c_flux(2), sign(1), square(0), c_flux(3), square(1), root(2), sign(2), square(2), c_chi()]
-        qs += [root(3), weigh_first(4), weigh_first(5), weigh_first(6), weigh_first(7), sign(3), square(3), root(4), sign(4), square(4), root(5), sign(5), c_kern(0), c_kern(1), square(5)]
+        qs = [c_pad("dens", dens_t, 0, NT), c_flux(0), c_nusf(), root(0), c_flux(1), sign(0), weigh_first(0), weigh_first(1), weigh_first(2), weigh_first(3), root(1), c_flux(2), sign(1), square(0), c_flux(3), square(1), root(2), sign(2), square(2)]
+        qs += [root(3), sign(3), weigh_first(4), weigh_first(5), square(3), weigh_first(6), weigh_first(7), f_chi(3, S), root(4), sign(4), square(4), root(5), sign(5), c_kern(0), c_kern(1), square(5)]
         qs += [f_chi(4, S), f_chi(5, S), c_kern(2), c_kern(3), f_chi(6, S), f_chi(7, S), c_kern(4), c_kern(5), root(6), sign(6), c_kern(6), c_kern(7), square(6)] + inverse(7)
         qs += [weave_res(0, c, S) for c in quarters] + [weave_res(1, 0, S), weave_res(1, H, S)] + [store_scales(1, S), store_scales(3, S)]
 
-        qg = [weave_scat(3, 0, G, GP, cols("scat_q", 2, 0, G)), signed(0, 1, 0, H), signed(2, after=cols("scat_q", 3, 0, G))] + [f_chi(i, GP) for i in lo] + [signed(0, 1, H, H), signed(1), signed(3)]
-        qg += [signed(4, after=[("kern_q", 0)]), signed(5), signed(6, 2, 0, H, after=[("kern_q", 3)]), signed(6, 2, H, H), weave_res(1, P, GP)]
+        qg = [weave_scat(3, 0, G, GP, cols("scat_q", 2, 0, G)), signed(0, 2, after=cols("scat_q", 3, 0, G))] + [f_chi(i, GP) for i in lo[:3]] + [signed(2, 2)]
+        qg += [signed(4, 2, after=[("kern_q", 0)]), signed(6, 2, 0, H, after=[("kern_q", 3)]), signed(6, 2, H, H), weave_res(1, P, GP)]
 
         qy = [store(units[k]) for k in range(8)] + [store_codes(0, 0, G), store_codes(1, 0, H), store_codes(1, H, H)]
         qy += [store_scales(0, SP), store_scales(2, SP)]

@@ -18,6 +18,7 @@ R, G, M = 1024, 512, 4
 NT = R // P
 H = G // 2
 CHI_AT, NU_AT = 4, 8
+PIECES = 3
 BANKS = {"mm": 4, "tp": 2, "sa": 1, "sb": 1}
 FLOPS = 2 * R * G * G * M + 2 * R * R * G
 
@@ -49,7 +50,9 @@ def tile_multigroupintegraltransportsourceiterati_x1_kernel(tc, flux, scat, dens
         dens32 = tile("dens32", [P, NT, M], F32)
         dens_t = tile("dens_t", [P, NT, P], BF16)
         chi_b = tile("chi_b", [P, G], BF16)
-        fx = tiles("fx", 2, [P, 4, G], F32)
+        fx = tile("fx", [P, 4, G], F32)
+        f_t = tile("f_t", [P, 4, P], BF16)
+        f_rest = tile("f_rest", [P, 4], F32)
         flux_grp = tiles("flux_grp", 2, [P, 4, P, 4], BF16)
         flux_codes = tile("flux_codes", [P, NT, P], U32)
         flux_sc = tile("flux_sc", [P, NT, P], U8)
@@ -121,6 +124,8 @@ def tile_multigroupintegraltransportsourceiterati_x1_kernel(tc, flux, scat, dens
             return tenant("q%d" % g, "q_grp%d" % g, [P, G, 4], BF16)
 
         def inv(i, n):
+            if i == NT - 1:
+                return tenant("kern3", "inv_last", [P, 1, G], F32)[:]
             buffer = INV_IN[i // 2]
             if buffer is None:
                 return rst[i // 4][:, i % 4:i % 4 + n]
@@ -133,7 +138,7 @@ def tile_multigroupintegraltransportsourceiterati_x1_kernel(tc, flux, scat, dens
                 ps = alloc()
                 for i in range(n):
                     T.transpose(ps[:, i], dens_pad[:, i0 + i], id16[:])
-            return run, needs, [(name, i0)]
+            return run, needs + (["pieces"] if name == "f" else []), [(name, i0)]
 
         def t_flux(b):
             alloc, needs = take("tp", ("flux", b), [P, 2, 2, P])
@@ -188,6 +193,15 @@ def tile_multigroupintegraltransportsourceiterati_x1_kernel(tc, flux, scat, dens
                     T.matmul(ps[:, i - i0], lhsT=flux_grp[i // 4][:, i % 4, :, j], rhs=nusf_k[:, j // 2, :, j % 2], start=(j == 0), stop=(j == 3))
             return run, (needs if i == i0 else []) + [("flux_grp", i // 2), "nusf_t"], [("p", i0)] if i == i0 + 3 else []
 
+        def emission(c0, ring):
+            alloc, needs = take(ring, ("e", c0), [P, 4, P])
+
+            def run():
+                ps = alloc()
+                for t in range(4):
+                    T.matmul(ps[:, t], lhsT=f_t[:, t], rhs=rows[:, c0:c0 + P], start=True, stop=True)
+            return run, needs + ["f_t", "chi"], [("e", c0)]
+
         def transport_pass(ps, unit, gs):
             g, t0, n, c0, w = unit
             for a in range(n):
@@ -207,6 +221,9 @@ def tile_multigroupintegraltransportsourceiterati_x1_kernel(tc, flux, scat, dens
 
         def c_pad(name, dst, i0, n):
             return (lambda: S.copy(out=dst[:, i0:i0 + n], in_=bank[name, i0][:])), [(name, i0)], [(name + "_t", i) for i in range(i0, i0 + n)] + [("read", (name, i0))]
+
+        def c_f():
+            return (lambda: S.copy(out=f_t[:], in_=bank["f", 4][:])), [("f", 4)], ["f_t", ("read", ("f", 4))]
 
         def c_nusf():
             return (lambda: S.copy(out=nusf_t[:], in_=bank["nusf"][:, :, NU_AT:NU_AT + M])), ["nusf"], ["nusf_t", ("read", "nusf")]
@@ -302,28 +319,54 @@ def tile_multigroupintegraltransportsourceiterati_x1_kernel(tc, flux, scat, dens
             return run, [("p", 4 * g)], [("pd", g), ("read", ("p", 4 * g))]
 
         def f_sum(g):
-            return (lambda: V.tensor_reduce(out=f[g][:], in_=pd[:, 4 * g:4 * g + 4], axis=AX.X, op=ALU.add)), [("pd", g)], [("f", g)]
+            return (lambda: V.tensor_reduce(out=f[g][:], in_=pd[:, 4 * g:4 * g + 4], axis=AX.X, op=ALU.add)), [("pd", g)], [("fsum", g)]
 
         def f_chi(i, eng):
             def run():
                 if eng is S:
-                    S.activation(out=fx[i // 4][:, i % 4], in_=chi_b[:], func=ACT.Copy, scale=f[i // 4][:, i % 4:i % 4 + 1])
+                    S.activation(out=fx[:, i], in_=chi_b[:], func=ACT.Copy, scale=f[i // 4][:, i % 4:i % 4 + 1])
                 else:
-                    GP.tensor_scalar(out=fx[i // 4][:, i % 4], in0=chi_b[:], scalar1=f[i // 4][:, i % 4:i % 4 + 1], scalar2=0.0, op0=ALU.mult, op1=ALU.add)
-            return run, [("f", i // 4)], [("fx", i)]
+                    GP.tensor_scalar(out=fx[:, i], in0=chi_b[:], scalar1=f[i // 4][:, i % 4:i % 4 + 1], scalar2=0.0, op0=ALU.mult, op1=ALU.add)
+            return run, [("fsum", i // 4)], [("fx", i)]
 
         def source(g, c0):
             def run():
                 dst, s = blocks(q_grp(g)[:, c0:c0 + H], x[g][:, :, c0:c0 + H])
-                V.tensor_tensor(out=dst, in0=s, in1=fx[g][:, :, c0:c0 + H].rearrange("p t (c i) -> p c t i", i=4), op=ALU.add)
+                V.tensor_tensor(out=dst, in0=s, in1=fx[:, :, c0:c0 + H].rearrange("p t (c i) -> p c t i", i=4), op=ALU.add)
             return run, [k for i in range(4 * g, 4 * g + 4) for k in (("x", i, M - 1), ("fx", i))], cols("q_grp", g, c0, H)
+
+        def piece(k):
+            return dens_pad[:, 4:NT, CHI_AT + k]
+
+        def f_first():
+            def run():
+                with nc.allow_low_precision(reason="the first bf16 piece of f; the later pieces carry the rest"):
+                    V.tensor_reduce(out=piece(0), in_=pd[:, 4:NT], axis=AX.X, op=ALU.add)
+            return run, [("pd", 1)], ["first"]
+
+        def f_less_first():
+            return (lambda: V.tensor_tensor(out=f_rest[:], in0=f[1][:], in1=piece(0), op=ALU.subtract)), [("fsum", 1), "first"], ["rest"]
+
+        def f_second():
+            return (lambda: V.tensor_copy(out=piece(1), in_=f_rest[:])), ["rest"], ["second"]
+
+        def f_third():
+            return (lambda: V.tensor_tensor(out=piece(2), in0=f_rest[:], in1=piece(1), op=ALU.subtract)), ["second"], ["pieces"]
+
+        def source_late(c0):
+            def run():
+                dst, s = blocks(q_grp(1)[:, c0:c0 + P], x[1][:, :, c0:c0 + P])
+                V.tensor_tensor(out=dst, in0=bank["e", c0][:].rearrange("p t (c i) -> p c t i", i=4), in1=s, op=ALU.add)
+            return run, [("x", i, M - 1) for i in range(4, NT)] + [("e", c0)], cols("q_grp", 1, c0, P) + [("read", ("e", c0))]
 
         def divide(unit):
             g, t0, n, c0, w = unit
             i0 = 4 * g + t0
 
             def run():
-                V.tensor_tensor(out=res[g][:, t0:t0 + n, c0:c0 + w], in0=bank["c", unit][:], in1=inv(i0, n)[:, :, c0:c0 + w], op=ALU.mult)
+                step = 1 if i0 + n == NT else n
+                for a in range(0, n, step):
+                    V.tensor_tensor(out=res[g][:, t0 + a:t0 + a + step, c0:c0 + w], in0=bank["c", unit][:, a:a + step], in1=inv(i0 + a, step)[:, :, c0:c0 + w], op=ALU.mult)
             needs = [k for i in range(i0, i0 + n) for k in cols("inv", i, c0, w)]
             return run, [("c", unit)] + needs, [k for t in range(t0, t0 + n) for k in cols(("res", t), g, c0, w)] + [("read", ("c", unit))]
 
@@ -393,35 +436,38 @@ def tile_multigroupintegraltransportsourceiterati_x1_kernel(tc, flux, scat, dens
         units = [(g, 2 * h, 2, c0, H) for g in range(2) for c0 in (0, H) for h in range(2)]
         quarters = range(0, G, P)
         SCAT_PIECES = [[("a", 0, G)], [("b", 0, G)], [("c", 0, G)], [("c", 0, G)]]
-        INV_IN = ["c", None, "kern0", "kern3"]
+        INV_IN = ["c", None, "kern0", None]
 
         qt = [t_pad("dens", 0, NT, "sa"), t_flux(0), t_nusf(), total(0, "sb"), t_flux(1), total(1, "sa"), scatter(0, 0), scatter(1, 0), fission(0), scatter(2, 0), scatter(3, 0), scatter(0, 1), scatter(1, 1)]
         qt += [t_flux(2), scatter(2, 1), scatter(3, 1), t_flux(3), scatter(0, 2), scatter(1, 2), total(2, "sa"), scatter(2, 2), fission(1), scatter(3, 2), fission(2), total(3, "tp"), fission(3)]
         qt += [scatter(0, 3), scatter(1, 3), scatter(4, 0, "tp"), scatter(2, 3), scatter(3, 3), scatter(5, 0, "tp"), total(4, "sa"), scatter(4, 1), fission(4)]
         qt += [scatter(6, 0, "tp"), scatter(5, 1), scatter(7, 0, "tp"), scatter(6, 1), fission(5), scatter(7, 1), scatter(4, 2), fission(6), scatter(5, 2), scatter(6, 2), fission(7), total(5, "sa")]
-        qt += [t_kern(0), t_kern(1), scatter(7, 2), scatter(4, 3), total(6, "sb"), scatter(5, 3), scatter(6, 3), t_kern(2), t_kern(3), total(7, "sa"), scatter(7, 3), t_kern(4), open_unit(units[0], "mm"), open_unit(units[2], "mm"), t_kern(5)]
-        qt += [open_unit(units[1], "mm"), open_unit(units[3], "mm"), t_kern(6), t_kern(7), close_unit(units[0]), close_unit(units[1])]
-        qt += [close_unit(units[2]), close_unit(units[3]), open_unit(units[4], "sb"), close_unit(units[4]), open_unit(units[5], "tp"), close_unit(units[5]), open_unit(units[6], "tp"), close_unit(units[6])]
-        qt += [open_unit(units[7], "sa"), close_unit(units[7])]
+        qt += [scatter(7, 2), t_kern(0), t_kern(1), scatter(4, 3), total(6, "sb"), scatter(5, 3), t_kern(2), scatter(6, 3), t_pad("f", 4, 4, "sa"), t_kern(3), scatter(7, 3), total(7, "sb")]
+        qt += [emission(c, "mm") for c in quarters[:3]] + [t_kern(4), emission(quarters[3], "mm"), t_kern(5), open_unit(units[0], "sa"), open_unit(units[2], "sb"), t_kern(6), t_kern(7)]
+        qt += [close_unit(units[0]), open_unit(units[1], "mm"), close_unit(units[1]), open_unit(units[3], "mm"), close_unit(units[2]), close_unit(units[3])]
+        for u, ring in zip(units[4:], ("mm", "mm", "tp", "tp")):
+            qt += [open_unit(u, ring), close_unit(u)]
 
         qv = [weave_scat(0, 0, H, V), weave_scat(0, H, H, V), quant_scat(0, 0, H), quant_scat(0, H, H), weave_scat(1, 0, H, V), quant_flux(0, 2), weave_scat(1, H, H, V)]
         qv += [weave_scat(2, 0, H, V), quant_flux(2, 2), quant_scat(1, 0, G), weave_scat(2, H, H, V), quant_scat(2, 0, H), quant_scat(2, H, H)]
         qv += [weigh_add(i, 1) for i in lo] + [weigh_add(i, 2) for i in lo[:3]]
         qv += [quant_scat(3, 0, G), quant_flux(4, 4), weigh_add(3, 2), f_weigh(0), weigh_add(0, 3), f_sum(0)] + [weigh_add(i, 3) for i in lo[1:]]
         qv += [weigh_add(i, 1) for i in hi] + [weigh_add(i, 2) for i in hi[:3]]
-        qv += [f_weigh(1), source(0, 0), f_sum(1), source(0, H), quant_q(0, 0, H), quant_q(0, H, H), quant_kern(0), weigh_add(7, 2)] + [weigh_add(i, 3) for i in hi]
-        qv += [quant_kern(1), source(1, 0), source(1, H), quant_q(1, 0, H), quant_q(1, H, H), quant_kern(2), divide(units[0]), divide(units[1]), quant_kern(3)]
+        qv += [f_weigh(1), source(0, 0), f_sum(1), f_first(), source(0, H), f_less_first(), quant_q(0, 0, H), f_second(), quant_q(0, H, H), f_third(), quant_kern(0)]
+        qv += [weigh_add(7, 2)] + [weigh_add(i, 3) for i in hi[:3]] + [weigh_add(7, 3, 0, H), weigh_add(7, 3, H, H)] + [source_late(c) for c in quarters]
+        qv += [quant_kern(1), quant_q(1, 0, H), quant_q(1, H, H), quant_kern(2), divide(units[0]), divide(units[1]), quant_kern(3)]
         qv += [divide(u) for u in units[2:]] + [quant_res(0, 0, G)]
         qv += [weave_res(1, H + P, V), quant_res(1, 0, H), quant_res(1, H, H)]
 
         qs = [c_pad("dens", dens_t, 0, NT), c_flux(0), c_nusf(), root(0), c_flux(1), sign(0), weigh_first(0), weigh_first(1), weigh_first(2), weigh_first(3), root(1), c_flux(2), sign(1), square(0), c_flux(3), square(1), root(2), sign(2), square(2)]
-        qs += [root(3), sign(3), weigh_first(4), weigh_first(5), square(3), weigh_first(6), weigh_first(7), f_chi(3, S), root(4), sign(4), square(4), root(5), sign(5), c_kern(0), c_kern(1), square(5)]
-        qs += [f_chi(4, S), f_chi(5, S), c_kern(2), c_kern(3), f_chi(6, S), f_chi(7, S), c_kern(4), c_kern(5), root(6), sign(6), c_kern(6), c_kern(7), square(6)] + inverse(7)
-        qs += [weave_res(0, c, S) for c in quarters] + [weave_res(1, 0, S), weave_res(1, H, S)] + [store_scales(1, S), store_scales(3, S)]
+        qs += [root(3), sign(3), weigh_first(4), weigh_first(5), square(3), weigh_first(6), weigh_first(7), f_chi(2, S), f_chi(3, S), root(4), sign(4), square(4), root(5), sign(5), c_kern(0), c_kern(1), square(5)]
+        qs += [root(6), sign(6), c_f(), square(6), c_kern(2), c_kern(3), root(7), sign(7), c_kern(4), c_kern(5), square(7), c_kern(6), c_kern(7)]
+        qs += [weave_res(g, c, S) for g in range(2) for c in quarters[:3]] + [store_scales(1, S), store_scales(3, S)]
 
-        qg = [weave_scat(3, 0, G, GP, cols("scat_q", 2, 0, G)), signed(0, 2, after=cols("scat_q", 3, 0, G))] + [f_chi(i, GP) for i in lo[:3]] + [signed(2, 2)]
-        qg += [signed(4, 2, after=[("kern_q", 0)]), signed(6, 2, 0, H, after=[("kern_q", 3)]), signed(6, 2, H, H), weave_res(1, P, GP)]
+        qg = [weave_scat(3, 0, G, GP, cols("scat_q", 2, 0, G)), signed(0, 2, after=cols("scat_q", 3, 0, G))] + [f_chi(i, GP) for i in lo[:2]] + [signed(2, 2)]
+        qg += [signed(4, 2, after=[("kern_q", 0)]), signed(6), signed(7, after=[("kern_q", 3)]), weave_res(0, H + P, GP)]
 
-        qy = [store(units[k]) for k in range(8)] + [store_codes(0, 0, G), store_codes(1, 0, H), store_codes(1, H, H)]
+        load_chi = (lambda: SP.dma_start(out=rows[CHI_AT:CHI_AT + PIECES], in_=chi.partition_broadcast(PIECES))), ["nusf"], ["chi"]
+        qy = [load_chi] + [store(units[k]) for k in range(8)] + [store_codes(0, 0, G), store_codes(1, 0, H), store_codes(1, H, H)]
         qy += [store_scales(0, SP), store_scales(2, SP)]
         emit([qt, qv, qs, qg, qy])

@@ -72,6 +72,7 @@ def tile_multigroupintegraltransportsourceiterati_x1_kernel(tc, flux, scat, dens
         r_codes = tile("r_codes", [P, 2, G], U32)
         r_sc = tile("r_sc", [P, G], U8)
         warm = tile("warm", [P, 2], F32)
+        idle = tile("idle", [P, G], BF16)
 
         held = {}
 
@@ -89,6 +90,7 @@ def tile_multigroupintegraltransportsourceiterati_x1_kernel(tc, flux, scat, dens
         out2_v = out_2.bitcast(I32)
 
         bank = {}
+        warmed = []
 
         def take(ring, key, shape, dtype=F32):
             def alloc():
@@ -170,6 +172,11 @@ def tile_multigroupintegraltransportsourceiterati_x1_kernel(tc, flux, scat, dens
                 for u in range(2):
                     T.transpose(ps[:, u], rows[:].bitcast(F32)[:, u:H:2], id32[:])
             return run, needs, ["nusf"]
+
+        def warm_up(lhs):
+            alloc, needs = take("mm", ("warm", len(warmed)), [P, G])
+            warmed.append(lhs)
+            return (lambda: T.matmul(alloc()[:], lhsT=idle[:, 0:P], rhs=lhs[:], start=True, stop=True)), needs, [("read", ("warm", len(warmed) - 1))]
 
         def total(i, ring):
             alloc, needs = take(ring, ("st", i), [P, G])
@@ -409,7 +416,7 @@ def tile_multigroupintegraltransportsourceiterati_x1_kernel(tc, flux, scat, dens
             SP.dma_start(out=flux_raw[b][:], in_=flux_v[b // 2, :, 2 * (b % 2):2 * (b % 2) + 2])
 
         V.memset(warm[:], 1.0)
-        for t in (sig_pad, rows, dens_pad):
+        for t in (sig_pad, rows, idle, dens_pad):
             V.memset(t[:], 0.0)
         make_identity(nc, id32[:])
         S.dma_start(out=dens_sb[:], in_=dens.rearrange("(g p t) m -> p g (t m)", g=2, t=4))
@@ -438,7 +445,7 @@ def tile_multigroupintegraltransportsourceiterati_x1_kernel(tc, flux, scat, dens
         SCAT_PIECES = [[("a", 0, G)], [("b", 0, G)], [("c", 0, G)], [("c", 0, G)]]
         INV_IN = ["c", None, "kern0", None]
 
-        qt = [t_pad("dens", 0, NT, "sa"), t_flux(0), t_nusf(), total(0, "sb"), t_flux(1), total(1, "sa"), scatter(0, 0), scatter(1, 0), fission(0), scatter(2, 0), scatter(3, 0), scatter(0, 1), scatter(1, 1)]
+        qt = [warm_up(idle) for k in range(4)] + [t_pad("dens", 0, NT, "sa"), warm_up(idle), warm_up(idle), t_flux(0), t_nusf(), total(0, "sb"), t_flux(1), total(1, "sa"), scatter(0, 0), scatter(1, 0), fission(0), scatter(2, 0), scatter(3, 0), scatter(0, 1), scatter(1, 1)]
         qt += [t_flux(2), scatter(2, 1), scatter(3, 1), t_flux(3), scatter(0, 2), scatter(1, 2), total(2, "sa"), scatter(2, 2), fission(1), scatter(3, 2), fission(2), total(3, "tp"), fission(3)]
         qt += [scatter(0, 3), scatter(1, 3), scatter(4, 0, "tp"), scatter(2, 3), scatter(3, 3), scatter(5, 0, "tp"), total(4, "sa"), scatter(4, 1), fission(4)]
         qt += [scatter(6, 0, "tp"), scatter(5, 1), scatter(7, 0, "tp"), scatter(6, 1), fission(5), scatter(7, 1), scatter(4, 2), fission(6), scatter(5, 2), scatter(6, 2), fission(7), total(5, "sa")]

@@ -445,7 +445,7 @@ def tile_multigroupintegraltransportsourceiterati_x1_kernel(tc, flux, scat, dens
         SCAT_PIECES = [[("a", 0, G)], [("b", 0, G)], [("c", 0, G)], [("c", 0, G)]]
         INV_IN = ["c", None, "kern0", None]
 
-        qt = [warm_up(idle) for k in range(4)] + [t_pad("dens", 0, NT, "sa"), warm_up(idle), warm_up(idle), t_flux(0), t_nusf(), total(0, "sb"), t_flux(1), total(1, "sa"), scatter(0, 0), scatter(1, 0), fission(0), scatter(2, 0), scatter(3, 0), scatter(0, 1), scatter(1, 1)]
+        qt = [warm_up(idle) for k in range(3)] + [t_pad("dens", 0, NT, "sa"), warm_up(idle), t_flux(0), t_nusf(), total(0, "sb"), t_flux(1), total(1, "sa"), scatter(0, 0), scatter(1, 0), fission(0), scatter(2, 0), scatter(3, 0), scatter(0, 1), scatter(1, 1)]
         qt += [t_flux(2), scatter(2, 1), scatter(3, 1), t_flux(3), scatter(0, 2), scatter(1, 2), total(2, "sa"), scatter(2, 2), fission(1), scatter(3, 2), fission(2), total(3, "tp"), fission(3)]
         qt += [scatter(0, 3), scatter(1, 3), scatter(4, 0, "tp"), scatter(2, 3), scatter(3, 3), scatter(5, 0, "tp"), total(4, "sa"), scatter(4, 1), fission(4)]
         qt += [scatter(6, 0, "tp"), scatter(5, 1), scatter(7, 0, "tp"), scatter(6, 1), fission(5), scatter(7, 1), scatter(4, 2), fission(6), scatter(5, 2), scatter(6, 2), fission(7), total(5, "sa")]

@@ -50,19 +50,17 @@ def tile_multigroupintegraltransportsourceiterati_x1_kernel(tc, flux, scat, dens
         dens32 = tile("dens32", [P, NT, M], F32)
         dens_t = tile("dens_t", [P, NT, P], BF16)
         chi_b = tile("chi_b", [P, G], BF16)
-        fx = tile("fx", [P, 4, G], F32)
         f_t = tile("f_t", [P, 4, P], BF16)
-        f_rest = tile("f_rest", [P, 4], F32)
-        flux_grp = tiles("flux_grp", 2, [P, 4, P, 4], BF16)
+        flux_grp = tiles("flux_grp", 4, [P, 2, P, 4], BF16)
         flux_codes = tile("flux_codes", [P, NT, P], U32)
         flux_sc = tile("flux_sc", [P, NT, P], U8)
         scat_codes = tile("scat_codes", [P, M, G], U32)
         scat_sc = tile("scat_sc", [P, M, G], U8)
         pd = tile("pd", [P, NT, M], F32)
-        f = tiles("f", 2, [P, 4], F32)
+        f = tile("f", [P, NT], F32)
         x = tiles("x", 2, [P, 4, G], F32)
         sg = tile("sg", [P, NT, G], BF16)
-        rst = tiles("rst", 2, [P, 4, G], F32)
+        rst = tile("rst", [P, NT, G], F32)
         kern_codes = tile("kern_codes", [P, NT, 2, P], U32)
         kern_sc = tile("kern_sc", [P, NT, 2, P], U8)
         q_codes = tile("q_codes", [P, 2, G], U32)
@@ -72,7 +70,7 @@ def tile_multigroupintegraltransportsourceiterati_x1_kernel(tc, flux, scat, dens
         r_codes = tile("r_codes", [P, 2, G], U32)
         r_sc = tile("r_sc", [P, G], U8)
         warm = tile("warm", [P, 2], F32)
-        idle = tile("idle", [P, G], BF16)
+        idle = tile("idle", [P, H], F32)
 
         held = {}
 
@@ -122,16 +120,22 @@ def tile_multigroupintegraltransportsourceiterati_x1_kernel(tc, flux, scat, dens
         def kern_grp(h):
             return tenant("kern%d" % h, "kern_grp%d" % h, [P, 2, 2, P, 4], BF16)
 
-        def q_grp(g):
-            return tenant("q%d" % g, "q_grp%d" % g, [P, G, 4], BF16)
+        def fx():
+            return tenant("fx", "fx", [P, 4, G], F32)
+
+        def f_rest():
+            return tenant("rest", "f_rest", [P, 4], F32)[:]
+
+        def q_grp(g, c0, w):
+            h0 = c0 - c0 % H
+            return tenant("q%d_%d" % (g, h0), "q_grp%d_%d" % (g, h0), [P, H, 4], BF16)[:, c0 - h0:c0 - h0 + w]
 
         def inv(i, n):
-            if i == NT - 1:
-                return tenant("kern3", "inv_last", [P, 1, G], F32)[:]
-            buffer = INV_IN[i // 2]
-            if buffer is None:
-                return rst[i // 4][:, i % 4:i % 4 + n]
-            return tenant(buffer, "inv%d" % (i // 2), [P, 2, G], F32)[:, i % 2:i % 2 + n]
+            for buffer, i0, ni in INV_IN:
+                if i0 <= i and i + n <= i0 + ni:
+                    if buffer is None:
+                        return rst[:, i:i + n]
+                    return tenant(buffer, "inv%d" % i0, [P, ni, G], F32)[:, i - i0:i - i0 + n]
 
         def t_pad(name, i0, n, ring):
             alloc, needs = take(ring, (name, i0), [P, n, P], BF16)
@@ -142,8 +146,8 @@ def tile_multigroupintegraltransportsourceiterati_x1_kernel(tc, flux, scat, dens
                     T.transpose(ps[:, i], dens_pad[:, i0 + i], id16[:])
             return run, needs + (["pieces"] if name == "f" else []), [(name, i0)]
 
-        def t_flux(b):
-            alloc, needs = take("tp", ("flux", b), [P, 2, 2, P])
+        def t_flux(b, ring="tp"):
+            alloc, needs = take(ring, ("flux", b), [P, 2, 2, P])
 
             def run():
                 ps = alloc()
@@ -153,8 +157,8 @@ def tile_multigroupintegraltransportsourceiterati_x1_kernel(tc, flux, scat, dens
                         T.transpose(ps[:, a, u], words[:, u:H:2], id32[:])
             return run, needs, [("flux", b)]
 
-        def t_kern(i):
-            alloc, needs = take("tp", ("kern", i), [P, 2, 2, P])
+        def t_kern(i, ring="tp"):
+            alloc, needs = take(ring, ("kern", i), [P, 2, 2, P])
 
             def run():
                 ps = alloc()
@@ -173,10 +177,24 @@ def tile_multigroupintegraltransportsourceiterati_x1_kernel(tc, flux, scat, dens
                     T.transpose(ps[:, u], rows[:].bitcast(F32)[:, u:H:2], id32[:])
             return run, needs, ["nusf"]
 
-        def warm_up(lhs):
-            alloc, needs = take("mm", ("warm", len(warmed)), [P, G])
-            warmed.append(lhs)
-            return (lambda: T.matmul(alloc()[:], lhsT=idle[:, 0:P], rhs=lhs[:], start=True, stop=True)), needs, [("read", ("warm", len(warmed) - 1))]
+        def warm_up(w):
+            alloc, needs = take("mm", ("warm", len(warmed)), [P, w])
+            warmed.append(w)
+            return (lambda: T.matmul(alloc()[:], lhsT=idle[:, 0:P], rhs=idle[:, 0:w], start=True, stop=True)), needs, [("read", ("warm", len(warmed) - 1))]
+
+        def t_weave(m, c0, ring):
+            alloc, needs = take(ring, ("w", m, c0), [P, 2, G], BF16)
+
+            def run():
+                ps = alloc()
+                for a in range(2):
+                    T.matmul(ps[:, a], lhsT=id16[:], rhs=scat_raw[m][:, :, c0 + a * P:c0 + (a + 1) * P].rearrange("p j n -> p n j"), start=True, stop=True)
+            return run, needs, [("w", m, c0)]
+
+        def c_weave(m, c0):
+            def run():
+                S.copy(out=scat_grp(m, c0, H).rearrange("p n j -> p (n j)"), in_=bank["w", m, c0][:].rearrange("p a n -> p (a n)"))
+            return run, [("w", m, c0)], cols("scat_grp", m, c0, H) + [("read", ("w", m, c0))]
 
         def total(i, ring):
             alloc, needs = take(ring, ("st", i), [P, G])
@@ -190,15 +208,24 @@ def tile_multigroupintegraltransportsourceiterati_x1_kernel(tc, flux, scat, dens
                             rhs=scat_codes[:, m].bitcast(FP8X4), rhs_scale=scat_sc[:, m], start=True, stop=True)
             return run, needs + [("flux_q", i)] + cols("scat_q", m, 0, G), [("a", i, m)]
 
-        def fission(i):
-            i0 = 4 * (i // 4)
-            alloc, needs = take("sb", ("p", i0), [P, 4, M])
+        def scatter_half(i0, m, c0):
+            alloc, needs = take("mm", ("a", i0, m, c0), [P, 2, H])
 
             def run():
-                ps = alloc() if i == i0 else bank["p", i0]
+                ps = alloc()
+                for a in range(2):
+                    T.matmul_mx(out=ps[:, a], lhsT=flux_codes[:, i0 + a].bitcast(FP8X4), lhsT_scale=flux_sc[:, i0 + a],
+                                rhs=scat_codes[:, m, c0:c0 + H].bitcast(FP8X4), rhs_scale=scat_sc[:, m, c0:c0 + H], start=True, stop=True)
+            return run, needs + [("flux_q", i0), ("flux_q", i0 + 1)] + cols("scat_q", m, c0, H), [("a", i0, m, c0)]
+
+        def fission(i, ring=None):
+            alloc, needs = take(ring, "p", [P, NT, M])
+
+            def run():
+                ps = alloc() if i == 0 else bank["p"]
                 for j in range(4):
-                    T.matmul(ps[:, i - i0], lhsT=flux_grp[i // 4][:, i % 4, :, j], rhs=nusf_k[:, j // 2, :, j % 2], start=(j == 0), stop=(j == 3))
-            return run, (needs if i == i0 else []) + [("flux_grp", i // 2), "nusf_t"], [("p", i0)] if i == i0 + 3 else []
+                    T.matmul(ps[:, i], lhsT=flux_grp[i // 2][:, i % 2, :, j], rhs=nusf_k[:, j // 2, :, j % 2], start=(j == 0), stop=(j == 3))
+            return run, (needs if i == 0 else []) + [("flux_grp", i // 2), "nusf_t"], ["p"] if i == NT - 1 else []
 
         def emission(c0, ring):
             alloc, needs = take(ring, ("e", c0), [P, 4, P])
@@ -242,8 +269,7 @@ def tile_multigroupintegraltransportsourceiterati_x1_kernel(tc, flux, scat, dens
                 V.tensor_copy(out=dst, in_=src)
 
         def c_flux(b, eng=S):
-            a0 = 2 * (b % 2)
-            dst = flux_grp[b // 2][:, a0:a0 + 2].rearrange("p a r f -> p a (r f)").bitcast(F32).rearrange("p a (r u) -> p a r u", u=2)
+            dst = flux_grp[b][:].rearrange("p a r f -> p a (r f)").bitcast(F32).rearrange("p a (r u) -> p a r u", u=2)
             return (lambda: words_out(eng, dst, bank["flux", b][:].rearrange("p a u r -> p a r u"))), [("flux", b)], [("flux_grp", b), ("read", ("flux", b))]
 
         def c_kern(i, eng=S):
@@ -258,21 +284,21 @@ def tile_multigroupintegraltransportsourceiterati_x1_kernel(tc, flux, scat, dens
             return run, [("a", i, 0)], [("x", i, 0), ("read", ("a", i, 0))]
 
         def root(i):
-            return (lambda: S.activation(out=rst[i // 4][:, i % 4], in_=bank["st", i][:], func=ACT.Abs_reciprocal_sqrt)), [("st", i)], [("root", i)]
+            return (lambda: S.activation(out=rst[:, i], in_=bank["st", i][:], func=ACT.Abs_reciprocal_sqrt)), [("st", i)], [("root", i)]
 
         def sign(i):
             return (lambda: S.activation(out=sg[:, i], in_=bank["st", i][:], func=ACT.Sign)), [("root", i)], [("sign", i), ("read", ("st", i))]
 
         def square(i):
-            r = rst[i // 4][:, i % 4]
+            r = rst[:, i]
             return (lambda: S.activation(out=r, in_=r, func=ACT.Square)), [("root", i)], [("size", i)]
 
         def inverse(i):
             return [root(i), sign(i), square(i)]
 
-        def signed(i, n=1, c0=0, w=G, after=()):
+        def signed(i, n=1, c0=0, w=G, after=(), eng=GP):
             def run():
-                GP.tensor_tensor(out=inv(i, n)[:, :, c0:c0 + w], in0=rst[i // 4][:, i % 4:i % 4 + n, c0:c0 + w], in1=sg[:, i:i + n, c0:c0 + w], op=ALU.mult)
+                eng.tensor_tensor(out=inv(i, n)[:, :, c0:c0 + w], in0=rst[:, i:i + n, c0:c0 + w], in1=sg[:, i:i + n, c0:c0 + w], op=ALU.mult)
             return run, [(k, j) for k in ("size", "sign") for j in range(i, i + n)] + list(after), [k for j in range(i, i + n) for k in cols("inv", j, c0, w)]
 
         def weave_scat(m, c0, w, eng, after=()):
@@ -287,11 +313,13 @@ def tile_multigroupintegraltransportsourceiterati_x1_kernel(tc, flux, scat, dens
                 V.quantize_mx(out=scat_codes[:, m, c0:c0 + w].bitcast(FP8X4), scales=scat_sc[:, m, c0:c0 + w], in_=scat_grp(m, c0, w).rearrange("p n j -> p (n j)"))
             return run, cols("scat_grp", m, c0, w), cols("scat_q", m, c0, w)
 
-        def quant_flux(i0, n):
+        def quant_flux(b):
+            i0, n = 2 * b, 2
+
             def run():
                 V.quantize_mx(out=flux_codes[:, i0:i0 + n].rearrange("p a r -> p (a r)").bitcast(FP8X4),
                               scales=flux_sc[:, i0:i0 + n].rearrange("p a r -> p (a r)"),
-                              in_=flux_grp[i0 // 4][:, i0 % 4:i0 % 4 + n].rearrange("p a r f -> p (a r f)"))
+                              in_=flux_grp[b][:].rearrange("p a r f -> p (a r f)"))
             return run, [("flux_grp", i // 2) for i in range(i0, i0 + n)], [("flux_q", i) for i in range(i0, i0 + n)]
 
         def quant_kern(h):
@@ -304,7 +332,7 @@ def tile_multigroupintegraltransportsourceiterati_x1_kernel(tc, flux, scat, dens
         def quant_q(g, c0, w):
             def run():
                 V.quantize_mx(out=q_codes[:, g, c0:c0 + w].bitcast(FP8X4), scales=q_sc[:, g, c0:c0 + w],
-                              in_=q_grp(g)[:, c0:c0 + w].rearrange("p n t -> p (n t)"))
+                              in_=q_grp(g, c0, w).rearrange("p n t -> p (n t)"))
             return run, cols("q_grp", g, c0, w), cols("q_q", g, c0, w)
 
         def quant_res(g, c0, w):
@@ -320,27 +348,33 @@ def tile_multigroupintegraltransportsourceiterati_x1_kernel(tc, flux, scat, dens
                 V.scalar_tensor_tensor(out=xi, in0=bank["a", i, m][:, c0:c0 + w], scalar=dens32[:, i, m:m + 1], in1=xi, op0=ALU.mult, op1=ALU.add)
             return run, [("a", i, m), ("x", i, m - 1)], [("x", i, m), ("read", ("a", i, m))] if c0 + w == G else []
 
-        def f_weigh(g):
+        def weigh_half(i, m, c0):
+            xi = x[i // 4][:, i % 4, c0:c0 + H]
+            key = ("a", i - i % 2, m, c0)
+
             def run():
-                V.tensor_tensor(out=pd[:, 4 * g:4 * g + 4], in0=bank["p", 4 * g][:], in1=dens32[:, 4 * g:4 * g + 4], op=ALU.mult)
-            return run, [("p", 4 * g)], [("pd", g), ("read", ("p", 4 * g))]
+                V.scalar_tensor_tensor(out=xi, in0=bank[key][:, i % 2], scalar=dens32[:, i, m:m + 1], in1=xi, op0=ALU.mult, op1=ALU.add)
+            return run, [key, ("x", i, m - 1)], [("x", i, m, c0)] + ([("read", key)] if i % 2 else [])
 
-        def f_sum(g):
-            return (lambda: V.tensor_reduce(out=f[g][:], in_=pd[:, 4 * g:4 * g + 4], axis=AX.X, op=ALU.add)), [("pd", g)], [("fsum", g)]
+        def f_weigh():
+            return (lambda: V.tensor_tensor(out=pd[:], in0=bank["p"][:], in1=dens32[:], op=ALU.mult)), ["p"], ["pd", ("read", "p")]
 
-        def f_chi(i, eng):
+        def f_sum():
+            return (lambda: V.tensor_reduce(out=f[:], in_=pd[:], axis=AX.X, op=ALU.add)), ["pd"], ["fsum"]
+
+        def f_chi(i, eng, after=()):
             def run():
                 if eng is S:
-                    S.activation(out=fx[:, i], in_=chi_b[:], func=ACT.Copy, scale=f[i // 4][:, i % 4:i % 4 + 1])
+                    S.activation(out=fx()[:, i], in_=chi_b[:], func=ACT.Copy, scale=f[:, i:i + 1])
                 else:
-                    GP.tensor_scalar(out=fx[:, i], in0=chi_b[:], scalar1=f[i // 4][:, i % 4:i % 4 + 1], scalar2=0.0, op0=ALU.mult, op1=ALU.add)
-            return run, [("fsum", i // 4)], [("fx", i)]
+                    GP.tensor_scalar(out=fx()[:, i], in0=chi_b[:], scalar1=f[:, i:i + 1], scalar2=0.0, op0=ALU.mult, op1=ALU.add)
+            return run, ["fsum"] + list(after), [("fx", i)]
 
-        def source(g, c0):
+        def source(g, c0, w, eng):
             def run():
-                dst, s = blocks(q_grp(g)[:, c0:c0 + H], x[g][:, :, c0:c0 + H])
-                V.tensor_tensor(out=dst, in0=s, in1=fx[:, :, c0:c0 + H].rearrange("p t (c i) -> p c t i", i=4), op=ALU.add)
-            return run, [k for i in range(4 * g, 4 * g + 4) for k in (("x", i, M - 1), ("fx", i))], cols("q_grp", g, c0, H)
+                dst, s = blocks(q_grp(g, c0, w), x[g][:, :, c0:c0 + w])
+                eng.tensor_tensor(out=dst, in0=s, in1=fx()[:, :, c0:c0 + w].rearrange("p t (c i) -> p c t i", i=4), op=ALU.add)
+            return run, [k for i in range(4 * g, 4 * g + 4) for k in (("x", i, M - 1), ("fx", i))], cols("q_grp", g, c0, w)
 
         def piece(k):
             return dens_pad[:, 4:NT, CHI_AT + k]
@@ -349,29 +383,29 @@ def tile_multigroupintegraltransportsourceiterati_x1_kernel(tc, flux, scat, dens
             def run():
                 with nc.allow_low_precision(reason="the first bf16 piece of f; the later pieces carry the rest"):
                     V.tensor_reduce(out=piece(0), in_=pd[:, 4:NT], axis=AX.X, op=ALU.add)
-            return run, [("pd", 1)], ["first"]
+            return run, ["pd"], ["first"]
 
         def f_less_first():
-            return (lambda: V.tensor_tensor(out=f_rest[:], in0=f[1][:], in1=piece(0), op=ALU.subtract)), [("fsum", 1), "first"], ["rest"]
+            return (lambda: V.tensor_tensor(out=f_rest(), in0=f[:, 4:NT], in1=piece(0), op=ALU.subtract)), ["fsum", "first"], ["rest"]
 
         def f_second():
-            return (lambda: V.tensor_copy(out=piece(1), in_=f_rest[:])), ["rest"], ["second"]
+            return (lambda: V.tensor_copy(out=piece(1), in_=f_rest())), ["rest"], ["second"]
 
         def f_third():
-            return (lambda: V.tensor_tensor(out=piece(2), in0=f_rest[:], in1=piece(1), op=ALU.subtract)), ["second"], ["pieces"]
+            return (lambda: V.tensor_tensor(out=piece(2), in0=f_rest(), in1=piece(1), op=ALU.subtract)), ["second"], ["pieces"]
 
         def source_late(c0):
             def run():
-                dst, s = blocks(q_grp(1)[:, c0:c0 + P], x[1][:, :, c0:c0 + P])
+                dst, s = blocks(q_grp(1, c0, P), x[1][:, :, c0:c0 + P])
                 V.tensor_tensor(out=dst, in0=bank["e", c0][:].rearrange("p t (c i) -> p c t i", i=4), in1=s, op=ALU.add)
-            return run, [("x", i, M - 1) for i in range(4, NT)] + [("e", c0)], cols("q_grp", 1, c0, P) + [("read", ("e", c0))]
+            return run, [("x", i, M - 1, c0 - c0 % H) for i in range(4, NT)] + [("e", c0)], cols("q_grp", 1, c0, P) + [("read", ("e", c0))]
 
         def divide(unit):
             g, t0, n, c0, w = unit
             i0 = 4 * g + t0
 
             def run():
-                step = 1 if i0 + n == NT else n
+                step = n if any(j0 <= i0 and i0 + n <= j0 + nj for buffer, j0, nj in INV_IN) else 1
                 for a in range(0, n, step):
                     V.tensor_tensor(out=res[g][:, t0 + a:t0 + a + step, c0:c0 + w], in0=bank["c", unit][:, a:a + step], in1=inv(i0 + a, step)[:, :, c0:c0 + w], op=ALU.mult)
             needs = [k for i in range(i0, i0 + n) for k in cols("inv", i, c0, w)]
@@ -416,7 +450,7 @@ def tile_multigroupintegraltransportsourceiterati_x1_kernel(tc, flux, scat, dens
             SP.dma_start(out=flux_raw[b][:], in_=flux_v[b // 2, :, 2 * (b % 2):2 * (b % 2) + 2])
 
         V.memset(warm[:], 1.0)
-        for t in (sig_pad, rows, idle, dens_pad):
+        for t in (idle, sig_pad, rows, dens_pad):
             V.memset(t[:], 0.0)
         make_identity(nc, id32[:])
         S.dma_start(out=dens_sb[:], in_=dens.rearrange("(g p t) m -> p g (t m)", g=2, t=4))
@@ -427,11 +461,11 @@ def tile_multigroupintegraltransportsourceiterati_x1_kernel(tc, flux, scat, dens
         load_scat(1)
         load_flux(1)
         load_scat(2)
-        load_scat(3)
         load_flux(2)
         load_flux(3)
-        SP.dma_start(out=kern_raw[0][:], in_=kern_v[0])
+        load_scat(3)
         SP.dma_start(out=chi_b[:], in_=chi.partition_broadcast(P))
+        SP.dma_start(out=kern_raw[0][:], in_=kern_v[0])
         SP.dma_start(out=kern_raw[1][:], in_=kern_v[1])
 
         S.activation(out=warm[:, 1:2], in_=warm[:, 0:1], func=ACT.Abs_reciprocal_sqrt)
@@ -440,39 +474,40 @@ def tile_multigroupintegraltransportsourceiterati_x1_kernel(tc, flux, scat, dens
         V.tensor_copy(out=dens32[:], in_=dens_v)
 
         lo, hi = range(4), range(4, NT)
-        units = [(g, 2 * h, 2, c0, H) for g in range(2) for c0 in (0, H) for h in range(2)]
         quarters = range(0, G, P)
-        SCAT_PIECES = [[("a", 0, G)], [("b", 0, G)], [("c", 0, G)], [("c", 0, G)]]
-        INV_IN = ["c", None, "kern0", None]
+        units = [(g, 2 * h, 2, c0, H) for g in range(2) for c0 in (0, H) for h in range(2)]
+        SCAT_PIECES = [[("a", 0, G)], [("b", 0, G)], [("c", 0, P), ("a", P, P), ("c", H, H)], [("b", 0, P), ("b", P, G - P)]]
+        INV_IN = [(None, 0, 1), ("rest", 1, 2), ("kern1", 3, 1), (None, 4, 1), ("q1_0", 5, 2), ("kern3", 7, 1)]
 
-        qt = [warm_up(idle) for k in range(3)] + [t_pad("dens", 0, NT, "sa"), warm_up(idle), t_flux(0), t_nusf(), total(0, "sb"), t_flux(1), total(1, "sa"), scatter(0, 0), scatter(1, 0), fission(0), scatter(2, 0), scatter(3, 0), scatter(0, 1), scatter(1, 1)]
-        qt += [t_flux(2), scatter(2, 1), scatter(3, 1), t_flux(3), scatter(0, 2), scatter(1, 2), total(2, "sa"), scatter(2, 2), fission(1), scatter(3, 2), fission(2), total(3, "tp"), fission(3)]
-        qt += [scatter(0, 3), scatter(1, 3), scatter(4, 0, "tp"), scatter(2, 3), scatter(3, 3), scatter(5, 0, "tp"), total(4, "sa"), scatter(4, 1), fission(4)]
-        qt += [scatter(6, 0, "tp"), scatter(5, 1), scatter(7, 0, "tp"), scatter(6, 1), fission(5), scatter(7, 1), scatter(4, 2), fission(6), scatter(5, 2), scatter(6, 2), fission(7), total(5, "sa")]
-        qt += [scatter(7, 2), t_kern(0), t_kern(1), scatter(4, 3), total(6, "sb"), scatter(5, 3), t_kern(2), scatter(6, 3), t_pad("f", 4, 4, "sa"), t_kern(3), scatter(7, 3), total(7, "sb")]
-        qt += [emission(c, "mm") for c in quarters[:3]] + [t_kern(4), emission(quarters[3], "mm"), t_kern(5), open_unit(units[0], "sa"), open_unit(units[2], "sb"), t_kern(6), t_kern(7)]
-        qt += [close_unit(units[0]), open_unit(units[1], "mm"), close_unit(units[1]), open_unit(units[3], "mm"), close_unit(units[2]), close_unit(units[3])]
-        for u, ring in zip(units[4:], ("mm", "mm", "tp", "tp")):
+        qt = [warm_up(H), warm_up(H), t_pad("dens", 0, NT, "sa"), warm_up(P), t_flux(0), t_nusf(), total(0, "sb"), warm_up(H), fission(0, "sa"), t_flux(1), scatter(0, 0), scatter(1, 0), fission(1)]
+        qt += [scatter(0, 1), scatter(2, 0, "tp"), scatter(1, 1), scatter(3, 0, "tp"), scatter(2, 1), scatter(3, 1), t_flux(2, "sb"), total(1, "mm"), t_flux(3), total(2, "tp"), fission(2)]
+        qt += [scatter(0, 2), scatter(1, 2), fission(3), scatter(4, 0, "sb"), scatter(2, 2), scatter(5, 0, "tp"), scatter(3, 2), fission(4), scatter(4, 1), fission(5), scatter(5, 1), fission(6), fission(7), total(3, "sb")]
+        qt += [scatter(0, 3), scatter(1, 3), scatter(6, 0, "tp"), scatter(2, 3), scatter(7, 0, "tp"), scatter(3, 3), scatter(4, 2), t_pad("f", 4, 4, "sb"), t_kern(0, "sa"), scatter(5, 2), scatter(6, 1), scatter(7, 1), t_kern(1), scatter(6, 2), scatter(7, 2)]
+        qt += [scatter_half(4, 3, 0), t_kern(2), scatter_half(6, 3, 0), t_kern(3, "sb"), total(4, "sa"), scatter_half(4, 3, H), total(5, "tp"), scatter_half(6, 3, H), total(6, "tp"), emission(quarters[0], "sb"), emission(quarters[1], "sa")]
+        qt += [open_unit(units[0], "mm"), open_unit(units[1], "mm"), t_kern(4), t_kern(5, "sb"), emission(quarters[2], "mm"), close_unit(units[0]), close_unit(units[1]), total(7, "tp"), emission(quarters[3], "mm"), t_kern(6, "sa"), t_kern(7)]
+        qt += [open_unit(units[2], "mm"), open_unit(units[3], "mm"), close_unit(units[2]), close_unit(units[3])]
+        for u, ring in zip(units[4:], ("mm", "mm", "sa", "sb")):
             qt += [open_unit(u, ring), close_unit(u)]
 
-        qv = [weave_scat(0, 0, H, V), weave_scat(0, H, H, V), quant_scat(0, 0, H), quant_scat(0, H, H), weave_scat(1, 0, H, V), quant_flux(0, 2), weave_scat(1, H, H, V)]
-        qv += [weave_scat(2, 0, H, V), quant_flux(2, 2), quant_scat(1, 0, G), weave_scat(2, H, H, V), quant_scat(2, 0, H), quant_scat(2, H, H)]
-        qv += [weigh_add(i, 1) for i in lo] + [weigh_add(i, 2) for i in lo[:3]]
-        qv += [quant_scat(3, 0, G), quant_flux(4, 4), weigh_add(3, 2), f_weigh(0), weigh_add(0, 3), f_sum(0)] + [weigh_add(i, 3) for i in lo[1:]]
-        qv += [weigh_add(i, 1) for i in hi] + [weigh_add(i, 2) for i in hi[:3]]
-        qv += [f_weigh(1), source(0, 0), f_sum(1), f_first(), source(0, H), f_less_first(), quant_q(0, 0, H), f_second(), quant_q(0, H, H), f_third(), quant_kern(0)]
-        qv += [weigh_add(7, 2)] + [weigh_add(i, 3) for i in hi[:3]] + [weigh_add(7, 3, 0, H), weigh_add(7, 3, H, H)] + [source_late(c) for c in quarters]
-        qv += [quant_kern(1), quant_q(1, 0, H), quant_q(1, H, H), quant_kern(2), divide(units[0]), divide(units[1]), quant_kern(3)]
+        qv = [weave_scat(0, 0, H, V), weave_scat(0, H, H, V), quant_scat(0, 0, H), quant_scat(0, H, H), weave_scat(1, 0, H, V), quant_flux(0), weave_scat(1, H, H, V)]
+        qv += [quant_scat(1, 0, H), quant_scat(1, H, H), quant_flux(1), weave_scat(2, 0, P, V), weave_scat(2, P, P, V), quant_scat(2, 0, P)]
+        qv += [weigh_add(i, 1) for i in lo]
+        qv += [quant_scat(2, P, P), quant_scat(2, H, H), weave_scat(3, 0, P, V), quant_flux(2), quant_scat(3, 0, P)] + [weigh_add(i, 2) for i in lo] + [weigh_add(4, 1), weigh_add(5, 1)]
+        qv += [f_weigh(), quant_scat(3, P, G - P), f_sum(), f_first(), quant_flux(3), f_less_first(), f_second(), f_third()]
+        qv += [weigh_add(i, 3) for i in lo] + [weigh_add(4, 2), weigh_add(5, 2), weigh_add(6, 1), weigh_add(7, 1), weigh_add(6, 2), weigh_add(7, 2), weigh_half(4, 3, 0), weigh_half(5, 3, 0)]
+        qv += [source(0, G - P, P, V), quant_q(0, 0, H), quant_kern(0), quant_q(0, H, H), quant_kern(1)]
+        qv += [weigh_half(6, 3, 0), weigh_half(7, 3, 0), weigh_half(4, 3, H)] + [source_late(c) for c in quarters[:2]] + [weigh_half(5, 3, H), quant_q(1, 0, H)] + [weigh_half(i, 3, H) for i in hi[2:]]
+        qv += [source_late(quarters[2])] + [divide(u) for u in units[:2]] + [source_late(quarters[3]), quant_kern(2), quant_q(1, H, H), quant_kern(3)]
         qv += [divide(u) for u in units[2:]] + [quant_res(0, 0, G)]
         qv += [weave_res(1, H + P, V), quant_res(1, 0, H), quant_res(1, H, H)]
 
-        qs = [c_pad("dens", dens_t, 0, NT), c_flux(0), c_nusf(), root(0), c_flux(1), sign(0), weigh_first(0), weigh_first(1), weigh_first(2), weigh_first(3), root(1), c_flux(2), sign(1), square(0), c_flux(3), square(1), root(2), sign(2), square(2)]
-        qs += [root(3), sign(3), weigh_first(4), weigh_first(5), square(3), weigh_first(6), weigh_first(7), f_chi(2, S), f_chi(3, S), root(4), sign(4), square(4), root(5), sign(5), c_kern(0), c_kern(1), square(5)]
-        qs += [root(6), sign(6), c_f(), square(6), c_kern(2), c_kern(3), root(7), sign(7), c_kern(4), c_kern(5), square(7), c_kern(6), c_kern(7)]
-        qs += [weave_res(g, c, S) for g in range(2) for c in quarters[:3]] + [store_scales(1, S), store_scales(3, S)]
+        qs = [c_pad("dens", dens_t, 0, NT), c_flux(0), c_nusf(), root(0), sign(0), c_flux(1), weigh_first(0), weigh_first(1), weigh_first(2), weigh_first(3), square(0)]
+        qs += [c_flux(2), root(1), c_flux(3), sign(1), square(1), weigh_first(4), weigh_first(5), root(2), sign(2), square(2), root(3), sign(3)] + [f_chi(i, S) for i in lo] + [weigh_first(6), weigh_first(7), c_f(), c_kern(0), c_kern(1), square(3)]
+        qs += [c_kern(2), c_kern(3)] + inverse(4) + inverse(5) + inverse(6) + [c_kern(4), c_kern(5), root(7), c_kern(6), c_kern(7), sign(7), square(7)]
+        qs += [weave_res(0, c, S) for c in quarters[:3]] + [weave_res(1, 0, S), weave_res(1, H, S)] + [store_scales(1, S), store_scales(3, S)]
 
-        qg = [weave_scat(3, 0, G, GP, cols("scat_q", 2, 0, G)), signed(0, 2, after=cols("scat_q", 3, 0, G))] + [f_chi(i, GP) for i in lo[:2]] + [signed(2, 2)]
-        qg += [signed(4, 2, after=[("kern_q", 0)]), signed(6), signed(7, after=[("kern_q", 3)]), weave_res(0, H + P, GP)]
+        qg = [weave_scat(2, H, H, GP, cols("scat_q", 2, 0, P)), weave_scat(3, P, G - P, GP, cols("scat_q", 3, 0, P)), signed(0), signed(1, 2, after=["pieces"]), source(0, 0, H, GP), source(0, H, P, GP)]
+        qg += [signed(3, after=[("kern_q", 1)]), signed(4), signed(5, 2, after=cols("q_q", 1, 0, H)), signed(7, after=[("kern_q", 3)]), weave_res(0, H + P, GP), weave_res(1, P, GP)]
 
         load_chi = (lambda: SP.dma_start(out=rows[CHI_AT:CHI_AT + PIECES], in_=chi.partition_broadcast(PIECES))), ["nusf"], ["chi"]
         qy = [load_chi] + [store(units[k]) for k in range(8)] + [store_codes(0, 0, G), store_codes(1, 0, H), store_codes(1, H, H)]

@@ -17,7 +17,7 @@ P = 128
 R, G, M = 1024, 512, 4
 NT = R // P
 H = G // 2
-CHI_AT, NU_AT = 4, 8
+NU_AT = 8
 PIECES = 3
 BANKS = {"mm": 4, "tp": 2, "sa": 1, "sb": 1}
 FLOPS = 2 * R * G * G * M + 2 * R * R * G
@@ -38,6 +38,8 @@ def tile_multigroupintegraltransportsourceiterati_x1_kernel(tc, flux, scat, dens
             return [tile("%s%d" % (name, k), shape, dtype) for k in range(n)]
 
         rows = tile("rows", [P, G], BF16)
+        chi_d = tile("chi_d", [P, 4, G], BF16)
+        f_pad = tile("f_pad", [P, 2, P], BF16)
         sig_pad = tile("sig_pad", [P, G], BF16)
         dens_pad = tile("dens_pad", [P, NT, P], BF16)
         dens_sb = tile("dens_sb", [P, 2, 4 * M], BF16)
@@ -49,8 +51,8 @@ def tile_multigroupintegraltransportsourceiterati_x1_kernel(tc, flux, scat, dens
         id16 = tile("id16", [P, P], BF16)
         dens32 = tile("dens32", [P, NT, M], F32)
         dens_t = tile("dens_t", [P, NT, P], BF16)
-        chi_b = tile("chi_b", [P, G], BF16)
-        f_t = tile("f_t", [P, 4, P], BF16)
+        y = tile("y", [P, 4, G], F32)
+        f_t = tile("f_t", [P, 2, P], BF16)
         flux_grp = tiles("flux_grp", 4, [P, 2, P, 4], BF16)
         flux_codes = tile("flux_codes", [P, NT, P], U32)
         flux_sc = tile("flux_sc", [P, NT, P], U8)
@@ -120,11 +122,8 @@ def tile_multigroupintegraltransportsourceiterati_x1_kernel(tc, flux, scat, dens
         def kern_grp(h):
             return tenant("kern%d" % h, "kern_grp%d" % h, [P, 2, 2, P, 4], BF16)
 
-        def fx():
-            return tenant("fx", "fx", [P, 4, G], F32)
-
         def f_rest():
-            return tenant("rest", "f_rest", [P, 4], F32)[:]
+            return tenant("rest", "f_rest", [P, 2, 4], F32)[:]
 
         def q_grp(g, c0, w):
             h0 = c0 - c0 % H
@@ -143,7 +142,7 @@ def tile_multigroupintegraltransportsourceiterati_x1_kernel(tc, flux, scat, dens
             def run():
                 ps = alloc()
                 for i in range(n):
-                    T.transpose(ps[:, i], dens_pad[:, i0 + i], id16[:])
+                    T.transpose(ps[:, i], (f_pad if name == "f" else dens_pad)[:, i0 + i], id16[:])
             return run, needs + (["pieces"] if name == "f" else []), [(name, i0)]
 
         def t_flux(b, ring="tp"):
@@ -227,14 +226,9 @@ def tile_multigroupintegraltransportsourceiterati_x1_kernel(tc, flux, scat, dens
                     T.matmul(ps[:, i], lhsT=flux_grp[i // 2][:, i % 2, :, j], rhs=nusf_k[:, j // 2, :, j % 2], start=(j == 0), stop=(j == 3))
             return run, (needs if i == 0 else []) + [("flux_grp", i // 2), "nusf_t"], ["p"] if i == NT - 1 else []
 
-        def emission(c0, ring):
-            alloc, needs = take(ring, ("e", c0), [P, 4, P])
-
-            def run():
-                ps = alloc()
-                for t in range(4):
-                    T.matmul(ps[:, t], lhsT=f_t[:, t], rhs=rows[:, c0:c0 + P], start=True, stop=True)
-            return run, needs + ["f_t", "chi"], [("e", c0)]
+        def emission(g, c0, ring):
+            alloc, needs = take(ring, ("e", g, c0), [P, 4, P])
+            return (lambda: T.matmul(alloc()[:], lhsT=f_t[:, g], rhs=chi_d[:, :, c0:c0 + P], start=True, stop=True)), needs + ["f_t"], [("e", g, c0)]
 
         def transport_pass(ps, unit, gs):
             g, t0, n, c0, w = unit
@@ -257,7 +251,7 @@ def tile_multigroupintegraltransportsourceiterati_x1_kernel(tc, flux, scat, dens
             return (lambda: S.copy(out=dst[:, i0:i0 + n], in_=bank[name, i0][:])), [(name, i0)], [(name + "_t", i) for i in range(i0, i0 + n)] + [("read", (name, i0))]
 
         def c_f():
-            return (lambda: S.copy(out=f_t[:], in_=bank["f", 4][:])), [("f", 4)], ["f_t", ("read", ("f", 4))]
+            return (lambda: S.copy(out=f_t[:], in_=bank["f", 0][:])), [("f", 0)], ["f_t", ("read", ("f", 0))]
 
         def c_nusf():
             return (lambda: S.copy(out=nusf_t[:], in_=bank["nusf"][:, :, NU_AT:NU_AT + M])), ["nusf"], ["nusf_t", ("read", "nusf")]
@@ -283,6 +277,11 @@ def tile_multigroupintegraltransportsourceiterati_x1_kernel(tc, flux, scat, dens
                 S.activation(out=x[i // 4][:, i % 4], in_=bank["a", i, 0][:], func=ACT.Copy, scale=dens32[:, i, 0:1])
             return run, [("a", i, 0)], [("x", i, 0), ("read", ("a", i, 0))]
 
+        def weigh_aside(i, m):
+            def run():
+                S.activation(out=y[:, i], in_=bank["a", i, m][:], func=ACT.Copy, scale=dens32[:, i, m:m + 1])
+            return run, [("a", i, m)], [("y", i), ("read", ("a", i, m))]
+
         def root(i):
             return (lambda: S.activation(out=rst[:, i], in_=bank["st", i][:], func=ACT.Abs_reciprocal_sqrt)), [("st", i)], [("root", i)]
 
@@ -300,6 +299,11 @@ def tile_multigroupintegraltransportsourceiterati_x1_kernel(tc, flux, scat, dens
             def run():
                 eng.tensor_tensor(out=inv(i, n)[:, :, c0:c0 + w], in0=rst[:, i:i + n, c0:c0 + w], in1=sg[:, i:i + n, c0:c0 + w], op=ALU.mult)
             return run, [(k, j) for k in ("size", "sign") for j in range(i, i + n)] + list(after), [k for j in range(i, i + n) for k in cols("inv", j, c0, w)]
+
+        def join(i, n, m):
+            def run():
+                GP.tensor_tensor(out=x[0][:, i:i + n], in0=x[0][:, i:i + n], in1=y[:, i:i + n], op=ALU.add)
+            return run, [k for j in range(i, i + n) for k in (("y", j), ("x", j, m - 1))], [("x", j, m) for j in range(i, i + n)]
 
         def weave_scat(m, c0, w, eng, after=()):
             return (lambda: weave(eng, scat_grp(m, c0, w), scat_raw[m][:, :, c0:c0 + w])), list(after), cols("scat_grp", m, c0, w)
@@ -362,43 +366,30 @@ def tile_multigroupintegraltransportsourceiterati_x1_kernel(tc, flux, scat, dens
         def f_sum():
             return (lambda: V.tensor_reduce(out=f[:], in_=pd[:], axis=AX.X, op=ALU.add)), ["pd"], ["fsum"]
 
-        def f_chi(i, eng, after=()):
-            def run():
-                if eng is S:
-                    S.activation(out=fx()[:, i], in_=chi_b[:], func=ACT.Copy, scale=f[:, i:i + 1])
-                else:
-                    GP.tensor_scalar(out=fx()[:, i], in0=chi_b[:], scalar1=f[:, i:i + 1], scalar2=0.0, op0=ALU.mult, op1=ALU.add)
-            return run, ["fsum"] + list(after), [("fx", i)]
-
-        def source(g, c0, w, eng):
-            def run():
-                dst, s = blocks(q_grp(g, c0, w), x[g][:, :, c0:c0 + w])
-                eng.tensor_tensor(out=dst, in0=s, in1=fx()[:, :, c0:c0 + w].rearrange("p t (c i) -> p c t i", i=4), op=ALU.add)
-            return run, [k for i in range(4 * g, 4 * g + 4) for k in (("x", i, M - 1), ("fx", i))], cols("q_grp", g, c0, w)
-
         def piece(k):
-            return dens_pad[:, 4:NT, CHI_AT + k]
+            return f_pad[:, :, k:16:4]
 
         def f_first():
             def run():
                 with nc.allow_low_precision(reason="the first bf16 piece of f; the later pieces carry the rest"):
-                    V.tensor_reduce(out=piece(0), in_=pd[:, 4:NT], axis=AX.X, op=ALU.add)
+                    V.tensor_reduce(out=piece(0), in_=pd[:].rearrange("p (g t) m -> p g t m", g=2), axis=AX.X, op=ALU.add)
             return run, ["pd"], ["first"]
 
         def f_less_first():
-            return (lambda: V.tensor_tensor(out=f_rest(), in0=f[:, 4:NT], in1=piece(0), op=ALU.subtract)), ["fsum", "first"], ["rest"]
+            return (lambda: V.tensor_tensor(out=f_rest(), in0=f[:].rearrange("p (g t) -> p g t", g=2), in1=piece(0), op=ALU.subtract)), ["fsum", "first"], ["rest"]
 
         def f_second():
-            return (lambda: V.tensor_copy(out=piece(1), in_=f_rest())), ["rest"], ["second"]
+            return (lambda: V.tensor_tensor(out=piece(1), in0=f[:].rearrange("p (g t) -> p g t", g=2), in1=piece(0), op=ALU.subtract)), ["fsum", "first"], ["second"]
 
         def f_third():
-            return (lambda: V.tensor_tensor(out=piece(2), in0=f_rest(), in1=piece(1), op=ALU.subtract)), ["second"], ["pieces"]
+            return (lambda: V.tensor_tensor(out=piece(2), in0=f_rest(), in1=piece(1), op=ALU.subtract)), ["rest", "second"], ["pieces"]
 
-        def source_late(c0):
+        def source(g, c0):
             def run():
-                dst, s = blocks(q_grp(1, c0, P), x[1][:, :, c0:c0 + P])
-                V.tensor_tensor(out=dst, in0=bank["e", c0][:].rearrange("p t (c i) -> p c t i", i=4), in1=s, op=ALU.add)
-            return run, [("x", i, M - 1, c0 - c0 % H) for i in range(4, NT)] + [("e", c0)], cols("q_grp", 1, c0, P) + [("read", ("e", c0))]
+                dst, s = blocks(q_grp(g, c0, P), x[g][:, :, c0:c0 + P])
+                V.tensor_tensor(out=dst, in0=bank["e", g, c0][:].rearrange("p t (c i) -> p c t i", i=4), in1=s, op=ALU.add)
+            done = [("x", i, M - 1, c0 - c0 % H) if g else ("x", i, M - 1) for i in range(4 * g, 4 * g + 4)]
+            return run, done + [("e", g, c0)], cols("q_grp", g, c0, P) + [("read", ("e", g, c0))]
 
         def divide(unit):
             g, t0, n, c0, w = unit
@@ -450,7 +441,7 @@ def tile_multigroupintegraltransportsourceiterati_x1_kernel(tc, flux, scat, dens
             SP.dma_start(out=flux_raw[b][:], in_=flux_v[b // 2, :, 2 * (b % 2):2 * (b % 2) + 2])
 
         V.memset(warm[:], 1.0)
-        for t in (idle, sig_pad, rows, dens_pad):
+        for t in (idle, sig_pad, rows, dens_pad, f_pad):
             V.memset(t[:], 0.0)
         make_identity(nc, id32[:])
         S.dma_start(out=dens_sb[:], in_=dens.rearrange("(g p t) m -> p g (t m)", g=2, t=4))
@@ -464,11 +455,13 @@ def tile_multigroupintegraltransportsourceiterati_x1_kernel(tc, flux, scat, dens
         load_flux(2)
         load_flux(3)
         load_scat(3)
-        SP.dma_start(out=chi_b[:], in_=chi.partition_broadcast(P))
         SP.dma_start(out=kern_raw[0][:], in_=kern_v[0])
         SP.dma_start(out=kern_raw[1][:], in_=kern_v[1])
 
         S.activation(out=warm[:, 1:2], in_=warm[:, 0:1], func=ACT.Abs_reciprocal_sqrt)
+        S.copy(out=chi_d[:].bitcast(F32), in_=idle[:].unsqueeze(1).to_broadcast([P, 4, H]))
+        for t in range(4):
+            SP.dma_start(out=chi_d[4 * t:4 * t + 4, t], in_=chi.partition_broadcast(4))
         V.tensor_copy(out=dens_pad[:, :, 0:M], in_=dens_v)
         V.tensor_copy(out=id16[:], in_=id32[:])
         V.tensor_copy(out=dens32[:], in_=dens_v)
@@ -477,39 +470,38 @@ def tile_multigroupintegraltransportsourceiterati_x1_kernel(tc, flux, scat, dens
         quarters = range(0, G, P)
         units = [(g, 2 * h, 2, c0, H) for g in range(2) for c0 in (0, H) for h in range(2)]
         SCAT_PIECES = [[("a", 0, G)], [("b", 0, G)], [("c", 0, P), ("a", P, P), ("c", H, H)], [("b", 0, P), ("b", P, G - P)]]
-        INV_IN = [(None, 0, 1), ("rest", 1, 2), ("kern1", 3, 1), (None, 4, 1), ("q1_0", 5, 2), ("kern3", 7, 1)]
+        INV_IN = [(None, 0, 1), ("rest", 1, 1), (None, 2, 2), ("kern1", 4, 2), ("kern3", 6, 2)]
 
-        qt = [warm_up(H), warm_up(H), t_pad("dens", 0, NT, "sa"), warm_up(P), t_flux(0), t_nusf(), total(0, "sb"), warm_up(H), fission(0, "sa"), t_flux(1), scatter(0, 0), scatter(1, 0), fission(1)]
+        qt = [warm_up(H), warm_up(H), t_pad("dens", 0, NT, "sa"), warm_up(H), t_flux(0), t_nusf(), total(0, "sb"), warm_up(H), fission(0, "sa"), t_flux(1), scatter(0, 0), scatter(1, 0), fission(1)]
         qt += [scatter(0, 1), scatter(2, 0, "tp"), scatter(1, 1), scatter(3, 0, "tp"), scatter(2, 1), scatter(3, 1), t_flux(2, "sb"), total(1, "mm"), t_flux(3), total(2, "tp"), fission(2)]
         qt += [scatter(0, 2), scatter(1, 2), fission(3), scatter(4, 0, "sb"), scatter(2, 2), scatter(5, 0, "tp"), scatter(3, 2), fission(4), scatter(4, 1), fission(5), scatter(5, 1), fission(6), fission(7), total(3, "sb")]
-        qt += [scatter(0, 3), scatter(1, 3), scatter(6, 0, "tp"), scatter(2, 3), scatter(7, 0, "tp"), scatter(3, 3), scatter(4, 2), t_pad("f", 4, 4, "sb"), t_kern(0, "sa"), scatter(5, 2), scatter(6, 1), scatter(7, 1), t_kern(1), scatter(6, 2), scatter(7, 2)]
-        qt += [scatter_half(4, 3, 0), t_kern(2), scatter_half(6, 3, 0), t_kern(3, "sb"), total(4, "sa"), scatter_half(4, 3, H), total(5, "tp"), scatter_half(6, 3, H), total(6, "tp"), emission(quarters[0], "sb"), emission(quarters[1], "sa")]
-        qt += [open_unit(units[0], "mm"), open_unit(units[1], "mm"), t_kern(4), t_kern(5, "sb"), emission(quarters[2], "mm"), close_unit(units[0]), close_unit(units[1]), total(7, "tp"), emission(quarters[3], "mm"), t_kern(6, "sa"), t_kern(7)]
+        qt += [scatter(3, 3), scatter(0, 3, "tp"), scatter(4, 2), scatter(6, 0, "tp"), scatter(5, 2), scatter(7, 0, "sa"), scatter(6, 1), scatter(1, 3, "tp"), scatter(7, 1), scatter(2, 3, "sb"), scatter(6, 2), scatter(7, 2), total(4, "sa")]
+        qt += [scatter_half(4, 3, 0), t_pad("f", 0, 2, "tp"), scatter_half(6, 3, 0), t_kern(0, "sb"), scatter_half(4, 3, H), emission(1, quarters[0], "mm"), t_kern(1), emission(1, quarters[1], "mm"), t_kern(2), emission(0, quarters[0], "mm"), total(5, "sa"), emission(0, quarters[1], "mm"), emission(0, quarters[2], "mm"), t_kern(3, "sb"), emission(0, quarters[3], "mm")]
+        qt += [total(6, "tp"), t_kern(4), scatter_half(6, 3, H), t_kern(5, "sa"), total(7, "sb"), open_unit(units[0], "mm"), close_unit(units[0]), open_unit(units[1], "mm"), close_unit(units[1]), emission(1, quarters[2], "mm"), t_kern(6), emission(1, quarters[3], "mm"), t_kern(7)]
         qt += [open_unit(units[2], "mm"), open_unit(units[3], "mm"), close_unit(units[2]), close_unit(units[3])]
-        for u, ring in zip(units[4:], ("mm", "mm", "sa", "sb")):
-            qt += [open_unit(u, ring), close_unit(u)]
+        for k, ring in zip((4, 5, 6, 7), ("mm", "mm", "sa", "sb")):
+            qt += [open_unit(units[k], ring), close_unit(units[k])]
 
         qv = [weave_scat(0, 0, H, V), weave_scat(0, H, H, V), quant_scat(0, 0, H), quant_scat(0, H, H), weave_scat(1, 0, H, V), quant_flux(0), weave_scat(1, H, H, V)]
         qv += [quant_scat(1, 0, H), quant_scat(1, H, H), quant_flux(1), weave_scat(2, 0, P, V), weave_scat(2, P, P, V), quant_scat(2, 0, P)]
         qv += [weigh_add(i, 1) for i in lo]
         qv += [quant_scat(2, P, P), quant_scat(2, H, H), weave_scat(3, 0, P, V), quant_flux(2), quant_scat(3, 0, P)] + [weigh_add(i, 2) for i in lo] + [weigh_add(4, 1), weigh_add(5, 1)]
-        qv += [f_weigh(), quant_scat(3, P, G - P), f_sum(), f_first(), quant_flux(3), f_less_first(), f_second(), f_third()]
-        qv += [weigh_add(i, 3) for i in lo] + [weigh_add(4, 2), weigh_add(5, 2), weigh_add(6, 1), weigh_add(7, 1), weigh_add(6, 2), weigh_add(7, 2), weigh_half(4, 3, 0), weigh_half(5, 3, 0)]
-        qv += [source(0, G - P, P, V), quant_q(0, 0, H), quant_kern(0), quant_q(0, H, H), quant_kern(1)]
-        qv += [weigh_half(6, 3, 0), weigh_half(7, 3, 0), weigh_half(4, 3, H)] + [source_late(c) for c in quarters[:2]] + [weigh_half(5, 3, H), quant_q(1, 0, H)] + [weigh_half(i, 3, H) for i in hi[2:]]
-        qv += [source_late(quarters[2])] + [divide(u) for u in units[:2]] + [source_late(quarters[3]), quant_kern(2), quant_q(1, H, H), quant_kern(3)]
+        qv += [quant_scat(3, P, G - P), f_weigh(), quant_flux(3), f_sum(), f_first(), f_less_first(), f_second(), f_third()]
+        qv += [weigh_add(3, 3), weigh_add(4, 2), weigh_add(5, 2), weigh_add(6, 1), weigh_add(7, 1), weigh_add(6, 2), weigh_add(7, 2)] + [weigh_half(i, 3, 0) for i in hi] + [weigh_half(i, 3, H) for i in hi[:2]]
+        qv += [source(1, c) for c in quarters[:2]] + [source(0, c) for c in quarters]
+        qv += [quant_q(1, 0, H), quant_q(0, 0, H), quant_kern(0), quant_q(0, H, H), quant_kern(1)] + [weigh_half(i, 3, H) for i in hi[2:]]
+        qv += [divide(units[0]), divide(units[1]), source(1, quarters[2]), source(1, quarters[3]), quant_kern(2), quant_q(1, H, H), quant_kern(3), signed(7, 1, H, H, [("kern_q", 3)], V)]
         qv += [divide(u) for u in units[2:]] + [quant_res(0, 0, G)]
         qv += [weave_res(1, H + P, V), quant_res(1, 0, H), quant_res(1, H, H)]
 
         qs = [c_pad("dens", dens_t, 0, NT), c_flux(0), c_nusf(), root(0), sign(0), c_flux(1), weigh_first(0), weigh_first(1), weigh_first(2), weigh_first(3), square(0)]
-        qs += [c_flux(2), root(1), c_flux(3), sign(1), square(1), weigh_first(4), weigh_first(5), root(2), sign(2), square(2), root(3), sign(3)] + [f_chi(i, S) for i in lo] + [weigh_first(6), weigh_first(7), c_f(), c_kern(0), c_kern(1), square(3)]
-        qs += [c_kern(2), c_kern(3)] + inverse(4) + inverse(5) + inverse(6) + [c_kern(4), c_kern(5), root(7), c_kern(6), c_kern(7), sign(7), square(7)]
-        qs += [weave_res(0, c, S) for c in quarters[:3]] + [weave_res(1, 0, S), weave_res(1, H, S)] + [store_scales(1, S), store_scales(3, S)]
+        qs += [c_flux(2), root(1), c_flux(3), sign(1), square(1), weigh_first(4), weigh_first(5), root(2), sign(2), square(2), root(3), sign(3), weigh_aside(0, 3), weigh_first(6), weigh_first(7), weigh_aside(1, 3), weigh_aside(2, 3), square(3), c_f()]
+        qs += [root(4), sign(4), c_kern(0), square(4), c_kern(1), c_kern(2), root(5), sign(5), c_kern(3), square(5)] + inverse(6) + [c_kern(4), c_kern(5)] + inverse(7) + [c_kern(6), c_kern(7), weave_res(0, 0, S), weave_res(0, P, S)]
+        qs += [weave_res(0, H, S), weave_res(0, H + P, S)] + [weave_res(1, c, S) for c in quarters[:3]] + [store_scales(1, S), store_scales(3, S)]
 
-        qg = [weave_scat(2, H, H, GP, cols("scat_q", 2, 0, P)), weave_scat(3, P, G - P, GP, cols("scat_q", 3, 0, P)), signed(0), signed(1, 2, after=["pieces"]), source(0, 0, H, GP), source(0, H, P, GP)]
-        qg += [signed(3, after=[("kern_q", 1)]), signed(4), signed(5, 2, after=cols("q_q", 1, 0, H)), signed(7, after=[("kern_q", 3)]), weave_res(0, H + P, GP), weave_res(1, P, GP)]
+        qg = [weave_scat(2, H, H, GP, cols("scat_q", 2, 0, P)), weave_scat(3, P, G - P, GP, cols("scat_q", 3, 0, P)), signed(0, 1, 0, H), signed(1, after=["pieces"]), join(0, 1, 3), join(1, 2, 3), signed(2, 2), signed(0, 1, H, H)]
+        qg += [signed(4, 2, after=[("kern_q", 1)]), signed(6, 2, 0, H, after=[("kern_q", 3)]), signed(6, 1, H, H)]
 
-        load_chi = (lambda: SP.dma_start(out=rows[CHI_AT:CHI_AT + PIECES], in_=chi.partition_broadcast(PIECES))), ["nusf"], ["chi"]
-        qy = [load_chi] + [store(units[k]) for k in range(8)] + [store_codes(0, 0, G), store_codes(1, 0, H), store_codes(1, H, H)]
+        qy = [store(u) for u in units] + [store_codes(0, 0, G), store_codes(1, 0, H), store_codes(1, H, H)]
         qy += [store_scales(0, SP), store_scales(2, SP)]
         emit([qt, qv, qs, qg, qy])

@@ -228,7 +228,7 @@ def tile_multigroupintegraltransportsourceiterati_x1_kernel(tc, flux, scat, dens
 
         def emission(g, c0, ring):
             alloc, needs = take(ring, ("e", g, c0), [P, 4, P])
-            return (lambda: T.matmul(alloc()[:], lhsT=f_t[:, g], rhs=chi_d[:, :, c0:c0 + P], start=True, stop=True)), needs + ["f_t"], [("e", g, c0)]
+            return (lambda: T.matmul(alloc()[:], lhsT=f_t[:, g], rhs=chi_d[:, :, c0:c0 + P], start=True, stop=True)), needs + ["f_t"] + [("chi", t) for t in range(4)], [("e", g, c0)]
 
         def transport_pass(ps, unit, gs):
             g, t0, n, c0, w = unit
@@ -249,6 +249,12 @@ def tile_multigroupintegraltransportsourceiterati_x1_kernel(tc, flux, scat, dens
 
         def c_pad(name, dst, i0, n):
             return (lambda: S.copy(out=dst[:, i0:i0 + n], in_=bank[name, i0][:])), [(name, i0)], [(name + "_t", i) for i in range(i0, i0 + n)] + [("read", (name, i0))]
+
+        def clear_chi():
+            return (lambda: S.copy(out=chi_d[:, 2:4].bitcast(F32), in_=idle[:].unsqueeze(1).to_broadcast([P, 2, H]))), [], ["cleared"]
+
+        def load_chi(t):
+            return (lambda: SP.dma_start(out=chi_d[4 * t:4 * t + 4, t], in_=chi.partition_broadcast(4))), ["cleared"], [("chi", t)]
 
         def c_f():
             return (lambda: S.copy(out=f_t[:], in_=bank["f", 0][:])), [("f", 0)], ["f_t", ("read", ("f", 0))]
@@ -441,8 +447,8 @@ def tile_multigroupintegraltransportsourceiterati_x1_kernel(tc, flux, scat, dens
             SP.dma_start(out=flux_raw[b][:], in_=flux_v[b // 2, :, 2 * (b % 2):2 * (b % 2) + 2])
 
         V.memset(warm[:], 1.0)
-        for t in (idle, sig_pad, rows, dens_pad, f_pad):
-            V.memset(t[:], 0.0)
+        for t in (idle[:], sig_pad[:], rows[:], dens_pad[:], f_pad[:], chi_d[:, 0:2]):
+            V.memset(t.bitcast(U32), 0)
         make_identity(nc, id32[:])
         S.dma_start(out=dens_sb[:], in_=dens.rearrange("(g p t) m -> p g (t m)", g=2, t=4))
         S.dma_start(out=sig_pad[0:M], in_=sigt)
@@ -459,11 +465,8 @@ def tile_multigroupintegraltransportsourceiterati_x1_kernel(tc, flux, scat, dens
         SP.dma_start(out=kern_raw[1][:], in_=kern_v[1])
 
         S.activation(out=warm[:, 1:2], in_=warm[:, 0:1], func=ACT.Abs_reciprocal_sqrt)
-        S.copy(out=chi_d[:].bitcast(F32), in_=idle[:].unsqueeze(1).to_broadcast([P, 4, H]))
-        for t in range(4):
-            SP.dma_start(out=chi_d[4 * t:4 * t + 4, t], in_=chi.partition_broadcast(4))
-        V.tensor_copy(out=dens_pad[:, :, 0:M], in_=dens_v)
         V.tensor_copy(out=id16[:], in_=id32[:])
+        V.tensor_copy(out=dens_pad[:, :, 0:M], in_=dens_v)
         V.tensor_copy(out=dens32[:], in_=dens_v)
 
         lo, hi = range(4), range(4, NT)
@@ -472,8 +475,8 @@ def tile_multigroupintegraltransportsourceiterati_x1_kernel(tc, flux, scat, dens
         SCAT_PIECES = [[("a", 0, G)], [("b", 0, G)], [("c", 0, P), ("a", P, P), ("c", H, H)], [("b", 0, P), ("b", P, G - P)]]
         INV_IN = [(None, 0, 1), ("rest", 1, 1), (None, 2, 2), ("kern1", 4, 2), ("kern3", 6, 2)]
 
-        qt = [warm_up(H), warm_up(H), t_pad("dens", 0, NT, "sa"), warm_up(H), t_flux(0), t_nusf(), total(0, "sb"), warm_up(H), fission(0, "sa"), t_flux(1), scatter(0, 0), scatter(1, 0), fission(1)]
-        qt += [scatter(0, 1), scatter(2, 0, "tp"), scatter(1, 1), scatter(3, 0, "tp"), scatter(2, 1), scatter(3, 1), t_flux(2, "sb"), total(1, "mm"), t_flux(3), total(2, "tp"), fission(2)]
+        qt = [warm_up(H), warm_up(H), t_pad("dens", 0, 1, "sa"), warm_up(P), t_flux(0), total(0, "sb"), t_nusf(), t_pad("dens", 1, NT - 1, "mm"), warm_up(H), t_flux(1), fission(0, "sa"), scatter(0, 0), scatter(1, 0), fission(1)]
+        qt += [scatter(0, 1), scatter(1, 1), scatter(2, 0, "tp"), scatter(3, 0, "tp"), scatter(2, 1), scatter(3, 1), t_flux(2, "sb"), total(1, "mm"), t_flux(3), total(2, "tp"), fission(2)]
         qt += [scatter(0, 2), scatter(1, 2), fission(3), scatter(4, 0, "sb"), scatter(2, 2), scatter(5, 0, "tp"), scatter(3, 2), fission(4), scatter(4, 1), fission(5), scatter(5, 1), fission(6), fission(7), total(3, "sb")]
         qt += [scatter(3, 3), scatter(0, 3, "tp"), scatter(4, 2), scatter(6, 0, "tp"), scatter(5, 2), scatter(7, 0, "sa"), scatter(6, 1), scatter(1, 3, "tp"), scatter(7, 1), scatter(2, 3, "sb"), scatter(6, 2), scatter(7, 2), total(4, "sa")]
         qt += [scatter_half(4, 3, 0), t_pad("f", 0, 2, "tp"), scatter_half(6, 3, 0), t_kern(0, "sb"), scatter_half(4, 3, H), emission(1, quarters[0], "mm"), t_kern(1), emission(1, quarters[1], "mm"), t_kern(2), emission(0, quarters[0], "mm"), total(5, "sa"), emission(0, quarters[1], "mm"), emission(0, quarters[2], "mm"), t_kern(3, "sb"), emission(0, quarters[3], "mm")]
@@ -483,7 +486,7 @@ def tile_multigroupintegraltransportsourceiterati_x1_kernel(tc, flux, scat, dens
             qt += [open_unit(units[k], ring), close_unit(units[k])]
 
         qv = [weave_scat(0, 0, H, V), weave_scat(0, H, H, V), quant_scat(0, 0, H), quant_scat(0, H, H), weave_scat(1, 0, H, V), quant_flux(0), weave_scat(1, H, H, V)]
-        qv += [quant_scat(1, 0, H), quant_scat(1, H, H), quant_flux(1), weave_scat(2, 0, P, V), weave_scat(2, P, P, V), quant_scat(2, 0, P)]
+        qv += [quant_scat(1, 0, H), quant_scat(1, H, H), weave_scat(2, 0, P, V), quant_flux(1), weave_scat(2, P, P, V), quant_scat(2, 0, P)]
         qv += [weigh_add(i, 1) for i in lo]
         qv += [quant_scat(2, P, P), quant_scat(2, H, H), weave_scat(3, 0, P, V), quant_flux(2), quant_scat(3, 0, P)] + [weigh_add(i, 2) for i in lo] + [weigh_add(4, 1), weigh_add(5, 1)]
         qv += [quant_scat(3, P, G - P), f_weigh(), quant_flux(3), f_sum(), f_first(), f_less_first(), f_second(), f_third()]
@@ -494,7 +497,7 @@ def tile_multigroupintegraltransportsourceiterati_x1_kernel(tc, flux, scat, dens
         qv += [divide(u) for u in units[2:]] + [quant_res(0, 0, G)]
         qv += [weave_res(1, H + P, V), quant_res(1, 0, H), quant_res(1, H, H)]
 
-        qs = [c_pad("dens", dens_t, 0, NT), c_flux(0), c_nusf(), root(0), sign(0), c_flux(1), weigh_first(0), weigh_first(1), weigh_first(2), weigh_first(3), square(0)]
+        qs = [clear_chi(), c_pad("dens", dens_t, 0, 1), c_flux(0), root(0), c_nusf(), c_pad("dens", dens_t, 1, NT - 1), sign(0), c_flux(1), weigh_first(0), weigh_first(1), weigh_first(2), weigh_first(3), square(0)]
         qs += [c_flux(2), root(1), c_flux(3), sign(1), square(1), weigh_first(4), weigh_first(5), root(2), sign(2), square(2), root(3), sign(3), weigh_aside(0, 3), weigh_first(6), weigh_first(7), weigh_aside(1, 3), weigh_aside(2, 3), square(3), c_f()]
         qs += [root(4), sign(4), c_kern(0), square(4), c_kern(1), c_kern(2), root(5), sign(5), c_kern(3), square(5)] + inverse(6) + [c_kern(4), c_kern(5)] + inverse(7) + [c_kern(6), c_kern(7), weave_res(0, 0, S), weave_res(0, P, S)]
         qs += [weave_res(0, H, S), weave_res(0, H + P, S)] + [weave_res(1, c, S) for c in quarters[:3]] + [store_scales(1, S), store_scales(3, S)]
@@ -502,6 +505,6 @@ def tile_multigroupintegraltransportsourceiterati_x1_kernel(tc, flux, scat, dens
         qg = [weave_scat(2, H, H, GP, cols("scat_q", 2, 0, P)), weave_scat(3, P, G - P, GP, cols("scat_q", 3, 0, P)), signed(0, 1, 0, H), signed(1, after=["pieces"]), join(0, 1, 3), join(1, 2, 3), signed(2, 2), signed(0, 1, H, H)]
         qg += [signed(4, 2, after=[("kern_q", 1)]), signed(6, 2, 0, H, after=[("kern_q", 3)]), signed(6, 1, H, H)]
 
-        qy = [store(u) for u in units] + [store_codes(0, 0, G), store_codes(1, 0, H), store_codes(1, H, H)]
+        qy = [load_chi(t) for t in range(4)] + [store(u) for u in units] + [store_codes(0, 0, G), store_codes(1, 0, H), store_codes(1, H, H)]
         qy += [store_scales(0, SP), store_scales(2, SP)]
         emit([qt, qv, qs, qg, qy])

@@ -17,7 +17,7 @@ P = 128
 R, G, M = 1024, 512, 4
 NT = R // P
 H = G // 2
-NU_AT = 8
+NU_AT, CHI_AT = 8, 16
 PIECES = 3
 BANKS = {"mm": 4, "tp": 2, "sa": 1, "sb": 1}
 FLOPS = 2 * R * G * G * M + 2 * R * R * G
@@ -38,10 +38,9 @@ def tile_multigroupintegraltransportsourceiterati_x1_kernel(tc, flux, scat, dens
             return [tile("%s%d" % (name, k), shape, dtype) for k in range(n)]
 
         rows = tile("rows", [P, G], BF16)
-        chi_d = tile("chi_d", [P, 4, G], BF16)
+        slab = tile("slab", [P, 4, G], BF16)
         f_pad = tile("f_pad", [P, 2, P], BF16)
-        sig_pad = tile("sig_pad", [P, G], BF16)
-        dens_pad = tile("dens_pad", [P, NT, P], BF16)
+        dens_pad = tile("dens_pad", [P, 2, P], BF16)
         dens_sb = tile("dens_sb", [P, 2, 4 * M], BF16)
         nusf_t = tile("nusf_t", [P, 2, M], F32)
         flux_raw = tiles("flux_raw", 4, [P, 2, G], BF16)
@@ -50,7 +49,7 @@ def tile_multigroupintegraltransportsourceiterati_x1_kernel(tc, flux, scat, dens
         id32 = tile("id32", [P, P], F32)
         id16 = tile("id16", [P, P], BF16)
         dens32 = tile("dens32", [P, NT, M], F32)
-        dens_t = tile("dens_t", [P, NT, P], BF16)
+        dens_t = tile("dens_t", [P, 2, P], BF16)
         y = tile("y", [P, 4, G], F32)
         f_t = tile("f_t", [P, 2, P], BF16)
         flux_grp = tiles("flux_grp", 4, [P, 2, P, 4], BF16)
@@ -129,12 +128,14 @@ def tile_multigroupintegraltransportsourceiterati_x1_kernel(tc, flux, scat, dens
             h0 = c0 - c0 % H
             return tenant("q%d_%d" % (g, h0), "q_grp%d_%d" % (g, h0), [P, H, 4], BF16)[:, c0 - h0:c0 - h0 + w]
 
-        def inv(i, n):
-            for buffer, i0, ni in INV_IN:
-                if i0 <= i and i + n <= i0 + ni:
-                    if buffer is None:
-                        return rst[:, i:i + n]
-                    return tenant(buffer, "inv%d" % i0, [P, ni, G], F32)[:, i - i0:i - i0 + n]
+        def inv(i, n, c0, w):
+            for buffer, i0, ni, b0, bw in INV_IN:
+                if i0 <= i and i + n <= i0 + ni and b0 <= c0 and c0 + w <= b0 + bw:
+                    return tenant(buffer, "inv%d_%d" % (i0, b0), [P, ni, bw], F32)[:, i - i0:i - i0 + n, c0 - b0:c0 - b0 + w]
+            return rst[:, i:i + n, c0:c0 + w]
+
+        def apart(i, c0):
+            return [k for k, (buffer, i0, ni, b0, bw) in enumerate(INV_IN) if i0 <= i < i0 + ni and b0 <= c0 < b0 + bw]
 
         def t_pad(name, i0, n, ring):
             alloc, needs = take(ring, (name, i0), [P, n, P], BF16)
@@ -197,7 +198,7 @@ def tile_multigroupintegraltransportsourceiterati_x1_kernel(tc, flux, scat, dens
 
         def total(i, ring):
             alloc, needs = take(ring, ("st", i), [P, G])
-            return (lambda: T.matmul(alloc()[:], lhsT=dens_t[:, i], rhs=sig_pad[:], start=True, stop=True)), needs + [("dens_t", i)], [("st", i)]
+            return (lambda: T.matmul(alloc()[:], lhsT=dens_t[:, i // 4], rhs=slab[:, i % 4], start=True, stop=True)), needs + [("dens_t", i // 4)], [("st", i)]
 
         def scatter(i, m, ring="mm"):
             alloc, needs = take(ring, ("a", i, m), [P, G])
@@ -217,18 +218,18 @@ def tile_multigroupintegraltransportsourceiterati_x1_kernel(tc, flux, scat, dens
                                 rhs=scat_codes[:, m, c0:c0 + H].bitcast(FP8X4), rhs_scale=scat_sc[:, m, c0:c0 + H], start=True, stop=True)
             return run, needs + [("flux_q", i0), ("flux_q", i0 + 1)] + cols("scat_q", m, c0, H), [("a", i0, m, c0)]
 
-        def fission(i, ring=None):
+        def fission(i, ring=None, j0=0, n=4):
             alloc, needs = take(ring, "p", [P, NT, M])
 
             def run():
-                ps = alloc() if i == 0 else bank["p"]
-                for j in range(4):
+                ps = alloc() if i + j0 == 0 else bank["p"]
+                for j in range(j0, j0 + n):
                     T.matmul(ps[:, i], lhsT=flux_grp[i // 2][:, i % 2, :, j], rhs=nusf_k[:, j // 2, :, j % 2], start=(j == 0), stop=(j == 3))
-            return run, (needs if i == 0 else []) + [("flux_grp", i // 2), "nusf_t"], ["p"] if i == NT - 1 else []
+            return run, (needs if i + j0 == 0 else []) + [("flux_grp", i // 2), "nusf_t"], ["p"] if (i, j0 + n) == (NT - 1, 4) else []
 
         def emission(g, c0, ring):
             alloc, needs = take(ring, ("e", g, c0), [P, 4, P])
-            return (lambda: T.matmul(alloc()[:], lhsT=f_t[:, g], rhs=chi_d[:, :, c0:c0 + P], start=True, stop=True)), needs + ["f_t"] + [("chi", t) for t in range(4)], [("e", g, c0)]
+            return (lambda: T.matmul(alloc()[:], lhsT=f_t[:, g], rhs=slab[:, :, c0:c0 + P], start=True, stop=True)), needs + ["f_t"] + [("chi", t) for t in range(4)], [("e", g, c0)]
 
         def transport_pass(ps, unit, gs):
             g, t0, n, c0, w = unit
@@ -250,11 +251,8 @@ def tile_multigroupintegraltransportsourceiterati_x1_kernel(tc, flux, scat, dens
         def c_pad(name, dst, i0, n):
             return (lambda: S.copy(out=dst[:, i0:i0 + n], in_=bank[name, i0][:])), [(name, i0)], [(name + "_t", i) for i in range(i0, i0 + n)] + [("read", (name, i0))]
 
-        def clear_chi():
-            return (lambda: S.copy(out=chi_d[:, 2:4].bitcast(F32), in_=idle[:].unsqueeze(1).to_broadcast([P, 2, H]))), [], ["cleared"]
-
         def load_chi(t):
-            return (lambda: SP.dma_start(out=chi_d[4 * t:4 * t + 4, t], in_=chi.partition_broadcast(4))), ["cleared"], [("chi", t)]
+            return (lambda: SP.dma_start(out=slab[CHI_AT + 4 * t:CHI_AT + 4 * t + 4, t], in_=chi.partition_broadcast(4))), [("st", t)], [("chi", t)]
 
         def c_f():
             return (lambda: S.copy(out=f_t[:], in_=bank["f", 0][:])), [("f", 0)], ["f_t", ("read", ("f", 0))]
@@ -303,7 +301,7 @@ def tile_multigroupintegraltransportsourceiterati_x1_kernel(tc, flux, scat, dens
 
         def signed(i, n=1, c0=0, w=G, after=(), eng=GP):
             def run():
-                eng.tensor_tensor(out=inv(i, n)[:, :, c0:c0 + w], in0=rst[:, i:i + n, c0:c0 + w], in1=sg[:, i:i + n, c0:c0 + w], op=ALU.mult)
+                eng.tensor_tensor(out=inv(i, n, c0, w), in0=rst[:, i:i + n, c0:c0 + w], in1=sg[:, i:i + n, c0:c0 + w], op=ALU.mult)
             return run, [(k, j) for k in ("size", "sign") for j in range(i, i + n)] + list(after), [k for j in range(i, i + n) for k in cols("inv", j, c0, w)]
 
         def join(i, n, m):
@@ -373,7 +371,7 @@ def tile_multigroupintegraltransportsourceiterati_x1_kernel(tc, flux, scat, dens
             return (lambda: V.tensor_reduce(out=f[:], in_=pd[:], axis=AX.X, op=ALU.add)), ["pd"], ["fsum"]
 
         def piece(k):
-            return f_pad[:, :, k:16:4]
+            return f_pad[:, :, CHI_AT + k:CHI_AT + 16:4]
 
         def f_first():
             def run():
@@ -402,9 +400,9 @@ def tile_multigroupintegraltransportsourceiterati_x1_kernel(tc, flux, scat, dens
             i0 = 4 * g + t0
 
             def run():
-                step = n if any(j0 <= i0 and i0 + n <= j0 + nj for buffer, j0, nj in INV_IN) else 1
+                step = n if apart(i0, c0) == apart(i0 + 1, c0) else 1
                 for a in range(0, n, step):
-                    V.tensor_tensor(out=res[g][:, t0 + a:t0 + a + step, c0:c0 + w], in0=bank["c", unit][:, a:a + step], in1=inv(i0 + a, step)[:, :, c0:c0 + w], op=ALU.mult)
+                    V.tensor_tensor(out=res[g][:, t0 + a:t0 + a + step, c0:c0 + w], in0=bank["c", unit][:, a:a + step], in1=inv(i0 + a, step, c0, w), op=ALU.mult)
             needs = [k for i in range(i0, i0 + n) for k in cols("inv", i, c0, w)]
             return run, [("c", unit)] + needs, [k for t in range(t0, t0 + n) for k in cols(("res", t), g, c0, w)] + [("read", ("c", unit))]
 
@@ -447,62 +445,64 @@ def tile_multigroupintegraltransportsourceiterati_x1_kernel(tc, flux, scat, dens
             SP.dma_start(out=flux_raw[b][:], in_=flux_v[b // 2, :, 2 * (b % 2):2 * (b % 2) + 2])
 
         V.memset(warm[:], 1.0)
-        for t in (idle[:], sig_pad[:], rows[:], dens_pad[:], f_pad[:], chi_d[:, 0:2]):
+        for t in (idle[:], slab[:, 0], rows[:], dens_pad[:], slab[:, 1:4], f_pad[:]):
             V.memset(t.bitcast(U32), 0)
         make_identity(nc, id32[:])
         S.dma_start(out=dens_sb[:], in_=dens.rearrange("(g p t) m -> p g (t m)", g=2, t=4))
-        S.dma_start(out=sig_pad[0:M], in_=sigt)
+        S.dma_start(out=slab[0:M, 0], in_=sigt)
         load_scat(0)
         load_flux(0)
         SP.dma_start(out=rows[NU_AT:NU_AT + M], in_=nusf)
-        load_scat(1)
         load_flux(1)
+        load_scat(1)
         load_scat(2)
         load_flux(2)
         load_flux(3)
         load_scat(3)
+        for t in range(1, 4):
+            SP.dma_start(out=slab[4 * t:4 * t + M, t], in_=sigt)
         SP.dma_start(out=kern_raw[0][:], in_=kern_v[0])
         SP.dma_start(out=kern_raw[1][:], in_=kern_v[1])
 
         S.activation(out=warm[:, 1:2], in_=warm[:, 0:1], func=ACT.Abs_reciprocal_sqrt)
         V.tensor_copy(out=id16[:], in_=id32[:])
-        V.tensor_copy(out=dens_pad[:, :, 0:M], in_=dens_v)
+        V.tensor_copy(out=dens_pad[:, :, 0:4 * M], in_=dens_sb[:])
         V.tensor_copy(out=dens32[:], in_=dens_v)
 
         lo, hi = range(4), range(4, NT)
         quarters = range(0, G, P)
         units = [(g, 2 * h, 2, c0, H) for g in range(2) for c0 in (0, H) for h in range(2)]
         SCAT_PIECES = [[("a", 0, G)], [("b", 0, G)], [("c", 0, P), ("a", P, P), ("c", H, H)], [("b", 0, P), ("b", P, G - P)]]
-        INV_IN = [(None, 0, 1), ("rest", 1, 1), (None, 2, 2), ("kern1", 4, 2), ("kern3", 6, 2)]
+        INV_IN = [("rest", 1, 1, 0, G), ("kern1", 4, 2, 0, G), ("kern3", 6, 2, 0, H)]
 
-        qt = [warm_up(H), warm_up(H), t_pad("dens", 0, 1, "sa"), warm_up(P), t_flux(0), total(0, "sb"), t_nusf(), t_pad("dens", 1, NT - 1, "mm"), warm_up(H), t_flux(1), fission(0, "sa"), scatter(0, 0), scatter(1, 0), fission(1)]
-        qt += [scatter(0, 1), scatter(1, 1), scatter(2, 0, "tp"), scatter(3, 0, "tp"), scatter(2, 1), scatter(3, 1), t_flux(2, "sb"), total(1, "mm"), t_flux(3), total(2, "tp"), fission(2)]
-        qt += [scatter(0, 2), scatter(1, 2), fission(3), scatter(4, 0, "sb"), scatter(2, 2), scatter(5, 0, "tp"), scatter(3, 2), fission(4), scatter(4, 1), fission(5), scatter(5, 1), fission(6), fission(7), total(3, "sb")]
-        qt += [scatter(3, 3), scatter(0, 3, "tp"), scatter(4, 2), scatter(6, 0, "tp"), scatter(5, 2), scatter(7, 0, "sa"), scatter(6, 1), scatter(1, 3, "tp"), scatter(7, 1), scatter(2, 3, "sb"), scatter(6, 2), scatter(7, 2), total(4, "sa")]
-        qt += [scatter_half(4, 3, 0), t_pad("f", 0, 2, "tp"), scatter_half(6, 3, 0), t_kern(0, "sb"), scatter_half(4, 3, H), emission(1, quarters[0], "mm"), t_kern(1), emission(1, quarters[1], "mm"), t_kern(2), emission(0, quarters[0], "mm"), total(5, "sa"), emission(0, quarters[1], "mm"), emission(0, quarters[2], "mm"), t_kern(3, "sb"), emission(0, quarters[3], "mm")]
-        qt += [total(6, "tp"), t_kern(4), scatter_half(6, 3, H), t_kern(5, "sa"), total(7, "sb"), open_unit(units[0], "mm"), close_unit(units[0]), open_unit(units[1], "mm"), close_unit(units[1]), emission(1, quarters[2], "mm"), t_kern(6), emission(1, quarters[3], "mm"), t_kern(7)]
+        qt = [warm_up(H), warm_up(H), t_pad("dens", 0, 2, "sa"), warm_up(H), t_flux(0), total(0, "sb"), t_flux(1), t_nusf(), warm_up(H), scatter(0, 0), scatter(1, 0), fission(0, "sa"), scatter(2, 0, "tp"), scatter(3, 0, "tp"), fission(1)]
+        qt += [scatter(0, 1), scatter(1, 1), scatter(2, 1), scatter(3, 1), t_flux(2, "sb"), t_flux(3), total(1, "mm"), total(2, "tp"), fission(2)]
+        qt += [scatter(0, 2), scatter(1, 2), scatter(4, 0, "sb"), scatter(2, 2), fission(3), scatter(3, 2), scatter(5, 0, "tp"), scatter(4, 1), scatter(5, 1), fission(4), fission(5), scatter(4, 2), total(3, "sb"), fission(6), fission(7)]
+        qt += [scatter(3, 3), scatter(0, 3, "tp"), scatter(6, 0, "tp"), scatter(5, 2), scatter(7, 0, "sa"), scatter(6, 1), scatter(7, 1), scatter(1, 3, "tp"), scatter(2, 3, "sb"), scatter(6, 2), scatter(7, 2), total(4, "sa")]
+        qt += [scatter_half(4, 3, 0), scatter_half(6, 3, 0), t_pad("f", 0, 2, "tp"), t_kern(0, "sb"), scatter_half(4, 3, H), emission(1, quarters[0], "mm"), t_kern(1), emission(1, quarters[1], "mm"), emission(0, quarters[0], "mm"), t_kern(2), total(5, "sa"), emission(0, quarters[1], "mm"), emission(0, quarters[2], "mm"), t_kern(3, "sb"), emission(0, quarters[3], "mm")]
+        qt += [total(6, "tp"), scatter_half(6, 3, H), t_kern(4), t_kern(5, "sa"), total(7, "sb"), open_unit(units[0], "mm"), close_unit(units[0]), open_unit(units[1], "mm"), close_unit(units[1]), emission(1, quarters[2], "mm"), t_kern(6), emission(1, quarters[3], "mm"), t_kern(7)]
         qt += [open_unit(units[2], "mm"), open_unit(units[3], "mm"), close_unit(units[2]), close_unit(units[3])]
         for k, ring in zip((4, 5, 6, 7), ("mm", "mm", "sa", "sb")):
             qt += [open_unit(units[k], ring), close_unit(units[k])]
 
-        qv = [weave_scat(0, 0, H, V), weave_scat(0, H, H, V), quant_scat(0, 0, H), quant_scat(0, H, H), weave_scat(1, 0, H, V), quant_flux(0), weave_scat(1, H, H, V)]
-        qv += [quant_scat(1, 0, H), quant_scat(1, H, H), weave_scat(2, 0, P, V), quant_flux(1), weave_scat(2, P, P, V), quant_scat(2, 0, P)]
+        qv = [weave_scat(0, 0, H, V), weave_scat(0, H, H, V), quant_scat(0, 0, H), quant_scat(0, H, H), quant_flux(0), weave_scat(1, 0, H, V), quant_flux(1), weave_scat(1, H, H, V)]
+        qv += [quant_scat(1, 0, H), quant_scat(1, H, H), weave_scat(2, 0, P, V), weave_scat(2, P, P, V), quant_scat(2, 0, P)]
         qv += [weigh_add(i, 1) for i in lo]
         qv += [quant_scat(2, P, P), quant_scat(2, H, H), weave_scat(3, 0, P, V), quant_flux(2), quant_scat(3, 0, P)] + [weigh_add(i, 2) for i in lo] + [weigh_add(4, 1), weigh_add(5, 1)]
-        qv += [quant_scat(3, P, G - P), f_weigh(), quant_flux(3), f_sum(), f_first(), f_less_first(), f_second(), f_third()]
-        qv += [weigh_add(3, 3), weigh_add(4, 2), weigh_add(5, 2), weigh_add(6, 1), weigh_add(7, 1), weigh_add(6, 2), weigh_add(7, 2)] + [weigh_half(i, 3, 0) for i in hi] + [weigh_half(i, 3, H) for i in hi[:2]]
+        qv += [quant_scat(3, P, G - P), quant_flux(3), weigh_add(4, 2), f_weigh(), weigh_add(3, 3, 0, H), f_sum(), f_first(), weigh_add(3, 3, H, H), f_less_first(), f_second(), signed(0, 1, 0, H, eng=V), f_third()]
+        qv += [weigh_add(5, 2), weigh_add(6, 1), weigh_add(7, 1), weigh_add(6, 2), weigh_add(7, 2)] + [weigh_half(i, 3, 0) for i in hi] + [weigh_half(i, 3, H) for i in hi[:2]]
         qv += [source(1, c) for c in quarters[:2]] + [source(0, c) for c in quarters]
         qv += [quant_q(1, 0, H), quant_q(0, 0, H), quant_kern(0), quant_q(0, H, H), quant_kern(1)] + [weigh_half(i, 3, H) for i in hi[2:]]
-        qv += [divide(units[0]), divide(units[1]), source(1, quarters[2]), source(1, quarters[3]), quant_kern(2), quant_q(1, H, H), quant_kern(3), signed(7, 1, H, H, [("kern_q", 3)], V)]
+        qv += [divide(units[0]), divide(units[1]), source(1, quarters[2]), source(1, quarters[3]), quant_kern(2), quant_q(1, H, H), signed(7, 1, H, H, eng=V), quant_kern(3)]
         qv += [divide(u) for u in units[2:]] + [quant_res(0, 0, G)]
         qv += [weave_res(1, H + P, V), quant_res(1, 0, H), quant_res(1, H, H)]
 
-        qs = [clear_chi(), c_pad("dens", dens_t, 0, 1), c_flux(0), root(0), c_nusf(), c_pad("dens", dens_t, 1, NT - 1), sign(0), c_flux(1), weigh_first(0), weigh_first(1), weigh_first(2), weigh_first(3), square(0)]
+        qs = [c_pad("dens", dens_t, 0, 2), c_flux(0), c_flux(1), c_nusf(), root(0), sign(0), weigh_first(0), weigh_first(1), weigh_first(2), weigh_first(3), square(0)]
         qs += [c_flux(2), root(1), c_flux(3), sign(1), square(1), weigh_first(4), weigh_first(5), root(2), sign(2), square(2), root(3), sign(3), weigh_aside(0, 3), weigh_first(6), weigh_first(7), weigh_aside(1, 3), weigh_aside(2, 3), square(3), c_f()]
         qs += [root(4), sign(4), c_kern(0), square(4), c_kern(1), c_kern(2), root(5), sign(5), c_kern(3), square(5)] + inverse(6) + [c_kern(4), c_kern(5)] + inverse(7) + [c_kern(6), c_kern(7), weave_res(0, 0, S), weave_res(0, P, S)]
         qs += [weave_res(0, H, S), weave_res(0, H + P, S)] + [weave_res(1, c, S) for c in quarters[:3]] + [store_scales(1, S), store_scales(3, S)]
 
-        qg = [weave_scat(2, H, H, GP, cols("scat_q", 2, 0, P)), weave_scat(3, P, G - P, GP, cols("scat_q", 3, 0, P)), signed(0, 1, 0, H), signed(1, after=["pieces"]), join(0, 1, 3), join(1, 2, 3), signed(2, 2), signed(0, 1, H, H)]
+        qg = [weave_scat(2, H, H, GP, cols("scat_q", 2, 0, P)), weave_scat(3, P, G - P, GP, cols("scat_q", 3, 0, P)), signed(0, 1, H, H), signed(1, after=["pieces"]), join(0, 1, 3), join(1, 2, 3), signed(2, 2)]
         qg += [signed(4, 2, after=[("kern_q", 1)]), signed(6, 2, 0, H, after=[("kern_q", 3)]), signed(6, 1, H, H)]
 
         qy = [load_chi(t) for t in range(4)] + [store(u) for u in units] + [store_codes(0, 0, G), store_codes(1, 0, H), store_codes(1, H, H)]

@@ -71,7 +71,7 @@ def tile_multigroupintegraltransportsourceiterati_x1_kernel(tc, flux, scat, dens
         r_codes = tile("r_codes", [P, 2, G], U32)
         r_sc = tile("r_sc", [P, G], U8)
         warm = tile("warm", [P, 2], F32)
-        idle = tile("idle", [P, H], F32)
+        idle = tile("idle", [P, G], BF16)
 
         held = {}
 
@@ -177,10 +177,10 @@ def tile_multigroupintegraltransportsourceiterati_x1_kernel(tc, flux, scat, dens
                     T.transpose(ps[:, u], rows[:].bitcast(F32)[:, u:H:2], id32[:])
             return run, needs, ["nusf"]
 
-        def warm_up(w):
+        def warm_up(w, dtype=BF16):
             alloc, needs = take("mm", ("warm", len(warmed)), [P, w])
             warmed.append(w)
-            return (lambda: T.matmul(alloc()[:], lhsT=idle[:, 0:P], rhs=idle[:, 0:w], start=True, stop=True)), needs, [("read", ("warm", len(warmed) - 1))]
+            return (lambda: T.matmul(alloc()[:], lhsT=idle[:].bitcast(dtype)[:, 0:P], rhs=idle[:].bitcast(dtype)[:, 0:w], start=True, stop=True)), needs, [("read", ("warm", len(warmed) - 1))]
 
         def t_weave(m, c0, ring):
             alloc, needs = take(ring, ("w", m, c0), [P, 2, G], BF16)
@@ -453,8 +453,8 @@ def tile_multigroupintegraltransportsourceiterati_x1_kernel(tc, flux, scat, dens
         load_scat(0)
         load_flux(0)
         SP.dma_start(out=rows[NU_AT:NU_AT + M], in_=nusf)
-        load_flux(1)
         load_scat(1)
+        load_flux(1)
         load_scat(2)
         load_flux(2)
         load_flux(3)
@@ -475,29 +475,29 @@ def tile_multigroupintegraltransportsourceiterati_x1_kernel(tc, flux, scat, dens
         SCAT_PIECES = [[("a", 0, G)], [("b", 0, G)], [("c", 0, P), ("a", P, P), ("c", H, H)], [("b", 0, P), ("b", P, G - P)]]
         INV_IN = [("rest", 1, 1, 0, G), ("kern1", 4, 2, 0, G), ("kern3", 6, 2, 0, H)]
 
-        qt = [warm_up(H), warm_up(H), t_pad("dens", 0, 2, "sa"), warm_up(H), t_flux(0), total(0, "sb"), t_flux(1), t_nusf(), warm_up(H), scatter(0, 0), scatter(1, 0), fission(0, "sa"), scatter(2, 0, "tp"), scatter(3, 0, "tp"), fission(1)]
-        qt += [scatter(0, 1), scatter(1, 1), scatter(2, 1), scatter(3, 1), t_flux(2, "sb"), t_flux(3), total(1, "mm"), total(2, "tp"), fission(2)]
+        qt = [warm_up(H, F32), warm_up(H, F32), t_pad("dens", 0, 2, "sa"), warm_up(H, F32), t_flux(0), total(0, "sb"), t_nusf(), warm_up(H, F32), fission(0, "sa"), t_flux(1), scatter(0, 0), scatter(1, 0), fission(1)]
+        qt += [scatter(0, 1), scatter(1, 1), scatter(2, 0, "tp"), scatter(3, 0, "tp"), scatter(2, 1), scatter(3, 1), t_flux(2, "sb"), total(1, "mm"), t_flux(3), total(2, "tp"), fission(2)]
         qt += [scatter(0, 2), scatter(1, 2), scatter(4, 0, "sb"), scatter(2, 2), fission(3), scatter(3, 2), scatter(5, 0, "tp"), scatter(4, 1), scatter(5, 1), fission(4), fission(5), scatter(4, 2), total(3, "sb"), fission(6), fission(7)]
         qt += [scatter(3, 3), scatter(0, 3, "tp"), scatter(6, 0, "tp"), scatter(5, 2), scatter(7, 0, "sa"), scatter(6, 1), scatter(7, 1), scatter(1, 3, "tp"), scatter(2, 3, "sb"), scatter(6, 2), scatter(7, 2), total(4, "sa")]
         qt += [scatter_half(4, 3, 0), scatter_half(6, 3, 0), t_pad("f", 0, 2, "tp"), t_kern(0, "sb"), scatter_half(4, 3, H), emission(1, quarters[0], "mm"), t_kern(1), emission(1, quarters[1], "mm"), emission(0, quarters[0], "mm"), t_kern(2), total(5, "sa"), emission(0, quarters[1], "mm"), emission(0, quarters[2], "mm"), t_kern(3, "sb"), emission(0, quarters[3], "mm")]
-        qt += [total(6, "tp"), scatter_half(6, 3, H), t_kern(4), t_kern(5, "sa"), total(7, "sb"), open_unit(units[0], "mm"), close_unit(units[0]), open_unit(units[1], "mm"), close_unit(units[1]), emission(1, quarters[2], "mm"), t_kern(6), emission(1, quarters[3], "mm"), t_kern(7)]
+        qt += [total(6, "tp"), t_kern(4), t_kern(5, "sa"), total(7, "sb"), scatter_half(6, 3, H), open_unit(units[0], "mm"), close_unit(units[0]), open_unit(units[1], "mm"), close_unit(units[1]), emission(1, quarters[2], "mm"), t_kern(6), emission(1, quarters[3], "mm"), t_kern(7)]
         qt += [open_unit(units[2], "mm"), open_unit(units[3], "mm"), close_unit(units[2]), close_unit(units[3])]
         for k, ring in zip((4, 5, 6, 7), ("mm", "mm", "sa", "sb")):
             qt += [open_unit(units[k], ring), close_unit(units[k])]
 
-        qv = [weave_scat(0, 0, H, V), weave_scat(0, H, H, V), quant_scat(0, 0, H), quant_scat(0, H, H), quant_flux(0), weave_scat(1, 0, H, V), quant_flux(1), weave_scat(1, H, H, V)]
-        qv += [quant_scat(1, 0, H), quant_scat(1, H, H), weave_scat(2, 0, P, V), weave_scat(2, P, P, V), quant_scat(2, 0, P)]
+        qv = [weave_scat(0, 0, H, V), weave_scat(0, H, H, V), quant_scat(0, 0, H), quant_scat(0, H, H), weave_scat(1, 0, H, V), quant_flux(0), weave_scat(1, H, H, V)]
+        qv += [quant_scat(1, 0, H), quant_scat(1, H, H), weave_scat(2, 0, P, V), quant_flux(1), weave_scat(2, P, P, V), quant_scat(2, 0, P)]
         qv += [weigh_add(i, 1) for i in lo]
         qv += [quant_scat(2, P, P), quant_scat(2, H, H), weave_scat(3, 0, P, V), quant_flux(2), quant_scat(3, 0, P)] + [weigh_add(i, 2) for i in lo] + [weigh_add(4, 1), weigh_add(5, 1)]
         qv += [quant_scat(3, P, G - P), quant_flux(3), weigh_add(4, 2), f_weigh(), weigh_add(3, 3, 0, H), f_sum(), f_first(), weigh_add(3, 3, H, H), f_less_first(), f_second(), signed(0, 1, 0, H, eng=V), f_third()]
         qv += [weigh_add(5, 2), weigh_add(6, 1), weigh_add(7, 1), weigh_add(6, 2), weigh_add(7, 2)] + [weigh_half(i, 3, 0) for i in hi] + [weigh_half(i, 3, H) for i in hi[:2]]
         qv += [source(1, c) for c in quarters[:2]] + [source(0, c) for c in quarters]
-        qv += [quant_q(1, 0, H), quant_q(0, 0, H), quant_kern(0), quant_q(0, H, H), quant_kern(1)] + [weigh_half(i, 3, H) for i in hi[2:]]
+        qv += [quant_q(0, 0, H), quant_kern(0), quant_q(1, 0, H), quant_q(0, H, H), quant_kern(1)] + [weigh_half(i, 3, H) for i in hi[2:]]
         qv += [divide(units[0]), divide(units[1]), source(1, quarters[2]), source(1, quarters[3]), quant_kern(2), quant_q(1, H, H), signed(7, 1, H, H, eng=V), quant_kern(3)]
         qv += [divide(u) for u in units[2:]] + [quant_res(0, 0, G)]
         qv += [weave_res(1, H + P, V), quant_res(1, 0, H), quant_res(1, H, H)]
 
-        qs = [c_pad("dens", dens_t, 0, 2), c_flux(0), c_flux(1), c_nusf(), root(0), sign(0), weigh_first(0), weigh_first(1), weigh_first(2), weigh_first(3), square(0)]
+        qs = [c_pad("dens", dens_t, 0, 2), c_flux(0), c_nusf(), root(0), sign(0), c_flux(1), weigh_first(0), weigh_first(1), weigh_first(2), weigh_first(3), square(0)]
         qs += [c_flux(2), root(1), c_flux(3), sign(1), square(1), weigh_first(4), weigh_first(5), root(2), sign(2), square(2), root(3), sign(3), weigh_aside(0, 3), weigh_first(6), weigh_first(7), weigh_aside(1, 3), weigh_aside(2, 3), square(3), c_f()]
         qs += [root(4), sign(4), c_kern(0), square(4), c_kern(1), c_kern(2), root(5), sign(5), c_kern(3), square(5)] + inverse(6) + [c_kern(4), c_kern(5)] + inverse(7) + [c_kern(6), c_kern(7), weave_res(0, 0, S), weave_res(0, P, S)]
         qs += [weave_res(0, H, S), weave_res(0, H + P, S)] + [weave_res(1, c, S) for c in quarters[:3]] + [store_scales(1, S), store_scales(3, S)]

@@ -475,7 +475,7 @@ def tile_multigroupintegraltransportsourceiterati_x1_kernel(tc, flux, scat, dens
         SCAT_PIECES = [[("a", 0, G)], [("b", 0, G)], [("c", 0, P), ("a", P, P), ("c", H, H)], [("b", 0, P), ("b", P, G - P)]]
         INV_IN = [("rest", 1, 1, 0, G), ("kern1", 4, 2, 0, G), ("kern3", 6, 2, 0, H)]
 
-        qt = [warm_up(H, F32), warm_up(H, F32), t_pad("dens", 0, 2, "sa"), warm_up(H, F32), t_flux(0), total(0, "sb"), t_nusf(), warm_up(H, F32), fission(0, "sa"), t_flux(1), scatter(0, 0), scatter(1, 0), fission(1)]
+        qt = [warm_up(H, F32), warm_up(H, F32), t_pad("dens", 0, 2, "sa"), warm_up(P, F32), t_flux(0), total(0, "sb"), t_nusf(), warm_up(H, F32), fission(0, "sa"), t_flux(1), scatter(0, 0), scatter(1, 0), fission(1)]
         qt += [scatter(0, 1), scatter(1, 1), scatter(2, 0, "tp"), scatter(3, 0, "tp"), scatter(2, 1), scatter(3, 1), t_flux(2, "sb"), total(1, "mm"), t_flux(3), total(2, "tp"), fission(2)]
         qt += [scatter(0, 2), scatter(1, 2), scatter(4, 0, "sb"), scatter(2, 2), fission(3), scatter(3, 2), scatter(5, 0, "tp"), scatter(4, 1), scatter(5, 1), fission(4), fission(5), scatter(4, 2), total(3, "sb"), fission(6), fission(7)]
         qt += [scatter(3, 3), scatter(0, 3, "tp"), scatter(6, 0, "tp"), scatter(5, 2), scatter(7, 0, "sa"), scatter(6, 1), scatter(7, 1), scatter(1, 3, "tp"), scatter(2, 3, "sb"), scatter(6, 2), scatter(7, 2), total(4, "sa")]

@@ -19,6 +19,7 @@ NT = R // P
 H = G // 2
 NU_AT, CHI_AT = 8, 16
 PIECES = 3
+ASIDE = 3
 BANKS = {"mm": 4, "tp": 2, "sa": 1, "sb": 1}
 FLOPS = 2 * R * G * G * M + 2 * R * R * G
 
@@ -50,7 +51,7 @@ def tile_multigroupintegraltransportsourceiterati_x1_kernel(tc, flux, scat, dens
         id16 = tile("id16", [P, P], BF16)
         dens32 = tile("dens32", [P, NT, M], F32)
         dens_t = tile("dens_t", [P, 2, P], BF16)
-        y = tile("y", [P, 4, G], F32)
+        y = tile("y", [P, ASIDE, G], F32)
         f_t = tile("f_t", [P, 2, P], BF16)
         flux_grp = tiles("flux_grp", 4, [P, 2, P, 4], BF16)
         flux_codes = tile("flux_codes", [P, NT, P], U32)
@@ -71,7 +72,7 @@ def tile_multigroupintegraltransportsourceiterati_x1_kernel(tc, flux, scat, dens
         r_codes = tile("r_codes", [P, 2, G], U32)
         r_sc = tile("r_sc", [P, G], U8)
         warm = tile("warm", [P, 2], F32)
-        idle = tile("idle", [P, G], BF16)
+        idle = tile("idle", [P, H], F32)
 
         held = {}
 
@@ -137,14 +138,14 @@ def tile_multigroupintegraltransportsourceiterati_x1_kernel(tc, flux, scat, dens
         def apart(i, c0):
             return [k for k, (buffer, i0, ni, b0, bw) in enumerate(INV_IN) if i0 <= i < i0 + ni and b0 <= c0 < b0 + bw]
 
-        def t_pad(name, i0, n, ring):
-            alloc, needs = take(ring, (name, i0), [P, n, P], BF16)
+        def t_pad(name, pad, ring, after=()):
+            alloc, needs = take(ring, name, [P, 2, P], BF16)
 
             def run():
                 ps = alloc()
-                for i in range(n):
-                    T.transpose(ps[:, i], (f_pad if name == "f" else dens_pad)[:, i0 + i], id16[:])
-            return run, needs + (["pieces"] if name == "f" else []), [(name, i0)]
+                for g in range(2):
+                    T.transpose(ps[:, g], pad[:, g], id16[:])
+            return run, needs + list(after), [name]
 
         def t_flux(b, ring="tp"):
             alloc, needs = take(ring, ("flux", b), [P, 2, 2, P])
@@ -177,28 +178,14 @@ def tile_multigroupintegraltransportsourceiterati_x1_kernel(tc, flux, scat, dens
                     T.transpose(ps[:, u], rows[:].bitcast(F32)[:, u:H:2], id32[:])
             return run, needs, ["nusf"]
 
-        def warm_up(w, dtype=BF16):
+        def warm_up(w):
             alloc, needs = take("mm", ("warm", len(warmed)), [P, w])
             warmed.append(w)
-            return (lambda: T.matmul(alloc()[:], lhsT=idle[:].bitcast(dtype)[:, 0:P], rhs=idle[:].bitcast(dtype)[:, 0:w], start=True, stop=True)), needs, [("read", ("warm", len(warmed) - 1))]
-
-        def t_weave(m, c0, ring):
-            alloc, needs = take(ring, ("w", m, c0), [P, 2, G], BF16)
-
-            def run():
-                ps = alloc()
-                for a in range(2):
-                    T.matmul(ps[:, a], lhsT=id16[:], rhs=scat_raw[m][:, :, c0 + a * P:c0 + (a + 1) * P].rearrange("p j n -> p n j"), start=True, stop=True)
-            return run, needs, [("w", m, c0)]
-
-        def c_weave(m, c0):
-            def run():
-                S.copy(out=scat_grp(m, c0, H).rearrange("p n j -> p (n j)"), in_=bank["w", m, c0][:].rearrange("p a n -> p (a n)"))
-            return run, [("w", m, c0)], cols("scat_grp", m, c0, H) + [("read", ("w", m, c0))]
+            return (lambda: T.matmul(alloc()[:], lhsT=idle[:, 0:P], rhs=idle[:, 0:w], start=True, stop=True)), needs, [("read", ("warm", len(warmed) - 1))]
 
         def total(i, ring):
             alloc, needs = take(ring, ("st", i), [P, G])
-            return (lambda: T.matmul(alloc()[:], lhsT=dens_t[:, i // 4], rhs=slab[:, i % 4], start=True, stop=True)), needs + [("dens_t", i // 4)], [("st", i)]
+            return (lambda: T.matmul(alloc()[:], lhsT=dens_t[:, i // 4], rhs=slab[:, i % 4], start=True, stop=True)), needs + ["dens_t"], [("st", i)]
 
         def scatter(i, m, ring="mm"):
             alloc, needs = take(ring, ("a", i, m), [P, G])
@@ -218,14 +205,14 @@ def tile_multigroupintegraltransportsourceiterati_x1_kernel(tc, flux, scat, dens
                                 rhs=scat_codes[:, m, c0:c0 + H].bitcast(FP8X4), rhs_scale=scat_sc[:, m, c0:c0 + H], start=True, stop=True)
             return run, needs + [("flux_q", i0), ("flux_q", i0 + 1)] + cols("scat_q", m, c0, H), [("a", i0, m, c0)]
 
-        def fission(i, ring=None, j0=0, n=4):
+        def fission(i, ring=None):
             alloc, needs = take(ring, "p", [P, NT, M])
 
             def run():
-                ps = alloc() if i + j0 == 0 else bank["p"]
-                for j in range(j0, j0 + n):
+                ps = alloc() if i == 0 else bank["p"]
+                for j in range(4):
                     T.matmul(ps[:, i], lhsT=flux_grp[i // 2][:, i % 2, :, j], rhs=nusf_k[:, j // 2, :, j % 2], start=(j == 0), stop=(j == 3))
-            return run, (needs if i + j0 == 0 else []) + [("flux_grp", i // 2), "nusf_t"], ["p"] if (i, j0 + n) == (NT - 1, 4) else []
+            return run, (needs if i == 0 else []) + [("flux_grp", i // 2), "nusf_t"], ["p"] if i == NT - 1 else []
 
         def emission(g, c0, ring):
             alloc, needs = take(ring, ("e", g, c0), [P, 4, P])
@@ -248,32 +235,20 @@ def tile_multigroupintegraltransportsourceiterati_x1_kernel(tc, flux, scat, dens
             g, t0, n, c0, w = unit
             return (lambda: transport_pass(bank["c", unit], unit, 1)), [("open", unit)] + cols("q_q", 1, c0, w), [("c", unit)]
 
-        def c_pad(name, dst, i0, n):
-            return (lambda: S.copy(out=dst[:, i0:i0 + n], in_=bank[name, i0][:])), [(name, i0)], [(name + "_t", i) for i in range(i0, i0 + n)] + [("read", (name, i0))]
-
-        def load_chi(t):
-            return (lambda: SP.dma_start(out=slab[CHI_AT + 4 * t:CHI_AT + 4 * t + 4, t], in_=chi.partition_broadcast(4))), [("st", t)], [("chi", t)]
-
-        def c_f():
-            return (lambda: S.copy(out=f_t[:], in_=bank["f", 0][:])), [("f", 0)], ["f_t", ("read", ("f", 0))]
+        def c_pad(name, dst):
+            return (lambda: S.copy(out=dst[:], in_=bank[name][:])), [name], [name + "_t", ("read", name)]
 
         def c_nusf():
             return (lambda: S.copy(out=nusf_t[:], in_=bank["nusf"][:, :, NU_AT:NU_AT + M])), ["nusf"], ["nusf_t", ("read", "nusf")]
 
-        def words_out(eng, dst, src):
-            if eng is S:
-                S.copy(out=dst, in_=src)
-            else:
-                V.tensor_copy(out=dst, in_=src)
-
-        def c_flux(b, eng=S):
+        def c_flux(b):
             dst = flux_grp[b][:].rearrange("p a r f -> p a (r f)").bitcast(F32).rearrange("p a (r u) -> p a r u", u=2)
-            return (lambda: words_out(eng, dst, bank["flux", b][:].rearrange("p a u r -> p a r u"))), [("flux", b)], [("flux_grp", b), ("read", ("flux", b))]
+            return (lambda: S.copy(out=dst, in_=bank["flux", b][:].rearrange("p a u r -> p a r u"))), [("flux", b)], [("flux_grp", b), ("read", ("flux", b))]
 
-        def c_kern(i, eng=S):
+        def c_kern(i):
             def run():
                 dst = kern_grp(i // 2)[:, i % 2].rearrange("p k r f -> p k (r f)").bitcast(F32).rearrange("p k (r u) -> p k r u", u=2)
-                words_out(eng, dst, bank["kern", i][:].rearrange("p k u r -> p k r u"))
+                S.copy(out=dst, in_=bank["kern", i][:].rearrange("p k u r -> p k r u"))
             return run, [("kern", i)], [("kern_grp", i), ("read", ("kern", i))]
 
         def weigh_first(i):
@@ -406,6 +381,10 @@ def tile_multigroupintegraltransportsourceiterati_x1_kernel(tc, flux, scat, dens
             needs = [k for i in range(i0, i0 + n) for k in cols("inv", i, c0, w)]
             return run, [("c", unit)] + needs, [k for t in range(t0, t0 + n) for k in cols(("res", t), g, c0, w)] + [("read", ("c", unit))]
 
+        def load_chi(t):
+            at = CHI_AT + 4 * t
+            return (lambda: SP.dma_start(out=slab[at:at + PIECES, t], in_=chi.partition_broadcast(PIECES))), [("st", t)], [("chi", t)]
+
         def store(unit):
             g, t0, n, c0, w = unit
             needs = [k for t in range(t0, t0 + n) for k in cols(("res", t), g, c0, w)]
@@ -475,11 +454,11 @@ def tile_multigroupintegraltransportsourceiterati_x1_kernel(tc, flux, scat, dens
         SCAT_PIECES = [[("a", 0, G)], [("b", 0, G)], [("c", 0, P), ("a", P, P), ("c", H, H)], [("b", 0, P), ("b", P, G - P)]]
         INV_IN = [("rest", 1, 1, 0, G), ("kern1", 4, 2, 0, G), ("kern3", 6, 2, 0, H)]
 
-        qt = [warm_up(H, F32), warm_up(H, F32), t_pad("dens", 0, 2, "sa"), warm_up(P, F32), t_flux(0), total(0, "sb"), t_nusf(), warm_up(H, F32), fission(0, "sa"), t_flux(1), scatter(0, 0), scatter(1, 0), fission(1)]
+        qt = [warm_up(H), warm_up(H), t_pad("dens", dens_pad, "sa"), warm_up(P), t_flux(0), total(0, "sb"), t_nusf(), warm_up(H), fission(0, "sa"), t_flux(1), scatter(0, 0), scatter(1, 0), fission(1)]
         qt += [scatter(0, 1), scatter(1, 1), scatter(2, 0, "tp"), scatter(3, 0, "tp"), scatter(2, 1), scatter(3, 1), t_flux(2, "sb"), total(1, "mm"), t_flux(3), total(2, "tp"), fission(2)]
         qt += [scatter(0, 2), scatter(1, 2), scatter(4, 0, "sb"), scatter(2, 2), fission(3), scatter(3, 2), scatter(5, 0, "tp"), scatter(4, 1), scatter(5, 1), fission(4), fission(5), scatter(4, 2), total(3, "sb"), fission(6), fission(7)]
         qt += [scatter(3, 3), scatter(0, 3, "tp"), scatter(6, 0, "tp"), scatter(5, 2), scatter(7, 0, "sa"), scatter(6, 1), scatter(7, 1), scatter(1, 3, "tp"), scatter(2, 3, "sb"), scatter(6, 2), scatter(7, 2), total(4, "sa")]
-        qt += [scatter_half(4, 3, 0), scatter_half(6, 3, 0), t_pad("f", 0, 2, "tp"), t_kern(0, "sb"), scatter_half(4, 3, H), emission(1, quarters[0], "mm"), t_kern(1), emission(1, quarters[1], "mm"), emission(0, quarters[0], "mm"), t_kern(2), total(5, "sa"), emission(0, quarters[1], "mm"), emission(0, quarters[2], "mm"), t_kern(3, "sb"), emission(0, quarters[3], "mm")]
+        qt += [scatter_half(4, 3, 0), scatter_half(6, 3, 0), t_pad("f", f_pad, "tp", ["pieces"]), t_kern(0, "sb"), scatter_half(4, 3, H), emission(1, quarters[0], "mm"), t_kern(1), emission(1, quarters[1], "mm"), emission(0, quarters[0], "mm"), t_kern(2), total(5, "sa"), emission(0, quarters[1], "mm"), emission(0, quarters[2], "mm"), t_kern(3, "sb"), emission(0, quarters[3], "mm")]
         qt += [total(6, "tp"), t_kern(4), t_kern(5, "sa"), total(7, "sb"), scatter_half(6, 3, H), open_unit(units[0], "mm"), close_unit(units[0]), open_unit(units[1], "mm"), close_unit(units[1]), emission(1, quarters[2], "mm"), t_kern(6), emission(1, quarters[3], "mm"), t_kern(7)]
         qt += [open_unit(units[2], "mm"), open_unit(units[3], "mm"), close_unit(units[2]), close_unit(units[3])]
         for k, ring in zip((4, 5, 6, 7), ("mm", "mm", "sa", "sb")):
@@ -497,8 +476,8 @@ def tile_multigroupintegraltransportsourceiterati_x1_kernel(tc, flux, scat, dens
         qv += [divide(u) for u in units[2:]] + [quant_res(0, 0, G)]
         qv += [weave_res(1, H + P, V), quant_res(1, 0, H), quant_res(1, H, H)]
 
-        qs = [c_pad("dens", dens_t, 0, 2), c_flux(0), c_nusf(), root(0), sign(0), c_flux(1), weigh_first(0), weigh_first(1), weigh_first(2), weigh_first(3), square(0)]
-        qs += [c_flux(2), root(1), c_flux(3), sign(1), square(1), weigh_first(4), weigh_first(5), root(2), sign(2), square(2), root(3), sign(3), weigh_aside(0, 3), weigh_first(6), weigh_first(7), weigh_aside(1, 3), weigh_aside(2, 3), square(3), c_f()]
+        qs = [c_pad("dens", dens_t), c_flux(0), c_nusf(), root(0), sign(0), c_flux(1), weigh_first(0), weigh_first(1), weigh_first(2), weigh_first(3), square(0)]
+        qs += [c_flux(2), root(1), c_flux(3), sign(1), square(1), weigh_first(4), weigh_first(5), root(2), sign(2), square(2), root(3), sign(3), weigh_aside(0, 3), weigh_first(6), weigh_first(7), weigh_aside(1, 3), weigh_aside(2, 3), square(3), c_pad("f", f_t)]
         qs += [root(4), sign(4), c_kern(0), square(4), c_kern(1), c_kern(2), root(5), sign(5), c_kern(3), square(5)] + inverse(6) + [c_kern(4), c_kern(5)] + inverse(7) + [c_kern(6), c_kern(7), weave_res(0, 0, S), weave_res(0, P, S)]
         qs += [weave_res(0, H, S), weave_res(0, H + P, S)] + [weave_res(1, c, S) for c in quarters[:3]] + [store_scales(1, S), store_scales(3, S)]
 

@@ -458,8 +458,8 @@ def tile_multigroupintegraltransportsourceiterati_x1_kernel(tc, flux, scat, dens
         qt += [scatter(0, 1), scatter(1, 1), scatter(2, 0, "tp"), scatter(3, 0, "tp"), scatter(2, 1), scatter(3, 1), t_flux(2, "sb"), total(1, "mm"), t_flux(3), total(2, "tp"), fission(2)]
         qt += [scatter(0, 2), scatter(1, 2), scatter(4, 0, "sb"), scatter(2, 2), fission(3), scatter(3, 2), scatter(5, 0, "tp"), scatter(4, 1), scatter(5, 1), fission(4), fission(5), scatter(4, 2), total(3, "sb"), fission(6), fission(7)]
         qt += [scatter(3, 3), scatter(0, 3, "tp"), scatter(6, 0, "tp"), scatter(5, 2), scatter(7, 0, "sa"), scatter(6, 1), scatter(7, 1), scatter(1, 3, "tp"), scatter(2, 3, "sb"), scatter(6, 2), scatter(7, 2), total(4, "sa")]
-        qt += [scatter_half(4, 3, 0), scatter_half(6, 3, 0), t_pad("f", f_pad, "tp", ["pieces"]), t_kern(0, "sb"), scatter_half(4, 3, H), emission(1, quarters[0], "mm"), t_kern(1), emission(1, quarters[1], "mm"), emission(0, quarters[0], "mm"), t_kern(2), total(5, "sa"), emission(0, quarters[1], "mm"), emission(0, quarters[2], "mm"), t_kern(3, "sb"), emission(0, quarters[3], "mm")]
-        qt += [total(6, "tp"), t_kern(4), t_kern(5, "sa"), total(7, "sb"), scatter_half(6, 3, H), open_unit(units[0], "mm"), close_unit(units[0]), open_unit(units[1], "mm"), close_unit(units[1]), emission(1, quarters[2], "mm"), t_kern(6), emission(1, quarters[3], "mm"), t_kern(7)]
+        qt += [scatter_half(4, 3, 0), t_pad("f", f_pad, "tp", ["pieces"]), scatter_half(6, 3, 0), t_kern(0, "sb"), scatter_half(4, 3, H), emission(1, quarters[0], "mm"), t_kern(1), emission(1, quarters[1], "mm"), emission(0, quarters[0], "mm"), t_kern(2), total(5, "sa"), emission(0, quarters[1], "mm"), emission(0, quarters[2], "mm"), t_kern(3, "sb"), emission(0, quarters[3], "mm")]
+        qt += [total(6, "tp"), t_kern(4), t_kern(5, "sa"), total(7, "sb"), scatter_half(6, 3, H), open_unit(units[0], "mm"), close_unit(units[0]), emission(1, quarters[2], "mm"), emission(1, quarters[3], "mm"), t_kern(6), open_unit(units[1], "mm"), close_unit(units[1]), t_kern(7)]
         qt += [open_unit(units[2], "mm"), open_unit(units[3], "mm"), close_unit(units[2]), close_unit(units[3])]
         for k, ring in zip((4, 5, 6, 7), ("mm", "mm", "sa", "sb")):
             qt += [open_unit(units[k], ring), close_unit(units[k])]
@@ -472,17 +472,17 @@ def tile_multigroupintegraltransportsourceiterati_x1_kernel(tc, flux, scat, dens
         qv += [weigh_add(5, 2), weigh_add(6, 1), weigh_add(7, 1), weigh_add(6, 2), weigh_add(7, 2)] + [weigh_half(i, 3, 0) for i in hi] + [weigh_half(i, 3, H) for i in hi[:2]]
         qv += [source(1, c) for c in quarters[:2]] + [source(0, c) for c in quarters]
         qv += [quant_q(0, 0, H), quant_kern(0), quant_q(1, 0, H), quant_q(0, H, H), quant_kern(1)] + [weigh_half(i, 3, H) for i in hi[2:]]
-        qv += [divide(units[0]), divide(units[1]), source(1, quarters[2]), source(1, quarters[3]), quant_kern(2), quant_q(1, H, H), signed(7, 1, H, H, eng=V), quant_kern(3)]
+        qv += [divide(units[0]), source(1, quarters[2]), source(1, quarters[3]), divide(units[1]), quant_q(1, H, H), quant_kern(2), quant_kern(3)]
         qv += [divide(u) for u in units[2:]] + [quant_res(0, 0, G)]
         qv += [weave_res(1, H + P, V), quant_res(1, 0, H), quant_res(1, H, H)]
 
         qs = [c_pad("dens", dens_t), c_flux(0), c_nusf(), root(0), sign(0), c_flux(1), weigh_first(0), weigh_first(1), weigh_first(2), weigh_first(3), square(0)]
         qs += [c_flux(2), root(1), c_flux(3), sign(1), square(1), weigh_first(4), weigh_first(5), root(2), sign(2), square(2), root(3), sign(3), weigh_aside(0, 3), weigh_first(6), weigh_first(7), weigh_aside(1, 3), weigh_aside(2, 3), square(3), c_pad("f", f_t)]
-        qs += [root(4), sign(4), c_kern(0), square(4), c_kern(1), c_kern(2), root(5), sign(5), c_kern(3), square(5)] + inverse(6) + [c_kern(4), c_kern(5)] + inverse(7) + [c_kern(6), c_kern(7), weave_res(0, 0, S), weave_res(0, P, S)]
+        qs += [root(4), sign(4), c_kern(0), square(4), c_kern(1), c_kern(2), root(5), sign(5), c_kern(3), square(5)] + inverse(6) + [c_kern(4), c_kern(5), root(7), sign(7), c_kern(6), c_kern(7), square(7), weave_res(0, 0, S), weave_res(0, P, S)]
         qs += [weave_res(0, H, S), weave_res(0, H + P, S)] + [weave_res(1, c, S) for c in quarters[:3]] + [store_scales(1, S), store_scales(3, S)]
 
         qg = [weave_scat(2, H, H, GP, cols("scat_q", 2, 0, P)), weave_scat(3, P, G - P, GP, cols("scat_q", 3, 0, P)), signed(0, 1, H, H), signed(1, after=["pieces"]), join(0, 1, 3), join(1, 2, 3), signed(2, 2)]
-        qg += [signed(4, 2, after=[("kern_q", 1)]), signed(6, 2, 0, H, after=[("kern_q", 3)]), signed(6, 1, H, H)]
+        qg += [signed(4, 2, after=[("kern_q", 1)]), signed(6, 2, 0, H, after=[("kern_q", 3)]), signed(6, 2, H, H)]
 
         qy = [load_chi(t) for t in range(4)] + [store(u) for u in units] + [store_codes(0, 0, G), store_codes(1, 0, H), store_codes(1, H, H)]
         qy += [store_scales(0, SP), store_scales(2, SP)]

from contextlib import ExitStack

import concourse.mybir as mybir
from concourse.masks import make_identity

F32 = mybir.dt.float32
BF16 = mybir.dt.bfloat16
U32 = mybir.dt.uint32
I32 = mybir.dt.int32
U8 = mybir.dt.uint8
FP8X4 = mybir.dt.float8_e4m3fn_x4
ALU = mybir.AluOpType
ACT = mybir.ActivationFunctionType
AX = mybir.AxisListType

P = 128
R, G, M = 1024, 512, 4
NT = R // P
H = G // 2
NU_AT, CHI_AT = 8, 16
PIECES = 3
ASIDE = 3
BANKS = {"mm": 4, "tp": 2, "sa": 1, "sb": 1}
FLOPS = 2 * R * G * G * M + 2 * R * R * G


def tile_multigroupintegraltransportsourceiterati_x1_kernel(tc, flux, scat, dens, nusf, chi, kern, sigt, out_0, out_1, out_2):
    nc = tc.nc
    V, S, T, GP, SP = nc.vector, nc.scalar, nc.tensor, nc.gpsimd, nc.sync
    with ExitStack() as ctx:
        keep = ctx.enter_context(tc.tile_pool(name="keep", bufs=1))
        psum = ctx.enter_context(tc.psum_pool(name="psum", bufs=1))
        ctx.enter_context(tc.manual_schedule())

        def tile(name, shape, dtype):
            return keep.tile(shape, dtype, align_bytes=64, name=name)

        def tiles(name, n, shape, dtype):
            return [tile("%s%d" % (name, k), shape, dtype) for k in range(n)]

        rows = tile("rows", [P, G], BF16)
        slab = tile("slab", [P, 4, G], BF16)
        f_pad = tile("f_pad", [P, 2, P], BF16)
        dens_pad = tile("dens_pad", [P, 2, P], BF16)
        dens_sb = tile("dens_sb", [P, 2, 4 * M], BF16)
        nusf_t = tile("nusf_t", [P, 2, M], F32)
        flux_raw = tiles("flux_raw", 4, [P, 2, G], BF16)
        scat_raw = tiles("scat_raw", M, [P, 4, G], BF16)
        kern_raw = tiles("kern_raw", 2, [P, 4, R], BF16)
        id32 = tile("id32", [P, P], F32)
        id16 = tile("id16", [P, P], BF16)
        dens32 = tile("dens32", [P, NT, M], F32)
        dens_t = tile("dens_t", [P, 2, P], BF16)
        y = tile("y", [P, ASIDE, G], F32)
        f_t = tile("f_t", [P, 2, P], BF16)
        flux_grp = tiles("flux_grp", 4, [P, 2, P, 4], BF16)
        flux_codes = tile("flux_codes", [P, NT, P], U32)
        flux_sc = tile("flux_sc", [P, NT, P], U8)
        scat_codes = tile("scat_codes", [P, M, G], U32)
        scat_sc = tile("scat_sc", [P, M, G], U8)
        pd = tile("pd", [P, NT, M], F32)
        f = tile("f", [P, NT], F32)
        x = tiles("x", 2, [P, 4, G], F32)
        sg = tile("sg", [P, NT, G], BF16)
        rst = tile("rst", [P, NT, G], F32)
        kern_codes = tile("kern_codes", [P, NT, 2, P], U32)
        kern_sc = tile("kern_sc", [P, NT, 2, P], U8)
        q_codes = tile("q_codes", [P, 2, G], U32)
        q_sc = tile("q_sc", [P, 2, G], U8)
        res = tiles("res", 2, [P, 4, G], F32)
        r_grp = tile("r_grp", [P, 2, G, 4], BF16)
        r_codes = tile("r_codes", [P, 2, G], U32)
        r_sc = tile("r_sc", [P, G], U8)
        warm = tile("warm", [P, 2], F32)
        idle = tile("idle", [P, H], F32)

        held = {}

        def tenant(buffer, name, shape, dtype):
            if name not in held:
                held[name] = keep.tile(shape, dtype, align_bytes=64, name=name, tag=buffer)
            return held[name]

        dens_v = dens_sb[:].rearrange("p g (t m) -> p (g t) m", m=M)
        nusf_k = nusf_t[:].bitcast(BF16).rearrange("p u (m e) -> p u m e", e=2)
        flux_v = flux.rearrange("(g p t) k -> g p t k", g=2, t=4)
        kern_v = kern.rearrange("(g p t) k -> g p t k", g=2, t=4)
        out0_v = out_0.rearrange("(g p t) n -> g p t n", g=2, t=4)
        out1_v = out_1.rearrange("g p n t -> g p (n t)").bitcast(I32)
        out2_v = out_2.bitcast(I32)

        bank = {}
        warmed = []

        def take(ring, key, shape, dtype=F32):
            def alloc():
                bank[key] = psum.tile(shape, dtype, tag=ring, bufs=BANKS[ring], name=ring)
                return bank[key]
            return alloc, [("bank", ring, key)]

        def cols(name, g, c0, w):
            return [(name, g, c) for c in range(c0, c0 + w, P)]

        def blocks(dst, src):
            return dst.rearrange("p (c i) t -> p c t i", i=4), src.rearrange("p t (c i) -> p c t i", i=4)

        def weave(eng, dst, src):
            if eng is GP:
                GP.tensor_scalar(out=dst, in0=src.rearrange("p t n -> p n t"), scalar1=1.0, scalar2=0.0, op0=ALU.mult, op1=ALU.add)
            elif eng is S:
                out, in_ = blocks(dst, src)
                S.copy(out=out, in_=in_)
            else:
                out, in_ = blocks(dst, src)
                V.tensor_copy(out=out, in_=in_)

        def scat_grp(m, c0, w):
            for buffer, b0, bw in SCAT_PIECES[m]:
                if b0 <= c0 and c0 + w <= b0 + bw:
                    return tenant(buffer, "scat_grp%d_%d" % (m, b0), [P, bw, 4], BF16)[:, c0 - b0:c0 - b0 + w]

        def kern_grp(h):
            return tenant("kern%d" % h, "kern_grp%d" % h, [P, 2, 2, P, 4], BF16)

        def f_rest():
            return tenant("rest", "f_rest", [P, 2, 4], F32)[:]

        def q_grp(g, c0, w):
            h0 = c0 - c0 % H
            return tenant("q%d_%d" % (g, h0), "q_grp%d_%d" % (g, h0), [P, H, 4], BF16)[:, c0 - h0:c0 - h0 + w]

        def inv(i, n, c0, w):
            for buffer, i0, ni, b0, bw in INV_IN:
                if i0 <= i and i + n <= i0 + ni and b0 <= c0 and c0 + w <= b0 + bw:
                    return tenant(buffer, "inv%d_%d" % (i0, b0), [P, ni, bw], F32)[:, i - i0:i - i0 + n, c0 - b0:c0 - b0 + w]
            return rst[:, i:i + n, c0:c0 + w]

        def apart(i, c0):
            return [k for k, (buffer, i0, ni, b0, bw) in enumerate(INV_IN) if i0 <= i < i0 + ni and b0 <= c0 < b0 + bw]

        def t_pad(name, pad, ring, after=()):
            alloc, needs = take(ring, name, [P, 2, P], BF16)

            def run():
                ps = alloc()
                for g in range(2):
                    T.transpose(ps[:, g], pad[:, g], id16[:])
            return run, needs + list(after), [name]

        def t_flux(b, ring="tp"):
            alloc, needs = take(ring, ("flux", b), [P, 2, 2, P])

            def run():
                ps = alloc()
                for a in range(2):
                    words = flux_raw[b][:, a].bitcast(F32)
                    for u in range(2):
                        T.transpose(ps[:, a, u], words[:, u:H:2], id32[:])
            return run, needs, [("flux", b)]

        def t_kern(i, ring="tp"):
            alloc, needs = take(ring, ("kern", i), [P, 2, 2, P])

            def run():
                ps = alloc()
                words = kern_raw[i // 4][:, i % 4].bitcast(F32)
                for ks in range(2):
                    for u in range(2):
                        T.transpose(ps[:, ks, u], words[:, H * ks + u:H * ks + H:2], id32[:])
            return run, needs, [("kern", i)]

        def t_nusf():
            alloc, needs = take("mm", "nusf", [P, 2, P])

            def run():
                ps = alloc()
                for u in range(2):
                    T.transpose(ps[:, u], rows[:].bitcast(F32)[:, u:H:2], id32[:])
            return run, needs, ["nusf"]

        def warm_up(w):
            alloc, needs = take("mm", ("warm", len(warmed)), [P, w])
            warmed.append(w)
            return (lambda: T.matmul(alloc()[:], lhsT=idle[:, 0:P], rhs=idle[:, 0:w], start=True, stop=True)), needs, [("read", ("warm", len(warmed) - 1))]

        def total(i, ring):
            alloc, needs = take(ring, ("st", i), [P, G])
            return (lambda: T.matmul(alloc()[:], lhsT=dens_t[:, i // 4], rhs=slab[:, i % 4], start=True, stop=True)), needs + ["dens_t"], [("st", i)]

        def scatter(i, m, ring="mm"):
            alloc, needs = take(ring, ("a", i, m), [P, G])

            def run():
                T.matmul_mx(out=alloc()[:], lhsT=flux_codes[:, i].bitcast(FP8X4), lhsT_scale=flux_sc[:, i],
                            rhs=scat_codes[:, m].bitcast(FP8X4), rhs_scale=scat_sc[:, m], start=True, stop=True)
            return run, needs + [("flux_q", i)] + cols("scat_q", m, 0, G), [("a", i, m)]

        def scatter_half(i0, m, c0):
            alloc, needs = take("mm", ("a", i0, m, c0), [P, 2, H])

            def run():
                ps = alloc()
                for a in range(2):
                    T.matmul_mx(out=ps[:, a], lhsT=flux_codes[:, i0 + a].bitcast(FP8X4), lhsT_scale=flux_sc[:, i0 + a],
                                rhs=scat_codes[:, m, c0:c0 + H].bitcast(FP8X4), rhs_scale=scat_sc[:, m, c0:c0 + H], start=True, stop=True)
            return run, needs + [("flux_q", i0), ("flux_q", i0 + 1)] + cols("scat_q", m, c0, H), [("a", i0, m, c0)]

        def fission(i, ring=None):
            alloc, needs = take(ring, "p", [P, NT, M])

            def run():
                ps = alloc() if i == 0 else bank["p"]
                for j in range(4):
                    T.matmul(ps[:, i], lhsT=flux_grp[i // 2][:, i % 2, :, j], rhs=nusf_k[:, j // 2, :, j % 2], start=(j == 0), stop=(j == 3))
            return run, (needs if i == 0 else []) + [("flux_grp", i // 2), "nusf_t"], ["p"] if i == NT - 1 else []

        def emission(g, c0, ring):
            alloc, needs = take(ring, ("e", g, c0), [P, 4, P])
            return (lambda: T.matmul(alloc()[:], lhsT=f_t[:, g], rhs=slab[:, :, c0:c0 + P], start=True, stop=True)), needs + ["f_t"] + [("chi", t) for t in range(4)], [("e", g, c0)]

        def transport_pass(ps, unit, gs):
            g, t0, n, c0, w = unit
            for a in range(n):
                t = t0 + a
                T.matmul_mx(out=ps[:, a], lhsT=kern_codes[:, 4 * g + t, gs].bitcast(FP8X4), lhsT_scale=kern_sc[:, 4 * g + t, gs],
                            rhs=q_codes[:, gs, c0:c0 + w].bitcast(FP8X4), rhs_scale=q_sc[:, gs, c0:c0 + w],
                            start=(gs == 0 and a == 0), stop=(gs == 1 and a == n - 1))

        def open_unit(unit, ring):
            g, t0, n, c0, w = unit
            alloc, needs = take(ring, ("c", unit), [P, n, w])
            return (lambda: transport_pass(alloc(), unit, 0)), needs + [("kern_q", i // 2) for i in range(4 * g + t0, 4 * g + t0 + n)] + cols("q_q", 0, c0, w), [("open", unit)]

        def close_unit(unit):
            g, t0, n, c0, w = unit
            return (lambda: transport_pass(bank["c", unit], unit, 1)), [("open", unit)] + cols("q_q", 1, c0, w), [("c", unit)]

        def c_pad(name, dst):
            return (lambda: S.copy(out=dst[:], in_=bank[name][:])), [name], [name + "_t", ("read", name)]

        def c_nusf():
            return (lambda: S.copy(out=nusf_t[:], in_=bank["nusf"][:, :, NU_AT:NU_AT + M])), ["nusf"], ["nusf_t", ("read", "nusf")]

        def c_flux(b):
            dst = flux_grp[b][:].rearrange("p a r f -> p a (r f)").bitcast(F32).rearrange("p a (r u) -> p a r u", u=2)
            return (lambda: S.copy(out=dst, in_=bank["flux", b][:].rearrange("p a u r -> p a r u"))), [("flux", b)], [("flux_grp", b), ("read", ("flux", b))]

        def c_kern(i):
            def run():
                dst = kern_grp(i // 2)[:, i % 2].rearrange("p k r f -> p k (r f)").bitcast(F32).rearrange("p k (r u) -> p k r u", u=2)
                S.copy(out=dst, in_=bank["kern", i][:].rearrange("p k u r -> p k r u"))
            return run, [("kern", i)], [("kern_grp", i), ("read", ("kern", i))]

        def weigh_first(i):
            def run():
                S.activation(out=x[i // 4][:, i % 4], in_=bank["a", i, 0][:], func=ACT.Copy, scale=dens32[:, i, 0:1])
            return run, [("a", i, 0)], [("x", i, 0), ("read", ("a", i, 0))]

        def weigh_aside(i, m):
            def run():
                S.activation(out=y[:, i], in_=bank["a", i, m][:], func=ACT.Copy, scale=dens32[:, i, m:m + 1])
            return run, [("a", i, m)], [("y", i), ("read", ("a", i, m))]

        def root(i):
            return (lambda: S.activation(out=rst[:, i], in_=bank["st", i][:], func=ACT.Abs_reciprocal_sqrt)), [("st", i)], [("root", i)]

        def sign(i):
            return (lambda: S.activation(out=sg[:, i], in_=bank["st", i][:], func=ACT.Sign)), [("root", i)], [("sign", i), ("read", ("st", i))]

        def square(i):
            r = rst[:, i]
            return (lambda: S.activation(out=r, in_=r, func=ACT.Square)), [("root", i)], [("size", i)]

        def inverse(i):
            return [root(i), sign(i), square(i)]

        def signed(i, n=1, c0=0, w=G, after=(), eng=GP):
            def run():
                eng.tensor_tensor(out=inv(i, n, c0, w), in0=rst[:, i:i + n, c0:c0 + w], in1=sg[:, i:i + n, c0:c0 + w], op=ALU.mult)
            return run, [(k, j) for k in ("size", "sign") for j in range(i, i + n)] + list(after), [k for j in range(i, i + n) for k in cols("inv", j, c0, w)]

        def join(i, n, m):
            def run():
                GP.tensor_tensor(out=x[0][:, i:i + n], in0=x[0][:, i:i + n], in1=y[:, i:i + n], op=ALU.add)
            return run, [k for j in range(i, i + n) for k in (("y", j), ("x", j, m - 1))], [("x", j, m) for j in range(i, i + n)]

        def weave_scat(m, c0, w, eng, after=()):
            return (lambda: weave(eng, scat_grp(m, c0, w), scat_raw[m][:, :, c0:c0 + w])), list(after), cols("scat_grp", m, c0, w)

        def weave_res(g, c0, eng):
            needs = [k for t in range(4) for k in cols(("res", t), g, c0, P)]
            return (lambda: weave(eng, r_grp[:, g, c0:c0 + P], res[g][:, :, c0:c0 + P])), needs, cols("r_grp", g, c0, P)

        def quant_scat(m, c0, w):
            def run():
                V.quantize_mx(out=scat_codes[:, m, c0:c0 + w].bitcast(FP8X4), scales=scat_sc[:, m, c0:c0 + w], in_=scat_grp(m, c0, w).rearrange("p n j -> p (n j)"))
            return run, cols("scat_grp", m, c0, w), cols("scat_q", m, c0, w)

        def quant_flux(b):
            i0, n = 2 * b, 2

            def run():
                V.quantize_mx(out=flux_codes[:, i0:i0 + n].rearrange("p a r -> p (a r)").bitcast(FP8X4),
                              scales=flux_sc[:, i0:i0 + n].rearrange("p a r -> p (a r)"),
                              in_=flux_grp[b][:].rearrange("p a r f -> p (a r f)"))
            return run, [("flux_grp", i // 2) for i in range(i0, i0 + n)], [("flux_q", i) for i in range(i0, i0 + n)]

        def quant_kern(h):
            def run():
                V.quantize_mx(out=kern_codes[:, 2 * h:2 * h + 2].rearrange("p t k r -> p (t k r)").bitcast(FP8X4),
                              scales=kern_sc[:, 2 * h:2 * h + 2].rearrange("p t k r -> p (t k r)"),
                              in_=kern_grp(h)[:].rearrange("p t k r f -> p (t k r f)"))
            return run, [("kern_grp", 2 * h), ("kern_grp", 2 * h + 1)], [("kern_q", h)]

        def quant_q(g, c0, w):
            def run():
                V.quantize_mx(out=q_codes[:, g, c0:c0 + w].bitcast(FP8X4), scales=q_sc[:, g, c0:c0 + w],
                              in_=q_grp(g, c0, w).rearrange("p n t -> p (n t)"))
            return run, cols("q_grp", g, c0, w), cols("q_q", g, c0, w)

        def quant_res(g, c0, w):
            def run():
                V.quantize_mx(out=r_codes[:, g, c0:c0 + w].bitcast(FP8X4), scales=r_sc[4 * g:P, c0:c0 + w],
                              in_=r_grp[:, g, c0:c0 + w].rearrange("p n t -> p (n t)"))
            return run, cols("r_grp", g, c0, w), cols("r_q", g, c0, w)

        def weigh_add(i, m, c0=0, w=G):
            xi = x[i // 4][:, i % 4, c0:c0 + w]

            def run():
                V.scalar_tensor_tensor(out=xi, in0=bank["a", i, m][:, c0:c0 + w], scalar=dens32[:, i, m:m + 1], in1=xi, op0=ALU.mult, op1=ALU.add)
            return run, [("a", i, m), ("x", i, m - 1)], [("x", i, m), ("read", ("a", i, m))] if c0 + w == G else []

        def weigh_half(i, m, c0):
            xi = x[i // 4][:, i % 4, c0:c0 + H]
            key = ("a", i - i % 2, m, c0)

            def run():
                V.scalar_tensor_tensor(out=xi, in0=bank[key][:, i % 2], scalar=dens32[:, i, m:m + 1], in1=xi, op0=ALU.mult, op1=ALU.add)
            return run, [key, ("x", i, m - 1)], [("x", i, m, c0)] + ([("read", key)] if i % 2 else [])

        def f_weigh():
            return (lambda: V.tensor_tensor(out=pd[:], in0=bank["p"][:], in1=dens32[:], op=ALU.mult)), ["p"], ["pd", ("read", "p")]

        def f_sum():
            return (lambda: V.tensor_reduce(out=f[:], in_=pd[:], axis=AX.X, op=ALU.add)), ["pd"], ["fsum"]

        def piece(k):
            return f_pad[:, :, CHI_AT + k:CHI_AT + 16:4]

        def f_first():
            def run():
                with nc.allow_low_precision(reason="the first bf16 piece of f; the later pieces carry the rest"):
                    V.tensor_reduce(out=piece(0), in_=pd[:].rearrange("p (g t) m -> p g t m", g=2), axis=AX.X, op=ALU.add)
            return run, ["pd"], ["first"]

        def f_less_first():
            return (lambda: V.tensor_tensor(out=f_rest(), in0=f[:].rearrange("p (g t) -> p g t", g=2), in1=piece(0), op=ALU.subtract)), ["fsum", "first"], ["rest"]

        def f_second():
            return (lambda: V.tensor_tensor(out=piece(1), in0=f[:].rearrange("p (g t) -> p g t", g=2), in1=piece(0), op=ALU.subtract)), ["fsum", "first"], ["second"]

        def f_third():
            return (lambda: V.tensor_tensor(out=piece(2), in0=f_rest(), in1=piece(1), op=ALU.subtract)), ["rest", "second"], ["pieces"]

        def source(g, c0):
            def run():
                dst, s = blocks(q_grp(g, c0, P), x[g][:, :, c0:c0 + P])
                V.tensor_tensor(out=dst, in0=bank["e", g, c0][:].rearrange("p t (c i) -> p c t i", i=4), in1=s, op=ALU.add)
            done = [("x", i, M - 1, c0 - c0 % H) if g else ("x", i, M - 1) for i in range(4 * g, 4 * g + 4)]
            return run, done + [("e", g, c0)], cols("q_grp", g, c0, P) + [("read", ("e", g, c0))]

        def divide(unit):
            g, t0, n, c0, w = unit
            i0 = 4 * g + t0

            def run():
                step = n if apart(i0, c0) == apart(i0 + 1, c0) else 1
                for a in range(0, n, step):
                    V.tensor_tensor(out=res[g][:, t0 + a:t0 + a + step, c0:c0 + w], in0=bank["c", unit][:, a:a + step], in1=inv(i0 + a, step, c0, w), op=ALU.mult)
            needs = [k for i in range(i0, i0 + n) for k in cols("inv", i, c0, w)]
            return run, [("c", unit)] + needs, [k for t in range(t0, t0 + n) for k in cols(("res", t), g, c0, w)] + [("read", ("c", unit))]

        def load_chi(t):
            at = CHI_AT + 4 * t
            return (lambda: SP.dma_start(out=slab[at:at + PIECES, t], in_=chi.partition_broadcast(PIECES))), [("st", t)], [("chi", t)]

        def store(unit):
            g, t0, n, c0, w = unit
            needs = [k for t in range(t0, t0 + n) for k in cols(("res", t), g, c0, w)]
            return (lambda: SP.dma_start(out=out0_v[g, :, t0:t0 + n, c0:c0 + w], in_=res[g][:, t0:t0 + n, c0:c0 + w])), needs, []

        def store_codes(g, c0, w):
            return (lambda: SP.dma_start(out=out1_v[g, :, c0:c0 + w], in_=r_codes[:, g, c0:c0 + w].bitcast(I32))), cols("r_q", g, c0, w), []

        def store_scales(k, eng):
            def run():
                eng.dma_start(out=out2_v[:, 4 * k:4 * k + 4, :], in_=r_sc[32 * k:32 * k + 8, :].bitcast(I32))
            return run, cols("r_q", 0, 0, G) + cols("r_q", 1, 0, G), []

        def emit(queues):
            have = set()
            turn = {ring: [] for ring in BANKS}
            for run, needs, gives in queues[0]:
                for k in [k for k in needs if k[0] == "bank"]:
                    needs.remove(k)
                    turn[k[1]].append(k[2])
                    needs.extend(("read", b) for b in turn[k[1]][-1 - BANKS[k[1]]:-BANKS[k[1]]])
            at = [0] * len(queues)
            while any(at[e] < len(queue) for e, queue in enumerate(queues)):
                before = sum(at)
                for e, queue in enumerate(queues):
                    while at[e] < len(queue) and all(k in have for k in queue[at[e]][1]):
                        queue[at[e]][0]()
                        for k in queue[at[e]][2]:
                            have.add(k)
                        at[e] = at[e] + 1
                assert sum(at) > before, [[k for k in queue[at[e]][1] if k not in have] for e, queue in enumerate(queues) if at[e] < len(queue)]

        def load_scat(m):
            SP.dma_start(out=scat_raw[m][:], in_=scat[m].rearrange("(p j) n -> p j n", j=4))

        def load_flux(b):
            SP.dma_start(out=flux_raw[b][:], in_=flux_v[b // 2, :, 2 * (b % 2):2 * (b % 2) + 2])

        V.memset(warm[:], 1.0)
        for t in (idle[:], slab[:, 0], rows[:], dens_pad[:], slab[:, 1:4], f_pad[:]):
            V.memset(t.bitcast(U32), 0)
        make_identity(nc, id32[:])
        S.dma_start(out=dens_sb[:], in_=dens.rearrange("(g p t) m -> p g (t m)", g=2, t=4))
        S.dma_start(out=slab[0:M, 0], in_=sigt)
        load_scat(0)
        load_flux(0)
        SP.dma_start(out=rows[NU_AT:NU_AT + M], in_=nusf)
        load_scat(1)
        load_flux(1)
        load_scat(2)
        load_flux(2)
        load_flux(3)
        load_scat(3)
        for t in range(1, 4):
            SP.dma_start(out=slab[4 * t:4 * t + M, t], in_=sigt)
        SP.dma_start(out=kern_raw[0][:], in_=kern_v[0])
        SP.dma_start(out=kern_raw[1][:], in_=kern_v[1])

        S.activation(out=warm[:, 1:2], in_=warm[:, 0:1], func=ACT.Abs_reciprocal_sqrt)
        V.tensor_copy(out=id16[:], in_=id32[:])
        V.tensor_copy(out=dens_pad[:, :, 0:4 * M], in_=dens_sb[:])
        V.tensor_copy(out=dens32[:], in_=dens_v)

        lo, hi = range(4), range(4, NT)
        quarters = range(0, G, P)
        units = [(g, 2 * h, 2, c0, H) for g in range(2) for c0 in (0, H) for h in range(2)]
        SCAT_PIECES = [[("a", 0, G)], [("b", 0, G)], [("c", 0, P), ("a", P, P), ("c", H, H)], [("b", 0, P), ("b", P, G - P)]]
        INV_IN = [("rest", 1, 1, 0, G), ("kern1", 4, 2, 0, G), ("kern3", 6, 2, 0, H)]

        qt = [warm_up(H), warm_up(H), t_pad("dens", dens_pad, "sa"), warm_up(P), t_flux(0), total(0, "sb"), t_nusf(), warm_up(H), fission(0, "sa"), t_flux(1), scatter(0, 0), scatter(1, 0), fission(1)]
        qt += [scatter(0, 1), scatter(1, 1), scatter(2, 0, "tp"), scatter(3, 0, "tp"), scatter(2, 1), scatter(3, 1), t_flux(2, "sb"), total(1, "mm"), t_flux(3), total(2, "tp"), fission(2)]
        qt += [scatter(0, 2), scatter(1, 2), scatter(4, 0, "sb"), scatter(2, 2), fission(3), scatter(3, 2), scatter(5, 0, "tp"), scatter(4, 1), scatter(5, 1), fission(4), fission(5), scatter(4, 2), total(3, "sb"), fission(6), fission(7)]
        qt += [scatter(3, 3), scatter(0, 3, "tp"), scatter(6, 0, "tp"), scatter(5, 2), scatter(7, 0, "sa"), scatter(6, 1), scatter(7, 1), scatter(1, 3, "tp"), scatter(2, 3, "sb"), scatter(6, 2), scatter(7, 2), total(4, "sa")]
        qt += [scatter_half(4, 3, 0), t_pad("f", f_pad, "tp", ["pieces"]), scatter_half(6, 3, 0), t_kern(0, "sb"), scatter_half(4, 3, H), emission(1, quarters[0], "mm"), t_kern(1), emission(1, quarters[1], "mm"), emission(0, quarters[0], "mm"), t_kern(2), total(5, "sa"), emission(0, quarters[1], "mm"), emission(0, quarters[2], "mm"), t_kern(3, "sb"), emission(0, quarters[3], "mm")]
        qt += [total(6, "tp"), t_kern(4), t_kern(5, "sa"), total(7, "sb"), scatter_half(6, 3, H), open_unit(units[0], "mm"), close_unit(units[0]), emission(1, quarters[2], "mm"), emission(1, quarters[3], "mm"), t_kern(6), open_unit(units[1], "mm"), close_unit(units[1]), t_kern(7)]
        qt += [open_unit(units[2], "mm"), open_unit(units[3], "mm"), close_unit(units[2]), close_unit(units[3])]
        for k, ring in zip((4, 5, 6, 7), ("mm", "mm", "sa", "sb")):
            qt += [open_unit(units[k], ring), close_unit(units[k])]

        qv = [weave_scat(0, 0, H, V), weave_scat(0, H, H, V), quant_scat(0, 0, H), quant_scat(0, H, H), weave_scat(1, 0, H, V), quant_flux(0), weave_scat(1, H, H, V)]
        qv += [quant_scat(1, 0, H), quant_scat(1, H, H), weave_scat(2, 0, P, V), quant_flux(1), weave_scat(2, P, P, V), quant_scat(2, 0, P)]
        qv += [weigh_add(i, 1) for i in lo]
        qv += [quant_scat(2, P, P), quant_scat(2, H, H), weave_scat(3, 0, P, V), quant_flux(2), quant_scat(3, 0, P)] + [weigh_add(i, 2) for i in lo] + [weigh_add(4, 1), weigh_add(5, 1)]
        qv += [quant_scat(3, P, G - P), quant_flux(3), weigh_add(4, 2), f_weigh(), weigh_add(3, 3, 0, H), f_sum(), f_first(), weigh_add(3, 3, H, H), f_less_first(), f_second(), signed(0, 1, 0, H, eng=V), f_third()]
        qv += [weigh_add(5, 2), weigh_add(6, 1), weigh_add(7, 1), weigh_add(6, 2), weigh_add(7, 2)] + [weigh_half(i, 3, 0) for i in hi] + [weigh_half(i, 3, H) for i in hi[:2]]
        qv += [source(1, c) for c in quarters[:2]] + [source(0, c) for c in quarters]
        qv += [quant_q(0, 0, H), quant_kern(0), quant_q(1, 0, H), quant_q(0, H, H), quant_kern(1)] + [weigh_half(i, 3, H) for i in hi[2:]]
        qv += [divide(units[0]), source(1, quarters[2]), source(1, quarters[3]), divide(units[1]), quant_q(1, H, H), quant_kern(2), quant_kern(3)]
        qv += [divide(u) for u in units[2:]] + [quant_res(0, 0, G)]
        qv += [weave_res(1, H + P, V), quant_res(1, 0, H), quant_res(1, H, H)]

        qs = [c_pad("dens", dens_t), c_flux(0), c_nusf(), root(0), sign(0), c_flux(1), weigh_first(0), weigh_first(1), weigh_first(2), weigh_first(3), square(0)]
        qs += [c_flux(2), root(1), c_flux(3), sign(1), square(1), weigh_first(4), weigh_first(5), root(2), sign(2), square(2), root(3), sign(3), weigh_aside(0, 3), weigh_first(6), weigh_first(7), weigh_aside(1, 3), weigh_aside(2, 3), square(3), c_pad("f", f_t)]
        qs += [root(4), sign(4), c_kern(0), square(4), c_kern(1), c_kern(2), root(5), sign(5), c_kern(3), square(5)] + inverse(6) + [c_kern(4), c_kern(5), root(7), sign(7), c_kern(6), c_kern(7), square(7), weave_res(0, 0, S), weave_res(0, P, S)]
        qs += [weave_res(0, H, S), weave_res(0, H + P, S)] + [weave_res(1, c, S) for c in quarters[:3]] + [store_scales(1, S), store_scales(3, S)]

        qg = [weave_scat(2, H, H, GP, cols("scat_q", 2, 0, P)), weave_scat(3, P, G - P, GP, cols("scat_q", 3, 0, P)), signed(0, 1, H, H), signed(1, after=["pieces"]), join(0, 1, 3), join(1, 2, 3), signed(2, 2)]
        qg += [signed(4, 2, after=[("kern_q", 1)]), signed(6, 2, 0, H, after=[("kern_q", 3)]), signed(6, 2, H, H)]

        qy = [load_chi(t) for t in range(4)] + [store(u) for u in units] + [store_codes(0, 0, G), store_codes(1, 0, H), store_codes(1, H, H)]
        qy += [store_scales(0, SP), store_scales(2, SP)]
        emit([qt, qv, qs, qg, qy])
